import numpy as np, ml_dtypes
CORES = [16,18,20,22]
N = 4
BF = ml_dtypes.bfloat16
def gentries(a):
    return np.ascontiguousarray(a.reshape(8, 16, -1).transpose(0, 2, 1)).reshape(8, -1)
def gtable(e):
    e = np.asarray(e); return np.ascontiguousarray(e.reshape(8, -1, 16).transpose(0, 2, 1)).reshape(128, -1).astype(np.int32)
W, LN, M, RO, C = 4096, 256, 16, 6, 16
PM = [1, 2]
TOP = M - RO
def mates():
    return np.arange(N)[:, None] ^ np.array(PM)[np.arange(LN) // (LN // len(PM))][None, :]
def hashed(l, s):
    s = s[..., None, :]
    return ((l * s >> 5) + l + 37 * np.arange(M)[:, None] + s) & (W - 1)
def noisy(rng, base, share):
    e = rng.integers(-1, 2, (N, 8, 16, W)) * ((rng.random((N, 8, 1, W)) < share) & (rng.random((N, 8, 16, W)) < rng.random((N, 8, 1, W))))
    return np.clip(base + e, 0, 15)
def parts(rng, lo):
    x = noisy(rng, rng.integers(0, 16, (1, 8, 16, W)), 0.015625)
    n = np.maximum(rng.integers(lo, TOP + 1, (1, 8, LN)) - rng.integers(0, 4, (N, 8, LN)) * (rng.random((N, 8, LN)) < 0.12), 0)
    cut = np.where(rng.random((N, 8, LN)) < 0.12, n - rng.integers(1, 6, (N, 8, LN)), M)
    l = np.where(np.arange(M)[:, None] >= cut[:, :, None, :], rng.integers(0, W, (N, 8, M, LN)), rng.integers(0, W, (1, 8, M, LN)))
    s = np.repeat(rng.integers(0, 4096, (1, 8, RO, LN)), N, 0); w = np.repeat(rng.integers(0, 4096, (1, 8, 16)), N, 0)
    q = rng.random((1, 8, LN)); k = np.where(q < 0.6, 1, np.where(q < 0.9, rng.integers(1, 9, (1, 8, LN)), rng.integers(1, 9, (N, 8, LN))))
    few = np.array([0, 0, 1, 2, 4, 8, 16, 40]); th = np.where(rng.random((1, 8, LN)) < 0.9, rng.choice(few, (1, 8, LN)), rng.choice(few, (N, 8, LN)))
    return x, l, s, n, k, th, w
def lists(a):
    return np.stack([gtable(v.reshape(8, -1)) for v in a])
def pack(x, l, s, n, k, th, w):
    return {"xt": np.ascontiguousarray(x.reshape(N, 128, W)).astype(np.float32).astype(BF), "tr": lists(l), "sd": lists(s), "n0": lists(n), "k0": lists(k), "th": lists(th),
            "wt": np.ascontiguousarray(w.reshape(N, 128, 1)).astype(np.int32)}
def setup_inputs(rng):
    return pack(*parts(rng, max(TOP - 4, 1)))
def setup_inputs_spread(rng):
    x, l, s, n, k, th, w = parts(rng, 0)
    x = noisy(rng, np.floor(np.exp2(4 * rng.random((1, 8, 1, W))) * rng.random((1, 8, 16, W))).astype(np.int64), 0.03)
    l = l * l * l // (W * W); s = s * s // 4096; w = w * w // 4096
    th = np.repeat(np.clip(np.exp2(8.01 * rng.random((1, 8, LN))).astype(np.int64) - 1, 0, 255), N, 0)
    return pack(x, l, s, n, k, th, w)
def setup_inputs_ends(rng):
    par = np.array([bin(r).count("1") & 1 for r in range(N)])
    def two(p, *sh):
        return np.repeat((rng.random((1,) + sh) < p).astype(np.int64), N, 0)
    x = 15 * two(0.5, 8, 16, W); x = np.where(rng.random((N, 8, 1, W)) < 0.01, 15 - x, x)
    l = (W - 1) * two(0.5, 8, M, LN); l = np.where(rng.random(l.shape) < 0.01, W - 1 - l, l)
    s = 4095 * two(0.5, 8, RO, LN); w = 4095 * two(0.5, 8, 16)
    n = TOP * two(0.8, 8, LN); n = np.where(rng.random(n.shape) < 0.04, TOP - n, n)
    k = 1 + 7 * two(0.3, 8, LN); k = np.where(rng.random(k.shape) < 0.05, 9 - k, k)
    th = 255 * two(0.5, 8, LN); th = np.where(rng.random(th.shape) < 0.05, 255 - th, th)
    big = np.array([5, LN - 2, LN - 1])
    x[:, 7] = 15; w[:, 7] = 4095; n[:, 7] = TOP; k[:, 7] = 1 + 7 * par[:, None]; l[:, 7] = l[0, 7].copy()
    k7 = k[:, 7]; k7[:, big] = 1; s7 = s[:, 7]; s7[:, :, big] = 0
    k7[:, 9] = 1; l[:, 7, :, 9] = W - 1; s7[:, :, 9] = 0; s7[:, RO - 1, 9] = 4095; th[:, 7, 9] = 0
    z = (((W - 1) * 4095 >> 5) + W - 1 + 4095) & (W - 1); x7 = x[:, 7]; x7[par == 1, :, z] = 0
    x[:, 6] = 15 * par[:, None, None]; n[:, 6, LN - 1] = TOP
    x[:, 5] = x[0, 5].copy(); l[:, 5] = l[0, 5].copy()
    for r in range(N):
        y = x[r, 5]; y[15, 0] = 0; y[15, 37] = 0; y[3, 0] = 0; y[3, 74] = 0
        if par[r]:
            y[:, 0] = 15 - y[:, 0]; y[15, 37] = 15; y[3, 74] = 15
    for i in (4, LN - 1):
        n[:, 5, i] = TOP; k[:, 5, i] = 1; th[:, 5, i] = 255; s[:, 5, 0, i] = 0; l[:, 5, 0, i] = 0; l[:, 5, 1, i] = 0; l[:, 5, 2, i] = 0 if i == 4 else W - 1
    def alone(g, cols):
        own = cols // C; kg = k[:, g]; kg[:, own] = 1 + 7 * par[:, None]; i = int(np.setdiff1d(np.arange(LN), own)[-1])
        n[:, g, i] = TOP; k[:, g, i] = 1; l[:, g, :, i] = 0; s[:, g, :, i] = 0
        return i
    e0 = 37 * np.arange(M); e1 = (e0 - 1) & (W - 1); i = alone(4, np.concatenate([e0, e1])); y = x[:, 4]
    y[:, :, e0] = y[:1, :, e0]; y[:, :, e1] = y[:1, :, e1]; y[:, 15, e1] = 15 * par[:, None]
    w[:, 4] = 0; s[:, 4, RO - 1, i] = 4095; th[:, 4, i] = 120
    z = np.arange(65520, 0, -1); v = 15 * (M - 1) * z; ws = int(z[((v & 4095) == 4095) & ((v >> 12 & 1) == 1)][0])
    u = (15 * ws * np.arange(M)) & 4095; e0 = (np.where(np.arange(M) < TOP, 0, (u * u >> 5) + 37 * u) + 37 * np.arange(M)) & (W - 1)
    alone(3, e0); y = x[:, 3]; y[:, :, e0] = 15; w[:, 3] = np.clip(ws - 4095 * np.arange(16), 0, 4095)
    return pack(x, l, s, n, k, th, w)
def setup_inputs_corners(rng):
    x, l, s, n, k, th, w = parts(rng, 1)
    jj = np.arange(M)[:, None]; own = rng.integers(0, W, (N, 8, M, LN))
    kk = np.array([1, 1, 1, 2, 3, 4, 7, 8])
    n[:, 0] = 0; k[:, 0] = np.where(rng.random((1, LN)) < 0.7, rng.choice(kk, (1, LN)), rng.choice(kk, (N, LN)))
    x[:, 1] = x[0, 1].copy(); l[:, 1] = l[0, 1].copy(); n[:, 1] = TOP; k[:, 1] = 1; th[:, 1] = 0
    if W == 4096:
        l[:, 1, 0, ::4] = 4095; s[:, 1, :, ::4] = 4065
        l[:, 1, 0, 1::4] = 4093; s[:, 1, :, 1::4] = 4075
    x[:, 2] = x[0, 2].copy(); n[:, 2] = TOP; k[:, 2] = 8; th[:, 2] = 0; l[:, 2] = np.where(jj == TOP - 1, own[:, 2], l[0, 2].copy())
    x[:, 3] = x[0, 3].copy(); k[:, 3] = 6; th[:, 3] = 0; n[:, 3] = rng.integers(4, TOP + 1, (1, LN))
    cut = n[:, 3] - rng.integers(0, 5, (N, LN)); l[:, 3] = np.where(jj >= cut[:, None, :], own[:, 3], l[0, 3].copy())
    s[:, 4] = rng.integers(0, 4096, (N, RO, LN)); w[:, 4] = rng.integers(0, 4096, (N, 16)); k[:, 4] = rng.integers(1, 9, (N, LN)); th[:, 4] = rng.choice(np.array([0, 60, 255]), (N, LN))
    n[:, 5] = rng.choice(np.array([0, 1, TOP]), (N, LN)); n[:, 5, :LN // 2] = rng.choice(np.array([0, 1, TOP]), (1, LN // 2))
    n[:, 6] = n[0, 6].copy(); k[:, 6] = 1
    ix = hashed(l[:, 6], s[:, 6, 0]); v = np.take_along_axis(x[:, 6], ix.reshape(N, 1, -1), 2).reshape(N, 16, M, LN)
    p = np.add.reduce(np.where(jj < n[:, 6][:, None, None, :], v, 0), axis=2)
    d = np.add.reduce(np.abs(p - np.take_along_axis(p, mates()[:, None, :], 0)), axis=1)
    th[:, 6] = np.clip(d + rng.integers(-1, 2, d.shape), 0, 255)
    return pack(x, l, s, n, k, th, w)
def setup_inputs_crowd(rng):
    x, l, s, n, k, th, w = parts(rng, 1)
    par = np.array([bin(r).count("1") & 1 for r in range(N)]); jj = np.arange(M)[:, None]
    x = np.repeat(x[:1], N, 0); l = np.repeat(l[:1], N, 0); nb = rng.integers(1, TOP, (1, 8, LN))
    l[:, 2] = l[:, 2, :, :1].copy(); s[:, 2] = s[:, 2, :, :1].copy(); nb[:, 2] = nb[:, 2, :1].copy()
    l[:, 4, :, :LN - 1] = l[:, 4, :, :1].copy(); s[:, 4, :, :LN - 1] = s[:, 4, :, :1].copy()
    nb[:, 3] = rng.integers(3, min(TOP, 7), (1, LN))
    hit = hashed(l[0, 3], s[0, 3, 0])[:, :LN - 2][jj <= nb[0, 3, :LN - 2][None, :]]; left = np.setdiff1d(np.arange(W), hit)
    c0 = int(rng.choice(left)); c1 = int(rng.choice(left[((left - c0) % W > 128) & ((c0 - left) % W > 128)]))
    for i, c in ((LN - 1, c0), (LN - 2, c1)):
        l[:, 3, :, i] = (c - 37 * np.arange(M)) & (W - 1); s[:, 3, 0, i] = 1; s[:, 3, 1, i] = 0; nb[:, 3, i] = 3
    n = nb + par[:, None, None]; k = np.ones((N, 8, LN), np.int64); th = np.zeros((N, 8, LN), np.int64)
    for r in (0, PM[-1]):
        k[r, 7, LN - 1] = 2; th[r, 7, LN - 1] = 255
    ix = hashed(l[0], s[0, :, 0]); live = jj <= nb[0][:, None, :]
    used = np.zeros((8, W), bool); np.put_along_axis(used, np.where(live, ix, ix[:, :1]).reshape(8, -1), True, 1)
    e = rng.integers(-1, 2, x.shape) * ((rng.random((N, 8, 1, W)) < 0.04) & (rng.random(x.shape) < 0.2) & ~used[None, :, None, :])
    x = np.clip(x + e, 0, 15)
    z = hashed(l[0, 7], s[0, 7, 1])[:, LN - 1]; x7 = x[:, 7]; x7[:, :, z] = x7[:1, :, z]; x7[:, :, int(z[nb[0, 7, LN - 1]])] = 0
    y = np.where(par[:, None, None] == 1, rng.integers(5, 10, (N, 16, W)), rng.integers(0, 4, (N, 16, W)))
    x[:, 3] = np.where(used[3], x[:, 3], y)
    for c, g in ((c0, 87), (c1, 90)):
        x[:, 3, :, c] = x[0, 3, :, c].copy(); x[:, 3, :8, c] = par[:, None] * ((g + np.arange(8)) >> 3)
    ix = hashed(l[:, 3], s[:, 3, 1]); v = np.take_along_axis(x[:, 3], ix.reshape(N, 1, -1), 2).reshape(N, 16, M, LN)
    p = np.add.reduce(np.where(jj < nb[0, 3][None, :], v, 0), axis=2)
    d = np.add.reduce(np.abs(p - np.take_along_axis(p, mates()[:, None, :], 0)), axis=1)
    for r in (0, PM[-1]):
        th[r, 3] = np.clip(d[r] - 15 + rng.integers(-1, 2, LN), 0, 255)
        th[r, 3, LN - 1] = 245; th[r, 3, LN - 2] = 255
    return pack(x, l, s, n, k, th, w)
def setup_inputs_few(rng):
    x, l, s, n, k, th, w = parts(rng, 1)
    par = np.array([bin(r).count("1") & 1 for r in range(N)]); h = LN // 2
    x = np.repeat(x[:1], N, 0); l = np.repeat(l[:1], N, 0); n = np.repeat(n[:1], N, 0); k = np.repeat(k[:1], N, 0)
    n[:, 3:] = rng.integers(1, min(TOP, 15), (1, 5, LN)) + par[:, None, None]; k[:, 3:] = 8
    D = rng.integers(1, 17, (4, 1, 1)); e = (np.argsort(rng.random((4, 16, W)), axis=1) < D).astype(np.int64)
    x[:, 3:7] = np.minimum(x[:, 3:7], 14) + e[None] * par[:, None, None, None]
    l[:, 3:7, :, h:] = rng.integers(0, W // 8, (1, 4, M, LN - h)); s[:, 3:7, :, h:] = rng.integers(0, 32, (1, 4, RO, LN - h))
    m = rng.integers(5, 7, (4, LN - h)); n[:, 3:7, h:] = m
    z = np.stack([rng.permutation(LN - h) % 10 for g in range(4)])
    th[:, 3:7, h:] = np.where(par[:, None, None] == z // 5, m * D[:, :, 0] - z % 5, 0)
    ty = rng.permutation(N) % 4; o = rng.permutation(h)
    for r in range(N):
        for j in range(int(ty[r])):
            n[r, 7 - j, o[r]] = 0; k[r, 7 - j, o[r]] = (1, 6, 5)[j]
    return pack(x, l, s, n, k, th, w)
def check_inputs(d):
    bad = []
    for a, lo, hi in (("xt", 0, 15), ("tr", 0, W - 1), ("sd", 0, 4095), ("n0", 0, TOP), ("k0", 1, 8), ("th", 0, 255), ("wt", 0, 4095)):
        v = np.asarray(d[a]).astype(np.float64)
        if not (np.all(v >= lo) and np.all(v <= hi)): bad.append("range of " + a)
        elif np.any(v != np.floor(v)): bad.append("whole numbers in " + a)
    return bad
def reference(xt, tr, sd, n0, k0, th, wt):
    X = xt.astype(np.float32).astype(np.int32).reshape(N, 8, 16, W); wv = wt.astype(np.int64).reshape(N, 8, 16, 1)
    L = np.stack([gentries(a) for a in tr]).astype(np.int64).reshape(N, 8, M, LN)
    S = np.stack([gentries(a) for a in sd]).astype(np.int64).reshape(N, 8, RO, LN)
    n = np.stack([gentries(a) for a in n0]).astype(np.int64); k = np.stack([gentries(a) for a in k0]).astype(np.int64)
    t0 = np.stack([gentries(a) for a in th]).astype(np.int64)
    v1 = np.zeros((N, 8, LN), np.int64); v2 = np.zeros((N, 8, LN), np.int64); A = np.zeros((N, 1, 1), np.int64)
    mate = mates(); jj = np.arange(M)[:, None]; ii = np.arange(LN)
    def other(a):
        return np.take_along_axis(a, mate.reshape((N,) + (1,) * (a.ndim - 2) + (LN,)), 0)
    for rnd in range(RO):
        ix = hashed(L, S[:, :, rnd])
        V = np.take_along_axis(X, ix.reshape(N, 8, 1, M * LN), 3).reshape(N, 8, 16, M, LN)
        R = np.concatenate([np.zeros((N, 8, 16, 1, LN), np.int32), np.add.accumulate(V, axis=3, dtype=np.int32)], axis=3)
        K = np.where(k >= 8, 8, np.where(k >= 4, 4, np.where(k >= 2, 2, 1)))
        m1 = n - (n & (K - 1)); m2 = np.maximum(m1 - K, 0)
        Pn, P1, P2 = [np.take_along_axis(R, m[:, :, None, None, :], 3)[:, :, :, 0] for m in (n, m1, m2)]
        lim = t0 + (A & 15)
        def agree(a, la, b, lb):
            return (la == lb) & (np.add.reduce(np.abs(a - b), axis=2) <= lim)
        Q1, q1, Q2, q2 = other(P1), other(m1), other(P2), other(m2)
        ok = agree(Pn, n, other(Pn), other(n)) & (k == other(k))
        a1 = agree(P1, m1, Q1, q1) | agree(P1, m1, Q2, q2)
        a2 = agree(P2, m2, Q1, q1) | agree(P2, m2, Q2, q2)
        u = np.add.reduce(wv * Pn, axis=2) & 4095; new = ((u * u >> 5) + 37 * u) & (W - 1)
        L = np.where((jj == n[:, :, None, :]) & ok[:, :, None, :], new[:, :, None, :], L)
        col = (C * ii + (u & (C - 1)))[:, :, None, :]
        np.put_along_axis(X, col, np.where(ok[:, :, None, :], Pn >> 4, np.take_along_axis(X, col, 3)).astype(np.int32), 3)
        c1 = v1 + a1; c2 = v2 + a2; full = ~ok & (k + 1 == 2 * K)
        b1 = full & (2 * c1 >= K); b2 = full & ~b1 & (2 * c2 >= K)
        n = np.where(ok, n + 1, np.where(b1, m1, np.where(b2, m2, n)))
        k = np.where(ok | b1 | b2, 1, k + 1)
        v1 = np.where(ok | full, 0, c1); v2 = np.where(ok | full, 0, c2)
        A = np.add.reduce((b1 | b2).astype(np.int64), axis=(1, 2), keepdims=True)
    st = np.stack([n, k, v1, v2], axis=2)
    return {"yt": lists(L).astype(np.float32), "yst": lists(st).astype(np.float32), "yx": np.ascontiguousarray(X.reshape(N, 128, W)).astype(np.float32).astype(BF)}

@@ -1,0 +1,659 @@
+from concourse.bass import DstId, RemoteDMATransfer
+from concourse.mybir import AluOpType as A, ActivationFunctionType as F
+import comms_topo
+
+RO = 6
+SL = [10, 10, 11, 12, 13, 14]
+LS = [s + 1 for s in SL]
+LSU = sorted(set(LS))
+VOFF = {}
+_o = 0
+for _l in LSU:
+    VOFF[_l] = _o
+    _o += 256 * _l
+VTOT = _o
+RW = 1920
+TB = 4096
+MULTI = True
+GP, TN = 0, 0
+NV0 = [3, 3, 4, 4, 5, 5]
+NV1 = [5, 3, 3, 4, 4, 5]
+KA, UA, UB, PRE = 3, 3, 5, 1
+MAGIC = 12582912.0
+
+f32, bf, i32, u16 = "float32", "bfloat16", "int32", "uint16"
+SCRATCH = {
+    "X": ("sbuf", [128, 12288], bf), "V": ("sbuf", [128, VTOT], bf), "ZR": ("sbuf", [128, RW], bf),
+    "AH": ("sbuf", [128, 2, 24], f32), "C": ("sbuf", [128, 2, 16], f32), "NF": ("sbuf", [128, 2, 16], f32),
+    "MR": ("sbuf", [128, 2, 16], f32), "D0F": ("sbuf", [128, 768], f32), "wj": ("sbuf", [128, 4], i32),
+    "RP0": ("sbuf", [128, RW + 384], bf), "RP1": ("sbuf", [128, RW + 384], bf),
+    "Q": ("sbuf", [128, 2 * RO * 384], bf), "DA": ("sbuf", [128, 768], bf),
+    "VN": ("sbuf", [128, 256], bf), "VT": ("sbuf", [128, 256], bf), "VAL": ("sbuf", [128, 256], bf),
+    "tri": ("sbuf", [128, 256], i32), "sdi": ("sbuf", [128, 96], i32), "ni": ("sbuf", [128, 16], i32),
+    "ki": ("sbuf", [128, 16], i32), "thi": ("sbuf", [128, 16], i32), "wi": ("sbuf", [128, 4], i32),
+    "TP": ("sbuf", [128, 256], f32), "S32": ("sbuf", [128, 96], f32), "B0": ("sbuf", [128, 96], f32),
+    "I96": ("sbuf", [128, 96], i32), "I96b": ("sbuf", [128, 96], i32),
+    "J128": ("sbuf", [128, 256], f32), "J1184": ("sbuf", [128, 256], f32),
+    "D0T": ("sbuf", [128, 1024], f32), "D1T": ("sbuf", [128, 6 * 1024], f32), "OT": ("sbuf", [128, 1024], f32),
+    "NI": ("sbuf", [128, 256], i32), "NJ": ("sbuf", [128, 256], i32), "N1": ("sbuf", [128, 256], f32), "N2": ("sbuf", [128, 256], f32),
+    "CT": ("sbuf", [128, 512], u16), "BC": ("sbuf", [128, 16], u16), "BC4": ("sbuf", [128, 8], u16),
+    "OFU": ("sbuf", [128, 2, 24], u16), "OAU": ("sbuf", [128, 16], u16), "SOU": ("sbuf", [128, 16], u16), "VOU": ("sbuf", [128, 16], u16),
+    "M": ("sbuf", [128, 2, 32], f32), "PM": ("sbuf", [128, 2 * RO, 24], f32), "E": ("sbuf", [128, 2, 40], f32),
+    "LIM": ("sbuf", [128, 2, 32], f32), "LP": ("sbuf", [128, 2, 32], f32), "TH4": ("sbuf", [128, 2, 32], f32),
+    "OF": ("sbuf", [128, 2, 24], f32), "BASE": ("sbuf", [128, 2 * len(LSU), 24], f32), "PNP": ("sbuf", [128, 32 * (RO + 1)], f32),
+    "D0": ("sbuf", [128, 64], f32), "D1": ("sbuf", [128, 64], f32), "D1R": ("sbuf", [128, 64], f32),
+    "ON": ("sbuf", [128, 64], f32), "NR": ("sbuf", [128, 64], f32),
+    "RES": ("sbuf", [128, 112], f32), "CAND": ("sbuf", [128, 112], f32),
+    "W": ("sbuf", [128, 16 * 48], f32), "WI": ("sbuf", [128, 16 * 16], i32),
+    "SIG": ("sbuf", [128, 32], f32), "NP": ("sbuf", [128, 32], f32),
+    "PI": ("sbuf", [128, 16], i32), "PC": ("sbuf", [128, 16], f32), "XR": ("sbuf", [128, 144], f32),
+    "Z": ("sbuf", [128, 144], bf), "ZW": ("sbuf", [128, 144], "float16"),
+    "ID": ("sbuf", [128, 128], bf), "NID": ("sbuf", [128, 128], bf),
+    "ONE": ("sbuf", [128, 128], f32), "NONE": ("sbuf", [128, 128], f32),
+    "YT": ("sbuf", [128, 256], f32), "YS": ("sbuf", [128, 4, 16], f32),
+    "pU": ("psum", [128, 512], f32), "pN0": ("psum", [128, 512], f32), "pN1": ("psum", [128, 512], f32),
+    "pD0n": ("psum", [128, 512], f32), "pD1n": ("psum", [128, 512], f32),
+    "pD0v": ("psum", [128, 512], f32), "pD1v": ("psum", [128, 512], f32), "pS": ("psum", [128, 32, 16], f32),
+}
+SEMAPHORES = (["cV", "cS", "cP", "cG"] + ["ld%d" % i for i in range(8)] + ["st%d" % i for i in range(4)]
+              + ["ml%d" % t for t in range(RO)] + ["ma%d" % t for t in range(RO)]
+              + ["dl%d" % i for i in range(4 * RO)] + ["da%d" % i for i in range(4 * RO)])
+
+
+def rank_program(g, core, T, topo):
+    rank = T.rank_of(core)
+    if rank is None:
+        return
+    Q = {"V": g.vector, "S": g.scalar, "P": g.tensor, "G": g, "Y": g.sync}
+    CS = {"V": "cV", "S": "cS", "P": "cP", "G": "cG"}
+    cnt = {}
+    know = {e: {} for e in Q}
+    snap = {}
+    lastw, readers = {}, {}
+
+    def need(e, tok):
+        s, c = tok
+        if know[e].get(s, 0) >= c:
+            return
+        Q[e].wait_ge(T.sem[s], c)
+        know[e][s] = c
+        for s2, c2 in snap.get(tok, {}).items():
+            if know[e].get(s2, 0) < c2:
+                know[e][s2] = c2
+
+    def op(e, fn, rd, wr, sem=None, inc=1, auto=False, after=()):
+        deps = list(after)
+        for k in rd:
+            if k in lastw:
+                deps.append(lastw[k])
+            if k[0] == "p":
+                deps += [x for x in readers.get(k, []) if x[0] != CS.get(e)]
+        for k in wr:
+            if k in lastw:
+                deps.append(lastw[k])
+            deps += readers.get(k, [])
+        best = {}
+        for s, c in deps:
+            if e == "P" and s == "cP":
+                continue
+            best[s] = max(best.get(s, 0), c)
+        for s, c in best.items():
+            need(e, (s, c))
+        s = sem or CS[e]
+        ins = fn()
+        if not auto:
+            ins.then_inc(T.sem[s], inc)
+        cnt[s] = cnt.get(s, 0) + inc
+        tok = (s, cnt[s])
+        snap[tok] = dict(know[e])
+        for k in rd:
+            readers.setdefault(k, []).append(tok)
+        for k in wr:
+            lastw[k] = tok
+            readers[k] = []
+        return tok
+
+    def qv(name, q=0, n=1):
+        return ("%s.%d" % (name, q), lambda h: T[name][:, 16 * q:16 * (q + n)] if h is None else T[name][:, 16 * q + 8 * h:16 * q + 8 * h + 8], 0,
+                ["%s.%d" % (name, q + x) for x in range(n)])
+
+    def iv(name, s):
+        return (None, lambda h: T[name][:, s::4] if h is None else T[name][:, 32 * h + s:32 * h + 32:4], 0, ["%s.%d" % (name, s)])
+
+    def hv(name, q, n=1, r=0):
+        return (None, lambda h: T[name][:, r:r + 2, 8 * q:8 * (q + n)] if h is None else T[name][:, r + h, 8 * q:8 * (q + n)], 1,
+                ["%s.%d.%d" % (name, r, q + x) for x in range(n)])
+
+    def halves(vs, h):
+        if h is not None:
+            return [h]
+        kinds = set(v[2] for v in vs)
+        return [None] if (MULTI or len(kinds) == 1) else [1, 0]
+
+    def tt(o, a, b, alu, h=None, extra=()):
+        for x in halves([o, a, b], h):
+            op("V", lambda: g.vector.tensor_tensor(o[1](x), a[1](x), b[1](x), alu), a[3] + b[3] + list(extra), o[3])
+
+    def ts(o, a, s1, op0, s2=None, op1=None, h=None, extra=()):
+        for x in halves([o, a], h):
+            if op1 is None:
+                op("V", lambda: g.vector.tensor_scalar(o[1](x), a[1](x), s1, None, op0), a[3] + list(extra), o[3])
+            else:
+                op("V", lambda: g.vector.tensor_scalar(o[1](x), a[1](x), s1, s2, op0, op1), a[3] + list(extra), o[3])
+
+    def cp(o, a, h=None):
+        for x in halves([o, a], h):
+            op("V", lambda: g.vector.tensor_copy(o[1](x), a[1](x)), a[3], o[3])
+
+    def aff(o, a, scale=1.0, bias=0.0, h=None, extra=()):
+        for x in halves([o, a], h):
+            op("S", lambda: g.scalar.activation(o[1](x), a[1](x), F.Identity, bias=bias, scale=scale), a[3] + list(extra), o[3])
+
+    def raw(ap, *keys):
+        return (None, lambda h: ap, 0, list(keys))
+
+    def memset(ap, c, *keys):
+        op("V", lambda: g.vector.memset(ap, c), [], list(keys))
+
+    def iota(ap, pat, base, cm, key, fl=True):
+        if fl:
+            op("G", lambda: g.iota(ap, pat, base, cm, allow_small_or_imprecise_dtypes=True), [], [key])
+        else:
+            op("G", lambda: g.iota(ap, pat, base, cm), [], [key])
+
+    def dma(e, out, in_, sem, rd, wr):
+        return op(e, lambda: Q[e].dma_start(out, in_), rd, wr, sem=sem, inc=16)
+
+    Wn = {}
+
+    def w(name, n=1):
+        if name not in Wn:
+            Wn[name] = sum(v[1] for v in Wn.values()), n
+        return qv("W", Wn[name][0], n)
+
+    def wq(name, q):
+        return qv("W", Wn[name][0] + q, 1)
+
+    WIn = {}
+
+    def wi(name):
+        WIn.setdefault(name, len(WIn))
+        return qv("WI", WIn[name])
+
+    part = [T.cores[rank ^ 1], T.cores[rank ^ 2]]
+    RP = [T.RP0, T.RP1]
+    XK = ["X.0", "X.1"]
+    nn, nok = iv("ON", 3), iv("D0", 3)
+
+    def send_meta(t):
+        trs = []
+        tot = 0
+        for h in (0, 1):
+            rid, pid, _ = topo.addr(part[h])
+            en = topo.engines(core, part[h])
+            en = en[:len(en) // 2] if h == 0 else en[len(en) // 2:]
+            tot += len(en)
+            trs.append(RemoteDMATransfer(dst_ids=[DstId(rid=rid, pnc=pid)], dma_engine_mask=sum(1 << x for x in en),
+                                         remote_sem=T.sem["ma%d" % t], src=T.M[:, h, 0:24], dst=T.PM[:, 2 * t + h, :]))
+        op("G", lambda: g.remote_dma_fused(trs, local_sem=T.sem["ml%d" % t]), hv("M", 0, 3)[3], [], sem="ml%d" % t, inc=tot, auto=True)
+        for k in hv("PM", 0, 3, 2 * t)[3]:
+            lastw[k] = ("ma%d" % t, tot)
+        cnt["ma%d" % t] = tot
+
+    def send_data(t, h, p):
+        rid, pid, _ = topo.addr(part[h])
+        ne = len(topo.engines(core, part[h]))
+        i = 4 * t + (2 if p == "v" else 0) + h
+        a, b = (0 if "n" in p else 128), (384 if "v" in p else 128)
+        o = (2 * t + h) * 384
+        op("G", lambda: g.remote_dma(T.Q[:, o + a:o + b], RP[h][:, RW + a:RW + b], T.sem["da%d" % i], T.sem["dl%d" % i],
+                                     pid, rid, topo.mask(core, part[h])),
+           (["Pn%d" % h] if "n" in p else []) + (["PA%d" % h, "PB%d" % h] if "v" in p else []), [], sem="dl%d" % i, inc=ne, auto=True)
+        for x in p:
+            lastw["Q%d%d%s" % (t, h, x)] = ("da%d" % i, ne)
+        cnt["da%d" % i] = ne
+
+    dma("S", T.sdi[:], T.sd[:], "ld2", [], ["sdi"])
+    dma("Y", T.ki[:], T.k0[:], "ld1", [], ["ki.0"])
+    dma("S", T.ni[:], T.n0[:], "ld0", [], ["ni.0"])
+    dma("Y", T.tri[:], T.tr[:], "ld3", [], ["tri"])
+    dma("Y", T.X[:, TB:TB + 4096], T.xt[:], "ld4", [], XK)
+    dma("Y", T.wi[:, 0:1], T.wt[:], "ld6", [], ["wi0"])
+    dma("Y", T.thi[:], T.th[:], "ld5", [], ["thi.0"])
+
+    iota(T.PI[:], [[0, 16]], 0, 1, "PI.0", fl=False)
+    iota(T.PC[:], [[0, 2], [16, 8]], 0, 0, "PC.0")
+    iota(T.XR[:], [[1, 144]], 0, 0, "XR")
+    iota(T.J1184[:], [[1184, 16], [0, 16]], 0, 0, "J1184")
+    iota(T.J128[:], [[64, 16], [0, 16]], 16, 0, "J128")
+
+    tw = lambda t: 16 * (10 + t)
+    st = lambda t: 4 if t <= 4 else 3
+    w("col", 1)
+    c0 = 16 * Wn["col"][0]
+    memset(T.V[:, VOFF[LSU[0]]:VOFF[LSU[0]] + 256 * LSU[0]:LSU[0]], -256.0, "Vz%d" % LSU[0])
+    memset(T.X[:, TB - 16:TB], 0.0, "Xz")
+    memset(T.D0[:, 0::4], 0.0, "D0.0")
+    ts(wi("a"), qv("PI"), 15, A.bitwise_and)
+    ts(wi("a8"), qv("PI"), 7, A.bitwise_and)
+    ts(raw(T.wj[:, 0:1], "wj0"), raw(T.PI[:, 0:1], "PI.0"), 112, A.bitwise_and)
+    cp(raw(T.W[:, c0:c0 + 1], "c0"), raw(T.PI[:, 0:1], "PI.0"))
+    tt(w("li"), qv("PC"), wi("a"), A.add)
+    cp(qv("BC"), wi("a"))
+    ts(raw(T.W[:, c0 + 1:c0 + 2], "c1"), raw(T.wj[:, 0:1], "wj0"), 15.0, A.add)
+    memset(T.ZR[:], 0.0, "ZR")
+    memset(T.D0[:, 3::4], 1.0, "D0.3")
+    memset(T.D1R[:], 0.0, "D1R.0", "D1R.1", "D1R.2", "D1R.3")
+    memset(T.RES[:, 80:112], 0.0, "RES.5", "RES.6")
+    ts(raw(T.ID[:], "ID"), raw(T.XR[:, :128], "XR"), T.W[:, c0:c0 + 1], A.is_equal, extra=["c0"])
+    ts(raw(T.NID[:], "NID"), raw(T.XR[:, :128], "XR"), T.W[:, c0:c0 + 1], A.is_equal, -1.0, A.mult, extra=["c0"])
+    ts(raw(T.Z[:], "Z"), raw(T.XR[:], "XR"), T.W[:, c0 + 1:c0 + 2], A.is_equal, extra=["c1"])
+    memset(T.D1R[:, 0::4], 1.0, "D1R.0")
+    for li_, l in enumerate(LSU):
+        for q in range(3):
+            aff(hv("BASE", q, 1, 2 * li_), w("li"), float(l), -1.0 if q == 2 else 0.0)
+    for t in range(1, RO):
+        aff(qv("PNP", 2 * t + 1), w("li"), 1.0, 128.0 * LS[t] - 16.0)
+    aff(w("ci"), w("li"), 16.0, 4096.0, h=0)
+    aff(w("ci"), w("li"), 16.0, h=1)
+
+    def mid_constants():
+        for l in LSU[1:]:
+            memset(T.V[:, VOFF[l]:VOFF[l] + 256 * l:l], -256.0, "Vz%d" % l)
+
+    def late_constants():
+        memset(T.ONE[:], 1.0, "ONE")
+        memset(T.NONE[:], -1.0, "NONE")
+        memset(T.D0T[:, 0:4 * tw(4):4], 0.0, "D0T.0")
+        memset(T.D0T[:, 1:4 * tw(4):4], 1.0, "D0T.1")
+        memset(T.D0F[:, 0::3], 0.0, "D0F.0")
+        memset(T.D0F[:, 1::3], 1.0, "D0F.1")
+        a0, a8 = 16 * WIn["a"], 16 * WIn["a8"]
+        ts(raw(T.BC4[:, 0:5], "BC4"), raw(T.WI[:, a0:a0 + 5], *wi("a")[3]), 4.0, A.mult, 3.0, A.add)
+        ts(raw(T.BC4[:, 5:6], "BC5"), raw(T.WI[:, a8:a8 + 1], *wi("a8")[3]), 4.0, A.mult, 3.0, A.add)
+        ts(raw(T.BC4[:, 6:7], "BC6"), raw(T.WI[:, a8:a8 + 1], *wi("a8")[3]), 4.0, A.mult, 35.0, A.add)
+
+    def bc(name, col, L, *keys):
+        return raw(T[name][:, col:col + 16].indirect(T.BC[:, 0:L]), "BC.0", *keys)
+
+    def finish_c(t):
+        n = 16 * SL[t]
+        return [lambda: ts(raw(T.NJ[:, :n], "NJ"), raw(T.NI[:, :n], "NI"), 5, A.arith_shift_right, 4095, A.bitwise_and),
+                lambda: cp(raw(T.CT[:, 256 * (t % 2):256 * (t % 2) + n], "CT%d" % (t % 2)), raw(T.NJ[:, :n], "NJ"))]
+
+    def first_c(t):
+        n = 16 * SL[t]
+        return [
+            lambda: tt(raw(T.N2[:, :n], "N2"), bc("B0", 16 * t, SL[t], "B0"), raw(T.J1184[:, :n], "J1184"), A.add),
+            lambda: tt(raw(T.N1[:, :n], "N1"), bc("S32", 16 * t, SL[t], "S32"), raw(T.TP[:, :n], "TP"), A.mult),
+            lambda: tt(raw(T.NI[:, :n], "NI"), raw(T.N1[:, :n], "N1"), raw(T.N2[:, :n], "N2"), A.add),
+        ] + finish_c(t)
+
+    def weave(*lists):
+        lists = [list(x) for x in lists]
+        while any(lists):
+            for x in lists:
+                if x:
+                    x.pop(0)()
+
+    def t_seed(t):
+        n = tw(t)
+        op("S", lambda: g.scalar.activation(T.D0T[:, 3:4 * n:4], T.S32[:, 16 * (t + 1):16 * (t + 2)].indirect(T.BC[:, 0:n // 16]), F.Copy),
+           ["S32", "BC.0"], ["D0T.3"])
+
+    def t_operands():
+        for t in range(1, 7):
+            o, n, s = 1024 * (t - 1), tw(t), st(t)
+            lo = 0 if t == 1 else tw(t - 1)
+            aff(raw(T.D1T[:, o + s * lo + 1:o + s * n:s], "D1T%d.1b" % t), raw(T.TP[:, lo:n], "TP"), -1.0)
+            aff(raw(T.D1T[:, o + s * lo + 2:o + s * n:s], "D1T%d.2b" % t), raw(T.TP[:, lo:n], "TP"))
+        t_seed(1)
+
+    def t_b(t):
+        o, n = 1024 * (t - 1), tw(t)
+        tt(raw(T.D1T[:, o + 3:o + 4 * n:4], "D1T%d.3" % t), bc("B0", 16 * (t + 1), n // 16, "B0"), raw(T.J1184[:, :n], "J1184"), A.add)
+
+    def t_new(t):
+        o, n, s = 1024 * (t - 1), tw(t), st(t)
+        c = 16 * ((t - 1) % 2)
+        op("S", lambda: g.scalar.activation(T.D1T[:, o:o + s * n:s], T.NP[:, c:c + 16].indirect(T.BC[:, 0:n // 16]), F.Copy),
+           ["NP.%d" % ((t - 1) % 2), "BC.0"], ["D1T%d.0" % t])
+
+    def t_chain(t):
+        o, n, s = 1024 * (t - 1), tw(t), st(t)
+        d0 = "D0T" if s == 4 else "D0F"
+        k1 = ["D1T%d.%s" % (t, x) for x in ("0", "1", "1b", "2", "2b", "3")] + ["%s.%d" % (d0, x) for x in range(s)]
+        steps = [
+            lambda: tt(raw(T[d0][:, 2:s * n:s], d0 + ".2"), bc("SIG", 0, n // 16, "SIG.0"),
+                       raw(T.J128[:, :n], "J128") if t < 6 else raw(T.TP[:], "TP"), A.is_equal),
+            lambda: op("V", lambda: g.vector.tensor_tensor_scan(T.OT[:, :s * n], T[d0][:, :s * n], T.D1T[:, o:o + s * n], 0.0, A.mult, A.add), k1, ["OT"]),
+        ]
+        if s == 4:
+            steps += [lambda: cp(raw(T.NI[:, :n], "NI"), raw(T.OT[:, 3:4 * n:4], "OT"))] + finish_c(t + 1)
+
+        def carry():
+            if t == 6:
+                aff(raw(T.YT[:], "YT"), raw(T.OT[:, 2:s * n:s], "OT"), 1.0, 2048.0)
+                return
+            o2, s2 = 1024 * t, st(t + 1)
+            aff(raw(T.D1T[:, o2 + 1:o2 + s2 * n:s2], "D1T%d.1" % (t + 1)), raw(T.OT[:, 2:s * n:s], "OT"), -1.0)
+            aff(raw(T.D1T[:, o2 + 2:o2 + s2 * n:s2], "D1T%d.2" % (t + 1)), raw(T.OT[:, 2:s * n:s], "OT"))
+            if s2 == 4:
+                t_seed(t + 1)
+        return steps, carry
+
+    for x in range(3):
+        w("g%d" % x, 2)
+    w("KK", 2)
+    first = [lambda: cp(nn, qv("ni")), lambda: ts(qv("RES", 0), qv("ki"), -1.0, A.add)]
+    for x, (th_, c1, c2) in enumerate(((2, 1.0, -0.5), (4, 2.0, -0.25), (8, 4.0, -0.125))):
+        first.append(lambda x=x, a=th_, b=c1: ts(wq("g%d" % x, 0), qv("ki"), float(a), A.is_ge, b, A.mult))
+        first.append(lambda x=x, a=th_, b=c2: ts(wq("g%d" % x, 1), qv("ki"), float(a), A.is_ge, b, A.mult))
+    first2 = [
+        lambda: tt(w("g0", 2), w("g0", 2), w("g1", 2), A.add),
+        lambda: tt(qv("RES", 1, 2), w("g0", 2), w("g2", 2), A.add),
+        lambda: ts(w("KK", 2), qv("RES", 1, 2), 1.0, A.add),
+        lambda: tt(w("x1"), nn, wq("KK", 1), A.mult),
+        lambda: ts(wi("fl"), w("x1"), -0.4375, A.add),
+        lambda: tt(hv("M", 1), wi("fl"), wq("KK", 0), A.mult),
+        lambda: tt(w("x2"), hv("M", 1), qv("RES", 1), A.subtract),
+        lambda: ts(hv("M", 2), w("x2"), -1.0, A.add, 0.0, A.max),
+        lambda: send_meta(0),
+    ]
+    ts(raw(T.I96[:], "I96"), raw(T.sdi[:], "sdi"), 65.0, A.mult, 2048.0, A.add)
+    ts(raw(T.S32[:], "S32"), raw(T.sdi[:], "sdi"), 32.0, A.add)
+    ts(raw(T.I96b[:], "I96b"), raw(T.I96[:], "I96"), 4095, A.bitwise_and)
+    mid_constants()
+    weave(first)
+    ts(raw(T.B0[:], "B0"), raw(T.I96b[:], "I96b"), 32.0, A.mult)
+    weave(first2, [lambda: ts(qv("RES", 4), qv("ki"), -1.0, A.add, 0.0625, A.mult),
+                   lambda: ts(raw(T.TP[:], "TP"), raw(T.tri[:], "tri"), -2048.0, A.add),
+                   lambda: tt(hv("M", 0), nn, qv("RES", 4), A.add)] + first_c(0))
+    tt(qv("RES", 3), hv("M", 1), nn, A.subtract)
+    t_operands()
+    late_constants()
+    t_b(1)
+    t_b(2)
+    weights = [
+        lambda: (ts(raw(T.W[:, c0 + 2:c0 + 3], "c2"), raw(T.wi[:, 0:1], "wi0"), 2048.0, A.is_ge, -4096.0, A.mult), ts(w("th1"), qv("thi"), 1.0, A.add)),
+        lambda: tt(raw(T.W[:, c0 + 3:c0 + 4], "c3"), raw(T.W[:, c0 + 2:c0 + 3], "c2"), raw(T.wi[:, 0:1], "wi0"), A.add),
+        lambda: ts(raw(T.ZW[:], "ZW"), raw(T.XR[:], "XR"), T.W[:, c0 + 1:c0 + 2], A.is_equal, T.W[:, c0 + 3:c0 + 4], A.mult, extra=["c1", "c3"]),
+    ]
+
+    def mm(out, lhsT, rhs, a, b, rd, wr):
+        op("P", lambda: g.tensor.matmul(out, lhsT, rhs, a, b), rd, wr)
+
+    def post(t, fill=()):
+        last = t == RO - 1
+        d0 = ["D0.%d" % x for x in range(4)]
+        steps = [
+            lambda: (tt(hv("AH", 2), raw(T.pS[:, 0:2, 0:8], "pS"), hv("LIM", 3), A.is_lt),
+                     tt(hv("AH", 0, 2), raw(T.pS[:, 0:2, :], "pS"), hv("LIM", 1, 2), A.is_lt)),
+            lambda: tt(hv("AH", 1), hv("AH", 1), hv("AH", 2), A.max),
+            lambda: tt(hv("C", 0, 2), qv("RES", 5, 2), hv("AH", 0, 2), A.add),
+            lambda: (tt(iv("D0", 2), hv("C", 0), w("H"), A.is_lt), tt(iv("D0", 1), hv("C", 1), w("H"), A.is_lt),
+                     tt(qv("CAND", 5, 2), hv("C", 0, 2), hv("NF", 0, 2), A.min)),
+            lambda: (op("V", lambda: g.vector.tensor_tensor_scan(T.NR[:], T.D0[:], T.D1R[:], 0.0, A.mult, A.add), d0 + ["D1R.%d" % x for x in range(4)], ["NR.3"]),
+                     op("V", lambda: g.vector.tensor_tensor_scan(T.ON[:], T.D0[:], T.D1[:], 0.0, A.mult, A.add), d0 + ["D1.%d" % x for x in range(4)], ["ON.3"])),
+            lambda: tt(qv("RES", 0, 7), raw(T.NR[:, 0:64].indirect(T.BC4[:, 0:7]), "NR.3", "BC4", "BC5", "BC6"), qv("CAND", 0, 7), A.mult),
+        ]
+        if not last:
+            steps += [
+                lambda: (mm(T.pU[:, 16:32], T.ONE[:], T.D0[:, 3::4], True, False, ["ONE", "D0.3"], ["pU"]),
+                         mm(T.pU[:, 16:32], T.NONE[:], T.NR[:, 3::4], False, True, ["NONE", "NR.3"], ["pU"]),
+                         tt(hv("M", 1), nn, qv("RES", 3), A.add), tt(hv("M", 0), nn, qv("RES", 4), A.add)),
+                lambda: tt(w("x2"), hv("M", 1), qv("RES", 1), A.subtract),
+                lambda: (ts(hv("M", 2), w("x2"), -1.0, A.add, 0.0, A.max), send_meta(t + 1)),
+            ]
+        weave(steps, fill)
+
+    w("nk", 2)
+    w("FF", 2)
+    w("KI", 2)
+    w("acol", 1)
+    ac = 16 * Wn["acol"][0]
+    colap = lambda i: T.W[:, ac + i:ac + i + 1]
+
+    for t in range(RO):
+        S_, L, last = SL[t], LS[t], t == RO - 1
+        li_ = LSU.index(L)
+        vo = VOFF[L]
+        ctk = "CT%d" % (t % 2)
+
+        def gather(e, j, h):
+            out = T.V[:, vo + 128 * L * h + 1 + j:vo + 128 * L * (h + 1):L]
+            c = 256 * (t % 2) + 16 * j + 8 * h
+            src = T.X[:, TB:TB + 4096].indirect(T.CT[:, c:c + 8])
+            if e == "V":
+                op("V", lambda: g.vector.tensor_copy(out, src), XK + [ctk], ["V%d.%d.%d" % (L, j, h)])
+            else:
+                op("S", lambda: g.scalar.activation(out, src, F.Copy), XK + [ctk], ["V%d.%d.%d" % (L, j, h)])
+
+        def gather_new(h):
+            if t > 0:
+                op("S", lambda: g.scalar.activation(T.VN[:, 128 * h:128 * h + 128], T.X[:, TB - 16:TB + 4096].indirect(T.VOU[:, 8 * h:8 * h + 8]), F.Copy),
+                   XK + ["Xz", "VOU.0"], ["VN%d" % h])
+
+        nop = lambda: None
+        m3 = lambda: tt(hv("M", 3), nn, nok, A.add)
+        if t > 0:
+            aff(wq("nk", 0), nok, -8192.0, 16.0)
+            aff(wq("nk", 1), nok, -8192.0, 16.0)
+        for j in range(NV1[t], S_):
+            gather("S", j, 1)
+        pre = PRE if t > 0 else 0
+        for j in range(pre):
+            gather("V", j, 1)
+        if t > 0:
+            post(t - 1, [lambda: tt(w("vo"), wi("n3"), wq("nk", 0), A.add), lambda: tt(qv("SIG", 0, 2), qv("PNP", 2 * t, 2), w("nk", 2), A.add),
+                         lambda: cp(qv("VOU"), w("vo")), nop, nop, nop, nop, m3])
+            gather_new(1)
+            op("S", lambda: g.scalar.activation(w("junk")[1](None), T.pU[:, 16:32], F.Identity, accum_out=colap(0)), ["pU"], ["A0"] + w("junk")[3])
+        else:
+            m3()
+        aff(w("K2"), qv("RES", 1), 200.5, 0.5)
+        aff(w("hK"), qv("RES", 0), 100.0)
+        offs = [lambda: tt(hv("OF", 0, 3), hv("M", 1, 3), hv("BASE", 0, 3, 2 * li_), A.add), lambda: cp(hv("OFU", 1, 2), hv("OF", 1, 2))]
+        if t > 0:
+            offs.append(lambda: tt(hv("OF", 0), hv("OF", 0), qv("SIG", 1), A.max))
+        weave([lambda j=j: gather("V", j, 1) for j in range(pre, NV1[t])], offs, [nop, nop] + weights if t == 0 else [])
+        for j in range(NV0[t], S_):
+            gather("S", j, 0)
+        gather_new(0)
+
+        def scalar_operands():
+            if t == 0:
+                for q in range(4):
+                    aff(hv("TH4", q), w("th1"))
+            else:
+                aff(raw(colap(1), "A1"), raw(colap(0), "A0"), 0.0625, -0.46875)
+            aff(iv("D1", 2), qv("RES", 3), 1.0, -1.0)
+            if t > 0:
+                aff(raw(colap(2), "A2"), raw(colap(1), "A1"), 1.0, MAGIC)
+            aff(qv("CAND", 0), qv("RES", 0), 1.0, 1.0)
+            if t > 0:
+                aff(raw(colap(3), "A3"), raw(colap(2), "A2"), -16.0, 16.0 * MAGIC)
+            aff(iv("D1", 3), nn, 1.0, 1.0)
+            if t > 0:
+                aff(raw(colap(4), "A4"), raw(colap(0), "A0"), 1.0, colap(3), extra=["A3"])
+            aff(w("n1184"), nn, 1184.0)
+            if t > 0:
+                aff(hv("LP", 0, 4), hv("TH4", 0, 4), 1.0, colap(4), extra=["A4"])
+
+        def scan(h, a=0, b=128):
+            if a == b:
+                return
+            r0, v0 = RW - 128 * L, vo + 128 * L * h
+            op("V", lambda: g.vector.tensor_tensor_scan(RP[h][:, r0 + a * L:r0 + b * L], T.V[:, v0 + a * L:v0 + b * L],
+                                                        T.ZR[:, :(b - a) * L], 0.0, A.add, A.max),
+               ["ZR", "Vz%d" % L] + ["V%d.%d.%d" % (L, j, h) for j in range(S_)], ["R%d" % h])
+
+        def pick_n(h):
+            src = RP[h][:, RW - 128 * L:RW].indirect(T.OFU[:, h, 16:24])
+            if t > 0:
+                op("V", lambda: g.vector.tensor_tensor(RP[h][:, RW:RW + 128], src, T.VN[:, 128 * h:128 * h + 128], A.add),
+                   ["R%d" % h, "OFU.0.2", "VN%d" % h], ["Pn%d" % h])
+            else:
+                op("V", lambda: g.vector.tensor_copy(RP[h][:, RW:RW + 128], src), ["R%d" % h, "OFU.0.2"], ["Pn%d" % h])
+
+        def pick_ba(h, between=nop):
+            op("S", lambda: g.scalar.activation(RP[h][:, RW + 256:RW + 384], RP[h][:, RW - 128 * L:RW].indirect(T.OFU[:, h, 8:16]), F.Copy),
+               ["R%d" % h, "OFU.0.1"], ["PB%d" % h])
+            between()
+            op("S", lambda: g.scalar.activation(RP[h][:, RW + 128:RW + 256], RP[h][:, RW - 128 * L:RW + 128].indirect(T.OAU[:, 8 * h:8 * h + 8]), F.Copy),
+               ["R%d" % h, "Pn%d" % h, "OAU.0"], ["PA%d" % h])
+            send_data(t, h, "v")
+
+        def usum(h):
+            for a in range(16):
+                mm(T.pU[:, 8 * h:8 * h + 8], T.ZW[:, 15 - a:143 - a], RP[h][:, RW + a:RW + 128:16], a == 0, a == 15, ["ZW", "Pn%d" % h], ["pU"])
+
+        def val(h):
+            sl = slice(128 * h, 128 * h + 128)
+            aff(raw(T.VT[:, sl], "VT%d" % h), raw(RP[h][:, RW:RW + 128], "Pn%d" % h), 0.0625, 191.53125)
+            aff(raw(T.VAL[:, sl], "VAL%d" % h), raw(T.VT[:, sl], "VT%d" % h), 1.0, -192.0)
+
+        pieces = {"1n": (1, 0, 128, 128), "0n": (0, 0, 128, 0), "1v": (1, 128, 384, 512), "0v": (0, 128, 384, 256)}
+
+        def own(p):
+            h, a, b, _ = pieces[p]
+            mm(T["pD" + p][:, a:b], T.ID[:], RP[h][:, RW + a:RW + b], True, False,
+               ["ID"] + (["Pn%d" % h] if a == 0 else ["PA%d" % h, "PB%d" % h]), ["pD" + p])
+
+        def diff(p):
+            h, a, b, d = pieces[p]
+            i = 2 * t + h
+            mm(T["pD" + p][:, a:b], T.NID[:], T.Q[:, i * 384 + a:i * 384 + b], False, True, ["NID", "Q%d%s" % (t, p)], ["pD" + p])
+            op("S", lambda: g.scalar.activation(T.DA[:, d:d + b - a], T["pD" + p][:, a:b], F.Abs), ["pD" + p], ["DA" + p])
+
+        def sums(out, bk, a, b, *ps):
+            for x in range(16):
+                mm(out, T.Z[:, 15 - x:143 - x], T.DA[:, a + x:b:16], x == 0, x == 15, ["Z"] + ["DA" + p for p in ps], [bk])
+
+        def tail(h):
+            win = T.X[:, 0:6144] if h == 0 else T.X[:, 6144:12288]
+            return [
+                lambda: tt(nok, raw(T["pN%d" % h][:, 0:8], "pN%d" % h), hv("LIM", 0), A.is_ge, h=h),
+                lambda: tt(w("so"), w("colq"), nok, A.subtract if h == 0 else A.add, h=h),
+                lambda: ts(qv("SOU"), w("so"), 4096.0, A.mult, h=h),
+                lambda: op("V", lambda: g.vector.tensor_copy(win.indirect(T.SOU[:, 8 * h:8 * h + 8]), T.VAL[:, 128 * h:128 * h + 128]),
+                           ["SOU.0", "VAL%d" % h], [XK[h]] + (["Xz"] if h == 0 else [])),
+            ]
+
+        pm = lambda q, n=1: hv("PM", q, n, 2 * t)
+        relu = lambda o, a, sc, bi: op("S", lambda: g.scalar.activation(o[1](None), a[1](None), F.Relu, bias=bi, scale=sc), a[3], o[3])
+        scan(1)
+        pick_n(1)
+        send_data(t, 1, "n")
+        usum(1)
+        own("1n")
+        gl = [lambda j=j: gather("V", j, 0) for j in range(NV0[t])]
+        weave(gl)
+        scan(0, 0, GP)
+        weave([lambda: tt(w("g"), pm(1), hv("M", 1), A.is_ge), lambda: tt(w("gp"), w("g"), hv("OF", 0), A.mult),
+               lambda: tt(w("oa"), w("gp"), hv("OF", 1), A.max), lambda: cp(qv("OAU"), w("oa"))],
+              [lambda: tt(iv("D1", 0), nn, hv("M", 2), A.subtract), lambda: tt(iv("D1", 1), hv("M", 2), hv("M", 1), A.subtract),
+               lambda: tt(w("H"), w("K2"), w("hK"), A.subtract)])
+        scan(0, GP, 128)
+        pick_ba(1, (lambda: t_new(t)) if t > 0 and TN else nop)
+        own("1v")
+        if t > 0 and not TN:
+            t_new(t)
+        pick_n(0)
+        send_data(t, 0, "n")
+        usum(0)
+        pick_ba(0)
+        own("0n")
+        own("0v")
+        aff(hv("MR", 0), hv("M", 2))
+        aff(hv("MR", 1), hv("M", 1))
+        scalar_operands()
+        diff("1n")
+        sums(T.pN1[:, 0:8], "pN1", 128, 256, "1n")
+        relu(hv("NF", 0), w("H"), 1.0, -4.0)
+        aff(w("KI", 2), qv("RES", 1, 2), 1.0, 1.0)
+        if not last:
+            relu(w("f0"), hv("NF", 0), -1.0, 1.0)
+        val(1)
+        if not last:
+            aff(wq("FF", 0), w("f0"), 1.0, 1.0)
+            aff(wq("FF", 1), w("f0"), -0.5, 1.0)
+
+
+        ech = [
+            lambda: tt(hv("E", 0, 3), hv("M", 0, 3), pm(0, 3), A.is_equal),
+            lambda: tt(hv("E", 3, 2), hv("MR", 0, 2), pm(1, 2), A.is_equal),
+            lambda: tt(hv("E", 1), hv("E", 1), hv("E", 4), A.max),
+            lambda: tt(hv("LIM", 0, 4), hv("E", 0, 4), hv("LP" if t > 0 else "TH4", 0, 4), A.mult),
+        ]
+        kch = [
+            lambda: tt(w("KK", 2), w("KI", 2), w("FF", 2), A.mult),
+            lambda: tt(w("x1"), nn, wq("KK", 1), A.mult),
+            lambda: ts(wi("fl"), w("x1"), -0.4375, A.add),
+            lambda: tt(w("x3"), wi("fl"), wq("KK", 0), A.mult),
+            lambda: tt(qv("CAND", 3), w("x3"), nn, A.subtract),
+        ]
+        if last:
+            kch = []
+        uch = [
+            lambda: cp(wi("y"), raw(T.pU[:, 0:16], "pU")),
+            lambda: ts(wi("ul"), wi("y"), 15, A.bitwise_and),
+            lambda: ts(wi("u"), wi("y"), 4095, A.bitwise_and),
+            lambda: (tt(w("colx"), wi("ul"), w("ci"), A.add), aff(w("colq"), w("colx"), 1.0 / 4096)),
+            lambda: ts(w("ua"), wi("u"), 4096.0, A.add),
+            lambda: ts(w("ub"), wi("u"), -2912.0, A.add),
+        ]
+        uch2 = [
+            lambda: tt(wi("uw"), w("ua"), w("ub"), A.mult),
+            lambda: ts(wi("new"), wi("uw"), 5, A.arith_shift_right, 4095, A.bitwise_and),
+            lambda: ts(qv("NP", t % 2), wi("new"), -2048.0, A.add),
+        ]
+        if not last:
+            uch.append(lambda: tt(w("bn"), w("n1184"), raw(T.B0[:, 16 * (t + 1):16 * (t + 2)], "B0"), A.add))
+            uch2 += [
+                lambda: tt(w("n1"), qv("NP", t % 2), raw(T.S32[:, 16 * (t + 1):16 * (t + 2)], "S32"), A.mult),
+                lambda: tt(wi("n2"), w("n1"), w("bn"), A.add),
+                lambda: ts(wi("n3"), wi("n2"), 5, A.arith_shift_right, 4095, A.bitwise_and),
+            ]
+        if t > 0:
+            tch, carry = t_chain(t)
+        else:
+            tch, carry = first_c(1) + [lambda: t_b(3), lambda: t_b(4)], nop
+        weave(tch[:1], ech[:1], tch[1:2])
+        weave(uch, ech[1:])
+        carry()
+        weave(tch[2:], uch2[:UA])
+        weave(tail(1), uch2[UA:UB], kch[:KA])
+        if last:
+            dma("Y", T.yx[:, 2048:4096], T.X[:, TB + 2048:TB + 4096], "st0", ["X.1"], [])
+        diff("1v")
+        diff("0n")
+        sums(T.pN0[:, 0:8], "pN0", 0, 128, "0n")
+        val(0)
+        relu(hv("NF", 1), w("H"), 1.0, -4.0)
+        aff(qv("CAND", 4), qv("RES", 0), 0.0625, 0.0625)
+        if last:
+            aff(qv("PNP", 2 * RO), nn, 1.0 / 128, 1.0 / 512)
+        else:
+            aff(qv("PNP", 2 * t + 2), nn, 64.0)
+            aff(qv("CAND", 1, 2), w("KK", 2), 1.0, -1.0)
+        diff("0v")
+        if last:
+            t_new(6)
+        if t == 1:
+            aff(raw(T.TP[:], "TP"), raw(T.J128[:], "J128"), 1.0 / 8192)
+        sums(T.pS[:, 0:2, :], "pS", 256, 768, "0v", "1v")
+        weave(tail(0), kch[KA:] + uch2[UB:])
+
+    dma("Y", T.yx[:, 0:2048], T.X[:, TB:TB + 2048], "st1", ["X.0"], [])
+    tch, carry = t_chain(6)
+    tt(qv("SIG"), qv("PNP", 2 * RO), nok, A.subtract)
+    tch[0]()
+    post(RO - 1, [tch[1], carry, lambda: dma("S", T.yt[:], T.YT[:], "st3", ["YT"], [])])
+    cp(raw(T.YS[:, 0, :], "YS0"), nn)
+    ts(raw(T.YS[:, 1, :], "YS1"), qv("RES", 0), 1.0, A.add)
+    for h in (0, 1):
+        cp(raw(T.YS[:, 2:4, 8 * h:8 * h + 8], "YS%d" % (2 + h)), raw(T.RES[:, 80 + 16 * h:96 + 16 * h], "RES.5", "RES.6"))
+    dma("Y", T.yst[:], T.YS[:], "st2", ["YS0", "YS1", "YS2", "YS3"], [])
+    for s, c in cnt.items():
+        need("G", (s, c))

@@ -15,19 +15,20 @@ VTOT = _o
 RW = 1920
 TB = 4096
 MULTI = True
-GP, TN = 0, 0
-NV0 = [3, 3, 4, 4, 5, 5]
-NV1 = [5, 3, 3, 4, 4, 5]
+VM, SPLIT0, SO, V1F = 0, 1, 0, 0
+NV0 = [2, 2, 3, 3, 4, 4]
+NV1 = [5, 4, 4, 5, 5, 6]
+FILL = [(0, 1, 2, 3, 4)] + [tuple(range(n)) + (7, 11, 12) for n in NV1[1:]]
 KA, UA, UB, PRE = 3, 3, 5, 1
 MAGIC = 12582912.0
 
 f32, bf, i32, u16 = "float32", "bfloat16", "int32", "uint16"
 SCRATCH = {
     "X": ("sbuf", [128, 12288], bf), "V": ("sbuf", [128, VTOT], bf), "ZR": ("sbuf", [128, RW], bf),
-    "AH": ("sbuf", [128, 2, 24], f32), "C": ("sbuf", [128, 2, 16], f32), "NF": ("sbuf", [128, 2, 16], f32),
+    "AH": ("sbuf", [128, 2, 32], f32), "C": ("sbuf", [128, 2, 16], f32), "NF": ("sbuf", [128, 2, 16], f32),
     "MR": ("sbuf", [128, 2, 16], f32), "D0F": ("sbuf", [128, 768], f32), "wj": ("sbuf", [128, 4], i32),
     "RP0": ("sbuf", [128, RW + 384], bf), "RP1": ("sbuf", [128, RW + 384], bf),
-    "Q": ("sbuf", [128, 2 * RO * 384], bf), "DA": ("sbuf", [128, 768], bf),
+    "Q": ("sbuf", [128, 2 * RO * 384], bf), "DA": ("sbuf", [128, 1280], bf),
     "VN": ("sbuf", [128, 256], bf), "VT": ("sbuf", [128, 256], bf), "VAL": ("sbuf", [128, 256], bf),
     "tri": ("sbuf", [128, 256], i32), "sdi": ("sbuf", [128, 96], i32), "ni": ("sbuf", [128, 16], i32),
     "ki": ("sbuf", [128, 16], i32), "thi": ("sbuf", [128, 16], i32), "wi": ("sbuf", [128, 4], i32),
@@ -39,7 +40,7 @@ SCRATCH = {
     "CT": ("sbuf", [128, 512], u16), "BC": ("sbuf", [128, 16], u16), "BC4": ("sbuf", [128, 8], u16),
     "OFU": ("sbuf", [128, 2, 24], u16), "OAU": ("sbuf", [128, 16], u16), "SOU": ("sbuf", [128, 16], u16), "VOU": ("sbuf", [128, 16], u16),
     "M": ("sbuf", [128, 2, 32], f32), "PM": ("sbuf", [128, 2 * RO, 24], f32), "E": ("sbuf", [128, 2, 40], f32),
-    "LIM": ("sbuf", [128, 2, 32], f32), "LP": ("sbuf", [128, 2, 32], f32), "TH4": ("sbuf", [128, 2, 32], f32),
+    "LIM": ("sbuf", [128, 2, 40], f32), "LP": ("sbuf", [128, 2, 40], f32), "TH4": ("sbuf", [128, 2, 40], f32),
     "OF": ("sbuf", [128, 2, 24], f32), "BASE": ("sbuf", [128, 2 * len(LSU), 24], f32), "PNP": ("sbuf", [128, 32 * (RO + 1)], f32),
     "D0": ("sbuf", [128, 64], f32), "D1": ("sbuf", [128, 64], f32), "D1R": ("sbuf", [128, 64], f32),
     "ON": ("sbuf", [128, 64], f32), "NR": ("sbuf", [128, 64], f32),
@@ -51,9 +52,9 @@ SCRATCH = {
     "ID": ("sbuf", [128, 128], bf), "NID": ("sbuf", [128, 128], bf),
     "ONE": ("sbuf", [128, 128], f32), "NONE": ("sbuf", [128, 128], f32),
     "YT": ("sbuf", [128, 256], f32), "YS": ("sbuf", [128, 4, 16], f32),
-    "pU": ("psum", [128, 512], f32), "pN0": ("psum", [128, 512], f32), "pN1": ("psum", [128, 512], f32),
+    "pU": ("psum", [128, 512], f32), "pD0w": ("psum", [128, 512], f32), "pD1w": ("psum", [128, 512], f32),
     "pD0n": ("psum", [128, 512], f32), "pD1n": ("psum", [128, 512], f32),
-    "pD0v": ("psum", [128, 512], f32), "pD1v": ("psum", [128, 512], f32), "pS": ("psum", [128, 32, 16], f32),
+    "pD0v": ("psum", [128, 512], f32), "pD1v": ("psum", [128, 512], f32), "pS": ("psum", [128, 16, 32], f32),
 }
 SEMAPHORES = (["cV", "cS", "cP", "cG"] + ["ld%d" % i for i in range(8)] + ["st%d" % i for i in range(4)]
               + ["ml%d" % t for t in range(RO)] + ["ma%d" % t for t in range(RO)]
@@ -200,7 +201,24 @@ def rank_program(g, core, T, topo):
             lastw[k] = ("ma%d" % t, tot)
         cnt["ma%d" % t] = tot
 
+    def send_points(t):
+        trs, tot, i = [], 0, 4 * t + 2
+        for h in (0, 1):
+            rid, pid, _ = topo.addr(part[h])
+            en = topo.engines(core, part[h])
+            en = en[:len(en) // 2] if h == 0 else en[len(en) // 2:]
+            tot += len(en)
+            o = (2 * t + h) * 384
+            trs.append(RemoteDMATransfer(dst_ids=[DstId(rid=rid, pnc=pid)], dma_engine_mask=sum(1 << x for x in en), remote_sem=T.sem["da%d" % i],
+                                         src=RP[h][:, RW + 128:RW + 384], dst=T.Q[:, o + 128:o + 384]))
+        op("G", lambda: g.remote_dma_fused(trs, local_sem=T.sem["dl%d" % i]), ["PA0", "PB0", "PA1", "PB1"], [], sem="dl%d" % i, inc=tot, auto=True)
+        for h in (0, 1):
+            lastw["Q%d%dv" % (t, h)] = ("da%d" % i, tot)
+        cnt["da%d" % i] = tot
+
     def send_data(t, h, p):
+        if not p:
+            return
         rid, pid, _ = topo.addr(part[h])
         ne = len(topo.engines(core, part[h]))
         i = 4 * t + (2 if p == "v" else 0) + h
@@ -383,13 +401,12 @@ def rank_program(g, core, T, topo):
     def mm(out, lhsT, rhs, a, b, rd, wr):
         op("P", lambda: g.tensor.matmul(out, lhsT, rhs, a, b), rd, wr)
 
-    def post(t, fill=()):
+    def post(t):
         last = t == RO - 1
         d0 = ["D0.%d" % x for x in range(4)]
         steps = [
-            lambda: (tt(hv("AH", 2), raw(T.pS[:, 0:2, 0:8], "pS"), hv("LIM", 3), A.is_lt),
-                     tt(hv("AH", 0, 2), raw(T.pS[:, 0:2, :], "pS"), hv("LIM", 1, 2), A.is_lt)),
-            lambda: tt(hv("AH", 1), hv("AH", 1), hv("AH", 2), A.max),
+            lambda: tt(hv("AH", 0, 4), raw(T.pS[:, 0:2, :], "pS"), hv("LIM", 1, 4), A.is_lt),
+            lambda: tt(hv("AH", 0, 2), hv("AH", 0, 2), hv("AH", 2, 2), A.max),
             lambda: tt(hv("C", 0, 2), qv("RES", 5, 2), hv("AH", 0, 2), A.add),
             lambda: (tt(iv("D0", 2), hv("C", 0), w("H"), A.is_lt), tt(iv("D0", 1), hv("C", 1), w("H"), A.is_lt),
                      tt(qv("CAND", 5, 2), hv("C", 0, 2), hv("NF", 0, 2), A.min)),
@@ -405,7 +422,7 @@ def rank_program(g, core, T, topo):
                 lambda: tt(w("x2"), hv("M", 1), qv("RES", 1), A.subtract),
                 lambda: (ts(hv("M", 2), w("x2"), -1.0, A.add, 0.0, A.max), send_meta(t + 1)),
             ]
-        weave(steps, fill)
+        return steps
 
     w("nk", 2)
     w("FF", 2)
@@ -436,34 +453,14 @@ def rank_program(g, core, T, topo):
 
         nop = lambda: None
         m3 = lambda: tt(hv("M", 3), nn, nok, A.add)
-        if t > 0:
-            aff(wq("nk", 0), nok, -8192.0, 16.0)
-            aff(wq("nk", 1), nok, -8192.0, 16.0)
-        for j in range(NV1[t], S_):
-            gather("S", j, 1)
-        pre = PRE if t > 0 else 0
-        for j in range(pre):
-            gather("V", j, 1)
-        if t > 0:
-            post(t - 1, [lambda: tt(w("vo"), wi("n3"), wq("nk", 0), A.add), lambda: tt(qv("SIG", 0, 2), qv("PNP", 2 * t, 2), w("nk", 2), A.add),
-                         lambda: cp(qv("VOU"), w("vo")), nop, nop, nop, nop, m3])
-            gather_new(1)
-            op("S", lambda: g.scalar.activation(w("junk")[1](None), T.pU[:, 16:32], F.Identity, accum_out=colap(0)), ["pU"], ["A0"] + w("junk")[3])
-        else:
-            m3()
-        aff(w("K2"), qv("RES", 1), 200.5, 0.5)
-        aff(w("hK"), qv("RES", 0), 100.0)
-        offs = [lambda: tt(hv("OF", 0, 3), hv("M", 1, 3), hv("BASE", 0, 3, 2 * li_), A.add), lambda: cp(hv("OFU", 1, 2), hv("OF", 1, 2))]
+        offs = [lambda: tt(hv("OF", 0, 3), hv("M", 1, 3), hv("BASE", 0, 3, 2 * li_), A.add)]
         if t > 0:
             offs.append(lambda: tt(hv("OF", 0), hv("OF", 0), qv("SIG", 1), A.max))
-        weave([lambda j=j: gather("V", j, 1) for j in range(pre, NV1[t])], offs, [nop, nop] + weights if t == 0 else [])
-        for j in range(NV0[t], S_):
-            gather("S", j, 0)
-        gather_new(0)
+        offs.append(lambda: cp(hv("OFU", 0, 3), hv("OF", 0, 3)))
 
         def scalar_operands():
             if t == 0:
-                for q in range(4):
+                for q in range(5):
                     aff(hv("TH4", q), w("th1"))
             else:
                 aff(raw(colap(1), "A1"), raw(colap(0), "A0"), 0.0625, -0.46875)
@@ -478,7 +475,7 @@ def rank_program(g, core, T, topo):
                 aff(raw(colap(4), "A4"), raw(colap(0), "A0"), 1.0, colap(3), extra=["A3"])
             aff(w("n1184"), nn, 1184.0)
             if t > 0:
-                aff(hv("LP", 0, 4), hv("TH4", 0, 4), 1.0, colap(4), extra=["A4"])
+                aff(hv("LP", 0, 5), hv("TH4", 0, 5), 1.0, colap(4), extra=["A4"])
 
         def scan(h, a=0, b=128):
             if a == b:
@@ -496,13 +493,11 @@ def rank_program(g, core, T, topo):
             else:
                 op("V", lambda: g.vector.tensor_copy(RP[h][:, RW:RW + 128], src), ["R%d" % h, "OFU.0.2"], ["Pn%d" % h])
 
-        def pick_ba(h, between=nop):
+        def pick_ba(h):
             op("S", lambda: g.scalar.activation(RP[h][:, RW + 256:RW + 384], RP[h][:, RW - 128 * L:RW].indirect(T.OFU[:, h, 8:16]), F.Copy),
                ["R%d" % h, "OFU.0.1"], ["PB%d" % h])
-            between()
-            op("S", lambda: g.scalar.activation(RP[h][:, RW + 128:RW + 256], RP[h][:, RW - 128 * L:RW + 128].indirect(T.OAU[:, 8 * h:8 * h + 8]), F.Copy),
-               ["R%d" % h, "Pn%d" % h, "OAU.0"], ["PA%d" % h])
-            send_data(t, h, "v")
+            op("S", lambda: g.scalar.activation(RP[h][:, RW + 128:RW + 256], RP[h][:, RW - 128 * L:RW + 128].indirect(T.OFU[:, h, 0:8]), F.Copy),
+               ["R%d" % h, "Pn%d" % h, "OFU.0.0"], ["PA%d" % h])
 
         def usum(h):
             for a in range(16):
@@ -513,18 +508,26 @@ def rank_program(g, core, T, topo):
             aff(raw(T.VT[:, sl], "VT%d" % h), raw(RP[h][:, RW:RW + 128], "Pn%d" % h), 0.0625, 191.53125)
             aff(raw(T.VAL[:, sl], "VAL%d" % h), raw(T.VT[:, sl], "VT%d" % h), 1.0, -192.0)
 
-        pieces = {"1n": (1, 0, 128, 128), "0n": (0, 0, 128, 0), "1v": (1, 128, 384, 512), "0v": (0, 128, 384, 256)}
+        pieces = {"1n": (1, 0, 128, 128), "0n": (0, 0, 128, 0), "1v": (1, 128, 384, 768), "0v": (0, 128, 384, 256),
+                  "1w": (1, 128, 384, 1024), "0w": (0, 128, 384, 512)}
 
-        def own(p):
-            h, a, b, _ = pieces[p]
-            mm(T["pD" + p][:, a:b], T.ID[:], RP[h][:, RW + a:RW + b], True, False,
-               ["ID"] + (["Pn%d" % h] if a == 0 else ["PA%d" % h, "PB%d" % h]), ["pD" + p])
+        def own(*ps):
+            for p in ps:
+                h, a, b, _ = pieces[p]
+                mm(T["pD" + p][:, a:b], T.ID[:], RP[h][:, RW + a:RW + b], True, False,
+                   ["ID"] + (["Pn%d" % h] if a == 0 else ["PA%d" % h, "PB%d" % h]), ["pD" + p])
 
-        def diff(p):
-            h, a, b, d = pieces[p]
-            i = 2 * t + h
-            mm(T["pD" + p][:, a:b], T.NID[:], T.Q[:, i * 384 + a:i * 384 + b], False, True, ["NID", "Q%d%s" % (t, p)], ["pD" + p])
-            op("S", lambda: g.scalar.activation(T.DA[:, d:d + b - a], T["pD" + p][:, a:b], F.Abs), ["pD" + p], ["DA" + p])
+        def diff(*ps):
+            for p in ps:
+                h, a, b, d = pieces[p]
+                o = (2 * t + h) * 384
+                if p[1] == "w":
+                    k = ["NID", "Q%d%dv" % (t, h)]
+                    mm(T["pD" + p][:, 128:256], T.NID[:], T.Q[:, o + 256:o + 384], False, False, k, ["pD" + p])
+                    mm(T["pD" + p][:, 256:384], T.NID[:], T.Q[:, o + 128:o + 256], False, True, k, ["pD" + p])
+                else:
+                    mm(T["pD" + p][:, a:b], T.NID[:], T.Q[:, o + a:o + b], False, True, ["NID", "Q%d%s" % (t, p)], ["pD" + p])
+                op("S", lambda: g.scalar.activation(T.DA[:, d:d + b - a], T["pD" + p][:, a:b], F.Abs), ["pD" + p], ["DA" + p])
 
         def sums(out, bk, a, b, *ps):
             for x in range(16):
@@ -533,7 +536,7 @@ def rank_program(g, core, T, topo):
         def tail(h):
             win = T.X[:, 0:6144] if h == 0 else T.X[:, 6144:12288]
             return [
-                lambda: tt(nok, raw(T["pN%d" % h][:, 0:8], "pN%d" % h), hv("LIM", 0), A.is_ge, h=h),
+                lambda: tt(nok, raw(T["pD%dn" % h][:, 256:264], "pD%dn" % h), hv("LIM", 0), A.is_ge, h=h),
                 lambda: tt(w("so"), w("colq"), nok, A.subtract if h == 0 else A.add, h=h),
                 lambda: ts(qv("SOU"), w("so"), 4096.0, A.mult, h=h),
                 lambda: op("V", lambda: g.vector.tensor_copy(win.indirect(T.SOU[:, 8 * h:8 * h + 8]), T.VAL[:, 128 * h:128 * h + 128]),
@@ -542,34 +545,60 @@ def rank_program(g, core, T, topo):
 
         pm = lambda q, n=1: hv("PM", q, n, 2 * t)
         relu = lambda o, a, sc, bi: op("S", lambda: g.scalar.activation(o[1](None), a[1](None), F.Relu, bias=bi, scale=sc), a[3], o[3])
-        scan(1)
+        if t > 0:
+            aff(wq("nk", 0), nok, -8192.0, 16.0)
+            aff(wq("nk", 1), nok, -8192.0, 16.0)
+        for j in range(NV1[t], S_):
+            gather("S", j, 1)
+        long_ = [lambda j=j: gather("V", j, 1) for j in range(NV1[t])] + [lambda: scan(1)] + [lambda j=j: gather("V", j, 0) for j in range(NV0[t])]
+        s_rest = lambda: [gather("S", j, 0) for j in range(NV0[t], S_)]
+        if t > 0:
+            short = [lambda: (tt(w("vo"), wi("n3"), wq("nk", 0), A.add), tt(qv("SIG", 0, 2), qv("PNP", 2 * t, 2), w("nk", 2), A.add)),
+                     lambda: (cp(qv("VOU"), w("vo")), gather_new(1), s_rest())]
+            ps = post(t - 1)
+            short += ps[0:7] + [lambda: (ps[7](), m3())] + ps[8:] + offs
+        else:
+            s_rest()
+            short = [m3] + offs + weights
+        for x, step in enumerate(short):
+            step()
+            for _ in range(FILL[t].count(x)):
+                if long_:
+                    long_.pop(0)()
+        while len(long_) > NV0[t]:
+            long_.pop(0)()
+        if long_:
+            long_.pop(0)()
         pick_n(1)
         send_data(t, 1, "n")
+        weave(long_)
+        if t > 0:
+            op("S", lambda: g.scalar.activation(w("junk")[1](None), T.pU[:, 16:32], F.Identity, accum_out=colap(0)), ["pU"], ["A0"] + w("junk")[3])
+        gather_new(0)
         usum(1)
         own("1n")
-        gl = [lambda j=j: gather("V", j, 0) for j in range(NV0[t])]
-        weave(gl)
-        scan(0, 0, GP)
-        weave([lambda: tt(w("g"), pm(1), hv("M", 1), A.is_ge), lambda: tt(w("gp"), w("g"), hv("OF", 0), A.mult),
-               lambda: tt(w("oa"), w("gp"), hv("OF", 1), A.max), lambda: cp(qv("OAU"), w("oa"))],
-              [lambda: tt(iv("D1", 0), nn, hv("M", 2), A.subtract), lambda: tt(iv("D1", 1), hv("M", 2), hv("M", 1), A.subtract),
-               lambda: tt(w("H"), w("K2"), w("hK"), A.subtract)])
-        scan(0, GP, 128)
-        pick_ba(1, (lambda: t_new(t)) if t > 0 and TN else nop)
-        own("1v")
-        if t > 0 and not TN:
+        scan(0)
+        tt(iv("D1", 0), nn, hv("M", 2), A.subtract)
+        pick_ba(1)
+        send_data(t, 1, "v" if VM == 0 else "")
+        own("1v", "1w")
+        aff(w("K2"), qv("RES", 1), 200.5, 0.5)
+        aff(w("hK"), qv("RES", 0), 100.0)
+        if t > 0:
             t_new(t)
         pick_n(0)
-        send_data(t, 0, "n")
+        if SPLIT0:
+            send_data(t, 0, "n")
+        send_data(t, 1, "v" if VM == 1 else "")
+        tt(w("H"), w("K2"), w("hK"), A.subtract)
         usum(0)
         pick_ba(0)
-        own("0n")
-        own("0v")
-        aff(hv("MR", 0), hv("M", 2))
-        aff(hv("MR", 1), hv("M", 1))
+        if VM == 2:
+            send_points(t)
+        else:
+            send_data(t, 0, "v" if SPLIT0 else "nv")
+        own("0n", "0v", "0w")
         scalar_operands()
-        diff("1n")
-        sums(T.pN1[:, 0:8], "pN1", 128, 256, "1n")
         relu(hv("NF", 0), w("H"), 1.0, -4.0)
         aff(w("KI", 2), qv("RES", 1, 2), 1.0, 1.0)
         if not last:
@@ -578,13 +607,18 @@ def rank_program(g, core, T, topo):
         if not last:
             aff(wq("FF", 0), w("f0"), 1.0, 1.0)
             aff(wq("FF", 1), w("f0"), -0.5, 1.0)
+        aff(hv("MR", 0), pm(2))
+        aff(hv("MR", 1), pm(1))
+        if SO == 0:
+            diff("1n")
+            sums(T.pD1n[:, 256:264], "pD1n", 128, 256, "1n")
 
 
         ech = [
             lambda: tt(hv("E", 0, 3), hv("M", 0, 3), pm(0, 3), A.is_equal),
-            lambda: tt(hv("E", 3, 2), hv("MR", 0, 2), pm(1, 2), A.is_equal),
-            lambda: tt(hv("E", 1), hv("E", 1), hv("E", 4), A.max),
-            lambda: tt(hv("LIM", 0, 4), hv("E", 0, 4), hv("LP" if t > 0 else "TH4", 0, 4), A.mult),
+            lambda: tt(hv("E", 3, 2), hv("M", 1, 2), hv("MR", 0, 2), A.is_equal),
+            lambda: tt(iv("D1", 1), hv("M", 2), hv("M", 1), A.subtract),
+            lambda: tt(hv("LIM", 0, 5), hv("E", 0, 5), hv("LP" if t > 0 else "TH4", 0, 5), A.mult),
         ]
         kch = [
             lambda: tt(w("KK", 2), w("KI", 2), w("FF", 2), A.mult),
@@ -619,17 +653,25 @@ def rank_program(g, core, T, topo):
             tch, carry = t_chain(t)
         else:
             tch, carry = first_c(1) + [lambda: t_b(3), lambda: t_b(4)], nop
-        weave(tch[:1], ech[:1], tch[1:2])
-        weave(uch, ech[1:])
+        weave(tch[:1], ech[2:3], tch[1:2])
+        weave(uch, [nop, ech[0]])
+        if SO == 1:
+            diff("1n")
+            sums(T.pD1n[:, 256:264], "pD1n", 128, 256, "1n")
+        val(0)
         carry()
-        weave(tch[2:], uch2[:UA])
+        weave(tch[2:], uch2[:UA], [ech[1], ech[3]])
         weave(tail(1), uch2[UA:UB], kch[:KA])
         if last:
             dma("Y", T.yx[:, 2048:4096], T.X[:, TB + 2048:TB + 4096], "st0", ["X.1"], [])
-        diff("1v")
+        if VM == 0 and V1F:
+            diff("1v", "1w")
         diff("0n")
-        sums(T.pN0[:, 0:8], "pN0", 0, 128, "0n")
-        val(0)
+        if VM == 0 and not V1F:
+            diff("1v", "1w")
+        if not SPLIT0:
+            diff("0v", "0w")
+        sums(T.pD0n[:, 256:264], "pD0n", 0, 128, "0n")
         relu(hv("NF", 1), w("H"), 1.0, -4.0)
         aff(qv("CAND", 4), qv("RES", 0), 0.0625, 0.0625)
         if last:
@@ -637,19 +679,22 @@ def rank_program(g, core, T, topo):
         else:
             aff(qv("PNP", 2 * t + 2), nn, 64.0)
             aff(qv("CAND", 1, 2), w("KK", 2), 1.0, -1.0)
-        diff("0v")
+        if VM != 0:
+            diff("1v", "1w")
+        if SPLIT0:
+            diff("0v", "0w")
         if last:
             t_new(6)
         if t == 1:
             aff(raw(T.TP[:], "TP"), raw(T.J128[:], "J128"), 1.0 / 8192)
-        sums(T.pS[:, 0:2, :], "pS", 256, 768, "0v", "1v")
+        sums(T.pS[:, 0:2, :], "pS", 256, 1280, "0v", "1v", "0w", "1w")
         weave(tail(0), kch[KA:] + uch2[UB:])
 
     dma("Y", T.yx[:, 0:2048], T.X[:, TB:TB + 2048], "st1", ["X.0"], [])
     tch, carry = t_chain(6)
     tt(qv("SIG"), qv("PNP", 2 * RO), nok, A.subtract)
     tch[0]()
-    post(RO - 1, [tch[1], carry, lambda: dma("S", T.yt[:], T.YT[:], "st3", ["YT"], [])])
+    weave(post(RO - 1), [tch[1], carry, lambda: dma("S", T.yt[:], T.YT[:], "st3", ["YT"], [])])
     cp(raw(T.YS[:, 0, :], "YS0"), nn)
     ts(raw(T.YS[:, 1, :], "YS1"), qv("RES", 0), 1.0, A.add)
     for h in (0, 1):

@@ -15,11 +15,13 @@ VTOT = _o
 RW = 1920
 TB = 4096
 MULTI = True
-VM, SPLIT0, SO, V1F = 0, 1, 0, 0
+VM, SPLIT0, SO, V1F, VN0F = 0, 1, 0, 0, 1
+E0F = 0
+FV, FS = [0] * 6, [0] * 6
 NV0 = [2, 2, 3, 3, 4, 4]
 NV1 = [5, 4, 4, 5, 5, 6]
-FILL = [(0, 1, 2, 3, 4)] + [tuple(range(n)) + (7, 11, 12) for n in NV1[1:]]
-KA, UA, UB, PRE = 3, 3, 5, 1
+FILL = [(0, 1, 2, 3, 4)] + [tuple(range(min(n, 5))) + (4,) * max(n - 5, 0) + (6, 8, 9) for n in NV1[1:]]
+KA, UA, UB, PRE = 4, 3, 5, 1
 MAGIC = 12582912.0
 
 f32, bf, i32, u16 = "float32", "bfloat16", "int32", "uint16"
@@ -44,7 +46,7 @@ SCRATCH = {
     "OF": ("sbuf", [128, 2, 24], f32), "BASE": ("sbuf", [128, 2 * len(LSU), 24], f32), "PNP": ("sbuf", [128, 32 * (RO + 1)], f32),
     "D0": ("sbuf", [128, 64], f32), "D1": ("sbuf", [128, 64], f32), "D1R": ("sbuf", [128, 64], f32),
     "ON": ("sbuf", [128, 64], f32), "NR": ("sbuf", [128, 64], f32),
-    "RES": ("sbuf", [128, 112], f32), "CAND": ("sbuf", [128, 112], f32),
+    "RES": ("sbuf", [128, 128], f32), "CAND": ("sbuf", [128, 128], f32),
     "W": ("sbuf", [128, 16 * 48], f32), "WI": ("sbuf", [128, 16 * 16], i32),
     "SIG": ("sbuf", [128, 32], f32), "NP": ("sbuf", [128, 32], f32),
     "PI": ("sbuf", [128, 16], i32), "PC": ("sbuf", [128, 16], f32), "XR": ("sbuf", [128, 144], f32),
@@ -232,9 +234,9 @@ def rank_program(g, core, T, topo):
         cnt["da%d" % i] = ne
 
     dma("S", T.sdi[:], T.sd[:], "ld2", [], ["sdi"])
-    dma("Y", T.ki[:], T.k0[:], "ld1", [], ["ki.0"])
-    dma("S", T.ni[:], T.n0[:], "ld0", [], ["ni.0"])
     dma("Y", T.tri[:], T.tr[:], "ld3", [], ["tri"])
+    dma("S", T.ki[:], T.k0[:], "ld1", [], ["ki.0"])
+    dma("Y", T.ni[:], T.n0[:], "ld0", [], ["ni.0"])
     dma("Y", T.X[:, TB:TB + 4096], T.xt[:], "ld4", [], XK)
     dma("Y", T.wi[:, 0:1], T.wt[:], "ld6", [], ["wi0"])
     dma("Y", T.thi[:], T.th[:], "ld5", [], ["thi.0"])
@@ -276,18 +278,22 @@ def rank_program(g, core, T, topo):
     aff(w("ci"), w("li"), 16.0, h=1)
 
     def mid_constants():
-        for l in LSU[1:]:
-            memset(T.V[:, VOFF[l]:VOFF[l] + 256 * l:l], -256.0, "Vz%d" % l)
+        for l in LSU[1:3]:
+            iota(T.V[:, VOFF[l]:VOFF[l] + 256 * l:l], [[0, 256]], -256, 0, "Vz%d" % l)
+
+    iota(T.D0T[:, 0:4 * tw(4):4], [[0, tw(4)]], 0, 0, "D0T.0")
+    iota(T.D0T[:, 1:4 * tw(4):4], [[0, tw(4)]], 1, 0, "D0T.1")
+    iota(T.ONE[:], [[0, 128]], 1, 0, "ONE")
+    iota(T.NONE[:], [[0, 128]], -1, 0, "NONE")
+    iota(T.D0F[:, 0::3], [[0, 256]], 0, 0, "D0F.0")
+    iota(T.D0F[:, 1::3], [[0, 256]], 1, 0, "D0F.1")
+    for l in LSU[3:]:
+        iota(T.V[:, VOFF[l]:VOFF[l] + 256 * l:l], [[0, 256]], -256, 0, "Vz%d" % l)
 
     def late_constants():
-        memset(T.ONE[:], 1.0, "ONE")
-        memset(T.NONE[:], -1.0, "NONE")
-        memset(T.D0T[:, 0:4 * tw(4):4], 0.0, "D0T.0")
-        memset(T.D0T[:, 1:4 * tw(4):4], 1.0, "D0T.1")
-        memset(T.D0F[:, 0::3], 0.0, "D0F.0")
-        memset(T.D0F[:, 1::3], 1.0, "D0F.1")
         a0, a8 = 16 * WIn["a"], 16 * WIn["a8"]
         ts(raw(T.BC4[:, 0:5], "BC4"), raw(T.WI[:, a0:a0 + 5], *wi("a")[3]), 4.0, A.mult, 3.0, A.add)
+        ts(raw(T.BC4[:, 7:8], "BC7"), raw(T.WI[:, a0:a0 + 1], *wi("a")[3]), 4.0, A.mult, 3.0, A.add)
         ts(raw(T.BC4[:, 5:6], "BC5"), raw(T.WI[:, a8:a8 + 1], *wi("a8")[3]), 4.0, A.mult, 3.0, A.add)
         ts(raw(T.BC4[:, 6:7], "BC6"), raw(T.WI[:, a8:a8 + 1], *wi("a8")[3]), 4.0, A.mult, 35.0, A.add)
 
@@ -356,13 +362,12 @@ def rank_program(g, core, T, topo):
             o2, s2 = 1024 * t, st(t + 1)
             aff(raw(T.D1T[:, o2 + 1:o2 + s2 * n:s2], "D1T%d.1" % (t + 1)), raw(T.OT[:, 2:s * n:s], "OT"), -1.0)
             aff(raw(T.D1T[:, o2 + 2:o2 + s2 * n:s2], "D1T%d.2" % (t + 1)), raw(T.OT[:, 2:s * n:s], "OT"))
-            if s2 == 4:
-                t_seed(t + 1)
         return steps, carry
 
     for x in range(3):
         w("g%d" % x, 2)
     w("KK", 2)
+    nop0 = lambda: None
     first = [lambda: cp(nn, qv("ni")), lambda: ts(qv("RES", 0), qv("ki"), -1.0, A.add)]
     for x, (th_, c1, c2) in enumerate(((2, 1.0, -0.5), (4, 2.0, -0.25), (8, 4.0, -0.125))):
         first.append(lambda x=x, a=th_, b=c1: ts(wq("g%d" % x, 0), qv("ki"), float(a), A.is_ge, b, A.mult))
@@ -381,17 +386,19 @@ def rank_program(g, core, T, topo):
     ts(raw(T.I96[:], "I96"), raw(T.sdi[:], "sdi"), 65.0, A.mult, 2048.0, A.add)
     ts(raw(T.S32[:], "S32"), raw(T.sdi[:], "sdi"), 32.0, A.add)
     ts(raw(T.I96b[:], "I96b"), raw(T.I96[:], "I96"), 4095, A.bitwise_and)
-    mid_constants()
-    weave(first)
+    ts(raw(T.TP[:], "TP"), raw(T.tri[:], "tri"), -2048.0, A.add)
     ts(raw(T.B0[:], "B0"), raw(T.I96b[:], "I96b"), 32.0, A.mult)
-    weave(first2, [lambda: ts(qv("RES", 4), qv("ki"), -1.0, A.add, 0.0625, A.mult),
-                   lambda: ts(raw(T.TP[:], "TP"), raw(T.tri[:], "tri"), -2048.0, A.add),
-                   lambda: tt(hv("M", 0), nn, qv("RES", 4), A.add)] + first_c(0))
+    fc = first_c(0)
+    first.append(lambda: ts(qv("RES", 4), qv("ki"), -1.0, A.add, 0.0625, A.mult))
+    first2[1] = lambda a=first2[1]: (a(), tt(hv("M", 0), nn, qv("RES", 4), A.add), tt(hv("M", 3), nn, nok, A.add))
+    first2[7:] = [lambda a=first2[7], b=first2[8]: (a(), b())]
+    fc[1]()
+    fc[0]()
+    weave(first)
+    weave(first2, fc[2:] + [late_constants, lambda: t_b(1)])
+    mid_constants()
     tt(qv("RES", 3), hv("M", 1), nn, A.subtract)
     t_operands()
-    late_constants()
-    t_b(1)
-    t_b(2)
     weights = [
         lambda: (ts(raw(T.W[:, c0 + 2:c0 + 3], "c2"), raw(T.wi[:, 0:1], "wi0"), 2048.0, A.is_ge, -4096.0, A.mult), ts(w("th1"), qv("thi"), 1.0, A.add)),
         lambda: tt(raw(T.W[:, c0 + 3:c0 + 4], "c3"), raw(T.W[:, c0 + 2:c0 + 3], "c2"), raw(T.wi[:, 0:1], "wi0"), A.add),
@@ -404,27 +411,29 @@ def rank_program(g, core, T, topo):
     def post(t):
         last = t == RO - 1
         d0 = ["D0.%d" % x for x in range(4)]
+        nq = 7 if last else 8
         steps = [
             lambda: tt(hv("AH", 0, 4), raw(T.pS[:, 0:2, :], "pS"), hv("LIM", 1, 4), A.is_lt),
             lambda: tt(hv("AH", 0, 2), hv("AH", 0, 2), hv("AH", 2, 2), A.max),
             lambda: tt(hv("C", 0, 2), qv("RES", 5, 2), hv("AH", 0, 2), A.add),
-            lambda: (tt(iv("D0", 2), hv("C", 0), w("H"), A.is_lt), tt(iv("D0", 1), hv("C", 1), w("H"), A.is_lt),
+            lambda: (tt(iv("D0", 2), hv("C", 0), wq("H", 0), A.is_lt), tt(iv("D0", 1), hv("C", 1), wq("H", 0), A.is_lt),
                      tt(qv("CAND", 5, 2), hv("C", 0, 2), hv("NF", 0, 2), A.min)),
             lambda: (op("V", lambda: g.vector.tensor_tensor_scan(T.NR[:], T.D0[:], T.D1R[:], 0.0, A.mult, A.add), d0 + ["D1R.%d" % x for x in range(4)], ["NR.3"]),
                      op("V", lambda: g.vector.tensor_tensor_scan(T.ON[:], T.D0[:], T.D1[:], 0.0, A.mult, A.add), d0 + ["D1.%d" % x for x in range(4)], ["ON.3"])),
-            lambda: tt(qv("RES", 0, 7), raw(T.NR[:, 0:64].indirect(T.BC4[:, 0:7]), "NR.3", "BC4", "BC5", "BC6"), qv("CAND", 0, 7), A.mult),
+            lambda: tt(qv("RES", 0, nq), raw(T.NR[:, 0:64].indirect(T.BC4[:, 0:nq]), "NR.3", "BC4", "BC5", "BC6", "BC7"), qv("CAND", 0, nq), A.mult),
         ]
         if not last:
             steps += [
                 lambda: (mm(T.pU[:, 16:32], T.ONE[:], T.D0[:, 3::4], True, False, ["ONE", "D0.3"], ["pU"]),
                          mm(T.pU[:, 16:32], T.NONE[:], T.NR[:, 3::4], False, True, ["NONE", "NR.3"], ["pU"]),
-                         tt(hv("M", 1), nn, qv("RES", 3), A.add), tt(hv("M", 0), nn, qv("RES", 4), A.add)),
-                lambda: tt(w("x2"), hv("M", 1), qv("RES", 1), A.subtract),
+                         tt(w("x2"), nn, qv("RES", 7), A.add), tt(hv("M", 1), nn, qv("RES", 3), A.add), tt(hv("M", 0), nn, qv("RES", 4), A.add)),
                 lambda: (ts(hv("M", 2), w("x2"), -1.0, A.add, 0.0, A.max), send_meta(t + 1)),
             ]
         return steps
 
-    w("nk", 2)
+    seed_next = []
+    for x in ("nk", "K2", "hK", "H"):
+        w(x, 2)
     w("FF", 2)
     w("KI", 2)
     w("acol", 1)
@@ -438,13 +447,15 @@ def rank_program(g, core, T, topo):
         ctk = "CT%d" % (t % 2)
 
         def gather(e, j, h):
-            out = T.V[:, vo + 128 * L * h + 1 + j:vo + 128 * L * (h + 1):L]
-            c = 256 * (t % 2) + 16 * j + 8 * h
-            src = T.X[:, TB:TB + 4096].indirect(T.CT[:, c:c + 8])
+            a, b = (0, 2) if h == 2 else (h, h + 1)
+            out = T.V[:, vo + 128 * L * a + 1 + j:vo + 128 * L * b:L]
+            c = 256 * (t % 2) + 16 * j
+            src = T.X[:, TB:TB + 4096].indirect(T.CT[:, c + 8 * a:c + 8 * b])
+            k = ["V%d.%d.%d" % (L, j, x) for x in range(a, b)]
             if e == "V":
-                op("V", lambda: g.vector.tensor_copy(out, src), XK + [ctk], ["V%d.%d.%d" % (L, j, h)])
+                op("V", lambda: g.vector.tensor_copy(out, src), XK + [ctk], k)
             else:
-                op("S", lambda: g.scalar.activation(out, src, F.Copy), XK + [ctk], ["V%d.%d.%d" % (L, j, h)])
+                op("S", lambda: g.scalar.activation(out, src, F.Copy), XK + [ctk], k)
 
         def gather_new(h):
             if t > 0:
@@ -473,7 +484,6 @@ def rank_program(g, core, T, topo):
             aff(iv("D1", 3), nn, 1.0, 1.0)
             if t > 0:
                 aff(raw(colap(4), "A4"), raw(colap(0), "A0"), 1.0, colap(3), extra=["A3"])
-            aff(w("n1184"), nn, 1184.0)
             if t > 0:
                 aff(hv("LP", 0, 5), hv("TH4", 0, 5), 1.0, colap(4), extra=["A4"])
 
@@ -503,9 +513,11 @@ def rank_program(g, core, T, topo):
             for a in range(16):
                 mm(T.pU[:, 8 * h:8 * h + 8], T.ZW[:, 15 - a:143 - a], RP[h][:, RW + a:RW + 128:16], a == 0, a == 15, ["ZW", "Pn%d" % h], ["pU"])
 
+        def vt(h):
+            aff(raw(T.VT[:, 128 * h:128 * h + 128], "VT%d" % h), raw(RP[h][:, RW:RW + 128], "Pn%d" % h), 0.0625, 191.53125)
+
         def val(h):
             sl = slice(128 * h, 128 * h + 128)
-            aff(raw(T.VT[:, sl], "VT%d" % h), raw(RP[h][:, RW:RW + 128], "Pn%d" % h), 0.0625, 191.53125)
             aff(raw(T.VAL[:, sl], "VAL%d" % h), raw(T.VT[:, sl], "VT%d" % h), 1.0, -192.0)
 
         pieces = {"1n": (1, 0, 128, 128), "0n": (0, 0, 128, 0), "1v": (1, 128, 384, 768), "0v": (0, 128, 384, 256),
@@ -548,19 +560,23 @@ def rank_program(g, core, T, topo):
         if t > 0:
             aff(wq("nk", 0), nok, -8192.0, 16.0)
             aff(wq("nk", 1), nok, -8192.0, 16.0)
+        fv, sp = FV[t], S_ - FS[t]
         for j in range(NV1[t], S_):
-            gather("S", j, 1)
-        long_ = [lambda j=j: gather("V", j, 1) for j in range(NV1[t])] + [lambda: scan(1)] + [lambda j=j: gather("V", j, 0) for j in range(NV0[t])]
-        s_rest = lambda: [gather("S", j, 0) for j in range(NV0[t], S_)]
+            gather("S", j, 1 if j < sp else 2)
+        long_ = ([lambda j=j: gather("V", j, 2 if j < fv else 1) for j in range(NV1[t])] + [lambda: scan(1)]
+                 + [lambda j=j: gather("V", j, 0) for j in range(fv, fv + NV0[t])])
+        s_rest = lambda: [gather("S", j, 0) for j in range(fv + NV0[t], sp)]
         if t > 0:
             short = [lambda: (tt(w("vo"), wi("n3"), wq("nk", 0), A.add), tt(qv("SIG", 0, 2), qv("PNP", 2 * t, 2), w("nk", 2), A.add)),
                      lambda: (cp(qv("VOU"), w("vo")), gather_new(1), s_rest())]
             ps = post(t - 1)
-            short += ps[0:7] + [lambda: (ps[7](), m3())] + ps[8:] + offs
+            short = [short[0], lambda a=short[1]: (a(), ps[0]())] + ps[1:5] + [lambda: (ps[5](), m3()), ps[6], lambda: (
+                ps[7](), tt(hv("OF", 0), hv("M", 1), hv("BASE", 0, 1, 2 * li_), A.add)), lambda: (
+                tt(hv("OF", 1, 2), hv("M", 2, 2), hv("BASE", 1, 2, 2 * li_), A.add), offs[1]()), offs[2]]
         else:
             s_rest()
-            short = [m3] + offs + weights
-        for x, step in enumerate(short):
+            short = offs + weights
+        for x, step in enumerate([nop] + short, -1):
             step()
             for _ in range(FILL[t].count(x)):
                 if long_:
@@ -570,48 +586,66 @@ def rank_program(g, core, T, topo):
         if long_:
             long_.pop(0)()
         pick_n(1)
-        send_data(t, 1, "n")
+        send_data(t, 1, "n" if VM != 3 else "")
         weave(long_)
         if t > 0:
             op("S", lambda: g.scalar.activation(w("junk")[1](None), T.pU[:, 16:32], F.Identity, accum_out=colap(0)), ["pU"], ["A0"] + w("junk")[3])
-        gather_new(0)
+        if VN0F:
+            gather_new(0)
         usum(1)
         own("1n")
         scan(0)
         tt(iv("D1", 0), nn, hv("M", 2), A.subtract)
         pick_ba(1)
-        send_data(t, 1, "v" if VM == 0 else "")
+        send_data(t, 1, "v" if VM == 0 else "nv" if VM == 3 else "")
+        if not VN0F:
+            gather_new(0)
         own("1v", "1w")
-        aff(w("K2"), qv("RES", 1), 200.5, 0.5)
-        aff(w("hK"), qv("RES", 0), 100.0)
         if t > 0:
             t_new(t)
         pick_n(0)
         if SPLIT0:
             send_data(t, 0, "n")
         send_data(t, 1, "v" if VM == 1 else "")
-        tt(w("H"), w("K2"), w("hK"), A.subtract)
         usum(0)
         pick_ba(0)
+        while seed_next:
+            t_seed(seed_next.pop())
+        aff(wq("K2", 0), qv("RES", 1), 200.5, 0.5)
+        aff(wq("hK", 0), qv("RES", 0), 100.0)
+        if not last:
+            aff(wq("K2", 1), raw(T.B0[:, 16 * (t + 1):16 * (t + 2)], "B0"))
+            aff(wq("hK", 1), nn, -1184.0)
         if VM == 2:
             send_points(t)
         else:
             send_data(t, 0, "v" if SPLIT0 else "nv")
         own("0n", "0v", "0w")
+        if t > 0:
+            tch, carry = t_chain(t)
+        else:
+            tch, carry = first_c(1), nop
+        tch[0]()
+        tt(iv("D1", 1), hv("M", 2), hv("M", 1), A.subtract)
+        tch[1]()
+        nh = 1 if last else 2
+        tt(qv("W", Wn["H"][0], nh), qv("W", Wn["K2"][0], nh), qv("W", Wn["hK"][0], nh), A.subtract)
         scalar_operands()
-        relu(hv("NF", 0), w("H"), 1.0, -4.0)
+        relu(hv("NF", 0), wq("H", 0), 1.0, -4.0)
         aff(w("KI", 2), qv("RES", 1, 2), 1.0, 1.0)
+        vt(1)
         if not last:
             relu(w("f0"), hv("NF", 0), -1.0, 1.0)
-        val(1)
-        if not last:
-            aff(wq("FF", 0), w("f0"), 1.0, 1.0)
-            aff(wq("FF", 1), w("f0"), -0.5, 1.0)
         aff(hv("MR", 0), pm(2))
         aff(hv("MR", 1), pm(1))
+        val(1)
         if SO == 0:
             diff("1n")
             sums(T.pD1n[:, 256:264], "pD1n", 128, 256, "1n")
+        if not last:
+            aff(wq("FF", 0), w("f0"), 1.0, 1.0)
+            aff(wq("FF", 1), w("f0"), -0.5, 1.0)
+        vt(0)
 
 
         ech = [
@@ -626,6 +660,7 @@ def rank_program(g, core, T, topo):
             lambda: ts(wi("fl"), w("x1"), -0.4375, A.add),
             lambda: tt(w("x3"), wi("fl"), wq("KK", 0), A.mult),
             lambda: tt(qv("CAND", 3), w("x3"), nn, A.subtract),
+            lambda: tt(qv("CAND", 7), qv("CAND", 3), qv("CAND", 1), A.subtract),
         ]
         if last:
             kch = []
@@ -643,25 +678,23 @@ def rank_program(g, core, T, topo):
             lambda: ts(qv("NP", t % 2), wi("new"), -2048.0, A.add),
         ]
         if not last:
-            uch.append(lambda: tt(w("bn"), w("n1184"), raw(T.B0[:, 16 * (t + 1):16 * (t + 2)], "B0"), A.add))
             uch2 += [
                 lambda: tt(w("n1"), qv("NP", t % 2), raw(T.S32[:, 16 * (t + 1):16 * (t + 2)], "S32"), A.mult),
-                lambda: tt(wi("n2"), w("n1"), w("bn"), A.add),
+                lambda: tt(wi("n2"), w("n1"), wq("H", 1), A.add),
                 lambda: ts(wi("n3"), wi("n2"), 5, A.arith_shift_right, 4095, A.bitwise_and),
             ]
-        if t > 0:
-            tch, carry = t_chain(t)
-        else:
-            tch, carry = first_c(1) + [lambda: t_b(3), lambda: t_b(4)], nop
-        weave(tch[:1], ech[2:3], tch[1:2])
         weave(uch, [nop, ech[0]])
         if SO == 1:
             diff("1n")
             sums(T.pD1n[:, 256:264], "pD1n", 128, 256, "1n")
         val(0)
+        if VM == 3:
+            diff("1v", "1w")
         carry()
         weave(tch[2:], uch2[:UA], [ech[1], ech[3]])
         weave(tail(1), uch2[UA:UB], kch[:KA])
+        if t < 3:
+            t_b(t + 2)
         if last:
             dma("Y", T.yx[:, 2048:4096], T.X[:, TB + 2048:TB + 4096], "st0", ["X.1"], [])
         if VM == 0 and V1F:
@@ -672,17 +705,19 @@ def rank_program(g, core, T, topo):
         if not SPLIT0:
             diff("0v", "0w")
         sums(T.pD0n[:, 256:264], "pD0n", 0, 128, "0n")
-        relu(hv("NF", 1), w("H"), 1.0, -4.0)
+        relu(hv("NF", 1), wq("H", 0), 1.0, -4.0)
         aff(qv("CAND", 4), qv("RES", 0), 0.0625, 0.0625)
         if last:
             aff(qv("PNP", 2 * RO), nn, 1.0 / 128, 1.0 / 512)
         else:
             aff(qv("PNP", 2 * t + 2), nn, 64.0)
             aff(qv("CAND", 1, 2), w("KK", 2), 1.0, -1.0)
-        if VM != 0:
+        if VM in (1, 2):
             diff("1v", "1w")
         if SPLIT0:
             diff("0v", "0w")
+        if 0 < t < 4:
+            t_seed(t + 1)
         if last:
             t_new(6)
         if t == 1:
@@ -693,8 +728,9 @@ def rank_program(g, core, T, topo):
     dma("Y", T.yx[:, 0:2048], T.X[:, TB:TB + 2048], "st1", ["X.0"], [])
     tch, carry = t_chain(6)
     tt(qv("SIG"), qv("PNP", 2 * RO), nok, A.subtract)
-    tch[0]()
-    weave(post(RO - 1), [tch[1], carry, lambda: dma("S", T.yt[:], T.YT[:], "st3", ["YT"], [])])
+    ps = post(RO - 1)
+    weave(ps[:5], [tch[0], nop0, lambda: (tch[1](), carry(), dma("S", T.yt[:], T.YT[:], "st3", ["YT"], []))])
+    ps[5]()
     cp(raw(T.YS[:, 0, :], "YS0"), nn)
     ts(raw(T.YS[:, 1, :], "YS1"), qv("RES", 0), 1.0, A.add)
     for h in (0, 1):

@@ -20,8 +20,8 @@ E0F = 0
 FV, FS = [0] * 6, [0] * 6
 NV0 = [2, 2, 3, 3, 4, 4]
 NV1 = [5, 4, 4, 5, 5, 6]
-FILL = [(0, 1, 2, 3, 4)] + [tuple(range(min(n, 5))) + (4,) * max(n - 5, 0) + (6, 8, 9) for n in NV1[1:]]
-KA, UA, UB, PRE = 4, 3, 5, 1
+FILL = [(0, 1, 2, 3, 4, 5, 6, 7)] + [tuple(range(min(n, 5))) + (4,) * max(n - 5, 0) + (6, 8, 9) for n in NV1[1:]]
+KA, UA, UB, PRE = 3, 3, 5, 1
 MAGIC = 12582912.0
 
 f32, bf, i32, u16 = "float32", "bfloat16", "int32", "uint16"
@@ -236,8 +236,8 @@ def rank_program(g, core, T, topo):
     dma("S", T.sdi[:], T.sd[:], "ld2", [], ["sdi"])
     dma("Y", T.tri[:], T.tr[:], "ld3", [], ["tri"])
     dma("S", T.ki[:], T.k0[:], "ld1", [], ["ki.0"])
-    dma("Y", T.ni[:], T.n0[:], "ld0", [], ["ni.0"])
     dma("Y", T.X[:, TB:TB + 4096], T.xt[:], "ld4", [], XK)
+    dma("S", T.ni[:], T.n0[:], "ld0", [], ["ni.0"])
     dma("Y", T.wi[:, 0:1], T.wt[:], "ld6", [], ["wi0"])
     dma("Y", T.thi[:], T.th[:], "ld5", [], ["thi.0"])
 
@@ -335,7 +335,8 @@ def rank_program(g, core, T, topo):
 
     def t_b(t):
         o, n = 1024 * (t - 1), tw(t)
-        tt(raw(T.D1T[:, o + 3:o + 4 * n:4], "D1T%d.3" % t), bc("B0", 16 * (t + 1), n // 16, "B0"), raw(T.J1184[:, :n], "J1184"), A.add)
+        op("S", lambda: g.scalar.activation(T.D1T[:, o + 3:o + 4 * n:4], T.B0[:, 16 * (t + 1):16 * (t + 2)].indirect(T.BC[:, 0:n // 16]), F.Copy),
+           ["B0", "BC.0"], ["D1T%d.3" % t])
 
     def t_new(t):
         o, n, s = 1024 * (t - 1), tw(t), st(t)
@@ -353,7 +354,7 @@ def rank_program(g, core, T, topo):
             lambda: op("V", lambda: g.vector.tensor_tensor_scan(T.OT[:, :s * n], T[d0][:, :s * n], T.D1T[:, o:o + s * n], 0.0, A.mult, A.add), k1, ["OT"]),
         ]
         if s == 4:
-            steps += [lambda: cp(raw(T.NI[:, :n], "NI"), raw(T.OT[:, 3:4 * n:4], "OT"))] + finish_c(t + 1)
+            steps += [lambda: tt(raw(T.NI[:, :n], "NI"), raw(T.OT[:, 3:4 * n:4], "OT"), raw(T.J1184[:, :n], "J1184"), A.add)] + finish_c(t + 1)
 
         def carry():
             if t == 6:
@@ -368,7 +369,7 @@ def rank_program(g, core, T, topo):
         w("g%d" % x, 2)
     w("KK", 2)
     nop0 = lambda: None
-    first = [lambda: cp(nn, qv("ni")), lambda: ts(qv("RES", 0), qv("ki"), -1.0, A.add)]
+    first = [lambda: ts(qv("RES", 0), qv("ki"), -1.0, A.add)]
     for x, (th_, c1, c2) in enumerate(((2, 1.0, -0.5), (4, 2.0, -0.25), (8, 4.0, -0.125))):
         first.append(lambda x=x, a=th_, b=c1: ts(wq("g%d" % x, 0), qv("ki"), float(a), A.is_ge, b, A.mult))
         first.append(lambda x=x, a=th_, b=c2: ts(wq("g%d" % x, 1), qv("ki"), float(a), A.is_ge, b, A.mult))
@@ -390,15 +391,22 @@ def rank_program(g, core, T, topo):
     ts(raw(T.B0[:], "B0"), raw(T.I96b[:], "I96b"), 32.0, A.mult)
     fc = first_c(0)
     first.append(lambda: ts(qv("RES", 4), qv("ki"), -1.0, A.add, 0.0625, A.mult))
-    first2[1] = lambda a=first2[1]: (a(), tt(hv("M", 0), nn, qv("RES", 4), A.add), tt(hv("M", 3), nn, nok, A.add))
+    first2[2] = lambda a=first2[2]: (a(), cp(nn, qv("ni")))
+    first2[3] = lambda a=first2[3]: (a(), tt(hv("M", 0), nn, qv("RES", 4), A.add), tt(hv("M", 3), nn, nok, A.add))
     first2[7:] = [lambda a=first2[7], b=first2[8]: (a(), b())]
     fc[1]()
     fc[0]()
-    weave(first)
-    weave(first2, fc[2:] + [late_constants, lambda: t_b(1)])
+    late_constants()
+    fc[2]()
+    weave(first[:3])
+    fc[3]()
+    weave(first[3:6])
+    fc[4]()
+    weave(first[6:])
+    first2.append(lambda: tt(qv("RES", 3), hv("M", 1), nn, A.subtract))
     mid_constants()
-    tt(qv("RES", 3), hv("M", 1), nn, A.subtract)
     t_operands()
+    t_b(1)
     weights = [
         lambda: (ts(raw(T.W[:, c0 + 2:c0 + 3], "c2"), raw(T.wi[:, 0:1], "wi0"), 2048.0, A.is_ge, -4096.0, A.mult), ts(w("th1"), qv("thi"), 1.0, A.add)),
         lambda: tt(raw(T.W[:, c0 + 3:c0 + 4], "c3"), raw(T.W[:, c0 + 2:c0 + 3], "c2"), raw(T.wi[:, 0:1], "wi0"), A.add),
@@ -474,18 +482,14 @@ def rank_program(g, core, T, topo):
                 for q in range(5):
                     aff(hv("TH4", q), w("th1"))
             else:
-                aff(raw(colap(1), "A1"), raw(colap(0), "A0"), 0.0625, -0.46875)
-            aff(iv("D1", 2), qv("RES", 3), 1.0, -1.0)
-            if t > 0:
-                aff(raw(colap(2), "A2"), raw(colap(1), "A1"), 1.0, MAGIC)
-            aff(qv("CAND", 0), qv("RES", 0), 1.0, 1.0)
-            if t > 0:
-                aff(raw(colap(3), "A3"), raw(colap(2), "A2"), -16.0, 16.0 * MAGIC)
-            aff(iv("D1", 3), nn, 1.0, 1.0)
-            if t > 0:
-                aff(raw(colap(4), "A4"), raw(colap(0), "A0"), 1.0, colap(3), extra=["A3"])
-            if t > 0:
                 aff(hv("LP", 0, 5), hv("TH4", 0, 5), 1.0, colap(4), extra=["A4"])
+
+        def a_step(x):
+            if t > 0:
+                [lambda: aff(raw(colap(1), "A1"), raw(colap(0), "A0"), 0.0625, -0.46875),
+                 lambda: aff(raw(colap(2), "A2"), raw(colap(1), "A1"), 1.0, MAGIC),
+                 lambda: aff(raw(colap(3), "A3"), raw(colap(2), "A2"), -16.0, 16.0 * MAGIC),
+                 lambda: aff(raw(colap(4), "A4"), raw(colap(0), "A0"), 1.0, colap(3), extra=["A3"])][x]()
 
         def scan(h, a=0, b=128):
             if a == b:
@@ -575,7 +579,7 @@ def rank_program(g, core, T, topo):
                 tt(hv("OF", 1, 2), hv("M", 2, 2), hv("BASE", 1, 2, 2 * li_), A.add), offs[1]()), offs[2]]
         else:
             s_rest()
-            short = offs + weights
+            short = first2[:-1] + [lambda: (first2[-1](), offs[0](), weights[0]()), lambda: (offs[1](), weights[1]()), weights[2]]
         for x, step in enumerate([nop] + short, -1):
             step()
             for _ in range(FILL[t].count(x)):
@@ -590,27 +594,24 @@ def rank_program(g, core, T, topo):
         weave(long_)
         if t > 0:
             op("S", lambda: g.scalar.activation(w("junk")[1](None), T.pU[:, 16:32], F.Identity, accum_out=colap(0)), ["pU"], ["A0"] + w("junk")[3])
-        if VN0F:
-            gather_new(0)
+        gather_new(0)
+        a_step(0)
         usum(1)
         own("1n")
         scan(0)
         tt(iv("D1", 0), nn, hv("M", 2), A.subtract)
         pick_ba(1)
-        send_data(t, 1, "v" if VM == 0 else "nv" if VM == 3 else "")
-        if not VN0F:
-            gather_new(0)
+        send_data(t, 1, "v")
+        a_step(1)
         own("1v", "1w")
         if t > 0:
             t_new(t)
+        a_step(2)
         pick_n(0)
-        if SPLIT0:
-            send_data(t, 0, "n")
-        send_data(t, 1, "v" if VM == 1 else "")
+        send_data(t, 0, "n")
         usum(0)
         pick_ba(0)
-        while seed_next:
-            t_seed(seed_next.pop())
+        a_step(3)
         aff(wq("K2", 0), qv("RES", 1), 200.5, 0.5)
         aff(wq("hK", 0), qv("RES", 0), 100.0)
         if not last:
@@ -624,24 +625,26 @@ def rank_program(g, core, T, topo):
         if t > 0:
             tch, carry = t_chain(t)
         else:
-            tch, carry = first_c(1), nop
+            tch, carry = first_c(1), lambda: (t_b(2), t_b(3))
         tch[0]()
         tt(iv("D1", 1), hv("M", 2), hv("M", 1), A.subtract)
         tch[1]()
         nh = 1 if last else 2
         tt(qv("W", Wn["H"][0], nh), qv("W", Wn["K2"][0], nh), qv("W", Wn["hK"][0], nh), A.subtract)
-        scalar_operands()
-        relu(hv("NF", 0), wq("H", 0), 1.0, -4.0)
-        aff(w("KI", 2), qv("RES", 1, 2), 1.0, 1.0)
         vt(1)
-        if not last:
-            relu(w("f0"), hv("NF", 0), -1.0, 1.0)
+        scalar_operands()
+        val(1)
         aff(hv("MR", 0), pm(2))
         aff(hv("MR", 1), pm(1))
-        val(1)
-        if SO == 0:
-            diff("1n")
-            sums(T.pD1n[:, 256:264], "pD1n", 128, 256, "1n")
+        diff("1n")
+        sums(T.pD1n[:, 256:264], "pD1n", 128, 256, "1n")
+        relu(hv("NF", 0), wq("H", 0), 1.0, -4.0)
+        aff(w("KI", 2), qv("RES", 1, 2), 1.0, 1.0)
+        aff(iv("D1", 2), qv("RES", 3), 1.0, -1.0)
+        if not last:
+            relu(w("f0"), hv("NF", 0), -1.0, 1.0)
+        aff(qv("CAND", 0), qv("RES", 0), 1.0, 1.0)
+        aff(iv("D1", 3), nn, 1.0, 1.0)
         if not last:
             aff(wq("FF", 0), w("f0"), 1.0, 1.0)
             aff(wq("FF", 1), w("f0"), -0.5, 1.0)
@@ -683,18 +686,10 @@ def rank_program(g, core, T, topo):
                 lambda: tt(wi("n2"), w("n1"), wq("H", 1), A.add),
                 lambda: ts(wi("n3"), wi("n2"), 5, A.arith_shift_right, 4095, A.bitwise_and),
             ]
-        weave(uch, [nop, ech[0]])
-        if SO == 1:
-            diff("1n")
-            sums(T.pD1n[:, 256:264], "pD1n", 128, 256, "1n")
+        weave(uch[:1] + tch[2:3] + uch[1:3] + ech[:1] + uch[3:5] + ech[1:2] + uch[5:] + tch[3:4] + uch2[:1] + ech[3:])
         val(0)
-        if VM == 3:
-            diff("1v", "1w")
         carry()
-        weave(tch[2:], uch2[:UA], [ech[1], ech[3]])
-        weave(tail(1), uch2[UA:UB], kch[:KA])
-        if t < 3:
-            t_b(t + 2)
+        weave(tail(1), uch2[1:UB], tch[4:5] + kch[:KA])
         if last:
             dma("Y", T.yx[:, 2048:4096], T.X[:, TB + 2048:TB + 4096], "st0", ["X.1"], [])
         if VM == 0 and V1F:
@@ -718,21 +713,24 @@ def rank_program(g, core, T, topo):
             diff("0v", "0w")
         if 0 < t < 4:
             t_seed(t + 1)
+        if t == 0:
+            t_b(4)
         if last:
             t_new(6)
         if t == 1:
             aff(raw(T.TP[:], "TP"), raw(T.J128[:], "J128"), 1.0 / 8192)
         sums(T.pS[:, 0:2, :], "pS", 256, 1280, "0v", "1v", "0w", "1w")
-        weave(tail(0), kch[KA:] + uch2[UB:])
+        weave(tail(0), kch[KA:], uch2[UB:])
 
     dma("Y", T.yx[:, 0:2048], T.X[:, TB:TB + 2048], "st1", ["X.0"], [])
     tch, carry = t_chain(6)
     tt(qv("SIG"), qv("PNP", 2 * RO), nok, A.subtract)
     ps = post(RO - 1)
-    weave(ps[:5], [tch[0], nop0, lambda: (tch[1](), carry(), dma("S", T.yt[:], T.YT[:], "st3", ["YT"], []))])
+    tch[0]()
+    weave(ps[:5], [lambda: (tch[1](), carry(), dma("S", T.yt[:], T.YT[:], "st3", ["YT"], []))])
     ps[5]()
     cp(raw(T.YS[:, 0, :], "YS0"), nn)
-    ts(raw(T.YS[:, 1, :], "YS1"), qv("RES", 0), 1.0, A.add)
+    aff(raw(T.YS[:, 1, :], "YS1"), qv("RES", 0), 1.0, 1.0)
     for h in (0, 1):
         cp(raw(T.YS[:, 2:4, 8 * h:8 * h + 8], "YS%d" % (2 + h)), raw(T.RES[:, 80 + 16 * h:96 + 16 * h], "RES.5", "RES.6"))
     dma("Y", T.yst[:], T.YS[:], "st2", ["YS0", "YS1", "YS2", "YS3"], [])

@@ -13,50 +13,50 @@ for _l in LSU:
     _o += 256 * _l
 VTOT = _o
 RW = 1920
+PA = RW + 128
 TB = 4096
-MULTI = True
-VM, SPLIT0, SO, V1F, VN0F = 0, 1, 0, 0, 1
-E0F = 0
-FV, FS = [0] * 6, [0] * 6
-NV0 = [2, 2, 3, 3, 4, 4]
-NV1 = [5, 4, 4, 5, 5, 6]
-FILL = [(0, 1, 2, 3, 4, 5, 6, 7)] + [tuple(range(min(n, 5))) + (4,) * max(n - 5, 0) + (6, 8, 9) for n in NV1[1:]]
-KA, UA, UB, PRE = 3, 3, 5, 1
-MAGIC = 12582912.0
+E = 16
+NV = [4, 3, 3, 3, 4, 4]
+NS = [3, 3, 4, 4, 4, 5]
+NH = [0, 0, 0, 0, 0, 0]
+VMAX = (0, 0)
+CYC, PCYC, GATHER, SCATTER, VMIN, SMIN, PMIN = 0.84, 0.42, 1.2, 4.0, 45, 64, 48
+SAME, CROSS, PSUM, WAKE, ISSUE, REMOTE, FIRST, LOAD = 200, 250, 300, 100, 100, 1200, 1500, 4500
+PASSES, WIDE = 6, 8
+PLAN = []
 
-f32, bf, i32, u16 = "float32", "bfloat16", "int32", "uint16"
+f32, bf, f16, i32, u16 = "float32", "bfloat16", "float16", "int32", "uint16"
 SCRATCH = {
     "X": ("sbuf", [128, 12288], bf), "V": ("sbuf", [128, VTOT], bf), "ZR": ("sbuf", [128, RW], bf),
-    "AH": ("sbuf", [128, 2, 32], f32), "C": ("sbuf", [128, 2, 16], f32), "NF": ("sbuf", [128, 2, 16], f32),
-    "MR": ("sbuf", [128, 2, 16], f32), "D0F": ("sbuf", [128, 768], f32), "wj": ("sbuf", [128, 4], i32),
-    "RP0": ("sbuf", [128, RW + 384], bf), "RP1": ("sbuf", [128, RW + 384], bf),
-    "Q": ("sbuf", [128, 2 * RO * 384], bf), "DA": ("sbuf", [128, 1280], bf),
-    "VN": ("sbuf", [128, 256], bf), "VT": ("sbuf", [128, 256], bf), "VAL": ("sbuf", [128, 256], bf),
+    "RP": ("sbuf", [128, 2, RW + 384], bf), "Q": ("sbuf", [128, 2 * RO, 384], bf),
+    "DN": ("sbuf", [128, 2, 128], bf), "DV": ("sbuf", [128, 1024], bf),
+    "VN": ("sbuf", [128, 256], bf), "VT": ("sbuf", [128, 256], bf), "M192": ("sbuf", [128, 128], bf),
     "tri": ("sbuf", [128, 256], i32), "sdi": ("sbuf", [128, 96], i32), "ni": ("sbuf", [128, 16], i32),
-    "ki": ("sbuf", [128, 16], i32), "thi": ("sbuf", [128, 16], i32), "wi": ("sbuf", [128, 4], i32),
-    "TP": ("sbuf", [128, 256], f32), "S32": ("sbuf", [128, 96], f32), "B0": ("sbuf", [128, 96], f32),
-    "I96": ("sbuf", [128, 96], i32), "I96b": ("sbuf", [128, 96], i32),
-    "J128": ("sbuf", [128, 256], f32), "J1184": ("sbuf", [128, 256], f32),
-    "D0T": ("sbuf", [128, 1024], f32), "D1T": ("sbuf", [128, 6 * 1024], f32), "OT": ("sbuf", [128, 1024], f32),
-    "NI": ("sbuf", [128, 256], i32), "NJ": ("sbuf", [128, 256], i32), "N1": ("sbuf", [128, 256], f32), "N2": ("sbuf", [128, 256], f32),
-    "CT": ("sbuf", [128, 512], u16), "BC": ("sbuf", [128, 16], u16), "BC4": ("sbuf", [128, 8], u16),
-    "OFU": ("sbuf", [128, 2, 24], u16), "OAU": ("sbuf", [128, 16], u16), "SOU": ("sbuf", [128, 16], u16), "VOU": ("sbuf", [128, 16], u16),
-    "M": ("sbuf", [128, 2, 32], f32), "PM": ("sbuf", [128, 2 * RO, 24], f32), "E": ("sbuf", [128, 2, 40], f32),
-    "LIM": ("sbuf", [128, 2, 40], f32), "LP": ("sbuf", [128, 2, 40], f32), "TH4": ("sbuf", [128, 2, 40], f32),
-    "OF": ("sbuf", [128, 2, 24], f32), "BASE": ("sbuf", [128, 2 * len(LSU), 24], f32), "PNP": ("sbuf", [128, 32 * (RO + 1)], f32),
-    "D0": ("sbuf", [128, 64], f32), "D1": ("sbuf", [128, 64], f32), "D1R": ("sbuf", [128, 64], f32),
-    "ON": ("sbuf", [128, 64], f32), "NR": ("sbuf", [128, 64], f32),
-    "RES": ("sbuf", [128, 128], f32), "CAND": ("sbuf", [128, 128], f32),
-    "W": ("sbuf", [128, 16 * 48], f32), "WI": ("sbuf", [128, 16 * 16], i32),
-    "SIG": ("sbuf", [128, 32], f32), "NP": ("sbuf", [128, 32], f32),
+    "ki": ("sbuf", [128, 16], i32), "thi": ("sbuf", [128, 16], i32), "wi": ("sbuf", [128, 4], i32), "wj": ("sbuf", [128, 4], i32),
+    "TP": ("sbuf", [128, 256], f16), "TN": ("sbuf", [128, 2, 256], f16), "SR": ("sbuf", [128, RO, 64], f16),
+    "JJ": ("sbuf", [128, 256], f32), "J1184": ("sbuf", [128, 256], f16), "C2080": ("sbuf", [128, 256], f16), "C2048": ("sbuf", [128, 256], f16),
+    "MK": ("sbuf", [128, 256], f32), "WW": ("sbuf", [128, 256], f32), "Y0": ("sbuf", [128, 256], f32),
+    "NI": ("sbuf", [128, 256], i32), "NJ": ("sbuf", [128, 256], i32),
+    "CT": ("sbuf", [128, 512], u16), "BC": ("sbuf", [128, 16], u16), "BR": ("sbuf", [128, 8], u16), "BY": ("sbuf", [128, 4], u16),
+    "BV": ("sbuf", [128, 2], u16), "OFU": ("sbuf", [128, 2, 16], u16), "OFN": ("sbuf", [128, 16], u16),
+    "SOU": ("sbuf", [128, 16], u16), "VOU": ("sbuf", [128, 16], u16),
+    "OC": ("sbuf", [128, 2 * RO, 16], f16), "OL": ("sbuf", [128, 2 * RO, 16], f32),
+    "TH": ("sbuf", [128, 80], bf), "AH": ("sbuf", [128, 64], bf), "LIM": ("sbuf", [128, 64], f32), "ONES": ("sbuf", [128, 32], bf),
+    "SC": ("sbuf", [128, 48 * E], bf), "D1": ("sbuf", [128, 16 * E], bf), "D1R": ("sbuf", [128, 16 * E], bf),
+    "CA": ("sbuf", [128, 128], f32), "RES": ("sbuf", [128, 128], f16),
+    "M": ("sbuf", [128, 80], bf), "QM": ("sbuf", [128, 2 * RO, 80], bf), "DL": ("sbuf", [128, 96], bf),
+    "H2": ("sbuf", [128, 32], f32), "NF2": ("sbuf", [128, 32], f32), "VC": ("sbuf", [128, 32], f32), "VV": ("sbuf", [128, 32], bf),
+    "ND": ("sbuf", [128, 32], f32), "SIG": ("sbuf", [128, 16], f32), "FL": ("sbuf", [128, 16], f16),
+    "W": ("sbuf", [128, 16 * 40], f32), "WI": ("sbuf", [128, 16 * 16], i32),
     "PI": ("sbuf", [128, 16], i32), "PC": ("sbuf", [128, 16], f32), "XR": ("sbuf", [128, 144], f32),
-    "Z": ("sbuf", [128, 144], bf), "ZW": ("sbuf", [128, 144], "float16"),
-    "ID": ("sbuf", [128, 128], bf), "NID": ("sbuf", [128, 128], bf),
-    "ONE": ("sbuf", [128, 128], f32), "NONE": ("sbuf", [128, 128], f32),
-    "YT": ("sbuf", [128, 256], f32), "YS": ("sbuf", [128, 4, 16], f32),
-    "pU": ("psum", [128, 512], f32), "pD0w": ("psum", [128, 512], f32), "pD1w": ("psum", [128, 512], f32),
-    "pD0n": ("psum", [128, 512], f32), "pD1n": ("psum", [128, 512], f32),
-    "pD0v": ("psum", [128, 512], f32), "pD1v": ("psum", [128, 512], f32), "pS": ("psum", [128, 16, 32], f32),
+    "Z": ("sbuf", [128, 144], bf), "Z2": ("sbuf", [128, 144], bf), "NZ": ("sbuf", [128, 144], bf), "ZW": ("sbuf", [128, 144], f16),
+    "ID": ("sbuf", [128, 128], bf), "NID": ("sbuf", [128, 128], bf), "IB": ("sbuf", [128, 128], bf),
+    "I2080": ("sbuf", [128, 128], bf), "I1184": ("sbuf", [128, 128], bf),
+    "ONEQ": ("sbuf", [128, 128], bf), "NONE": ("sbuf", [128, 128], bf),
+    "YT": ("sbuf", [128, 256], f32), "YS": ("sbuf", [128, 64], f32),
+    "pN": ("psum", [128, 512], f32), "pV0": ("psum", [128, 8, 4, 16], f32), "pV1": ("psum", [128, 8, 4, 16], f32),
+    "pS": ("psum", [128, 512], f32), "pU": ("psum", [128, 512], f32),
+    "pT": ("psum", [128, 512], f32), "pY": ("psum", [128, 512], f32), "pK": ("psum", [128, 2, 256], f32),
 }
 SEMAPHORES = (["cV", "cS", "cP", "cG"] + ["ld%d" % i for i in range(8)] + ["st%d" % i for i in range(4)]
               + ["ml%d" % t for t in range(RO)] + ["ma%d" % t for t in range(RO)]
@@ -69,670 +69,605 @@ def rank_program(g, core, T, topo):
         return
     Q = {"V": g.vector, "S": g.scalar, "P": g.tensor, "G": g, "Y": g.sync}
     CS = {"V": "cV", "S": "cS", "P": "cP", "G": "cG"}
-    cnt = {}
-    know = {e: {} for e in Q}
-    snap = {}
-    lastw, readers = {}, {}
+    nodes, lastw, readers, chain = [], {}, {}, {}
 
-    def need(e, tok):
-        s, c = tok
-        if know[e].get(s, 0) >= c:
-            return
-        Q[e].wait_ge(T.sem[s], c)
-        know[e][s] = c
-        for s2, c2 in snap.get(tok, {}).items():
-            if know[e].get(s2, 0) < c2:
-                know[e][s2] = c2
-
-    def op(e, fn, rd, wr, sem=None, inc=1, auto=False, after=()):
-        deps = list(after)
+    def op(e, fn, args, kw, rd, wr, cost, done=None, sem=None, inc=1, auto=False, row=None):
+        deps = set()
         for k in rd:
-            if k in lastw:
-                deps.append(lastw[k])
+            deps.add(lastw[k])
             if k[0] == "p":
-                deps += [x for x in readers.get(k, []) if x[0] != CS.get(e)]
+                deps.update(x for x in readers.get(k, []) if nodes[x]["e"] != e)
         for k in wr:
             if k in lastw:
-                deps.append(lastw[k])
-            deps += readers.get(k, [])
-        best = {}
-        for s, c in deps:
-            if e == "P" and s == "cP":
-                continue
-            best[s] = max(best.get(s, 0), c)
-        for s, c in best.items():
-            need(e, (s, c))
-        s = sem or CS[e]
-        ins = fn()
-        if not auto:
-            ins.then_inc(T.sem[s], inc)
-        cnt[s] = cnt.get(s, 0) + inc
-        tok = (s, cnt[s])
-        snap[tok] = dict(know[e])
+                deps.add(lastw[k])
+            deps.update(readers.get(k, []))
+        i = len(nodes)
+        nodes.append(dict(e=e, fn=fn, args=args, kw=kw, deps=sorted(deps), cost=cost, done=cost if done is None else done,
+                          sem=sem or CS.get(e), inc=inc, auto=auto, after=chain.get(row)))
+        if row:
+            chain[row] = i
         for k in rd:
-            readers.setdefault(k, []).append(tok)
+            readers.setdefault(k, []).append(i)
         for k in wr:
-            lastw[k] = tok
+            lastw[k] = i
             readers[k] = []
-        return tok
 
-    def qv(name, q=0, n=1):
-        return ("%s.%d" % (name, q), lambda h: T[name][:, 16 * q:16 * (q + n)] if h is None else T[name][:, 16 * q + 8 * h:16 * q + 8 * h + 8], 0,
-                ["%s.%d" % (name, q + x) for x in range(n)])
+    def order():
+        n = len(nodes)
+        cost = [x["cost"] for x in nodes]
+        succ, back = [[] for _ in range(n)], [[] for _ in range(n)]
+        for i, x in enumerate(nodes):
+            pre = []
+            for d in x["deps"]:
+                y = nodes[d]
+                if y["e"] == x["e"] == "P" or x["e"] == "A":
+                    lag = 0
+                elif y["done"] != y["cost"] or y["e"] == "A":
+                    lag = WAKE
+                else:
+                    lag = SAME if y["e"] == x["e"] else PSUM if y["e"] == "P" else CROSS
+                pre.append((d, y["done"] + lag))
+            if x["after"] is not None:
+                pre.append((x["after"], cost[x["after"]]))
+            for d, lag in pre:
+                succ[d].append((i, lag))
+                back[i].append((d, lag + cost[i] - cost[d]))
+        left = [0.0] * n
+        for i in range(n - 1, -1, -1):
+            left[i] = max([nodes[i]["done"]] + [lag + left[j] for j, lag in succ[i]])
 
-    def iv(name, s):
-        return (None, lambda h: T[name][:, s::4] if h is None else T[name][:, 32 * h + s:32 * h + 32:4], 0, ["%s.%d" % (name, s)])
+        def counts(nxt):
+            todo = [0] * n
+            for i in range(n):
+                for j, _ in nxt[i]:
+                    todo[j] += 1
+            return todo
 
-    def hv(name, q, n=1, r=0):
-        return (None, lambda h: T[name][:, r:r + 2, 8 * q:8 * (q + n)] if h is None else T[name][:, r + h, 8 * q:8 * (q + n)], 1,
-                ["%s.%d.%d" % (name, r, q + x) for x in range(n)])
+        def place(nxt, ready, left):
+            ready, todo = list(ready), counts(nxt)
+            pool = sorted((-left[i], i) for i in range(n) if not todo[i])
+            busy = {e: [] for e in "VSPGYA"}
+            start = [0.0] * n
+            while pool:
+                i = pool.pop(0)[1]
+                b, s0 = busy[nodes[i]["e"]], ready[i]
+                k = len(b)
+                while k and b[k - 1][1] > s0:
+                    k -= 1
+                while k < len(b) and b[k][0] < s0 + cost[i]:
+                    s0 = max(s0, b[k][1])
+                    k += 1
+                b.insert(k, (s0, s0 + cost[i]))
+                start[i] = s0
+                new = []
+                for j, lag in nxt[i]:
+                    ready[j] = max(ready[j], s0 + lag)
+                    todo[j] -= 1
+                    if not todo[j]:
+                        new.append((-left[j], j))
+                if new:
+                    pool = sorted(pool + new)
+            return start
 
-    def halves(vs, h):
-        if h is not None:
-            return [h]
-        kinds = set(v[2] for v in vs)
-        return [None] if (MULTI or len(kinds) == 1) else [1, 0]
+        def follow(nxt, ready, left):
+            ready, todo = list(ready), counts(nxt)
+            pool = {e: [i for i in range(n) if nodes[i]["e"] == e and not todo[i]] for e in "VSPGYA"}
+            free = {e: 0.0 for e in pool}
+            start, pick = [0.0] * n, {}
+            for _ in range(n):
+                for e, c in pool.items():
+                    if e not in pick and c:
+                        c.sort(key=lambda i: -left[i])
+                        top = c[:WIDE] + [min(c, key=lambda i: ready[i])]
+                        pick[e] = min((max([max(free[e], ready[i]) + left[i]]
+                                           + [max(max(free[e], ready[i]) + cost[i], ready[j]) + left[j] for j in top if j != i]),
+                                       max(free[e], ready[i]), -left[i], i) for i in top)
+                e = min(pick, key=lambda e: pick[e][1])
+                _, s0, _, i = pick.pop(e)
+                pool[e].remove(i)
+                start[i], free[e] = s0, s0 + cost[i]
+                for j, lag in nxt[i]:
+                    ready[j] = max(ready[j], s0 + lag)
+                    todo[j] -= 1
+                    if not todo[j]:
+                        pool[nodes[j]["e"]].append(j)
+                        pick.pop(nodes[j]["e"], None)
+            return start
 
-    def tt(o, a, b, alu, h=None, extra=()):
-        for x in halves([o, a, b], h):
-            op("V", lambda: g.vector.tensor_tensor(o[1](x), a[1](x), b[1](x), alu), a[3] + b[3] + list(extra), o[3])
+        best = None
+        tail = [nodes[i]["done"] - cost[i] for i in range(n)]
+        for x in range(PASSES):
+            way = follow if x % 2 else place
+            start = way(succ, [0.0] * n, left)
+            end = max(start[i] + nodes[i]["done"] for i in range(n))
+            if best is None or end < best[0]:
+                best = (end, start)
+            late = way(back, tail, [best[1][i] + cost[i] for i in range(n)])
+            left = [late[i] + cost[i] for i in range(n)]
+        PLAN.append(best[0])
+        return sorted(range(n), key=lambda i: (best[1][i], i))
 
-    def ts(o, a, s1, op0, s2=None, op1=None, h=None, extra=()):
-        for x in halves([o, a], h):
-            if op1 is None:
-                op("V", lambda: g.vector.tensor_scalar(o[1](x), a[1](x), s1, None, op0), a[3] + list(extra), o[3])
-            else:
-                op("V", lambda: g.vector.tensor_scalar(o[1](x), a[1](x), s1, s2, op0, op1), a[3] + list(extra), o[3])
+    def emit():
+        cnt = {}
+        know = {e: {} for e in Q}
+        snap = {}
 
-    def cp(o, a, h=None):
-        for x in halves([o, a], h):
-            op("V", lambda: g.vector.tensor_copy(o[1](x), a[1](x)), a[3], o[3])
+        def need(e, s, c):
+            if know[e].get(s, 0) >= c:
+                return
+            Q[e].wait_ge(T.sem[s], c)
+            know[e][s] = c
+            for s2, c2 in snap.get((s, c), {}).items():
+                if know[e].get(s2, 0) < c2:
+                    know[e][s2] = c2
 
-    def aff(o, a, scale=1.0, bias=0.0, h=None, extra=()):
-        for x in halves([o, a], h):
-            op("S", lambda: g.scalar.activation(o[1](x), a[1](x), F.Identity, bias=bias, scale=scale), a[3] + list(extra), o[3])
+        for i in order():
+            x = nodes[i]
+            e, s = x["e"], x["sem"]
+            cnt[s] = cnt.get(s, 0) + x["inc"]
+            x["tok"] = (s, cnt[s])
+            if e == "A":
+                continue
+            best = {}
+            for d in x["deps"]:
+                s2, c2 = nodes[d]["tok"]
+                if not (e == "P" and s2 == "cP"):
+                    best[s2] = max(best.get(s2, 0), c2)
+            for s2, c2 in best.items():
+                need(e, s2, c2)
+            ins = x["fn"](*x["args"], **x["kw"])
+            if not x["auto"]:
+                ins.then_inc(T.sem[s], x["inc"])
+            snap[x["tok"]] = dict(know[e])
+        for s, c in cnt.items():
+            need("G", s, c)
 
-    def raw(ap, *keys):
-        return (None, lambda h: ap, 0, list(keys))
+    def R(ap, *keys):
+        n = 1
+        for x in ap.shape[1:]:
+            n *= x
+        return (ap, list(keys), n, "16" in str(ap.dtype), False)
 
-    def memset(ap, c, *keys):
-        op("V", lambda: g.vector.memset(ap, c), [], list(keys))
+    def IX(win, offs, *keys):
+        return (win.indirect(offs), list(keys), 16 * offs.shape[1], False, True)
 
-    def iota(ap, pat, base, cm, key, fl=True):
-        if fl:
-            op("G", lambda: g.iota(ap, pat, base, cm, allow_small_or_imprecise_dtypes=True), [], [key])
-        else:
-            op("G", lambda: g.iota(ap, pat, base, cm), [], [key])
+    def span(e, o, ins, per=None):
+        if o[4]:
+            return 50 + o[2] * SCATTER * CYC
+        if any(a[4] for a in ins):
+            return (50 if e == "V" else 65) + o[2] * GATHER * CYC
+        if per is None:
+            per = 0.5 if e == "V" and o[3] and all(a[3] for a in ins) else 1
+        return max(VMIN if e == "V" else SMIN, o[2] * per) * CYC
 
-    def dma(e, out, in_, sem, rd, wr):
-        return op(e, lambda: Q[e].dma_start(out, in_), rd, wr, sem=sem, inc=16)
+    def tt(o, a, b, alu):
+        per = 1 if a[1][0][0] == "p" or b[1][0][0] == "p" else 2
+        op("V", g.vector.tensor_tensor, (o[0], a[0], b[0], alu), {}, a[1] + b[1], o[1], span("V", o, [a, b], per))
 
-    Wn = {}
+    def ts(o, a, s1, op0, s2=None, op1=None, extra=()):
+        op("V", g.vector.tensor_scalar, (o[0], a[0], s1, s2, op0) + ((op1,) if op1 is not None else ()), {}, a[1] + list(extra), o[1], span("V", o, [a]))
 
-    def w(name, n=1):
+    def cp(o, a):
+        op("V", g.vector.tensor_copy, (o[0], a[0]), {}, a[1], o[1], span("V", o, [a]))
+
+    def scan(o, a, b, op0, op1):
+        op("V", g.vector.tensor_tensor_scan, (o[0], a[0], b[0], 0.0, op0, op1), {}, a[1] + b[1], o[1], span("V", o, [a, b]))
+
+    def act(o, a, fn, scale=1.0, bias=0.0, extra=(), accum=None):
+        kw = dict(bias=bias, scale=scale)
+        if accum:
+            kw["accum_out"] = accum[0]
+        op("S", g.scalar.activation, (o[0], a[0], fn), kw, a[1] + list(extra), o[1] + (accum[1] if accum else []), span("S", o, [a]))
+
+    def aff(o, a, scale=1.0, bias=0.0, extra=()):
+        act(o, a, F.Identity, scale, bias, extra)
+
+    def scp(o, a):
+        op("S", g.scalar.activation, (o[0], a[0], F.Copy), {}, a[1], o[1], span("S", o, [a]))
+
+    def memset(o, c):
+        op("V", g.vector.memset, (o[0], c), {}, [], o[1], span("V", o, []))
+
+    def iota(o, pat, base=0, cm=0, fl=True):
+        op("G", g.iota, (o[0], pat, base, cm), dict(allow_small_or_imprecise_dtypes=True) if fl else {}, [], o[1], 130 + 2 * CYC * o[2])
+
+    def dma(e, out, in_, sem, rd, wr, done):
+        op(e, Q[e].dma_start, (out, in_), {}, rd, wr, 60, done, sem=sem, inc=16, row="dma" + e)
+
+    def mm(o, l, r, start=False, stop=False):
+        op("P", g.tensor.matmul, (o[0], l[0], r[0], start, stop), {}, l[1] + r[1], o[1], max(PMIN, r[2]) * PCYC)
+
+    def whole(name):
+        return R(T[name][:], name)
+
+    Wn, WIn = {}, {}
+
+    def w(name, n=1, q=0, h=None):
         if name not in Wn:
             Wn[name] = sum(v[1] for v in Wn.values()), n
-        return qv("W", Wn[name][0], n)
+        c = Wn[name][0] + q
+        if h is not None:
+            return R(T.W[:, 16 * c + 8 * h:16 * c + 8 * h + 8], "W.%d" % c)
+        return R(T.W[:, 16 * c:16 * (c + n)], *["W.%d" % (c + x) for x in range(n)])
 
-    def wq(name, q):
-        return qv("W", Wn[name][0] + q, 1)
+    def wi(name, n=16):
+        c = WIn.setdefault(name, len(WIn))
+        return R(T.WI[:, 16 * c:16 * c + n], "WI.%d" % c)
 
-    WIn = {}
+    w("col")
 
-    def wi(name):
-        WIn.setdefault(name, len(WIn))
-        return qv("WI", WIn[name])
+    def col(i):
+        return R(T.W[:, i:i + 1], "c%d" % i)
+
+    def me(q, n=1):
+        return R(T.M[:, 16 * q:16 * (q + n)], *["ME%d" % x for x in range(q, q + n)])
+
+    D0, NR, ON = 0, 16 * E, 32 * E
+    D0K = ["D0.%d" % e for e in range(E)]
+    D1K = ["D1.%d" % e for e in range(E)]
+
+    def sc(base, e, h=None, step=E):
+        a, b = (0, 16 * E) if h is None else (8 * E * h, 8 * E * (h + 1))
+        return R(T.SC[:, base + a + e:base + b:step], *(["SC%d" % base] if base else D0K[e::step]))
+
+    def d1(e, h=None):
+        a, b = (0, 16 * E) if h is None else (8 * E * h, 8 * E * (h + 1))
+        return R(T.D1[:, a + e:b:E], D1K[e])
+
+    def tile(name, q, n=1):
+        return R(T[name][:, 16 * q:16 * (q + n)], *["%s.%d" % (name, x) for x in range(q, q + n)])
 
     part = [T.cores[rank ^ 1], T.cores[rank ^ 2]]
-    RP = [T.RP0, T.RP1]
     XK = ["X.0", "X.1"]
-    nn, nok = iv("ON", 3), iv("D0", 3)
+    nok4 = sc(D0, 14)
+    ID, NID, IB = whole("ID"), whole("NID"), whole("IB")
 
-    def send_meta(t):
-        trs = []
-        tot = 0
+    def send(t, h, p):
+        rid, pid, _ = topo.addr(part[h])
+        ne = len(topo.engines(core, part[h]))
+        i = 4 * t + (2 if p == "v" else 0) + h
+        a, b = (0, 128) if p == "n" else (128, 384)
+        op("G", g.remote_dma, (T.Q[:, 2 * t + h, a:b], T.RP[:, h, RW + a:RW + b], T.sem["da%d" % i], T.sem["dl%d" % i], pid, rid, topo.mask(core, part[h])), {},
+           ["Pn%d" % h] if p == "n" else ["PA%d" % h], ["sent%d" % i], ISSUE, REMOTE, sem="dl%d" % i, inc=ne, auto=True)
+        op("A", None, (), {}, ["sent%d" % i], ["Q%d%d%s" % (t, h, p)], 0, sem="da%d" % i, inc=ne)
+
+    def send_lengths(t):
+        trs, tot = [], 0
         for h in (0, 1):
             rid, pid, _ = topo.addr(part[h])
             en = topo.engines(core, part[h])
             en = en[:len(en) // 2] if h == 0 else en[len(en) // 2:]
             tot += len(en)
             trs.append(RemoteDMATransfer(dst_ids=[DstId(rid=rid, pnc=pid)], dma_engine_mask=sum(1 << x for x in en),
-                                         remote_sem=T.sem["ma%d" % t], src=T.M[:, h, 0:24], dst=T.PM[:, 2 * t + h, :]))
-        op("G", lambda: g.remote_dma_fused(trs, local_sem=T.sem["ml%d" % t]), hv("M", 0, 3)[3], [], sem="ml%d" % t, inc=tot, auto=True)
-        for k in hv("PM", 0, 3, 2 * t)[3]:
-            lastw[k] = ("ma%d" % t, tot)
-        cnt["ma%d" % t] = tot
+                                         remote_sem=T.sem["ma%d" % t], src=me(0, 4)[0], dst=T.QM[:, 2 * t + h, 8 - 8 * h:72 - 8 * h]))
+        late = FIRST if t == 0 else 0
+        op("G", g.remote_dma_fused, (trs,), dict(local_sem=T.sem["ml%d" % t]), me(0, 4)[1], ["sentm%d" % t], ISSUE + late, REMOTE + late,
+           sem="ml%d" % t, inc=tot, auto=True)
+        op("A", None, (), {}, ["sentm%d" % t], ["Q%dm" % t], 0, sem="ma%d" % t, inc=tot)
 
-    def send_points(t):
-        trs, tot, i = [], 0, 4 * t + 2
-        for h in (0, 1):
-            rid, pid, _ = topo.addr(part[h])
-            en = topo.engines(core, part[h])
-            en = en[:len(en) // 2] if h == 0 else en[len(en) // 2:]
-            tot += len(en)
-            o = (2 * t + h) * 384
-            trs.append(RemoteDMATransfer(dst_ids=[DstId(rid=rid, pnc=pid)], dma_engine_mask=sum(1 << x for x in en), remote_sem=T.sem["da%d" % i],
-                                         src=RP[h][:, RW + 128:RW + 384], dst=T.Q[:, o + 128:o + 384]))
-        op("G", lambda: g.remote_dma_fused(trs, local_sem=T.sem["dl%d" % i]), ["PA0", "PB0", "PA1", "PB1"], [], sem="dl%d" % i, inc=tot, auto=True)
-        for h in (0, 1):
-            lastw["Q%d%dv" % (t, h)] = ("da%d" % i, tot)
-        cnt["da%d" % i] = tot
+    dma("S", T.sdi[:], T.sd[:], "ld2", [], ["sdi"], 2200)
+    dma("Y", T.tri[:], T.tr[:], "ld3", [], ["tri"], 2600)
+    dma("S", T.ki[:], T.k0[:], "ld1", [], ["ki"], 2300)
+    dma("Y", T.ni[:], T.n0[:], "ld0", [], ["ni"], 3000)
+    dma("Y", T.X[:, TB:TB + 4096], T.xt[:], "ld4", [], XK, LOAD)
+    dma("S", T.wi[:, 0:1], T.wt[:], "ld6", [], ["wi0"], LOAD + 200)
+    dma("S", T.thi[:], T.th[:], "ld5", [], ["thi"], LOAD + 200)
 
-    def send_data(t, h, p):
-        if not p:
-            return
-        rid, pid, _ = topo.addr(part[h])
-        ne = len(topo.engines(core, part[h]))
-        i = 4 * t + (2 if p == "v" else 0) + h
-        a, b = (0 if "n" in p else 128), (384 if "v" in p else 128)
-        o = (2 * t + h) * 384
-        op("G", lambda: g.remote_dma(T.Q[:, o + a:o + b], RP[h][:, RW + a:RW + b], T.sem["da%d" % i], T.sem["dl%d" % i],
-                                     pid, rid, topo.mask(core, part[h])),
-           (["Pn%d" % h] if "n" in p else []) + (["PA%d" % h, "PB%d" % h] if "v" in p else []), [], sem="dl%d" % i, inc=ne, auto=True)
-        for x in p:
-            lastw["Q%d%d%s" % (t, h, x)] = ("da%d" % i, ne)
-        cnt["da%d" % i] = ne
+    iota(whole("PI"), [[0, 16]], 0, 1, fl=False)
+    iota(whole("XR"), [[1, 144]])
+    iota(whole("PC"), [[0, 2], [16, 8]])
+    iota(whole("JJ"), [[1, 16], [0, 16]])
+    iota(whole("ONEQ"), [[0, 128]], 1)
+    iota(whole("NONE"), [[0, 128]], -1)
+    for l in LSU[1:]:
+        iota(R(T.V[:, VOFF[l]:VOFF[l] + 256 * l:l], "Vz%d" % l), [[0, 256]], -256)
+    memset(R(T.V[:, VOFF[LSU[0]]:VOFF[LSU[0]] + 256 * LSU[0]:LSU[0]], "Vz%d" % LSU[0]), -256.0)
+    for name, c in (("C2080", 2080.0), ("ZR", 0.0), ("C2048", 2048.0), ("M192", -192.0), ("D1R", 0.0), ("ONES", 1.0), ("VV", 0.0), ("OL", 0.0)):
+        memset(whole(name), c)
+    memset(R(T.X[:, TB + 4096:TB + 4112], "Xz"), 0.0)
+    memset(col(9), 0.0)
+    PI1 = R(T.PI[:, 0:1], "PI")
+    cp(col(0), PI1)
+    ts(wi("a"), whole("PI"), 15, A.bitwise_and)
+    ts(R(T.wj[:, 0:1], "wj0"), PI1, 112, A.bitwise_and)
+    for name, c in (("ID", 1.0), ("I2080", 2080.0), ("NID", -1.0), ("IB", 512.0), ("I1184", 1184.0)):
+        ts(whole(name), R(T.XR[:, :128], "XR"), col(0)[0], A.is_equal, c, A.mult, extra=["c0"])
+    ts(col(1), R(T.wj[:, 0:1], "wj0"), 15.0, A.add)
+    for name, c in (("Z", 1.0), ("Z2", 2.0), ("NZ", -1.0)):
+        ts(whole(name), whole("XR"), col(1)[0], A.is_equal, c, A.mult, extra=["c1"])
+    tt(w("li"), whole("PC"), wi("a"), A.add)
+    cp(whole("BC"), wi("a"))
+    aff(whole("J1184"), whole("JJ"), 1184.0)
+    aff(whole("ONEQ"), whole("ONEQ"), 1.0 / 4096)
+    oc = lambda t, q: R(T.OC[:, 2 * t:2 * t + 2, 8 * q:8 * q + 8], "OC%d.%d" % (t, q))
+    base = lambda t: R(T.OL[:, 2 * t:2 * t + 2, 8:16], "OL%d" % t)
+    for t in range(RO):
+        l = float(LS[t])
+        aff(oc(t, 0), w("li"), *((l, 0.0) if t == 0 else (1.0, 128 * l - 1)))
+        aff(oc(t, 1), w("li"), l, -1.0)
+        aff(base(t), w("li"), l, extra=["OL"])
+    aff(w("ci", h=0), w("li", h=0), 16.0, 4096.0)
+    aff(w("ci", h=1), w("li", h=1), 16.0)
 
-    dma("S", T.sdi[:], T.sd[:], "ld2", [], ["sdi"])
-    dma("Y", T.tri[:], T.tr[:], "ld3", [], ["tri"])
-    dma("S", T.ki[:], T.k0[:], "ld1", [], ["ki.0"])
-    dma("Y", T.X[:, TB:TB + 4096], T.xt[:], "ld4", [], XK)
-    dma("S", T.ni[:], T.n0[:], "ld0", [], ["ni.0"])
-    dma("Y", T.wi[:, 0:1], T.wt[:], "ld6", [], ["wi0"])
-    dma("Y", T.thi[:], T.th[:], "ld5", [], ["thi.0"])
+    ts(wi("a2"), wi("a"), 1, A.arith_shift_right)
+    memset(R(T.SC[:, 0:16 * E], *D0K), 1.0)
+    memset(R(T.D1[:], *D1K), 0.0)
+    memset(tile("CA", 0), 0.0)
+    memset(sc(D0, 0), 0.0)
+    memset(sc(D0, 6), 1.0 / 4096)
+    memset(R(T.D1R[:, 0::E], "D1R"), 1.0)
+    for h in (0, 1):
+        ts(R(T.BV[:, h:h + 1], "BV%d" % h), wi("a2", 1), float(E), A.mult, NR + 14.0 + 8 * E * h, A.add)
+    ts(R(T.BR[:, 0:6], "BR0"), wi("a", 6), float(E), A.mult, NR + 14.0, A.add)
+    ts(R(T.BR[:, 6:8], "BR6"), wi("a", 2), float(E), A.mult, D0 + 14.0, A.add)
+    ts(R(T.BY[:], "BY"), wi("a", 4), float(E), A.mult, ON + 15.0, A.add)
+    memset(R(T.BY[:, 1:2], "BY"), D0 + 2)
+    WT = R(T.wi[:, 0:1], "wi0")
+    ts(col(6), WT, 2048.0, A.is_ge, -4096.0, A.mult)
+    tt(col(7), col(6), WT, A.add)
+    ts(whole("ZW"), whole("XR"), col(1)[0], A.is_equal, col(7)[0], A.mult, extra=["c1", "c7"])
+    aff(R(T.TH[:, 0:16], "TH"), whole("thi"))
+    for q in range(4):
+        aff(R(T.TH[:, 16 + q:80:4], "TH%d" % q), whole("thi"))
 
-    iota(T.PI[:], [[0, 16]], 0, 1, "PI.0", fl=False)
-    iota(T.PC[:], [[0, 2], [16, 8]], 0, 0, "PC.0")
-    iota(T.XR[:], [[1, 144]], 0, 0, "XR")
-    iota(T.J1184[:], [[1184, 16], [0, 16]], 0, 0, "J1184")
-    iota(T.J128[:], [[64, 16], [0, 16]], 16, 0, "J128")
+    def tn(t, a, b):
+        return R(T.TN[:, t % 2, 16 * a:16 * b], *(["TN%d" % (t % 2)] * (a < 10 + t) + ["NP%d" % (t % 2)] * (b > 10 + t)))
 
-    tw = lambda t: 16 * (10 + t)
-    st = lambda t: 4 if t <= 4 else 3
-    w("col", 1)
-    c0 = 16 * Wn["col"][0]
-    memset(T.V[:, VOFF[LSU[0]]:VOFF[LSU[0]] + 256 * LSU[0]:LSU[0]], -256.0, "Vz%d" % LSU[0])
-    memset(T.X[:, TB - 16:TB], 0.0, "Xz")
-    memset(T.D0[:, 0::4], 0.0, "D0.0")
-    ts(wi("a"), qv("PI"), 15, A.bitwise_and)
-    ts(wi("a8"), qv("PI"), 7, A.bitwise_and)
-    ts(raw(T.wj[:, 0:1], "wj0"), raw(T.PI[:, 0:1], "PI.0"), 112, A.bitwise_and)
-    cp(raw(T.W[:, c0:c0 + 1], "c0"), raw(T.PI[:, 0:1], "PI.0"))
-    tt(w("li"), qv("PC"), wi("a"), A.add)
-    cp(qv("BC"), wi("a"))
-    ts(raw(T.W[:, c0 + 1:c0 + 2], "c1"), raw(T.wj[:, 0:1], "wj0"), 15.0, A.add)
-    memset(T.ZR[:], 0.0, "ZR")
-    memset(T.D0[:, 3::4], 1.0, "D0.3")
-    memset(T.D1R[:], 0.0, "D1R.0", "D1R.1", "D1R.2", "D1R.3")
-    memset(T.RES[:, 80:112], 0.0, "RES.5", "RES.6")
-    ts(raw(T.ID[:], "ID"), raw(T.XR[:, :128], "XR"), T.W[:, c0:c0 + 1], A.is_equal, extra=["c0"])
-    ts(raw(T.NID[:], "NID"), raw(T.XR[:, :128], "XR"), T.W[:, c0:c0 + 1], A.is_equal, -1.0, A.mult, extra=["c0"])
-    ts(raw(T.Z[:], "Z"), raw(T.XR[:], "XR"), T.W[:, c0 + 1:c0 + 2], A.is_equal, extra=["c1"])
-    memset(T.D1R[:, 0::4], 1.0, "D1R.0")
-    for li_, l in enumerate(LSU):
-        for q in range(3):
-            aff(hv("BASE", q, 1, 2 * li_), w("li"), float(l), -1.0 if q == 2 else 0.0)
-    for t in range(1, RO):
-        aff(qv("PNP", 2 * t + 1), w("li"), 1.0, 128.0 * LS[t] - 16.0)
-    aff(w("ci"), w("li"), 16.0, 4096.0, h=0)
-    aff(w("ci"), w("li"), 16.0, h=1)
+    def seeds(t, nb, extra):
+        n = 16 * (nb + extra)
+        mm(R(T.pY[:, :n], "pY"), ID, R(T.C2080[:, :n], "C2080"), start=True)
+        mm(R(T.pY[:, 256:256 + 16 * nb], "pY"), ID, R(T.J1184[:, :16 * nb], "J1184"))
+        sr = lambda k: R(T.SR[:, t, :k], "SR0", "SR1", "SR2", "SR3")
+        for c in range(0, n, 64):
+            mm(R(T.pY[:, c:min(c + 64, n)], "pY"), ID, sr(min(64, n - c)))
+        for c in range(0, 16 * nb, 64):
+            k = min(64, 16 * nb - c)
+            mm(R(T.pY[:, 256 + c:256 + c + k], "pY"), whole("I2080"), sr(k), stop=c + k == n)
+        if extra:
+            mm(R(T.pY[:, 256 + 16 * nb:256 + n], "pY"), whole("I2080"), sr(16))
+            mm(R(T.pY[:, 256 + 16 * nb:256 + n], "pY"), whole("I1184"), me(0), stop=True)
 
-    def mid_constants():
-        for l in LSU[1:3]:
-            iota(T.V[:, VOFF[l]:VOFF[l] + 256 * l:l], [[0, 256]], -256, 0, "Vz%d" % l)
+    def columns(src, a, b, key):
+        part_ = lambda name: R(T[name][:, 16 * a:16 * b], name + key)
+        tt(part_("Y0"), R(T.pY[:, 16 * a:16 * b], "pY"), src, A.mult)
+        tt(part_("NI"), R(T.pY[:, 256 + 16 * a:256 + 16 * b], "pY"), part_("Y0"), A.add)
+        ts(part_("NJ"), part_("NI"), 5, A.arith_shift_right, 4095, A.bitwise_and)
+        return part_("NJ")
 
-    iota(T.D0T[:, 0:4 * tw(4):4], [[0, tw(4)]], 0, 0, "D0T.0")
-    iota(T.D0T[:, 1:4 * tw(4):4], [[0, tw(4)]], 1, 0, "D0T.1")
-    iota(T.ONE[:], [[0, 128]], 1, 0, "ONE")
-    iota(T.NONE[:], [[0, 128]], -1, 0, "NONE")
-    iota(T.D0F[:, 0::3], [[0, 256]], 0, 0, "D0F.0")
-    iota(T.D0F[:, 1::3], [[0, 256]], 1, 0, "D0F.1")
-    for l in LSU[3:]:
-        iota(T.V[:, VOFF[l]:VOFF[l] + 256 * l:l], [[0, 256]], -256, 0, "Vz%d" % l)
+    ct = lambda t, nb: R(T.CT[:, 256 * (t % 2):256 * (t % 2) + 16 * nb], "CT%d" % (t % 2))
 
-    def late_constants():
-        a0, a8 = 16 * WIn["a"], 16 * WIn["a8"]
-        ts(raw(T.BC4[:, 0:5], "BC4"), raw(T.WI[:, a0:a0 + 5], *wi("a")[3]), 4.0, A.mult, 3.0, A.add)
-        ts(raw(T.BC4[:, 7:8], "BC7"), raw(T.WI[:, a0:a0 + 1], *wi("a")[3]), 4.0, A.mult, 3.0, A.add)
-        ts(raw(T.BC4[:, 5:6], "BC5"), raw(T.WI[:, a8:a8 + 1], *wi("a8")[3]), 4.0, A.mult, 3.0, A.add)
-        ts(raw(T.BC4[:, 6:7], "BC6"), raw(T.WI[:, a8:a8 + 1], *wi("a8")[3]), 4.0, A.mult, 35.0, A.add)
+    def update(t):
+        nb = 10 + t
+        n = 16 * nb
+        old, last, new = tn(t - 1, 0, nb - 1), R(T.TP[:, n - 16:n], "TP"), tn(t - 1, nb - 1, nb)
+        for x, (o, l) in enumerate(((0, NID), (256, ID))):
+            mm(R(T.pT[:, o:o + n - 16], "pT"), l, old, start=x == 0)
+            mm(R(T.pT[:, o + n - 16:o + n], "pT"), l, last)
+        if t == RO:
+            mm(R(T.pT[:, 256:512], "pT"), ID, whole("C2048"))
+        for j in range(nb):
+            mm(R(T.pT[:, 16 * j:16 * j + 16], "pT"), ID, new, stop=j == nb - 1)
+        tt(whole("SIG"), me(0), nok4, A.add)
+        tt(R(T.MK[:, :n], "MK"), IX(T.SIG[:], T.BC[:, 0:nb], "SIG", "BC"), R(T.JJ[:, :n], "JJ"), A.is_equal)
+        tt(R(T.WW[:, :n], "WW"), R(T.pT[:, :n], "pT"), R(T.MK[:, :n], "MK"), A.mult)
+        tt(whole("YT") if t == RO else tn(t, 0, nb), R(T.pT[:, 256:256 + n], "pT"), R(T.WW[:, :n], "WW"), A.add)
 
-    def bc(name, col, L, *keys):
-        return raw(T[name][:, col:col + 16].indirect(T.BC[:, 0:L]), "BC.0", *keys)
+    def offsets(t):
+        of = lambda q: R(T.pK[:, :, 8 * q:8 * q + 8], "pK")
+        tt(whole("OFN"), sc(ON, 14) if t else me(0), base(t), A.add)
+        mm(R(T.pK[:, :, 0:16], "pK"), ID, R(T.OC[:, 2 * t:2 * t + 2, :], "OC%d.0" % t, "OC%d.1" % t), start=True)
+        terms = ((0, d1(14)), (0, sc(ON, 15)), (1, sc(ON, 15)), (0, tile("RES", 6)), (0, tile("RES", 7)), (0, tile("RES", 2)), (1, tile("RES", 3)))
+        terms = terms if t else ((0, me(2)), (1, me(3)))
+        for x, (q, r) in enumerate(terms):
+            mm(of(q), NID if t and x == 0 else ID, r, stop=x == len(terms) - 1)
+        tt(whole("OFU"), R(T.pK[:, :, 0:16], "pK"), R(T.OL[:, 2 * t:2 * t + 2, :], "OL", "OL%d" % t), A.max)
 
-    def finish_c(t):
-        n = 16 * SL[t]
-        return [lambda: ts(raw(T.NJ[:, :n], "NJ"), raw(T.NI[:, :n], "NI"), 5, A.arith_shift_right, 4095, A.bitwise_and),
-                lambda: cp(raw(T.CT[:, 256 * (t % 2):256 * (t % 2) + n], "CT%d" % (t % 2)), raw(T.NJ[:, :n], "NJ"))]
-
-    def first_c(t):
-        n = 16 * SL[t]
-        return [
-            lambda: tt(raw(T.N2[:, :n], "N2"), bc("B0", 16 * t, SL[t], "B0"), raw(T.J1184[:, :n], "J1184"), A.add),
-            lambda: tt(raw(T.N1[:, :n], "N1"), bc("S32", 16 * t, SL[t], "S32"), raw(T.TP[:, :n], "TP"), A.mult),
-            lambda: tt(raw(T.NI[:, :n], "NI"), raw(T.N1[:, :n], "N1"), raw(T.N2[:, :n], "N2"), A.add),
-        ] + finish_c(t)
-
-    def weave(*lists):
-        lists = [list(x) for x in lists]
-        while any(lists):
-            for x in lists:
-                if x:
-                    x.pop(0)()
-
-    def t_seed(t):
-        n = tw(t)
-        op("S", lambda: g.scalar.activation(T.D0T[:, 3:4 * n:4], T.S32[:, 16 * (t + 1):16 * (t + 2)].indirect(T.BC[:, 0:n // 16]), F.Copy),
-           ["S32", "BC.0"], ["D0T.3"])
-
-    def t_operands():
-        for t in range(1, 7):
-            o, n, s = 1024 * (t - 1), tw(t), st(t)
-            lo = 0 if t == 1 else tw(t - 1)
-            aff(raw(T.D1T[:, o + s * lo + 1:o + s * n:s], "D1T%d.1b" % t), raw(T.TP[:, lo:n], "TP"), -1.0)
-            aff(raw(T.D1T[:, o + s * lo + 2:o + s * n:s], "D1T%d.2b" % t), raw(T.TP[:, lo:n], "TP"))
-        t_seed(1)
-
-    def t_b(t):
-        o, n = 1024 * (t - 1), tw(t)
-        op("S", lambda: g.scalar.activation(T.D1T[:, o + 3:o + 4 * n:4], T.B0[:, 16 * (t + 1):16 * (t + 2)].indirect(T.BC[:, 0:n // 16]), F.Copy),
-           ["B0", "BC.0"], ["D1T%d.3" % t])
-
-    def t_new(t):
-        o, n, s = 1024 * (t - 1), tw(t), st(t)
-        c = 16 * ((t - 1) % 2)
-        op("S", lambda: g.scalar.activation(T.D1T[:, o:o + s * n:s], T.NP[:, c:c + 16].indirect(T.BC[:, 0:n // 16]), F.Copy),
-           ["NP.%d" % ((t - 1) % 2), "BC.0"], ["D1T%d.0" % t])
-
-    def t_chain(t):
-        o, n, s = 1024 * (t - 1), tw(t), st(t)
-        d0 = "D0T" if s == 4 else "D0F"
-        k1 = ["D1T%d.%s" % (t, x) for x in ("0", "1", "1b", "2", "2b", "3")] + ["%s.%d" % (d0, x) for x in range(s)]
-        steps = [
-            lambda: tt(raw(T[d0][:, 2:s * n:s], d0 + ".2"), bc("SIG", 0, n // 16, "SIG.0"),
-                       raw(T.J128[:, :n], "J128") if t < 6 else raw(T.TP[:], "TP"), A.is_equal),
-            lambda: op("V", lambda: g.vector.tensor_tensor_scan(T.OT[:, :s * n], T[d0][:, :s * n], T.D1T[:, o:o + s * n], 0.0, A.mult, A.add), k1, ["OT"]),
-        ]
-        if s == 4:
-            steps += [lambda: tt(raw(T.NI[:, :n], "NI"), raw(T.OT[:, 3:4 * n:4], "OT"), raw(T.J1184[:, :n], "J1184"), A.add)] + finish_c(t + 1)
-
-        def carry():
-            if t == 6:
-                aff(raw(T.YT[:], "YT"), raw(T.OT[:, 2:s * n:s], "OT"), 1.0, 2048.0)
-                return
-            o2, s2 = 1024 * t, st(t + 1)
-            aff(raw(T.D1T[:, o2 + 1:o2 + s2 * n:s2], "D1T%d.1" % (t + 1)), raw(T.OT[:, 2:s * n:s], "OT"), -1.0)
-            aff(raw(T.D1T[:, o2 + 2:o2 + s2 * n:s2], "D1T%d.2" % (t + 1)), raw(T.OT[:, 2:s * n:s], "OT"))
-        return steps, carry
-
-    for x in range(3):
+    for r in (0, 1):
+        ts(R(T.SR[:, :, 16 * r:16 * r + 16], "SR%d" % r), whole("sdi"), -2048.0, A.add)
+        aff(R(T.SR[:, :, 16 * r + 32:16 * r + 48], "SR%d" % (r + 2)), whole("sdi"), 1.0, -2048.0)
+    ts(whole("TP"), whole("tri"), -2048.0, A.add)
+    seeds(0, 10, 0)
+    cp(ct(0, 10), columns(R(T.TP[:, :160], "TP"), 0, 10, "a"))
+    aff(tn(0, 0, 10), R(T.tri[:, :160], "tri"), 1.0, -2048.0)
+    for x, (least, c1, c2) in enumerate(((2.0, 1.0, -0.5), (4.0, 2.0, -0.25), (8.0, 4.0, -0.125))):
         w("g%d" % x, 2)
-    w("KK", 2)
-    nop0 = lambda: None
-    first = [lambda: ts(qv("RES", 0), qv("ki"), -1.0, A.add)]
-    for x, (th_, c1, c2) in enumerate(((2, 1.0, -0.5), (4, 2.0, -0.25), (8, 4.0, -0.125))):
-        first.append(lambda x=x, a=th_, b=c1: ts(wq("g%d" % x, 0), qv("ki"), float(a), A.is_ge, b, A.mult))
-        first.append(lambda x=x, a=th_, b=c2: ts(wq("g%d" % x, 1), qv("ki"), float(a), A.is_ge, b, A.mult))
-    first2 = [
-        lambda: tt(w("g0", 2), w("g0", 2), w("g1", 2), A.add),
-        lambda: tt(qv("RES", 1, 2), w("g0", 2), w("g2", 2), A.add),
-        lambda: ts(w("KK", 2), qv("RES", 1, 2), 1.0, A.add),
-        lambda: tt(w("x1"), nn, wq("KK", 1), A.mult),
-        lambda: ts(wi("fl"), w("x1"), -0.4375, A.add),
-        lambda: tt(hv("M", 1), wi("fl"), wq("KK", 0), A.mult),
-        lambda: tt(w("x2"), hv("M", 1), qv("RES", 1), A.subtract),
-        lambda: ts(hv("M", 2), w("x2"), -1.0, A.add, 0.0, A.max),
-        lambda: send_meta(0),
-    ]
-    ts(raw(T.I96[:], "I96"), raw(T.sdi[:], "sdi"), 65.0, A.mult, 2048.0, A.add)
-    ts(raw(T.S32[:], "S32"), raw(T.sdi[:], "sdi"), 32.0, A.add)
-    ts(raw(T.I96b[:], "I96b"), raw(T.I96[:], "I96"), 4095, A.bitwise_and)
-    ts(raw(T.TP[:], "TP"), raw(T.tri[:], "tri"), -2048.0, A.add)
-    ts(raw(T.B0[:], "B0"), raw(T.I96b[:], "I96b"), 32.0, A.mult)
-    fc = first_c(0)
-    first.append(lambda: ts(qv("RES", 4), qv("ki"), -1.0, A.add, 0.0625, A.mult))
-    first2[2] = lambda a=first2[2]: (a(), cp(nn, qv("ni")))
-    first2[3] = lambda a=first2[3]: (a(), tt(hv("M", 0), nn, qv("RES", 4), A.add), tt(hv("M", 3), nn, nok, A.add))
-    first2[7:] = [lambda a=first2[7], b=first2[8]: (a(), b())]
-    fc[1]()
-    fc[0]()
-    late_constants()
-    fc[2]()
-    weave(first[:3])
-    fc[3]()
-    weave(first[3:6])
-    fc[4]()
-    weave(first[6:])
-    first2.append(lambda: tt(qv("RES", 3), hv("M", 1), nn, A.subtract))
-    mid_constants()
-    t_operands()
-    t_b(1)
-    weights = [
-        lambda: (ts(raw(T.W[:, c0 + 2:c0 + 3], "c2"), raw(T.wi[:, 0:1], "wi0"), 2048.0, A.is_ge, -4096.0, A.mult), ts(w("th1"), qv("thi"), 1.0, A.add)),
-        lambda: tt(raw(T.W[:, c0 + 3:c0 + 4], "c3"), raw(T.W[:, c0 + 2:c0 + 3], "c2"), raw(T.wi[:, 0:1], "wi0"), A.add),
-        lambda: ts(raw(T.ZW[:], "ZW"), raw(T.XR[:], "XR"), T.W[:, c0 + 1:c0 + 2], A.is_equal, T.W[:, c0 + 3:c0 + 4], A.mult, extra=["c1", "c3"]),
-    ]
+        ts(w("g%d" % x, 1, 0), whole("ki"), least, A.is_ge, c1, A.mult)
+        ts(w("g%d" % x, 1, 1), whole("ki"), least, A.is_ge, c2, A.mult)
+    tt(w("g0", 2), w("g0", 2), w("g1", 2), A.add)
+    aff(me(0), whole("ni"))
+    aff(me(1), whole("ki"))
+    tt(tile("RES", 4, 2), w("g0", 2), w("g2", 2), A.add)
+    ts(w("KK", 2), tile("RES", 4, 2), 1.0, A.add)
+    tt(w("x1"), whole("ni"), w("KK", 1, 1), A.mult)
+    ts(wi("fl"), w("x1"), -0.4375, A.add)
+    tt(me(2), wi("fl"), w("KK", 1, 0), A.mult)
+    tt(me(3), me(2), tile("RES", 4), A.subtract)
+    tt(tile("RES", 2), me(2), me(0), A.subtract)
+    ts(me(4), me(3), -1.0, A.add, 0.0, A.max)
+    offsets(0)
 
-    def mm(out, lhsT, rhs, a, b, rd, wr):
-        op("P", lambda: g.tensor.matmul(out, lhsT, rhs, a, b), rd, wr)
+    pC = R(T.pU[:, 64:96], "pU")
+    sums = R(T.pS[:, 16:80], "pS")
 
     def post(t):
-        last = t == RO - 1
-        d0 = ["D0.%d" % x for x in range(4)]
-        nq = 7 if last else 8
-        steps = [
-            lambda: tt(hv("AH", 0, 4), raw(T.pS[:, 0:2, :], "pS"), hv("LIM", 1, 4), A.is_lt),
-            lambda: tt(hv("AH", 0, 2), hv("AH", 0, 2), hv("AH", 2, 2), A.max),
-            lambda: tt(hv("C", 0, 2), qv("RES", 5, 2), hv("AH", 0, 2), A.add),
-            lambda: (tt(iv("D0", 2), hv("C", 0), wq("H", 0), A.is_lt), tt(iv("D0", 1), hv("C", 1), wq("H", 0), A.is_lt),
-                     tt(qv("CAND", 5, 2), hv("C", 0, 2), hv("NF", 0, 2), A.min)),
-            lambda: (op("V", lambda: g.vector.tensor_tensor_scan(T.NR[:], T.D0[:], T.D1R[:], 0.0, A.mult, A.add), d0 + ["D1R.%d" % x for x in range(4)], ["NR.3"]),
-                     op("V", lambda: g.vector.tensor_tensor_scan(T.ON[:], T.D0[:], T.D1[:], 0.0, A.mult, A.add), d0 + ["D1.%d" % x for x in range(4)], ["ON.3"])),
-            lambda: tt(qv("RES", 0, nq), raw(T.NR[:, 0:64].indirect(T.BC4[:, 0:nq]), "NR.3", "BC4", "BC5", "BC6", "BC7"), qv("CAND", 0, nq), A.mult),
-        ]
-        if not last:
-            steps += [
-                lambda: (mm(T.pU[:, 16:32], T.ONE[:], T.D0[:, 3::4], True, False, ["ONE", "D0.3"], ["pU"]),
-                         mm(T.pU[:, 16:32], T.NONE[:], T.NR[:, 3::4], False, True, ["NONE", "NR.3"], ["pU"]),
-                         tt(w("x2"), nn, qv("RES", 7), A.add), tt(hv("M", 1), nn, qv("RES", 3), A.add), tt(hv("M", 0), nn, qv("RES", 4), A.add)),
-                lambda: (ts(hv("M", 2), w("x2"), -1.0, A.add, 0.0, A.max), send_meta(t + 1)),
-            ]
-        return steps
+        tt(sc(D0, 1, step=4), sums, R(T.LIM[:], "LIM0", "LIM1"), A.is_gt)
+        scan(R(T.SC[:, ON:ON + 16 * E], "SC%d" % ON), R(T.SC[:, 0:16 * E], *D0K), R(T.D1[:], *D1K), A.mult, A.add)
+        scan(R(T.SC[:, NR:NR + 16 * E], "SC%d" % NR), R(T.SC[:, 0:16 * E], *D0K), whole("D1R"), A.mult, A.add)
+        ts(whole("AH"), sums, col(9)[0], A.is_le, extra=["c9"])
+        mm(pC, ID, whole("VV"), start=True)
+        for x in (0, 1):
+            mm(pC, ID, R(T.AH[:, x::2], "AH"), stop=x == 1)
+        tt(whole("VC"), pC, whole("NF2"), A.min)
+        if t == RO - 1:
+            return
+        tt(whole("VV"), IX(T.SC[:, 0:ON], T.BV[:], "SC%d" % NR, "BV0", "BV1", *D0K), whole("VC"), A.mult)
+        tt(tile("RES", 0, 8), IX(T.SC[:, 0:ON], T.BR[:], "SC%d" % NR, "BR0", "BR6", *D0K), tile("CA", 0, 8), A.mult)
+        offsets(t + 1)
+        mm(R(T.pU[:, 16:32], "pU"), whole("ONEQ"), nok4, start=True)
+        mm(R(T.pU[:, 16:32], "pU"), whole("NONE"), sc(NR, 14), stop=True)
+        tt(me(0, 4), IX(T.SC[:], T.BY[:], "SC%d" % ON, "SC%d" % NR, "BY", *D0K), tile("RES", 0, 4), A.add)
+        ts(me(4), me(3), -1.0, A.add, 0.0, A.max)
+        act(w("junk"), R(T.pU[:, 16:32], "pU"), F.Identity, 1.0, 1100.0, accum=col(8))
+        aff(R(T.FL[:, 0:1], "FL"), col(8), 0.0625, -0.46875)
+        aff(col(9), R(T.FL[:, 0:1], "FL"), -16.0, col(8)[0], extra=["c8"])
 
-    seed_next = []
-    for x in ("nk", "K2", "hK", "H"):
-        w(x, 2)
     w("FF", 2)
-    w("KI", 2)
-    w("acol", 1)
-    ac = 16 * Wn["acol"][0]
-    colap = lambda i: T.W[:, ac + i:ac + i + 1]
 
     for t in range(RO):
         S_, L, last = SL[t], LS[t], t == RO - 1
-        li_ = LSU.index(L)
         vo = VOFF[L]
-        ctk = "CT%d" % (t % 2)
 
         def gather(e, j, h):
             a, b = (0, 2) if h == 2 else (h, h + 1)
-            out = T.V[:, vo + 128 * L * a + 1 + j:vo + 128 * L * b:L]
             c = 256 * (t % 2) + 16 * j
-            src = T.X[:, TB:TB + 4096].indirect(T.CT[:, c + 8 * a:c + 8 * b])
-            k = ["V%d.%d.%d" % (L, j, x) for x in range(a, b)]
-            if e == "V":
-                op("V", lambda: g.vector.tensor_copy(out, src), XK + [ctk], k)
-            else:
-                op("S", lambda: g.scalar.activation(out, src, F.Copy), XK + [ctk], k)
+            (cp if e == "V" else scp)(R(T.V[:, vo + 128 * L * a + 1 + j:vo + 128 * L * b:L], *["V%d.%d.%d" % (L, j, x) for x in range(a, b)]),
+                                      IX(T.X[:, TB:TB + 4096], T.CT[:, c + 8 * a:c + 8 * b], "CT%d" % (t % 2), *XK))
 
-        def gather_new(h):
-            if t > 0:
-                op("S", lambda: g.scalar.activation(T.VN[:, 128 * h:128 * h + 128], T.X[:, TB - 16:TB + 4096].indirect(T.VOU[:, 8 * h:8 * h + 8]), F.Copy),
-                   XK + ["Xz", "VOU.0"], ["VN%d" % h])
+        pn = lambda h, a=0, s=1: R(T.RP[:, h, RW + a:RW + 128:s], "Pn%d" % h)
 
-        nop = lambda: None
-        m3 = lambda: tt(hv("M", 3), nn, nok, A.add)
-        offs = [lambda: tt(hv("OF", 0, 3), hv("M", 1, 3), hv("BASE", 0, 3, 2 * li_), A.add)]
-        if t > 0:
-            offs.append(lambda: tt(hv("OF", 0), hv("OF", 0), qv("SIG", 1), A.max))
-        offs.append(lambda: cp(hv("OFU", 0, 3), hv("OF", 0, 3)))
-
-        def scalar_operands():
-            if t == 0:
-                for q in range(5):
-                    aff(hv("TH4", q), w("th1"))
-            else:
-                aff(hv("LP", 0, 5), hv("TH4", 0, 5), 1.0, colap(4), extra=["A4"])
-
-        def a_step(x):
-            if t > 0:
-                [lambda: aff(raw(colap(1), "A1"), raw(colap(0), "A0"), 0.0625, -0.46875),
-                 lambda: aff(raw(colap(2), "A2"), raw(colap(1), "A1"), 1.0, MAGIC),
-                 lambda: aff(raw(colap(3), "A3"), raw(colap(2), "A2"), -16.0, 16.0 * MAGIC),
-                 lambda: aff(raw(colap(4), "A4"), raw(colap(0), "A0"), 1.0, colap(3), extra=["A3"])][x]()
-
-        def scan(h, a=0, b=128):
-            if a == b:
-                return
+        def folds(h):
             r0, v0 = RW - 128 * L, vo + 128 * L * h
-            op("V", lambda: g.vector.tensor_tensor_scan(RP[h][:, r0 + a * L:r0 + b * L], T.V[:, v0 + a * L:v0 + b * L],
-                                                        T.ZR[:, :(b - a) * L], 0.0, A.add, A.max),
-               ["ZR", "Vz%d" % L] + ["V%d.%d.%d" % (L, j, h) for j in range(S_)], ["R%d" % h])
-
-        def pick_n(h):
-            src = RP[h][:, RW - 128 * L:RW].indirect(T.OFU[:, h, 16:24])
+            scan(R(T.RP[:, h, r0:RW], "R%d" % h), R(T.V[:, v0:v0 + 128 * L], "Vz%d" % L, *["V%d.%d.%d" % (L, j, h) for j in range(S_)]),
+                 R(T.ZR[:, :128 * L], "ZR"), A.add, A.max)
+            src = IX(T.RP[:, h, r0:RW], T.OFN[:, 8 * h:8 * h + 8], "R%d" % h, "OFN")
             if t > 0:
-                op("V", lambda: g.vector.tensor_tensor(RP[h][:, RW:RW + 128], src, T.VN[:, 128 * h:128 * h + 128], A.add),
-                   ["R%d" % h, "OFU.0.2", "VN%d" % h], ["Pn%d" % h])
+                tt(pn(h), src, R(T.VN[:, 128 * h:128 * h + 128], "VN"), A.add)
             else:
-                op("V", lambda: g.vector.tensor_copy(RP[h][:, RW:RW + 128], src), ["R%d" % h, "OFU.0.2"], ["Pn%d" % h])
+                cp(pn(h), src)
+            send(t, h, "n")
+            scp(R(T.RP[:, h, PA:PA + 256], "PA%d" % h), IX(T.RP[:, h, r0:RW + 128], T.OFU[:, h, :], "R%d" % h, "Pn%d" % h, "OFU"))
+            send(t, h, "v")
+            aff(R(T.VT[:, 128 * h:128 * h + 128], "VT%d" % h), pn(h), 0.0625, 191.53125)
 
-        def pick_ba(h):
-            op("S", lambda: g.scalar.activation(RP[h][:, RW + 256:RW + 384], RP[h][:, RW - 128 * L:RW].indirect(T.OFU[:, h, 8:16]), F.Copy),
-               ["R%d" % h, "OFU.0.1"], ["PB%d" % h])
-            op("S", lambda: g.scalar.activation(RP[h][:, RW + 128:RW + 256], RP[h][:, RW - 128 * L:RW + 128].indirect(T.OFU[:, h, 0:8]), F.Copy),
-               ["R%d" % h, "Pn%d" % h, "OFU.0.0"], ["PA%d" % h])
+        def compare_lengths():
+            pl = lambda a, n=1: R(T.pN[:, 128 + 16 * a:128 + 16 * (a + n)], "pN")
+            mm(pl(0, 2), ID, me(0, 2), start=True)
+            for c, q in ((2, 4), (3, 4), (4, 2), (5, 2)):
+                mm(pl(c), ID, me(q))
+            for c in (2, 5):
+                mm(pl(c), ID, R(T.ONES[:, :16], "ONES"))
+            for c, q in enumerate((0, 1, 3, 2, 2, 3)):
+                mm(pl(c), NID, R(T.QM[:, 2 * t:2 * t + 2, 8 + 16 * q:16 + 16 * q], "Q%dm" % t, "PA1"), stop=c == 5)
+            act(whole("DL"), pl(0, 6), F.Abs)
 
-        def usum(h):
-            for a in range(16):
-                mm(T.pU[:, 8 * h:8 * h + 8], T.ZW[:, 15 - a:143 - a], RP[h][:, RW + a:RW + 128:16], a == 0, a == 15, ["ZW", "Pn%d" % h], ["pU"])
-
-        def vt(h):
-            aff(raw(T.VT[:, 128 * h:128 * h + 128], "VT%d" % h), raw(RP[h][:, RW:RW + 128], "Pn%d" % h), 0.0625, 191.53125)
-
-        def val(h):
-            sl = slice(128 * h, 128 * h + 128)
-            aff(raw(T.VAL[:, sl], "VAL%d" % h), raw(T.VT[:, sl], "VT%d" % h), 1.0, -192.0)
-
-        pieces = {"1n": (1, 0, 128, 128), "0n": (0, 0, 128, 0), "1v": (1, 128, 384, 768), "0v": (0, 128, 384, 256),
-                  "1w": (1, 128, 384, 1024), "0w": (0, 128, 384, 512)}
-
-        def own(*ps):
-            for p in ps:
-                h, a, b, _ = pieces[p]
-                mm(T["pD" + p][:, a:b], T.ID[:], RP[h][:, RW + a:RW + b], True, False,
-                   ["ID"] + (["Pn%d" % h] if a == 0 else ["PA%d" % h, "PB%d" % h]), ["pD" + p])
-
-        def diff(*ps):
-            for p in ps:
-                h, a, b, d = pieces[p]
-                o = (2 * t + h) * 384
-                if p[1] == "w":
-                    k = ["NID", "Q%d%dv" % (t, h)]
-                    mm(T["pD" + p][:, 128:256], T.NID[:], T.Q[:, o + 256:o + 384], False, False, k, ["pD" + p])
-                    mm(T["pD" + p][:, 256:384], T.NID[:], T.Q[:, o + 128:o + 256], False, True, k, ["pD" + p])
-                else:
-                    mm(T["pD" + p][:, a:b], T.NID[:], T.Q[:, o + a:o + b], False, True, ["NID", "Q%d%s" % (t, p)], ["pD" + p])
-                op("S", lambda: g.scalar.activation(T.DA[:, d:d + b - a], T["pD" + p][:, a:b], F.Abs), ["pD" + p], ["DA" + p])
-
-        def sums(out, bk, a, b, *ps):
+        def compare_n(h):
+            qn = lambda a=0, s=1: R(T.Q[:, 2 * t + h, a:128:s], "Q%d%dn" % (t, h))
+            dn = lambda a=0, s=1: R(T.DN[:, h, a:128:s], "DN%d" % h)
+            rows = lambda name, x: R(T[name][:, 15 - x:143 - x], name)
+            o = R(T.pS[:, 0:8], "pS") if h else R(T.pK[:, 0, 32:40], "pK")
+            mm(o, NID, R(T.TH[:, 8 * h:8 * h + 8], "TH"), start=True)
+            if VMAX[h]:
+                for x in range(16):
+                    mm(o, rows("NZ", x), pn(h, x, 16))
+            for q in (0, 1):
+                mm(o, IB, R(T.DL[:, 16 * q + 8 * h:16 * q + 8 * h + 8], "DL"))
+            if VMAX[h]:
+                for x in range(16):
+                    mm(o, rows("NZ", x), qn(x, 16))
+                tt(dn(), pn(h), qn(), A.max)
+            else:
+                pn_ = R(T.pN[:, 0:128], "pN")
+                mm(pn_, ID, pn(h), start=True)
+                mm(pn_, NID, qn(), stop=True)
+                act(dn(), pn_, F.Abs)
             for x in range(16):
-                mm(out, T.Z[:, 15 - x:143 - x], T.DA[:, a + x:b:16], x == 0, x == 15, ["Z"] + ["DA" + p for p in ps], [bk])
+                mm(o, rows("Z2" if VMAX[h] else "Z", x), dn(x, 16), stop=x == 15)
+            so = R(T.SOU[:, 8 * h:8 * h + 8], "SOU%d" % h)
+            ts(sc(D0, 14, h), o, col(9)[0], A.is_gt, 4096.0, A.mult, extra=["c9"])
+            tt(so, w("colx", h=h), sc(D0, 14, h), A.subtract if h == 0 else A.add)
+            tt(IX(T.X[:, 6144 * h:6144 * h + 6144], so[0], XK[h], *["Xz"] * h),
+               R(T.VT[:, 128 * h:128 * h + 128], "VT%d" % h, *so[1]), whole("M192"), A.add)
+            ts(d1(15, h), o, col(9)[0], A.is_le, extra=["c9"])
 
-        def tail(h):
-            win = T.X[:, 0:6144] if h == 0 else T.X[:, 6144:12288]
-            return [
-                lambda: tt(nok, raw(T["pD%dn" % h][:, 256:264], "pD%dn" % h), hv("LIM", 0), A.is_ge, h=h),
-                lambda: tt(w("so"), w("colq"), nok, A.subtract if h == 0 else A.add, h=h),
-                lambda: ts(qv("SOU"), w("so"), 4096.0, A.mult, h=h),
-                lambda: op("V", lambda: g.vector.tensor_copy(win.indirect(T.SOU[:, 8 * h:8 * h + 8]), T.VAL[:, 128 * h:128 * h + 128]),
-                           ["SOU.0", "VAL%d" % h], [XK[h]] + (["Xz"] if h == 0 else [])),
-            ]
+        def compare_v(h):
+            bk = "pV%d" % h
+            for x, a in enumerate((128, 128, 0, 0)):
+                mm(R(T[bk][:, :, x, :], bk), ID, R(T.RP[:, h, PA + a:PA + a + 128], "PA%d" % h), start=x == 0)
+            for x, a in enumerate((256, 128, 128, 256)):
+                mm(R(T[bk][:, :, x, :], bk), NID, R(T.Q[:, 2 * t + h, a:a + 128], "Q%d%dv" % (t, h)), stop=x == 3)
+            act(R(T.DV[:, 512 * h:512 * h + 512], "DV%d" % h), whole(bk), F.Abs)
 
-        pm = lambda q, n=1: hv("PM", q, n, 2 * t)
-        relu = lambda o, a, sc, bi: op("S", lambda: g.scalar.activation(o[1](None), a[1](None), F.Relu, bias=bi, scale=sc), a[3], o[3])
         if t > 0:
-            aff(wq("nk", 0), nok, -8192.0, 16.0)
-            aff(wq("nk", 1), nok, -8192.0, 16.0)
-        fv, sp = FV[t], S_ - FS[t]
-        for j in range(NV1[t], S_):
-            gather("S", j, 1 if j < sp else 2)
-        long_ = ([lambda j=j: gather("V", j, 2 if j < fv else 1) for j in range(NV1[t])] + [lambda: scan(1)]
-                 + [lambda j=j: gather("V", j, 0) for j in range(fv, fv + NV0[t])])
-        s_rest = lambda: [gather("S", j, 0) for j in range(fv + NV0[t], sp)]
-        if t > 0:
-            short = [lambda: (tt(w("vo"), wi("n3"), wq("nk", 0), A.add), tt(qv("SIG", 0, 2), qv("PNP", 2 * t, 2), w("nk", 2), A.add)),
-                     lambda: (cp(qv("VOU"), w("vo")), gather_new(1), s_rest())]
-            ps = post(t - 1)
-            short = [short[0], lambda a=short[1]: (a(), ps[0]())] + ps[1:5] + [lambda: (ps[5](), m3()), ps[6], lambda: (
-                ps[7](), tt(hv("OF", 0), hv("M", 1), hv("BASE", 0, 1, 2 * li_), A.add)), lambda: (
-                tt(hv("OF", 1, 2), hv("M", 2, 2), hv("BASE", 1, 2, 2 * li_), A.add), offs[1]()), offs[2]]
-        else:
-            s_rest()
-            short = first2[:-1] + [lambda: (first2[-1](), offs[0](), weights[0]()), lambda: (offs[1](), weights[1]()), weights[2]]
-        for x, step in enumerate([nop] + short, -1):
-            step()
-            for _ in range(FILL[t].count(x)):
-                if long_:
-                    long_.pop(0)()
-        while len(long_) > NV0[t]:
-            long_.pop(0)()
-        if long_:
-            long_.pop(0)()
-        pick_n(1)
-        send_data(t, 1, "n" if VM != 3 else "")
-        weave(long_)
-        if t > 0:
-            op("S", lambda: g.scalar.activation(w("junk")[1](None), T.pU[:, 16:32], F.Identity, accum_out=colap(0)), ["pU"], ["A0"] + w("junk")[3])
-        gather_new(0)
-        a_step(0)
-        usum(1)
-        own("1n")
-        scan(0)
-        tt(iv("D1", 0), nn, hv("M", 2), A.subtract)
-        pick_ba(1)
-        send_data(t, 1, "v")
-        a_step(1)
-        own("1v", "1w")
-        if t > 0:
-            t_new(t)
-        a_step(2)
-        pick_n(0)
-        send_data(t, 0, "n")
-        usum(0)
-        pick_ba(0)
-        a_step(3)
-        aff(wq("K2", 0), qv("RES", 1), 200.5, 0.5)
-        aff(wq("hK", 0), qv("RES", 0), 100.0)
+            scp(whole("VN"), IX(T.X[:, TB:TB + 4112], T.VOU[:], "Xz", "VOU", *XK))
+            update(t)
+            post(t - 1)
+        send_lengths(t)
+        for j in range(S_):
+            if j < NV[t] + NS[t]:
+                gather("V" if j < NV[t] else "S", j, 2)
+            else:
+                gather("S", j, 1)
+                gather("V" if j >= S_ - NH[t] else "S", j, 0)
         if not last:
-            aff(wq("K2", 1), raw(T.B0[:, 16 * (t + 1):16 * (t + 2)], "B0"))
-            aff(wq("hK", 1), nn, -1184.0)
-        if VM == 2:
-            send_points(t)
+            seeds(t + 1, 10 + t, 1)
+            cp(ct(t + 1, 10 + t), columns(tn(t, 0, 10 + t), 0, 10 + t, "a"))
+        folds(1)
+        folds(0)
+        for a in range(16):
+            mm(R(T.pU[:, 0:16], "pU"), R(T.ZW[:, 15 - a:143 - a], "ZW"), R(T.RP[:, :, RW + a:RW + 128:16], "Pn0", "Pn1"), a == 0, a == 15)
+        cp(wi("y"), R(T.pU[:, 0:16], "pU"))
+        ts(wi("u"), wi("y"), 4095, A.bitwise_and)
+        ts(wi("ul"), wi("y"), 15, A.bitwise_and)
+        tt(w("colx"), wi("ul"), w("ci"), A.add)
+        ts(w("ua"), wi("u"), 4096.0, A.add)
+        ts(w("ub"), wi("u"), -2912.0, A.add)
+        tt(wi("uw"), w("ua"), w("ub"), A.mult)
+        ts(wi("new"), wi("uw"), 5, A.arith_shift_right, 4095, A.bitwise_and)
+        ts(tn(t, 10 + t, 11 + t), wi("new"), -2048.0, A.add)
+        tt(d1(0), me(0), me(4), A.subtract)
+        tt(d1(5), me(4), me(2), A.subtract)
+        aff(d1(13), tile("RES", 2), 1.0 / 4096)
+        aff(d1(14), me(0))
+        aff(w("K2"), tile("RES", 4), 200.5, 99.5)
+        aff(w("hK"), me(1), 100.0)
+        tt(w("H"), w("K2"), w("hK"), A.subtract)
+        for x in (0, 1):
+            act(R(T.H2[:, x::2], "H2%d" % x), w("H"), F.Relu)
+        act(whole("NF2"), R(T.H2[:], "H20", "H21"), F.Relu, 1.0, -3.0)
+        tt(whole("ND"), R(T.H2[:], "H20", "H21"), whole("VV"), A.subtract)
+        for x in (0, 1):
+            aff(R(T.LIM[:, x::2], "LIM%d" % x), whole("ND"), -16384.0, col(9)[0], extra=["c9"])
+        if last:
+            aff(sc(D0, 15), me(1))
+            memset(R(T.D1R[:, 15::E], "D1R"), 1.0)
         else:
-            send_data(t, 0, "v" if SPLIT0 else "nv")
-        own("0n", "0v", "0w")
-        if t > 0:
-            tch, carry = t_chain(t)
-        else:
-            tch, carry = first_c(1), lambda: (t_b(2), t_b(3))
-        tch[0]()
-        tt(iv("D1", 1), hv("M", 2), hv("M", 1), A.subtract)
-        tch[1]()
-        nh = 1 if last else 2
-        tt(qv("W", Wn["H"][0], nh), qv("W", Wn["K2"][0], nh), qv("W", Wn["hK"][0], nh), A.subtract)
-        vt(1)
-        scalar_operands()
-        val(1)
-        aff(hv("MR", 0), pm(2))
-        aff(hv("MR", 1), pm(1))
-        diff("1n")
-        sums(T.pD1n[:, 256:264], "pD1n", 128, 256, "1n")
-        relu(hv("NF", 0), wq("H", 0), 1.0, -4.0)
-        aff(w("KI", 2), qv("RES", 1, 2), 1.0, 1.0)
-        aff(iv("D1", 2), qv("RES", 3), 1.0, -1.0)
+            act(w("f0"), R(T.NF2[:, 0::2], "NF2"), F.Relu, -1.0, 1.0)
+            aff(w("FF", 1, 0), w("f0"), 1.0, 1.0)
+            aff(w("FF", 1, 1), w("f0"), -0.5, 1.0)
+            aff(w("KI", 2), tile("RES", 4, 2), 1.0, 1.0)
+            tt(w("KK", 2), w("KI", 2), w("FF", 2), A.mult)
+            aff(tile("CA", 4, 2), w("KK", 2), 1.0, -1.0)
+            tt(w("x1"), me(0), w("KK", 1, 1), A.mult)
+            ts(wi("fl"), w("x1"), -0.4375, A.add)
+            tt(w("x3"), wi("fl"), w("KK", 1, 0), A.mult)
+            tt(tile("CA", 2), w("x3"), me(0), A.subtract)
+            tt(tile("CA", 3), tile("CA", 2), tile("CA", 4), A.subtract)
+            aff(tile("CA", 1), me(1))
+            aff(tile("CA", 6), w("li"), (LS[t + 1] - 1) / 4096, -LS[t + 1] / 32)
+            aff(tile("CA", 7), me(0), 1.0 / 4096, 1.0 / 4096)
+        compare_lengths()
+        compare_n(1)
+        if last:
+            dma("Y", T.yx[:, 2048:4096], T.X[:, TB + 2048:TB + 4096], "st0", ["X.1"], [], 3000)
+        compare_v(1)
+        compare_n(0)
         if not last:
-            relu(w("f0"), hv("NF", 0), -1.0, 1.0)
-        aff(qv("CAND", 0), qv("RES", 0), 1.0, 1.0)
-        aff(iv("D1", 3), nn, 1.0, 1.0)
-        if not last:
-            aff(wq("FF", 0), w("f0"), 1.0, 1.0)
-            aff(wq("FF", 1), w("f0"), -0.5, 1.0)
-        vt(0)
+            tt(whole("VOU"), columns(tn(t, 10 + t, 11 + t), 10 + t, 11 + t, "b"), nok4, A.max)
+        compare_v(0)
+        mm(sums, NID, R(T.TH[:, 16:80], "TH0", "TH1", "TH2", "TH3"), start=True)
+        for x in range(4):
+            mm(R(T.pS[:, 16 + x:80:4], "pS"), IB, R(T.DL[:, 32 + 16 * x:48 + 16 * x], "DL"))
+        for x in range(16):
+            mm(sums, R(T.Z[:, 15 - x:143 - x], "Z"), R(T.DV[:, x::16], "DV0", "DV1"), stop=x == 15)
 
-
-        ech = [
-            lambda: tt(hv("E", 0, 3), hv("M", 0, 3), pm(0, 3), A.is_equal),
-            lambda: tt(hv("E", 3, 2), hv("M", 1, 2), hv("MR", 0, 2), A.is_equal),
-            lambda: tt(iv("D1", 1), hv("M", 2), hv("M", 1), A.subtract),
-            lambda: tt(hv("LIM", 0, 5), hv("E", 0, 5), hv("LP" if t > 0 else "TH4", 0, 5), A.mult),
-        ]
-        kch = [
-            lambda: tt(w("KK", 2), w("KI", 2), w("FF", 2), A.mult),
-            lambda: tt(w("x1"), nn, wq("KK", 1), A.mult),
-            lambda: ts(wi("fl"), w("x1"), -0.4375, A.add),
-            lambda: tt(w("x3"), wi("fl"), wq("KK", 0), A.mult),
-            lambda: tt(qv("CAND", 3), w("x3"), nn, A.subtract),
-            lambda: tt(qv("CAND", 7), qv("CAND", 3), qv("CAND", 1), A.subtract),
-        ]
-        if last:
-            kch = []
-        uch = [
-            lambda: cp(wi("y"), raw(T.pU[:, 0:16], "pU")),
-            lambda: ts(wi("ul"), wi("y"), 15, A.bitwise_and),
-            lambda: ts(wi("u"), wi("y"), 4095, A.bitwise_and),
-            lambda: (tt(w("colx"), wi("ul"), w("ci"), A.add), aff(w("colq"), w("colx"), 1.0 / 4096)),
-            lambda: ts(w("ua"), wi("u"), 4096.0, A.add),
-            lambda: ts(w("ub"), wi("u"), -2912.0, A.add),
-        ]
-        uch2 = [
-            lambda: tt(wi("uw"), w("ua"), w("ub"), A.mult),
-            lambda: ts(wi("new"), wi("uw"), 5, A.arith_shift_right, 4095, A.bitwise_and),
-            lambda: ts(qv("NP", t % 2), wi("new"), -2048.0, A.add),
-        ]
-        if not last:
-            uch2 += [
-                lambda: tt(w("n1"), qv("NP", t % 2), raw(T.S32[:, 16 * (t + 1):16 * (t + 2)], "S32"), A.mult),
-                lambda: tt(wi("n2"), w("n1"), wq("H", 1), A.add),
-                lambda: ts(wi("n3"), wi("n2"), 5, A.arith_shift_right, 4095, A.bitwise_and),
-            ]
-        weave(uch[:1] + tch[2:3] + uch[1:3] + ech[:1] + uch[3:5] + ech[1:2] + uch[5:] + tch[3:4] + uch2[:1] + ech[3:])
-        val(0)
-        carry()
-        weave(tail(1), uch2[1:UB], tch[4:5] + kch[:KA])
-        if last:
-            dma("Y", T.yx[:, 2048:4096], T.X[:, TB + 2048:TB + 4096], "st0", ["X.1"], [])
-        if VM == 0 and V1F:
-            diff("1v", "1w")
-        diff("0n")
-        if VM == 0 and not V1F:
-            diff("1v", "1w")
-        if not SPLIT0:
-            diff("0v", "0w")
-        sums(T.pD0n[:, 256:264], "pD0n", 0, 128, "0n")
-        relu(hv("NF", 1), wq("H", 0), 1.0, -4.0)
-        aff(qv("CAND", 4), qv("RES", 0), 0.0625, 0.0625)
-        if last:
-            aff(qv("PNP", 2 * RO), nn, 1.0 / 128, 1.0 / 512)
-        else:
-            aff(qv("PNP", 2 * t + 2), nn, 64.0)
-            aff(qv("CAND", 1, 2), w("KK", 2), 1.0, -1.0)
-        if VM in (1, 2):
-            diff("1v", "1w")
-        if SPLIT0:
-            diff("0v", "0w")
-        if 0 < t < 4:
-            t_seed(t + 1)
-        if t == 0:
-            t_b(4)
-        if last:
-            t_new(6)
-        if t == 1:
-            aff(raw(T.TP[:], "TP"), raw(T.J128[:], "J128"), 1.0 / 8192)
-        sums(T.pS[:, 0:2, :], "pS", 256, 1280, "0v", "1v", "0w", "1w")
-        weave(tail(0), kch[KA:], uch2[UB:])
-
-    dma("Y", T.yx[:, 0:2048], T.X[:, TB:TB + 2048], "st1", ["X.0"], [])
-    tch, carry = t_chain(6)
-    tt(qv("SIG"), qv("PNP", 2 * RO), nok, A.subtract)
-    ps = post(RO - 1)
-    tch[0]()
-    weave(ps[:5], [lambda: (tch[1](), carry(), dma("S", T.yt[:], T.YT[:], "st3", ["YT"], []))])
-    ps[5]()
-    cp(raw(T.YS[:, 0, :], "YS0"), nn)
-    aff(raw(T.YS[:, 1, :], "YS1"), qv("RES", 0), 1.0, 1.0)
-    for h in (0, 1):
-        cp(raw(T.YS[:, 2:4, 8 * h:8 * h + 8], "YS%d" % (2 + h)), raw(T.RES[:, 80 + 16 * h:96 + 16 * h], "RES.5", "RES.6"))
-    dma("Y", T.yst[:], T.YS[:], "st2", ["YS0", "YS1", "YS2", "YS3"], [])
-    for s, c in cnt.items():
-        need("G", (s, c))
+    dma("Y", T.yx[:, 0:2048], T.X[:, TB:TB + 2048], "st1", ["X.0"], [], 3000)
+    update(RO)
+    post(RO - 1)
+    dma("S", T.yt[:], T.YT[:], "st3", ["YT"], [], 2200)
+    ys = lambda q: R(T.YS[:, 16 * q:16 * q + 16], "YS%d" % q)
+    tt(ys(0), sc(ON, 14), d1(15), A.add)
+    cp(ys(1), sc(NR, 15))
+    tt(ys(2), sc(NR, 14), R(T.VC[:, 1::2], "VC"), A.mult)
+    tt(ys(3), sc(NR, 14), R(T.VC[:, 0::2], "VC"), A.mult)
+    dma("Y", T.yst[:], T.YS[:], "st2", ["YS0", "YS1", "YS2", "YS3"], [], 2000)
+    emit()

@@ -19,10 +19,11 @@ E = 16
 NV = [4, 3, 3, 3, 4, 4]
 NS = [3, 3, 4, 4, 4, 5]
 NH = [0, 0, 0, 0, 0, 0]
-VMAX = (0, 0)
-CYC, PCYC, GATHER, SCATTER, VMIN, SMIN, PMIN = 0.84, 0.42, 1.2, 4.0, 45, 64, 48
-SAME, CROSS, PSUM, WAKE, ISSUE, REMOTE, FIRST, LOAD = 200, 250, 300, 100, 100, 1200, 1500, 4500
-PASSES, WIDE = 6, 8
+VMAX = (1, 0)
+ROWS = ["gS2 gS1 new gS0", "pick1 scan0", "write1 ok0", "points1 lengths", "sum0 votes", "size1 size0 sizes1 sizes0"]
+CYC, PCYC, GATHER, SCATTER, VMIN, SMIN, PMIN = 0.84, 0.42, 1.15, 4.0, 45, 62, 44
+SAME, CROSS, PSUM, WAKE, ISSUE, REMOTE, FIRST, SMALL, LOAD = 200, 250, 300, 110, 90, 1150, 1500, 1700, 4200
+PASSES, WIDE = 4, 8
 PLAN = []
 
 f32, bf, f16, i32, u16 = "float32", "bfloat16", "float16", "int32", "uint16"
@@ -37,15 +38,15 @@ SCRATCH = {
     "JJ": ("sbuf", [128, 256], f32), "J1184": ("sbuf", [128, 256], f16), "C2080": ("sbuf", [128, 256], f16), "C2048": ("sbuf", [128, 256], f16),
     "MK": ("sbuf", [128, 256], f32), "WW": ("sbuf", [128, 256], f32), "Y0": ("sbuf", [128, 256], f32),
     "NI": ("sbuf", [128, 256], i32), "NJ": ("sbuf", [128, 256], i32),
-    "CT": ("sbuf", [128, 512], u16), "BC": ("sbuf", [128, 16], u16), "BR": ("sbuf", [128, 8], u16), "BY": ("sbuf", [128, 4], u16),
+    "CT": ("sbuf", [128, 512], u16), "BC": ("sbuf", [128, 16], u16), "BR": ("sbuf", [128, 10], u16), "BY": ("sbuf", [128, 4], u16),
     "BV": ("sbuf", [128, 2], u16), "OFU": ("sbuf", [128, 2, 16], u16), "OFN": ("sbuf", [128, 16], u16),
     "SOU": ("sbuf", [128, 16], u16), "VOU": ("sbuf", [128, 16], u16),
     "OC": ("sbuf", [128, 2 * RO, 16], f16), "OL": ("sbuf", [128, 2 * RO, 16], f32),
     "TH": ("sbuf", [128, 80], bf), "AH": ("sbuf", [128, 64], bf), "LIM": ("sbuf", [128, 64], f32), "ONES": ("sbuf", [128, 32], bf),
     "SC": ("sbuf", [128, 48 * E], bf), "D1": ("sbuf", [128, 16 * E], bf), "D1R": ("sbuf", [128, 16 * E], bf),
-    "CA": ("sbuf", [128, 128], f32), "RES": ("sbuf", [128, 128], f16),
+    "CA": ("sbuf", [128, 160], f32), "RES": ("sbuf", [128, 160], f16),
     "M": ("sbuf", [128, 80], bf), "QM": ("sbuf", [128, 2 * RO, 80], bf), "DL": ("sbuf", [128, 96], bf),
-    "H2": ("sbuf", [128, 32], f32), "NF2": ("sbuf", [128, 32], f32), "VC": ("sbuf", [128, 32], f32), "VV": ("sbuf", [128, 32], bf),
+    "NF2": ("sbuf", [128, 32], f32), "VC": ("sbuf", [128, 32], f32), "VV": ("sbuf", [128, 32], bf),
     "ND": ("sbuf", [128, 32], f32), "SIG": ("sbuf", [128, 16], f32), "FL": ("sbuf", [128, 16], f16),
     "W": ("sbuf", [128, 16 * 40], f32), "WI": ("sbuf", [128, 16 * 16], i32),
     "PI": ("sbuf", [128, 16], i32), "PC": ("sbuf", [128, 16], f32), "XR": ("sbuf", [128, 144], f32),
@@ -69,7 +70,7 @@ def rank_program(g, core, T, topo):
         return
     Q = {"V": g.vector, "S": g.scalar, "P": g.tensor, "G": g, "Y": g.sync}
     CS = {"V": "cV", "S": "cS", "P": "cP", "G": "cG"}
-    nodes, lastw, readers, chain = [], {}, {}, {}
+    nodes, lastw, readers, chain, marks = [], {}, {}, {}, {}
 
     def op(e, fn, args, kw, rd, wr, cost, done=None, sem=None, inc=1, auto=False, row=None):
         deps = set()
@@ -83,7 +84,7 @@ def rank_program(g, core, T, topo):
             deps.update(readers.get(k, []))
         i = len(nodes)
         nodes.append(dict(e=e, fn=fn, args=args, kw=kw, deps=sorted(deps), cost=cost, done=cost if done is None else done,
-                          sem=sem or CS.get(e), inc=inc, auto=auto, after=chain.get(row)))
+                          sem=sem or CS.get(e), inc=inc, auto=auto, after=[chain[row]] if row in chain else []))
         if row:
             chain[row] = i
         for k in rd:
@@ -92,12 +93,21 @@ def rank_program(g, core, T, topo):
             lastw[k] = i
             readers[k] = []
 
+    def mark(name, t):
+        marks.setdefault((name, t), []).append(len(nodes) - 1)
+
     def order():
+        for t in range(RO):
+            for row in ROWS:
+                row = [marks[x, t] for x in row.split() if (x, t) in marks]
+                for a, b in zip(row, row[1:]):
+                    for i in b:
+                        nodes[i]["after"] += a
         n = len(nodes)
         cost = [x["cost"] for x in nodes]
         succ, back = [[] for _ in range(n)], [[] for _ in range(n)]
         for i, x in enumerate(nodes):
-            pre = []
+            pre = [(d, cost[d]) for d in x["after"]]
             for d in x["deps"]:
                 y = nodes[d]
                 if y["e"] == x["e"] == "P" or x["e"] == "A":
@@ -107,14 +117,13 @@ def rank_program(g, core, T, topo):
                 else:
                     lag = SAME if y["e"] == x["e"] else PSUM if y["e"] == "P" else CROSS
                 pre.append((d, y["done"] + lag))
-            if x["after"] is not None:
-                pre.append((x["after"], cost[x["after"]]))
             for d, lag in pre:
                 succ[d].append((i, lag))
                 back[i].append((d, lag + cost[i] - cost[d]))
         left = [0.0] * n
-        for i in range(n - 1, -1, -1):
-            left[i] = max([nodes[i]["done"]] + [lag + left[j] for j, lag in succ[i]])
+        for _ in range(3):
+            for i in range(n - 1, -1, -1):
+                left[i] = max([nodes[i]["done"]] + [lag + left[j] for j, lag in succ[i]])
 
         def counts(nxt):
             todo = [0] * n
@@ -269,7 +278,7 @@ def rank_program(g, core, T, topo):
         op("V", g.vector.memset, (o[0], c), {}, [], o[1], span("V", o, []))
 
     def iota(o, pat, base=0, cm=0, fl=True):
-        op("G", g.iota, (o[0], pat, base, cm), dict(allow_small_or_imprecise_dtypes=True) if fl else {}, [], o[1], 130 + 2 * CYC * o[2])
+        op("G", g.iota, (o[0], pat, base, cm), dict(allow_small_or_imprecise_dtypes=True) if fl else {}, [], o[1], 130 + 2 * CYC * o[2], row="iota")
 
     def dma(e, out, in_, sem, rd, wr, done):
         op(e, Q[e].dma_start, (out, in_), {}, rd, wr, 60, done, sem=sem, inc=16, row="dma" + e)
@@ -294,7 +303,8 @@ def rank_program(g, core, T, topo):
         c = WIn.setdefault(name, len(WIn))
         return R(T.WI[:, 16 * c:16 * c + n], "WI.%d" % c)
 
-    w("col")
+    for name, n in (("col", 1), ("g0", 2), ("g1", 2), ("g2", 2), ("KK", 2), ("Ka", 2), ("kb", 2), ("FF", 2), ("KI", 2)):
+        w(name, n)
 
     def col(i):
         return R(T.W[:, i:i + 1], "c%d" % i)
@@ -345,24 +355,22 @@ def rank_program(g, core, T, topo):
            sem="ml%d" % t, inc=tot, auto=True)
         op("A", None, (), {}, ["sentm%d" % t], ["Q%dm" % t], 0, sem="ma%d" % t, inc=tot)
 
-    dma("S", T.sdi[:], T.sd[:], "ld2", [], ["sdi"], 2200)
-    dma("Y", T.tri[:], T.tr[:], "ld3", [], ["tri"], 2600)
-    dma("S", T.ki[:], T.k0[:], "ld1", [], ["ki"], 2300)
-    dma("Y", T.ni[:], T.n0[:], "ld0", [], ["ni"], 3000)
+    dma("S", T.sdi[:], T.sd[:], "ld2", [], ["sdi"], SMALL)
+    dma("Y", T.tri[:], T.tr[:], "ld3", [], ["tri"], SMALL + 300)
+    dma("S", T.ki[:], T.k0[:], "ld1", [], ["ki"], SMALL + 200)
+    dma("Y", T.ni[:], T.n0[:], "ld0", [], ["ni"], SMALL + 400)
     dma("Y", T.X[:, TB:TB + 4096], T.xt[:], "ld4", [], XK, LOAD)
     dma("S", T.wi[:, 0:1], T.wt[:], "ld6", [], ["wi0"], LOAD + 200)
     dma("S", T.thi[:], T.th[:], "ld5", [], ["thi"], LOAD + 200)
 
     iota(whole("PI"), [[0, 16]], 0, 1, fl=False)
-    iota(whole("XR"), [[1, 144]])
-    iota(whole("PC"), [[0, 2], [16, 8]])
     iota(whole("JJ"), [[1, 16], [0, 16]])
-    iota(whole("ONEQ"), [[0, 128]], 1)
-    iota(whole("NONE"), [[0, 128]], -1)
-    for l in LSU[1:]:
-        iota(R(T.V[:, VOFF[l]:VOFF[l] + 256 * l:l], "Vz%d" % l), [[0, 256]], -256)
-    memset(R(T.V[:, VOFF[LSU[0]]:VOFF[LSU[0]] + 256 * LSU[0]:LSU[0]], "Vz%d" % LSU[0]), -256.0)
-    for name, c in (("C2080", 2080.0), ("ZR", 0.0), ("C2048", 2048.0), ("M192", -192.0), ("D1R", 0.0), ("ONES", 1.0), ("VV", 0.0), ("OL", 0.0)):
+    iota(whole("PC"), [[0, 2], [16, 8]])
+    iota(whole("XR"), [[1, 144]])
+    for l in LSU:
+        memset(R(T.V[:, VOFF[l]:VOFF[l] + 256 * l:l], "Vz%d" % l), -256.0)
+    for name, c in (("C2080", 2080.0), ("ZR", 0.0), ("C2048", 2048.0), ("M192", -192.0), ("D1R", 0.0), ("ONES", 1.0),
+                    ("ONEQ", 1.0 / 4096), ("NONE", -1.0), ("VV", 0.0), ("OL", 0.0)):
         memset(whole(name), c)
     memset(R(T.X[:, TB + 4096:TB + 4112], "Xz"), 0.0)
     memset(col(9), 0.0)
@@ -370,15 +378,16 @@ def rank_program(g, core, T, topo):
     cp(col(0), PI1)
     ts(wi("a"), whole("PI"), 15, A.bitwise_and)
     ts(R(T.wj[:, 0:1], "wj0"), PI1, 112, A.bitwise_and)
-    for name, c in (("ID", 1.0), ("I2080", 2080.0), ("NID", -1.0), ("IB", 512.0), ("I1184", 1184.0)):
-        ts(whole(name), R(T.XR[:, :128], "XR"), col(0)[0], A.is_equal, c, A.mult, extra=["c0"])
+    ts(ID, R(T.XR[:, :128], "XR"), col(0)[0], A.is_equal, extra=["c0"])
+    for name, c in (("I2080", 2080.0), ("NID", -1.0), ("IB", 512.0), ("I1184", 1184.0)):
+        aff(whole(name), ID, c)
     ts(col(1), R(T.wj[:, 0:1], "wj0"), 15.0, A.add)
-    for name, c in (("Z", 1.0), ("Z2", 2.0), ("NZ", -1.0)):
-        ts(whole(name), whole("XR"), col(1)[0], A.is_equal, c, A.mult, extra=["c1"])
+    ts(whole("Z"), whole("XR"), col(1)[0], A.is_equal, extra=["c1"])
+    for name, c in (("Z2", 2.0), ("NZ", -1.0)) if any(VMAX) else ():
+        aff(whole(name), whole("Z"), c)
     tt(w("li"), whole("PC"), wi("a"), A.add)
     cp(whole("BC"), wi("a"))
     aff(whole("J1184"), whole("JJ"), 1184.0)
-    aff(whole("ONEQ"), whole("ONEQ"), 1.0 / 4096)
     oc = lambda t, q: R(T.OC[:, 2 * t:2 * t + 2, 8 * q:8 * q + 8], "OC%d.%d" % (t, q))
     base = lambda t: R(T.OL[:, 2 * t:2 * t + 2, 8:16], "OL%d" % t)
     for t in range(RO):
@@ -398,14 +407,14 @@ def rank_program(g, core, T, topo):
     memset(R(T.D1R[:, 0::E], "D1R"), 1.0)
     for h in (0, 1):
         ts(R(T.BV[:, h:h + 1], "BV%d" % h), wi("a2", 1), float(E), A.mult, NR + 14.0 + 8 * E * h, A.add)
-    ts(R(T.BR[:, 0:6], "BR0"), wi("a", 6), float(E), A.mult, NR + 14.0, A.add)
-    ts(R(T.BR[:, 6:8], "BR6"), wi("a", 2), float(E), A.mult, D0 + 14.0, A.add)
+    ts(R(T.BR[:, 0:8], "BR0"), wi("a", 8), float(E), A.mult, NR + 14.0, A.add)
+    ts(R(T.BR[:, 8:10], "BR8"), wi("a", 2), float(E), A.mult, D0 + 14.0, A.add)
     ts(R(T.BY[:], "BY"), wi("a", 4), float(E), A.mult, ON + 15.0, A.add)
     memset(R(T.BY[:, 1:2], "BY"), D0 + 2)
     WT = R(T.wi[:, 0:1], "wi0")
     ts(col(6), WT, 2048.0, A.is_ge, -4096.0, A.mult)
     tt(col(7), col(6), WT, A.add)
-    ts(whole("ZW"), whole("XR"), col(1)[0], A.is_equal, col(7)[0], A.mult, extra=["c1", "c7"])
+    aff(whole("ZW"), whole("Z"), col(7)[0], extra=["c7"])
     aff(R(T.TH[:, 0:16], "TH"), whole("thi"))
     for q in range(4):
         aff(R(T.TH[:, 16 + q:80:4], "TH%d" % q), whole("thi"))
@@ -413,19 +422,17 @@ def rank_program(g, core, T, topo):
     def tn(t, a, b):
         return R(T.TN[:, t % 2, 16 * a:16 * b], *(["TN%d" % (t % 2)] * (a < 10 + t) + ["NP%d" % (t % 2)] * (b > 10 + t)))
 
-    def seeds(t, nb, extra):
-        n = 16 * (nb + extra)
-        mm(R(T.pY[:, :n], "pY"), ID, R(T.C2080[:, :n], "C2080"), start=True)
-        mm(R(T.pY[:, 256:256 + 16 * nb], "pY"), ID, R(T.J1184[:, :16 * nb], "J1184"))
+    def seeds(t, nb):
+        n = 16 * nb
+        mm(R(T.pY[:, :n + 16], "pY"), ID, R(T.C2080[:, :n + 16], "C2080"), start=True)
+        mm(R(T.pY[:, 256:256 + n], "pY"), ID, R(T.J1184[:, :n], "J1184"))
         sr = lambda k: R(T.SR[:, t, :k], "SR0", "SR1", "SR2", "SR3")
+        for c in range(0, n + 16, 64):
+            mm(R(T.pY[:, c:min(c + 64, n + 16)], "pY"), ID, sr(min(64, n + 16 - c)))
         for c in range(0, n, 64):
-            mm(R(T.pY[:, c:min(c + 64, n)], "pY"), ID, sr(min(64, n - c)))
-        for c in range(0, 16 * nb, 64):
-            k = min(64, 16 * nb - c)
-            mm(R(T.pY[:, 256 + c:256 + c + k], "pY"), whole("I2080"), sr(k), stop=c + k == n)
-        if extra:
-            mm(R(T.pY[:, 256 + 16 * nb:256 + n], "pY"), whole("I2080"), sr(16))
-            mm(R(T.pY[:, 256 + 16 * nb:256 + n], "pY"), whole("I1184"), me(0), stop=True)
+            mm(R(T.pY[:, 256 + c:256 + min(c + 64, n)], "pY"), whole("I2080"), sr(min(64, n - c)))
+        mm(R(T.pY[:, 256 + n:272 + n], "pY"), whole("I2080"), sr(16))
+        mm(R(T.pY[:, 256 + n:272 + n], "pY"), whole("I1184"), me(0), stop=True)
 
     def columns(src, a, b, key):
         part_ = lambda name: R(T[name][:, 16 * a:16 * b], name + key)
@@ -456,21 +463,27 @@ def rank_program(g, core, T, topo):
         of = lambda q: R(T.pK[:, :, 8 * q:8 * q + 8], "pK")
         tt(whole("OFN"), sc(ON, 14) if t else me(0), base(t), A.add)
         mm(R(T.pK[:, :, 0:16], "pK"), ID, R(T.OC[:, 2 * t:2 * t + 2, :], "OC%d.0" % t, "OC%d.1" % t), start=True)
-        terms = ((0, d1(14)), (0, sc(ON, 15)), (1, sc(ON, 15)), (0, tile("RES", 6)), (0, tile("RES", 7)), (0, tile("RES", 2)), (1, tile("RES", 3)))
+        terms = ((0, d1(14)), (0, sc(ON, 15)), (1, sc(ON, 15)), (0, tile("RES", 8)), (0, tile("RES", 9)), (0, tile("RES", 2)), (1, tile("RES", 3)))
         terms = terms if t else ((0, me(2)), (1, me(3)))
         for x, (q, r) in enumerate(terms):
             mm(of(q), NID if t and x == 0 else ID, r, stop=x == len(terms) - 1)
         tt(whole("OFU"), R(T.pK[:, :, 0:16], "pK"), R(T.OL[:, 2 * t:2 * t + 2, :], "OL", "OL%d" % t), A.max)
 
-    for r in (0, 1):
-        ts(R(T.SR[:, :, 16 * r:16 * r + 16], "SR%d" % r), whole("sdi"), -2048.0, A.add)
-        aff(R(T.SR[:, :, 16 * r + 32:16 * r + 48], "SR%d" % (r + 2)), whole("sdi"), 1.0, -2048.0)
-    ts(whole("TP"), whole("tri"), -2048.0, A.add)
-    seeds(0, 10, 0)
-    cp(ct(0, 10), columns(R(T.TP[:, :160], "TP"), 0, 10, "a"))
+    for r in range(4):
+        aff(R(T.SR[:, :, 16 * r:16 * r + 16], "SR%d" % r), whole("sdi"), 1.0, -2048.0)
+    aff(R(T.TP[:, 160:], "TP"), R(T.tri[:, 160:], "tri"), 1.0, -2048.0)
     aff(tn(0, 0, 10), R(T.tri[:, :160], "tri"), 1.0, -2048.0)
+    first = lambda name, key="a": R(T[name][:, :160], name + key)
+    s0 = R(T.sdi[:, 0:16], "sdi")
+    ts(w("s0"), s0, 32.0, A.add)
+    ts(w("b0"), s0, -2048.0, A.add, 2080.0, A.mult)
+    ts(first("WW", ""), first("tri", ""), -2048.0, A.add)
+    tt(first("MK", ""), IX(w("b0")[0], T.BC[:, 0:10], "BC", *w("b0")[1]), first("J1184", ""), A.add)
+    tt(first("Y0"), IX(w("s0")[0], T.BC[:, 0:10], "BC", *w("s0")[1]), first("WW", ""), A.mult)
+    tt(first("NI"), first("Y0"), first("MK", ""), A.add)
+    ts(first("NJ"), first("NI"), 5, A.arith_shift_right, 4095, A.bitwise_and)
+    cp(ct(0, 10), first("NJ"))
     for x, (least, c1, c2) in enumerate(((2.0, 1.0, -0.5), (4.0, 2.0, -0.25), (8.0, 4.0, -0.125))):
-        w("g%d" % x, 2)
         ts(w("g%d" % x, 1, 0), whole("ki"), least, A.is_ge, c1, A.mult)
         ts(w("g%d" % x, 1, 1), whole("ki"), least, A.is_ge, c2, A.mult)
     tt(w("g0", 2), w("g0", 2), w("g1", 2), A.add)
@@ -485,33 +498,38 @@ def rank_program(g, core, T, topo):
     tt(tile("RES", 2), me(2), me(0), A.subtract)
     ts(me(4), me(3), -1.0, A.add, 0.0, A.max)
     offsets(0)
+    act(w("Ka", 1, 0), w("KK", 1, 0), F.Relu, 0.5, -1.0)
+    aff(w("Ka", 1, 1), w("KK", 1, 0), 2.0, -1.0)
+    tt(tile("RES", 7), w("Ka", 1, 1), whole("ki"), A.subtract)
+    aff(w("kb", 1, 0), tile("RES", 7), 8.0)
+    tt(tile("RES", 6), w("Ka", 1, 0), w("kb", 1, 0), A.add)
 
     pC = R(T.pU[:, 64:96], "pU")
     sums = R(T.pS[:, 16:80], "pS")
 
     def post(t):
+        last = t == RO - 1
         tt(sc(D0, 1, step=4), sums, R(T.LIM[:], "LIM0", "LIM1"), A.is_gt)
         scan(R(T.SC[:, ON:ON + 16 * E], "SC%d" % ON), R(T.SC[:, 0:16 * E], *D0K), R(T.D1[:], *D1K), A.mult, A.add)
         scan(R(T.SC[:, NR:NR + 16 * E], "SC%d" % NR), R(T.SC[:, 0:16 * E], *D0K), whole("D1R"), A.mult, A.add)
         ts(whole("AH"), sums, col(9)[0], A.is_le, extra=["c9"])
+        if not last:
+            mm(R(T.pU[:, 16:32], "pU"), whole("ONEQ"), nok4, start=True)
+            mm(R(T.pU[:, 16:32], "pU"), whole("NONE"), sc(NR, 14), stop=True)
+            act(w("junk"), R(T.pU[:, 16:32], "pU"), F.Identity, 1.0, 1100.0, accum=col(8))
+            aff(R(T.FL[:, 0:1], "FL"), col(8), 0.0625, -0.46875)
+            aff(col(9), R(T.FL[:, 0:1], "FL"), -16.0, col(8)[0], extra=["c8"])
         mm(pC, ID, whole("VV"), start=True)
         for x in (0, 1):
             mm(pC, ID, R(T.AH[:, x::2], "AH"), stop=x == 1)
-        tt(whole("VC"), pC, whole("NF2"), A.min)
-        if t == RO - 1:
+        tt(whole("VC"), pC, R(T.NF2[:], "NF0", "NF1"), A.min)
+        if last:
             return
         tt(whole("VV"), IX(T.SC[:, 0:ON], T.BV[:], "SC%d" % NR, "BV0", "BV1", *D0K), whole("VC"), A.mult)
-        tt(tile("RES", 0, 8), IX(T.SC[:, 0:ON], T.BR[:], "SC%d" % NR, "BR0", "BR6", *D0K), tile("CA", 0, 8), A.mult)
+        tt(tile("RES", 0, 10), IX(T.SC[:, 0:ON], T.BR[:], "SC%d" % NR, "BR0", "BR8", *D0K), tile("CA", 0, 10), A.mult)
         offsets(t + 1)
-        mm(R(T.pU[:, 16:32], "pU"), whole("ONEQ"), nok4, start=True)
-        mm(R(T.pU[:, 16:32], "pU"), whole("NONE"), sc(NR, 14), stop=True)
         tt(me(0, 4), IX(T.SC[:], T.BY[:], "SC%d" % ON, "SC%d" % NR, "BY", *D0K), tile("RES", 0, 4), A.add)
         ts(me(4), me(3), -1.0, A.add, 0.0, A.max)
-        act(w("junk"), R(T.pU[:, 16:32], "pU"), F.Identity, 1.0, 1100.0, accum=col(8))
-        aff(R(T.FL[:, 0:1], "FL"), col(8), 0.0625, -0.46875)
-        aff(col(9), R(T.FL[:, 0:1], "FL"), -16.0, col(8)[0], extra=["c8"])
-
-    w("FF", 2)
 
     for t in range(RO):
         S_, L, last = SL[t], LS[t], t == RO - 1
@@ -522,6 +540,7 @@ def rank_program(g, core, T, topo):
             c = 256 * (t % 2) + 16 * j
             (cp if e == "V" else scp)(R(T.V[:, vo + 128 * L * a + 1 + j:vo + 128 * L * b:L], *["V%d.%d.%d" % (L, j, x) for x in range(a, b)]),
                                       IX(T.X[:, TB:TB + 4096], T.CT[:, c + 8 * a:c + 8 * b], "CT%d" % (t % 2), *XK))
+            mark("g%s%d" % (e, h), t)
 
         pn = lambda h, a=0, s=1: R(T.RP[:, h, RW + a:RW + 128:s], "Pn%d" % h)
 
@@ -529,26 +548,30 @@ def rank_program(g, core, T, topo):
             r0, v0 = RW - 128 * L, vo + 128 * L * h
             scan(R(T.RP[:, h, r0:RW], "R%d" % h), R(T.V[:, v0:v0 + 128 * L], "Vz%d" % L, *["V%d.%d.%d" % (L, j, h) for j in range(S_)]),
                  R(T.ZR[:, :128 * L], "ZR"), A.add, A.max)
+            mark("scan%d" % h, t)
             src = IX(T.RP[:, h, r0:RW], T.OFN[:, 8 * h:8 * h + 8], "R%d" % h, "OFN")
             if t > 0:
                 tt(pn(h), src, R(T.VN[:, 128 * h:128 * h + 128], "VN"), A.add)
             else:
                 cp(pn(h), src)
+            mark("pick%d" % h, t)
             send(t, h, "n")
             scp(R(T.RP[:, h, PA:PA + 256], "PA%d" % h), IX(T.RP[:, h, r0:RW + 128], T.OFU[:, h, :], "R%d" % h, "Pn%d" % h, "OFU"))
+            mark("points%d" % h, t)
             send(t, h, "v")
             aff(R(T.VT[:, 128 * h:128 * h + 128], "VT%d" % h), pn(h), 0.0625, 191.53125)
 
         def compare_lengths():
-            pl = lambda a, n=1: R(T.pN[:, 128 + 16 * a:128 + 16 * (a + n)], "pN")
+            pl = lambda a, n=1: R(T.pV0[:, a:a + n, 0, :], "pV0")
             mm(pl(0, 2), ID, me(0, 2), start=True)
             for c, q in ((2, 4), (3, 4), (4, 2), (5, 2)):
                 mm(pl(c), ID, me(q))
             for c in (2, 5):
                 mm(pl(c), ID, R(T.ONES[:, :16], "ONES"))
             for c, q in enumerate((0, 1, 3, 2, 2, 3)):
-                mm(pl(c), NID, R(T.QM[:, 2 * t:2 * t + 2, 8 + 16 * q:16 + 16 * q], "Q%dm" % t, "PA1"), stop=c == 5)
+                mm(pl(c), NID, R(T.QM[:, 2 * t:2 * t + 2, 8 + 16 * q:16 + 16 * q], "Q%dm" % t), stop=c == 5)
             act(whole("DL"), pl(0, 6), F.Abs)
+            mark("lengths", t)
 
         def compare_n(h):
             qn = lambda a=0, s=1: R(T.Q[:, 2 * t + h, a:128:s], "Q%d%dn" % (t, h))
@@ -564,31 +587,42 @@ def rank_program(g, core, T, topo):
             if VMAX[h]:
                 for x in range(16):
                     mm(o, rows("NZ", x), qn(x, 16))
+                    mark("diff%d" % h, t)
                 tt(dn(), pn(h), qn(), A.max)
+                mark("max%d" % h, t)
             else:
                 pn_ = R(T.pN[:, 0:128], "pN")
                 mm(pn_, ID, pn(h), start=True)
                 mm(pn_, NID, qn(), stop=True)
+                mark("diff%d" % h, t)
                 act(dn(), pn_, F.Abs)
+                mark("size%d" % h, t)
             for x in range(16):
                 mm(o, rows("Z2" if VMAX[h] else "Z", x), dn(x, 16), stop=x == 15)
+                mark("sum%d" % h, t)
             so = R(T.SOU[:, 8 * h:8 * h + 8], "SOU%d" % h)
             ts(sc(D0, 14, h), o, col(9)[0], A.is_gt, 4096.0, A.mult, extra=["c9"])
+            mark("ok%d" % h, t)
             tt(so, w("colx", h=h), sc(D0, 14, h), A.subtract if h == 0 else A.add)
             tt(IX(T.X[:, 6144 * h:6144 * h + 6144], so[0], XK[h], *["Xz"] * h),
                R(T.VT[:, 128 * h:128 * h + 128], "VT%d" % h, *so[1]), whole("M192"), A.add)
-            ts(d1(15, h), o, col(9)[0], A.is_le, extra=["c9"])
+            mark("write%d" % h, t)
+            ts(d1(15, h), sc(D0, 14, h), 0.0, A.is_equal)
 
         def compare_v(h):
             bk = "pV%d" % h
             for x, a in enumerate((128, 128, 0, 0)):
                 mm(R(T[bk][:, :, x, :], bk), ID, R(T.RP[:, h, PA + a:PA + a + 128], "PA%d" % h), start=x == 0)
+                mark("own%d" % h, t)
             for x, a in enumerate((256, 128, 128, 256)):
                 mm(R(T[bk][:, :, x, :], bk), NID, R(T.Q[:, 2 * t + h, a:a + 128], "Q%d%dv" % (t, h)), stop=x == 3)
+                mark("diffs%d" % h, t)
             act(R(T.DV[:, 512 * h:512 * h + 512], "DV%d" % h), whole(bk), F.Abs)
+            mark("sizes%d" % h, t)
 
         if t > 0:
             scp(whole("VN"), IX(T.X[:, TB:TB + 4112], T.VOU[:], "Xz", "VOU", *XK))
+            mark("new", t)
             update(t)
             post(t - 1)
         send_lengths(t)
@@ -599,8 +633,8 @@ def rank_program(g, core, T, topo):
                 gather("S", j, 1)
                 gather("V" if j >= S_ - NH[t] else "S", j, 0)
         if not last:
-            seeds(t + 1, 10 + t, 1)
-            cp(ct(t + 1, 10 + t), columns(tn(t, 0, 10 + t), 0, 10 + t, "a"))
+            seeds(t + 1, 10 + t)
+            aff(ct(t + 1, 10 + t), columns(tn(t, 0, 10 + t), 0, 10 + t, "a"))
         folds(1)
         folds(0)
         for a in range(16):
@@ -618,33 +652,36 @@ def rank_program(g, core, T, topo):
         tt(d1(5), me(4), me(2), A.subtract)
         aff(d1(13), tile("RES", 2), 1.0 / 4096)
         aff(d1(14), me(0))
-        aff(w("K2"), tile("RES", 4), 200.5, 99.5)
-        aff(w("hK"), me(1), 100.0)
-        tt(w("H"), w("K2"), w("hK"), A.subtract)
         for x in (0, 1):
-            act(R(T.H2[:, x::2], "H2%d" % x), w("H"), F.Relu)
-        act(whole("NF2"), R(T.H2[:], "H20", "H21"), F.Relu, 1.0, -3.0)
-        tt(whole("ND"), R(T.H2[:], "H20", "H21"), whole("VV"), A.subtract)
+            aff(R(T.NF2[:, x::2], "NF%d" % x), tile("RES", 7), 8.0)
+            tt(R(T.ND[:, x::2], "ND%d" % x), tile("RES", 6), R(T.VV[:, x::2], "VV"), A.subtract)
         for x in (0, 1):
-            aff(R(T.LIM[:, x::2], "LIM%d" % x), whole("ND"), -16384.0, col(9)[0], extra=["c9"])
+            aff(R(T.LIM[:, x::2], "LIM%d" % x), R(T.ND[:], "ND0", "ND1"), -16384.0, col(9)[0], extra=["c9"])
         if last:
             aff(sc(D0, 15), me(1))
             memset(R(T.D1R[:, 15::E], "D1R"), 1.0)
         else:
-            act(w("f0"), R(T.NF2[:, 0::2], "NF2"), F.Relu, -1.0, 1.0)
-            aff(w("FF", 1, 0), w("f0"), 1.0, 1.0)
-            aff(w("FF", 1, 1), w("f0"), -0.5, 1.0)
-            aff(w("KI", 2), tile("RES", 4, 2), 1.0, 1.0)
+            ts(w("FF", 1, 0), tile("RES", 7), 0.0, A.is_equal, 1.0, A.add)
+            ts(w("FF", 1, 1), tile("RES", 7), 0.0, A.not_equal, 1.0, A.add)
+            aff(w("KI", 1, 0), tile("RES", 4), 1.0, 1.0)
+            aff(w("KI", 1, 1), tile("RES", 5), 0.5, 0.5)
             tt(w("KK", 2), w("KI", 2), w("FF", 2), A.mult)
             aff(tile("CA", 4, 2), w("KK", 2), 1.0, -1.0)
             tt(w("x1"), me(0), w("KK", 1, 1), A.mult)
             ts(wi("fl"), w("x1"), -0.4375, A.add)
             tt(w("x3"), wi("fl"), w("KK", 1, 0), A.mult)
             tt(tile("CA", 2), w("x3"), me(0), A.subtract)
-            tt(tile("CA", 3), tile("CA", 2), tile("CA", 4), A.subtract)
+            aff(w("n1"), me(0), 1.0, -1.0)
+            tt(w("nK"), w("n1"), w("KK", 1, 0), A.add)
+            tt(tile("CA", 3), w("x3"), w("nK"), A.subtract)
             aff(tile("CA", 1), me(1))
-            aff(tile("CA", 6), w("li"), (LS[t + 1] - 1) / 4096, -LS[t + 1] / 32)
-            aff(tile("CA", 7), me(0), 1.0 / 4096, 1.0 / 4096)
+            aff(w("kb", 1, 0), me(1), 8.0)
+            aff(w("kb", 1, 1), me(1))
+            aff(w("Ka", 1, 0), w("KK", 1, 0), 16.5, -17.0)
+            aff(w("Ka", 1, 1), w("KK", 1, 0), 2.0, -2.0)
+            tt(tile("CA", 6, 2), w("Ka", 2), w("kb", 2), A.subtract)
+            aff(tile("CA", 8), w("li"), (LS[t + 1] - 1) / 4096, -LS[t + 1] / 32)
+            aff(tile("CA", 9), me(0), 1.0 / 4096, 1.0 / 4096)
         compare_lengths()
         compare_n(1)
         if last:
@@ -655,6 +692,7 @@ def rank_program(g, core, T, topo):
             tt(whole("VOU"), columns(tn(t, 10 + t, 11 + t), 10 + t, 11 + t, "b"), nok4, A.max)
         compare_v(0)
         mm(sums, NID, R(T.TH[:, 16:80], "TH0", "TH1", "TH2", "TH3"), start=True)
+        mark("votes", t)
         for x in range(4):
             mm(R(T.pS[:, 16 + x:80:4], "pS"), IB, R(T.DL[:, 32 + 16 * x:48 + 16 * x], "DL"))
         for x in range(16):

@@ -16,15 +16,18 @@ RW = 1920
 PA = RW + 128
 TB = 4096
 E = 16
-NV = [4, 3, 3, 3, 4, 4]
-NS = [3, 3, 4, 4, 4, 5]
+NV = [4, 3, 4, 4, 4, 5]
+NS = [2, 3, 3, 3, 4, 4]
 NH = [0, 0, 0, 0, 0, 0]
-VMAX = (1, 0)
-ROWS = ["gS2 gS1 new gS0", "pick1 scan0", "write1 ok0", "points1 lengths", "sum0 votes", "size1 size0 sizes1 sizes0"]
+N2, CUT = [2] * 6, 64
+MKP = 1
+VMAX = (1, 1)
+ROWS = ["gSabc gSc new gSab gSa gSb", "pick1 scanab scana scanb", "write1 ok0", "points0 lengths", "sum0 votes", "size1 size0 sizes1 sizes0"]
 CYC, PCYC, GATHER, SCATTER, VMIN, SMIN, PMIN = 0.84, 0.42, 1.15, 4.0, 45, 62, 44
-SAME, CROSS, PSUM, WAKE, ISSUE, REMOTE, FIRST, SMALL, LOAD = 200, 250, 300, 110, 90, 1150, 1500, 1700, 4200
-PASSES, WIDE = 4, 8
-PLAN = []
+SAME, CROSS, PSUM, WAKE, ISSUE, REMOTE, FIRST, SMALL, LOAD = 200, 250, 300, 110, 90, 1150, 1500, 1700, 3900
+STORE = 1800
+PASSES, WIDE, TRIES = 6, 8, 1000
+PLAN, ORDER = [], []
 
 f32, bf, f16, i32, u16 = "float32", "bfloat16", "float16", "int32", "uint16"
 SCRATCH = {
@@ -42,7 +45,9 @@ SCRATCH = {
     "BV": ("sbuf", [128, 2], u16), "OFU": ("sbuf", [128, 2, 16], u16), "OFN": ("sbuf", [128, 16], u16),
     "SOU": ("sbuf", [128, 16], u16), "VOU": ("sbuf", [128, 16], u16),
     "OC": ("sbuf", [128, 2 * RO, 16], f16), "OL": ("sbuf", [128, 2 * RO, 16], f32),
-    "TH": ("sbuf", [128, 80], bf), "AH": ("sbuf", [128, 64], bf), "LIM": ("sbuf", [128, 64], f32), "ONES": ("sbuf", [128, 32], bf),
+    "TH": ("sbuf", [128, 80], bf), "AH": ("sbuf", [128, 64], bf), "LIM": ("sbuf", [128, 64], f32), "ONES": ("sbuf", [128, 16], bf),
+    "GG": ("sbuf", [128, 144], bf), "NB": ("sbuf", [128, 48], i32), "I2": ("sbuf", [128, 128], bf), "IG": ("sbuf", [128, 128], bf),
+    "JB": ("sbuf", [128, 256], bf), "SB": ("sbuf", [128, 16], bf),
     "SC": ("sbuf", [128, 48 * E], bf), "D1": ("sbuf", [128, 16 * E], bf), "D1R": ("sbuf", [128, 16 * E], bf),
     "CA": ("sbuf", [128, 160], f32), "RES": ("sbuf", [128, 160], f16),
     "M": ("sbuf", [128, 80], bf), "QM": ("sbuf", [128, 2 * RO, 80], bf), "DL": ("sbuf", [128, 96], bf),
@@ -59,7 +64,7 @@ SCRATCH = {
     "pS": ("psum", [128, 512], f32), "pU": ("psum", [128, 512], f32),
     "pT": ("psum", [128, 512], f32), "pY": ("psum", [128, 512], f32), "pK": ("psum", [128, 2, 256], f32),
 }
-SEMAPHORES = (["cV", "cS", "cP", "cG"] + ["ld%d" % i for i in range(8)] + ["st%d" % i for i in range(4)]
+SEMAPHORES = (["cV", "cS", "cP", "cG"] + ["ld%d" % i for i in range(8)] + ["st%d" % i for i in range(5)]
               + ["ml%d" % t for t in range(RO)] + ["ma%d" % t for t in range(RO)]
               + ["dl%d" % i for i in range(4 * RO)] + ["da%d" % i for i in range(4 * RO)])
 
@@ -193,7 +198,29 @@ def rank_program(g, core, T, topo):
                 best = (end, start)
             late = way(back, tail, [best[1][i] + cost[i] for i in range(n)])
             left = [late[i] + cost[i] for i in range(n)]
-        PLAN.append(best[0])
+        stones = [marks[x, t][-1] for t in range(RO) for x in ("write0", "pick0", "pick1", "write1")]
+        worth = lambda s: max(s[i] + nodes[i]["done"] for i in range(n)) + 0.1 * sum(s[i] for i in stones)
+        seed = [1]
+
+        def draw():
+            seed[0] = (seed[0] * 1103515245 + 12345) % 2147483648
+            return seed[0] / 2147483648
+
+        pick = lambda xs: xs[int(draw() * len(xs))]
+        now = best = (worth(best[1]), best[1])
+        for x in range(TRIES):
+            mid, wide, step = draw() * end, pick((1000, 2500, 5000, 60000)), pick((100, 300, 800, 1500))
+            queues, share = pick(("V", "S", "P", "VS", "VSP")), pick((0.05, 0.3))
+            rank_ = [-s + (step * (2 * draw() - 1) if abs(s - mid) < wide and y["e"] in queues and draw() < share else 0)
+                     for s, y in zip(now[1], nodes)]
+            if x % 4 == 3:
+                late = place(back, tail, [cost[i] - rank_[i] for i in range(n)])
+                rank_ = [late[i] + cost[i] for i in range(n)]
+            start = place(succ, [0.0] * n, rank_)
+            if worth(start) <= now[0] + 60 * (1 - x / TRIES):
+                now = (worth(start), start)
+                best = min(best, now)
+        PLAN.append(max(best[1][i] + nodes[i]["done"] for i in range(n)))
         return sorted(range(n), key=lambda i: (best[1][i], i))
 
     def emit():
@@ -210,7 +237,9 @@ def rank_program(g, core, T, topo):
                 if know[e].get(s2, 0) < c2:
                     know[e][s2] = c2
 
-        for i in order():
+        if not ORDER:
+            ORDER.extend(order())
+        for i in ORDER:
             x = nodes[i]
             e, s = x["e"], x["sem"]
             cnt[s] = cnt.get(s, 0) + x["inc"]
@@ -379,7 +408,7 @@ def rank_program(g, core, T, topo):
     ts(wi("a"), whole("PI"), 15, A.bitwise_and)
     ts(R(T.wj[:, 0:1], "wj0"), PI1, 112, A.bitwise_and)
     ts(ID, R(T.XR[:, :128], "XR"), col(0)[0], A.is_equal, extra=["c0"])
-    for name, c in (("I2080", 2080.0), ("NID", -1.0), ("IB", 512.0), ("I1184", 1184.0)):
+    for name, c in (("I2080", 2080.0), ("NID", -1.0), ("IB", 512.0), ("I1184", 1184.0), ("I2", 2.0), ("IG", 2.0625)):
         aff(whole(name), ID, c)
     ts(col(1), R(T.wj[:, 0:1], "wj0"), 15.0, A.add)
     ts(whole("Z"), whole("XR"), col(1)[0], A.is_equal, extra=["c1"])
@@ -388,6 +417,7 @@ def rank_program(g, core, T, topo):
     tt(w("li"), whole("PC"), wi("a"), A.add)
     cp(whole("BC"), wi("a"))
     aff(whole("J1184"), whole("JJ"), 1184.0)
+    aff(whole("JB"), whole("JJ"), -1.0)
     oc = lambda t, q: R(T.OC[:, 2 * t:2 * t + 2, 8 * q:8 * q + 8], "OC%d.%d" % (t, q))
     base = lambda t: R(T.OL[:, 2 * t:2 * t + 2, 8:16], "OL%d" % t)
     for t in range(RO):
@@ -403,7 +433,7 @@ def rank_program(g, core, T, topo):
     memset(R(T.D1[:], *D1K), 0.0)
     memset(tile("CA", 0), 0.0)
     memset(sc(D0, 0), 0.0)
-    memset(sc(D0, 6), 1.0 / 4096)
+    memset(sc(D0, 10), 1.0 / 4096)
     memset(R(T.D1R[:, 0::E], "D1R"), 1.0)
     for h in (0, 1):
         ts(R(T.BV[:, h:h + 1], "BV%d" % h), wi("a2", 1), float(E), A.mult, NR + 14.0 + 8 * E * h, A.add)
@@ -454,8 +484,15 @@ def rank_program(g, core, T, topo):
             mm(R(T.pT[:, 256:512], "pT"), ID, whole("C2048"))
         for j in range(nb):
             mm(R(T.pT[:, 16 * j:16 * j + 16], "pT"), ID, new, stop=j == nb - 1)
-        tt(whole("SIG"), me(0), nok4, A.add)
-        tt(R(T.MK[:, :n], "MK"), IX(T.SIG[:], T.BC[:, 0:nb], "SIG", "BC"), R(T.JJ[:, :n], "JJ"), A.is_equal)
+        if MKP and t < RO:
+            tt(whole("SB"), me(0), nok4, A.add)
+            mm(R(T.pN[:, :n], "pN"), ID, R(T.JB[:, :n], "JB"), start=True)
+            for j in range(nb):
+                mm(R(T.pN[:, 16 * j:16 * j + 16], "pN"), ID, whole("SB"), stop=j == nb - 1)
+            ts(R(T.MK[:, :n], "MK"), R(T.pN[:, :n], "pN"), 0.0, A.is_equal)
+        else:
+            tt(whole("SIG"), me(0), nok4, A.add)
+            tt(R(T.MK[:, :n], "MK"), IX(T.SIG[:], T.BC[:, 0:nb], "SIG", "BC"), R(T.JJ[:, :n], "JJ"), A.is_equal)
         tt(R(T.WW[:, :n], "WW"), R(T.pT[:, :n], "pT"), R(T.MK[:, :n], "MK"), A.mult)
         tt(whole("YT") if t == RO else tn(t, 0, nb), R(T.pT[:, 256:256 + n], "pT"), R(T.WW[:, :n], "WW"), A.add)
 
@@ -483,28 +520,32 @@ def rank_program(g, core, T, topo):
     tt(first("NI"), first("Y0"), first("MK", ""), A.add)
     ts(first("NJ"), first("NI"), 5, A.arith_shift_right, 4095, A.bitwise_and)
     cp(ct(0, 10), first("NJ"))
-    for x, (least, c1, c2) in enumerate(((2.0, 1.0, -0.5), (4.0, 2.0, -0.25), (8.0, 4.0, -0.125))):
-        ts(w("g%d" % x, 1, 0), whole("ki"), least, A.is_ge, c1, A.mult)
-        ts(w("g%d" % x, 1, 1), whole("ki"), least, A.is_ge, c2, A.mult)
-    tt(w("g0", 2), w("g0", 2), w("g1", 2), A.add)
+    gt = lambda q, n=1: R(T.GG[:, 16 * q:16 * (q + n)], *["GG%d" % x for x in range(q, q + n)])
+    for x in range(3):
+        ts(gt(x), whole("ki"), 2.0 ** (x + 1), A.is_ge, 2.0 ** x, A.mult)
+        aff(gt(3 + x), gt(x), -0.5 / 4 ** x)
+        ts(R(T.NB[:, 16 * x:16 * x + 16], "NB%d" % x), whole("ni"), x, A.arith_shift_right, 1, A.bitwise_and)
+    tt(gt(6, 3), gt(0, 3), R(T.NB[:], "NB0", "NB1", "NB2"), A.mult)
     aff(me(0), whole("ni"))
     aff(me(1), whole("ki"))
-    tt(tile("RES", 4, 2), w("g0", 2), w("g2", 2), A.add)
-    ts(w("KK", 2), tile("RES", 4, 2), 1.0, A.add)
-    tt(w("x1"), whole("ni"), w("KK", 1, 1), A.mult)
-    ts(wi("fl"), w("x1"), -0.4375, A.add)
-    tt(me(2), wi("fl"), w("KK", 1, 0), A.mult)
-    tt(me(3), me(2), tile("RES", 4), A.subtract)
-    tt(tile("RES", 2), me(2), me(0), A.subtract)
-    ts(me(4), me(3), -1.0, A.add, 0.0, A.max)
-    offsets(0)
-    act(w("Ka", 1, 0), w("KK", 1, 0), F.Relu, 0.5, -1.0)
-    aff(w("Ka", 1, 1), w("KK", 1, 0), 2.0, -1.0)
-    tt(tile("RES", 7), w("Ka", 1, 1), whole("ki"), A.subtract)
-    aff(w("kb", 1, 0), tile("RES", 7), 8.0)
-    tt(tile("RES", 6), w("Ka", 1, 0), w("kb", 1, 0), A.add)
 
-    pC = R(T.pU[:, 64:96], "pU")
+    def tiles(bank, terms):
+        for x, (q, l, r) in enumerate(terms):
+            mm(R(T[bank][:, 16 * q:16 * q + 16], bank), l, r, x == 0, x == len(terms) - 1)
+
+    tiles("pT", [(0, ID, me(0)), (1, ID, me(0))] + [(1, NID, gt(x)) for x in range(3)] + [(q, NID, gt(x)) for x in (6, 7, 8) for q in (0, 1)])
+    aff(me(2, 2), R(T.pT[:, 0:32], "pT"))
+    act(me(4), R(T.pT[:, 16:32], "pT"), F.Relu, 1.0, -1.0)
+    offsets(0)
+    tiles("pY", [(4, ID, gt(x)) for x in range(3)] + [(5, ID, gt(x)) for x in (3, 4, 5)] + [(q, NID, me(1)) for q in (6, 7)]
+          + [(q, ID, whole("ONES")) for q in (6, 7)] + [(7, whole("I2"), gt(x)) for x in range(3)]
+          + [(6, whole("IG" if x else "I2"), gt(x)) for x in range(3)])
+    aff(tile("RES", 4, 2), R(T.pY[:, 64:96], "pY"))
+    aff(tile("RES", 6), R(T.pY[:, 96:112], "pY"), 8.0)
+    aff(tile("RES", 7), R(T.pY[:, 112:128], "pY"))
+    tt(tile("RES", 2), me(2), me(0), A.subtract)
+
+    pC = R(T.pN[:, 256:288], "pN")
     sums = R(T.pS[:, 16:80], "pS")
 
     def post(t):
@@ -535,28 +576,34 @@ def rank_program(g, core, T, topo):
         S_, L, last = SL[t], LS[t], t == RO - 1
         vo = VOFF[L]
 
-        def gather(e, j, h):
-            a, b = (0, 2) if h == 2 else (h, h + 1)
+        runs = {"a": (0, CUT), "b": (CUT, 128), "c": (128, 256)}
+
+        def gather(e, j, xs):
+            a, b = runs[xs[0]][0], runs[xs[-1]][1]
             c = 256 * (t % 2) + 16 * j
-            (cp if e == "V" else scp)(R(T.V[:, vo + 128 * L * a + 1 + j:vo + 128 * L * b:L], *["V%d.%d.%d" % (L, j, x) for x in range(a, b)]),
-                                      IX(T.X[:, TB:TB + 4096], T.CT[:, c + 8 * a:c + 8 * b], "CT%d" % (t % 2), *XK))
-            mark("g%s%d" % (e, h), t)
+            (cp if e == "V" else scp)(R(T.V[:, vo + L * a + 1 + j:vo + L * b:L], *["V%d.%d.%s" % (L, j, x) for x in xs]),
+                                      IX(T.X[:, TB:TB + 4096], T.CT[:, c + a // 16:c + b // 16], "CT%d" % (t % 2), *XK))
+            mark("g" + e + xs, t)
 
         pn = lambda h, a=0, s=1: R(T.RP[:, h, RW + a:RW + 128:s], "Pn%d" % h)
 
         def folds(h):
-            r0, v0 = RW - 128 * L, vo + 128 * L * h
-            scan(R(T.RP[:, h, r0:RW], "R%d" % h), R(T.V[:, v0:v0 + 128 * L], "Vz%d" % L, *["V%d.%d.%d" % (L, j, h) for j in range(S_)]),
-                 R(T.ZR[:, :128 * L], "ZR"), A.add, A.max)
-            mark("scan%d" % h, t)
-            src = IX(T.RP[:, h, r0:RW], T.OFN[:, 8 * h:8 * h + 8], "R%d" % h, "OFN")
+            r0 = RW - 128 * L
+            for xs in ["c"] if h else ["a", "b"] if N2[t] else ["ab"]:
+                a, b = runs[xs[0]][0], runs[xs[-1]][1]
+                scan(R(T.RP[:, h, r0 + (a - 128 * h) * L:r0 + (b - 128 * h) * L], *["R" + x for x in xs]),
+                     R(T.V[:, vo + a * L:vo + b * L], "Vz%d" % L, *["V%d.%d.%s" % (L, j, x) for j in range(S_) for x in xs]),
+                     R(T.ZR[:, :(b - a) * L], "ZR"), A.add, A.max)
+                mark("scan" + xs, t)
+            rk = ["Rc"] if h else ["Ra", "Rb"]
+            src = IX(T.RP[:, h, r0:RW], T.OFN[:, 8 * h:8 * h + 8], "OFN", *rk)
             if t > 0:
                 tt(pn(h), src, R(T.VN[:, 128 * h:128 * h + 128], "VN"), A.add)
             else:
                 cp(pn(h), src)
             mark("pick%d" % h, t)
             send(t, h, "n")
-            scp(R(T.RP[:, h, PA:PA + 256], "PA%d" % h), IX(T.RP[:, h, r0:RW + 128], T.OFU[:, h, :], "R%d" % h, "Pn%d" % h, "OFU"))
+            scp(R(T.RP[:, h, PA:PA + 256], "PA%d" % h), IX(T.RP[:, h, r0:RW + 128], T.OFU[:, h, :], "Pn%d" % h, "OFU", *rk))
             mark("points%d" % h, t)
             send(t, h, "v")
             aff(R(T.VT[:, 128 * h:128 * h + 128], "VT%d" % h), pn(h), 0.0625, 191.53125)
@@ -567,7 +614,7 @@ def rank_program(g, core, T, topo):
             for c, q in ((2, 4), (3, 4), (4, 2), (5, 2)):
                 mm(pl(c), ID, me(q))
             for c in (2, 5):
-                mm(pl(c), ID, R(T.ONES[:, :16], "ONES"))
+                mm(pl(c), ID, whole("ONES"))
             for c, q in enumerate((0, 1, 3, 2, 2, 3)):
                 mm(pl(c), NID, R(T.QM[:, 2 * t:2 * t + 2, 8 + 16 * q:16 + 16 * q], "Q%dm" % t), stop=c == 5)
             act(whole("DL"), pl(0, 6), F.Abs)
@@ -575,39 +622,50 @@ def rank_program(g, core, T, topo):
 
         def compare_n(h):
             qn = lambda a=0, s=1: R(T.Q[:, 2 * t + h, a:128:s], "Q%d%dn" % (t, h))
-            dn = lambda a=0, s=1: R(T.DN[:, h, a:128:s], "DN%d" % h)
+            dn = lambda a, s, *xs: R(T.DN[:, h, a:128:s], *["DN%d.%d" % (h, x) for x in xs])
             rows = lambda name, x: R(T[name][:, 15 - x:143 - x], name)
             o = R(T.pS[:, 0:8], "pS") if h else R(T.pK[:, 0, 32:40], "pK")
             mm(o, NID, R(T.TH[:, 8 * h:8 * h + 8], "TH"), start=True)
             if VMAX[h]:
                 for x in range(16):
                     mm(o, rows("NZ", x), pn(h, x, 16))
-            for q in (0, 1):
-                mm(o, IB, R(T.DL[:, 16 * q + 8 * h:16 * q + 8 * h + 8], "DL"))
+            def lengths(stop):
+                for q in (0, 1):
+                    mm(o, IB, R(T.DL[:, 16 * q + 8 * h:16 * q + 8 * h + 8], "DL"), stop=stop and q == 1)
+
+            if h == 0:
+                lengths(False)
             if VMAX[h]:
                 for x in range(16):
                     mm(o, rows("NZ", x), qn(x, 16))
                     mark("diff%d" % h, t)
-                tt(dn(), pn(h), qn(), A.max)
-                mark("max%d" % h, t)
+                for x in (0, 1):
+                    tt(dn(x, 2, x), pn(h, x, 2), qn(x, 2), A.max)
+                    mark("max%d" % h, t)
             else:
                 pn_ = R(T.pN[:, 0:128], "pN")
                 mm(pn_, ID, pn(h), start=True)
                 mm(pn_, NID, qn(), stop=True)
                 mark("diff%d" % h, t)
-                act(dn(), pn_, F.Abs)
+                act(dn(0, 1, 0, 1), pn_, F.Abs)
                 mark("size%d" % h, t)
-            for x in range(16):
-                mm(o, rows("Z2" if VMAX[h] else "Z", x), dn(x, 16), stop=x == 15)
+            for x in list(range(0, 16, 2)) + list(range(1, 16, 2)):
+                mm(o, rows("Z2" if VMAX[h] else "Z", x), dn(x, 16, x % 2), stop=x == 15 and h == 0)
                 mark("sum%d" % h, t)
+            if h == 1:
+                lengths(True)
             so = R(T.SOU[:, 8 * h:8 * h + 8], "SOU%d" % h)
             ts(sc(D0, 14, h), o, col(9)[0], A.is_gt, 4096.0, A.mult, extra=["c9"])
             mark("ok%d" % h, t)
             tt(so, w("colx", h=h), sc(D0, 14, h), A.subtract if h == 0 else A.add)
-            tt(IX(T.X[:, 6144 * h:6144 * h + 6144], so[0], XK[h], *["Xz"] * h),
-               R(T.VT[:, 128 * h:128 * h + 128], "VT%d" % h, *so[1]), whole("M192"), A.add)
+            if last and h == 0:
+                tt(IX(T.X[:, 0:6144], T.SOU[:, 4:8], "X.0", "X.0b"), R(T.VT[:, 64:128], "VT0", *so[1]), R(T.M192[:, :64], "M192"), A.add)
+                dma("Y", T.yx[:, 1024:2048], T.X[:, TB + 1024:TB + 2048], "st4", ["X.0b"], [], STORE + 250)
+                tt(IX(T.X[:, 0:5120], T.SOU[:, 0:4], "X.0"), R(T.VT[:, 0:64], "VT0", *so[1]), R(T.M192[:, :64], "M192"), A.add)
+            else:
+                tt(IX(T.X[:, 6144 * h:6144 * h + 6144], so[0], XK[h], *["Xz"] * h),
+                   R(T.VT[:, 128 * h:128 * h + 128], "VT%d" % h, *so[1]), whole("M192"), A.add)
             mark("write%d" % h, t)
-            ts(d1(15, h), sc(D0, 14, h), 0.0, A.is_equal)
 
         def compare_v(h):
             bk = "pV%d" % h
@@ -628,10 +686,14 @@ def rank_program(g, core, T, topo):
         send_lengths(t)
         for j in range(S_):
             if j < NV[t] + NS[t]:
-                gather("V" if j < NV[t] else "S", j, 2)
+                gather("V" if j < NV[t] else "S", j, "abc")
             else:
-                gather("S", j, 1)
-                gather("V" if j >= S_ - NH[t] else "S", j, 0)
+                gather("S", j, "c")
+                if j >= S_ - N2[t]:
+                    gather("S", j, "a")
+                    gather("S", j, "b")
+                else:
+                    gather("V" if j < NV[t] + NS[t] + NH[t] else "S", j, "ab")
         if not last:
             seeds(t + 1, 10 + t)
             aff(ct(t + 1, 10 + t), columns(tn(t, 0, 10 + t), 0, 10 + t, "a"))
@@ -648,8 +710,9 @@ def rank_program(g, core, T, topo):
         tt(wi("uw"), w("ua"), w("ub"), A.mult)
         ts(wi("new"), wi("uw"), 5, A.arith_shift_right, 4095, A.bitwise_and)
         ts(tn(t, 10 + t, 11 + t), wi("new"), -2048.0, A.add)
-        tt(d1(0), me(0), me(4), A.subtract)
-        tt(d1(5), me(4), me(2), A.subtract)
+        for x, (o, l, q) in enumerate(((0, ID, 0), (1, ID, 4), (0, NID, 4), (1, NID, 2))):
+            mm(R(T.pV1[:, 0, 0:2, o::2], "pV1"), l, me(q), x == 0, x == 3)
+        aff(R(T.D1[:, 0::8], D1K[0], D1K[8]), R(T.pV1[:, 0, 0:2, :], "pV1"))
         aff(d1(13), tile("RES", 2), 1.0 / 4096)
         aff(d1(14), me(0))
         for x in (0, 1):
@@ -685,11 +748,12 @@ def rank_program(g, core, T, topo):
         compare_lengths()
         compare_n(1)
         if last:
-            dma("Y", T.yx[:, 2048:4096], T.X[:, TB + 2048:TB + 4096], "st0", ["X.1"], [], 3000)
+            dma("Y", T.yx[:, 2048:4096], T.X[:, TB + 2048:TB + 4096], "st0", ["X.1"], [], STORE + 700)
         compare_v(1)
         compare_n(0)
         if not last:
             tt(whole("VOU"), columns(tn(t, 10 + t, 11 + t), 10 + t, 11 + t, "b"), nok4, A.max)
+        aff(d1(15), nok4, -1.0 / 4096, 1.0)
         compare_v(0)
         mm(sums, NID, R(T.TH[:, 16:80], "TH0", "TH1", "TH2", "TH3"), start=True)
         mark("votes", t)
@@ -698,14 +762,14 @@ def rank_program(g, core, T, topo):
         for x in range(16):
             mm(sums, R(T.Z[:, 15 - x:143 - x], "Z"), R(T.DV[:, x::16], "DV0", "DV1"), stop=x == 15)
 
-    dma("Y", T.yx[:, 0:2048], T.X[:, TB:TB + 2048], "st1", ["X.0"], [], 3000)
+    dma("Y", T.yx[:, 0:1024], T.X[:, TB:TB + 1024], "st1", ["X.0"], [], STORE + 250)
     update(RO)
     post(RO - 1)
-    dma("S", T.yt[:], T.YT[:], "st3", ["YT"], [], 2200)
+    dma("S", T.yt[:], T.YT[:], "st3", ["YT"], [], STORE + 100)
     ys = lambda q: R(T.YS[:, 16 * q:16 * q + 16], "YS%d" % q)
     tt(ys(0), sc(ON, 14), d1(15), A.add)
     cp(ys(1), sc(NR, 15))
     tt(ys(2), sc(NR, 14), R(T.VC[:, 1::2], "VC"), A.mult)
     tt(ys(3), sc(NR, 14), R(T.VC[:, 0::2], "VC"), A.mult)
-    dma("Y", T.yst[:], T.YS[:], "st2", ["YS0", "YS1", "YS2", "YS3"], [], 2000)
+    dma("Y", T.yst[:], T.YS[:], "st2", ["YS0", "YS1", "YS2", "YS3"], [], STORE)
     emit()

@@ -6,33 +6,35 @@ RO = 6
 SL = [10, 10, 11, 12, 13, 14]
 LS = [s + 1 for s in SL]
 LSU = sorted(set(LS))
-VOFF = {}
-_o = 0
-for _l in LSU:
-    VOFF[_l] = _o
-    _o += 256 * _l
-VTOT = _o
+VOFF = {l: 256 * sum(LSU[:x]) for x, l in enumerate(LSU)}
 RW = 1920
 PA = RW + 128
-TB = 4096
-E = 16
-NV = [4, 3, 4, 4, 4, 5]
-NS = [2, 3, 3, 3, 4, 4]
-NH = [0, 0, 0, 0, 0, 0]
+TB = 128
+SP = 2064
+B = 16384.0
+NV = [4, 4, 5, 5, 5, 6]
+NS = [2, 2, 2, 3, 4, 4]
 N2, CUT = [2] * 6, 64
-MKP = 1
-VMAX = (1, 1)
-ROWS = ["gSabc gSc new gSab gSa gSb", "pick1 scanab scana scanb", "write1 ok0", "points0 lengths", "sum0 votes", "size1 size0 sizes1 sizes0"]
-CYC, PCYC, GATHER, SCATTER, VMIN, SMIN, PMIN = 0.84, 0.42, 1.15, 4.0, 45, 62, 44
-SAME, CROSS, PSUM, WAKE, ISSUE, REMOTE, FIRST, SMALL, LOAD = 200, 250, 300, 110, 90, 1150, 1500, 1700, 3900
-STORE = 1800
-PASSES, WIDE, TRIES = 6, 8, 1000
+UY, USQ, UT, UX, HALF = "V", 1, "V", "S", 1
+ROWS = ["gSabc gSc new gSab gSa gSb", "pick1 scanab scana scanb", "write1 ok0", "points0 lengths", "sizes1 sizes0", "sendv0 lead", "led sendm"]
+CYC, PCYC, GATHER, SCATTER, VMIN, SMIN, PFIX, BOTH = 0.84, 0.42, 1.44, 3.3, 36, 50, 7, 2.0
+LAG = {"V": 205, "S": 180, "P": 220, "G": 200}
+CROSS, WAKE, ISSUE, REMOTE, BYTE, FIRST, SMALL, LOAD = 50, 150, 250, 760, 0.004, 2000, 1200, 3000
+STORE = 1200
+RUN, FS = 8, 6
+CASES = ((0.8, 0.7, 1.2, 0.9, 400, 500), (1.2, 1.3, 0.9, 1.15, -150, -200))
+VD = ("I2080", "IF", "N129", "NID")
+PASSES, WIDE, TRIES = 6, 8, 7000
 PLAN, ORDER = [], []
 
 f32, bf, f16, i32, u16 = "float32", "bfloat16", "float16", "int32", "uint16"
+DIAG = {"NID": -1.0, "I2": 2.0, "I8": 8.0, "N8": -8.0, "IE": 0.125, "I13": 1.625, "IL": 16.5, "IF": 128.5, "N129": -129.0, "IB": 512.0,
+        "I1184": 1184.0, "I2080": 2080.0, "NQ": -1.0 / 4096, "IP": B, "IN": -B, "JP": 16 * B, "JN": -16 * B}
 SCRATCH = {
-    "X": ("sbuf", [128, 12288], bf), "V": ("sbuf", [128, VTOT], bf), "ZR": ("sbuf", [128, RW], bf),
+    "X": ("sbuf", [128, TB + 2048 + SP + 128], bf), "V": ("sbuf", [128, 256 * sum(LSU)], bf), "ZR": ("sbuf", [128, 960], bf),
     "RP": ("sbuf", [128, 2, RW + 384], bf), "Q": ("sbuf", [128, 2 * RO, 384], bf),
+    "THD": ("sbuf", [128, 128], f16), "CS": ("sbuf", [128, 128], f32), "SO": ("sbuf", [128, 128], f32),
+    "AW": ("sbuf", [128, 32], bf), "DG": ("sbuf", [128, 64], f32), "DH": ("sbuf", [128, 64], f32), "BS": ("sbuf", [128, 8], u16),
     "DN": ("sbuf", [128, 2, 128], bf), "DV": ("sbuf", [128, 1024], bf),
     "VN": ("sbuf", [128, 256], bf), "VT": ("sbuf", [128, 256], bf), "M192": ("sbuf", [128, 128], bf),
     "tri": ("sbuf", [128, 256], i32), "sdi": ("sbuf", [128, 96], i32), "ni": ("sbuf", [128, 16], i32),
@@ -41,29 +43,23 @@ SCRATCH = {
     "JJ": ("sbuf", [128, 256], f32), "J1184": ("sbuf", [128, 256], f16), "C2080": ("sbuf", [128, 256], f16), "C2048": ("sbuf", [128, 256], f16),
     "MK": ("sbuf", [128, 256], f32), "WW": ("sbuf", [128, 256], f32), "Y0": ("sbuf", [128, 256], f32),
     "NI": ("sbuf", [128, 256], i32), "NJ": ("sbuf", [128, 256], i32),
-    "CT": ("sbuf", [128, 512], u16), "BC": ("sbuf", [128, 16], u16), "BR": ("sbuf", [128, 10], u16), "BY": ("sbuf", [128, 4], u16),
-    "BV": ("sbuf", [128, 2], u16), "OFU": ("sbuf", [128, 2, 16], u16), "OFN": ("sbuf", [128, 16], u16),
-    "SOU": ("sbuf", [128, 16], u16), "VOU": ("sbuf", [128, 16], u16),
-    "OC": ("sbuf", [128, 2 * RO, 16], f16), "OL": ("sbuf", [128, 2 * RO, 16], f32),
-    "TH": ("sbuf", [128, 80], bf), "AH": ("sbuf", [128, 64], bf), "LIM": ("sbuf", [128, 64], f32), "ONES": ("sbuf", [128, 16], bf),
-    "GG": ("sbuf", [128, 144], bf), "NB": ("sbuf", [128, 48], i32), "I2": ("sbuf", [128, 128], bf), "IG": ("sbuf", [128, 128], bf),
-    "JB": ("sbuf", [128, 256], bf), "SB": ("sbuf", [128, 16], bf),
-    "SC": ("sbuf", [128, 48 * E], bf), "D1": ("sbuf", [128, 16 * E], bf), "D1R": ("sbuf", [128, 16 * E], bf),
-    "CA": ("sbuf", [128, 160], f32), "RES": ("sbuf", [128, 160], f16),
-    "M": ("sbuf", [128, 80], bf), "QM": ("sbuf", [128, 2 * RO, 80], bf), "DL": ("sbuf", [128, 96], bf),
-    "NF2": ("sbuf", [128, 32], f32), "VC": ("sbuf", [128, 32], f32), "VV": ("sbuf", [128, 32], bf),
-    "ND": ("sbuf", [128, 32], f32), "SIG": ("sbuf", [128, 16], f32), "FL": ("sbuf", [128, 16], f16),
-    "W": ("sbuf", [128, 16 * 40], f32), "WI": ("sbuf", [128, 16 * 16], i32),
+    "CT": ("sbuf", [128, 512], u16), "OF": ("sbuf", [128, 2, 24], u16), "SOU": ("sbuf", [128, 16], u16), "VOU": ("sbuf", [128, 16], u16),
+    "OB": ("sbuf", [128, len(LSU), 16], f16), "OD": ("sbuf", [128, len(LSU), 16], f16), "LI": ("sbuf", [128, 16], f32),
+    "TH": ("sbuf", [128, 96], bf), "LIM": ("sbuf", [128, 96], f32), "D0": ("sbuf", [128, 96], bf), "DZ": ("sbuf", [128, 96], bf),
+    "D1": ("sbuf", [128, 3, 96], f16), "SC": ("sbuf", [128, 4, 96], f16), "VC": ("sbuf", [128, 32], f32), "AH": ("sbuf", [128, 64], bf),
+    "ONES": ("sbuf", [128, 16], bf), "JB": ("sbuf", [128, 256], bf), "SB": ("sbuf", [128, 16], bf), "NK": ("sbuf", [128, 16], bf),
+    "M": ("sbuf", [128, 224], bf), "MZ": ("sbuf", [128, 64], bf), "MX": ("sbuf", [128, 16], bf), "QM": ("sbuf", [128, 2 * RO, 80], bf),
+    "DL": ("sbuf", [128, 64], bf), "CH": ("sbuf", [128, 240], bf), "CL": ("sbuf", [128, 304], f16), "FL": ("sbuf", [128, 16], f16),
+    "W": ("sbuf", [128, 16 * 16], f32), "WI": ("sbuf", [128, 16 * 16], i32),
     "PI": ("sbuf", [128, 16], i32), "PC": ("sbuf", [128, 16], f32), "XR": ("sbuf", [128, 144], f32),
-    "Z": ("sbuf", [128, 144], bf), "Z2": ("sbuf", [128, 144], bf), "NZ": ("sbuf", [128, 144], bf), "ZW": ("sbuf", [128, 144], f16),
-    "ID": ("sbuf", [128, 128], bf), "NID": ("sbuf", [128, 128], bf), "IB": ("sbuf", [128, 128], bf),
-    "I2080": ("sbuf", [128, 128], bf), "I1184": ("sbuf", [128, 128], bf),
-    "ONEQ": ("sbuf", [128, 128], bf), "NONE": ("sbuf", [128, 128], bf),
+    "Z": ("sbuf", [128, 144], bf), "ZW": ("sbuf", [128, 144], f16), "BK": ("sbuf", [128, 144], bf), "BK2": ("sbuf", [128, 144], bf),
+    "ID": ("sbuf", [128, 128], bf), "ONEQ": ("sbuf", [128, 128], bf), "NONE": ("sbuf", [128, 128], bf),
     "YT": ("sbuf", [128, 256], f32), "YS": ("sbuf", [128, 64], f32),
-    "pN": ("psum", [128, 512], f32), "pV0": ("psum", [128, 8, 4, 16], f32), "pV1": ("psum", [128, 8, 4, 16], f32),
-    "pS": ("psum", [128, 512], f32), "pU": ("psum", [128, 512], f32),
-    "pT": ("psum", [128, 512], f32), "pY": ("psum", [128, 512], f32), "pK": ("psum", [128, 2, 256], f32),
+    "pN": ("psum", [128, 512], f32), "pV0": ("psum", [128, 32, 16], f32), "pV1": ("psum", [128, 32, 16], f32),
+    "pS": ("psum", [128, 85, 6], f32), "pU": ("psum", [128, 512], f32),
+    "pT": ("psum", [128, 512], f32), "pY": ("psum", [128, 512], f32), "pK": ("psum", [128, 512], f32),
 }
+SCRATCH.update({name: ("sbuf", [128, 128], f16 if name == "IF" else bf) for name in DIAG})
 SEMAPHORES = (["cV", "cS", "cP", "cG"] + ["ld%d" % i for i in range(8)] + ["st%d" % i for i in range(5)]
               + ["ml%d" % t for t in range(RO)] + ["ma%d" % t for t in range(RO)]
               + ["dl%d" % i for i in range(4 * RO)] + ["da%d" % i for i in range(4 * RO)])
@@ -75,7 +71,7 @@ def rank_program(g, core, T, topo):
         return
     Q = {"V": g.vector, "S": g.scalar, "P": g.tensor, "G": g, "Y": g.sync}
     CS = {"V": "cV", "S": "cS", "P": "cP", "G": "cG"}
-    nodes, lastw, readers, chain, marks = [], {}, {}, {}, {}
+    nodes, lastw, readers, chain, marks, fixed, kind = [], {}, {}, {}, {}, [0], []
 
     def op(e, fn, args, kw, rd, wr, cost, done=None, sem=None, inc=1, auto=False, row=None):
         deps = set()
@@ -88,7 +84,15 @@ def rank_program(g, core, T, topo):
                 deps.add(lastw[k])
             deps.update(readers.get(k, []))
         i = len(nodes)
-        nodes.append(dict(e=e, fn=fn, args=args, kw=kw, deps=sorted(deps), cost=cost, done=cost if done is None else done,
+        y = nodes[-1] if nodes else None
+        if e == "P" and y["e"] == "P" and y["wr"] == wr and len(y["more"]) < RUN - 1 and all(d in y["deps"] or d == i - 1 or d < fixed[0] for d in deps):
+            y["more"].append(args)
+            y["deps"] = sorted(set(y["deps"]) | deps - {i - 1})
+            y["cost"] = y["done"] = y["cost"] + cost
+            for k in rd:
+                readers.setdefault(k, []).append(i - 1)
+            return
+        nodes.append(dict(e=e, fn=fn, args=args, kw=kw, deps=sorted(deps), wr=wr, more=[], kind=kind.pop() if kind else e, cost=cost, done=cost if done is None else done,
                           sem=sem or CS.get(e), inc=inc, auto=auto, after=[chain[row]] if row in chain else []))
         if row:
             chain[row] = i
@@ -120,7 +124,7 @@ def rank_program(g, core, T, topo):
                 elif y["done"] != y["cost"] or y["e"] == "A":
                     lag = WAKE
                 else:
-                    lag = SAME if y["e"] == x["e"] else PSUM if y["e"] == "P" else CROSS
+                    lag = LAG[y["e"]] + (0 if y["e"] == x["e"] else CROSS)
                 pre.append((d, y["done"] + lag))
             for d, lag in pre:
                 succ[d].append((i, lag))
@@ -199,7 +203,28 @@ def rank_program(g, core, T, topo):
             late = way(back, tail, [best[1][i] + cost[i] for i in range(n)])
             left = [late[i] + cost[i] for i in range(n)]
         stones = [marks[x, t][-1] for t in range(RO) for x in ("write0", "pick0", "pick1", "write1")]
-        worth = lambda s: max(s[i] + nodes[i]["done"] for i in range(n)) + 0.1 * sum(s[i] for i in stones)
+        cases = []
+        for ga, sc_, pe, wait, far, load in CASES:
+            c = [x["cost"] * {"g": ga, "s": sc_, "P": pe}.get(x["kind"], 1) for x in nodes]
+            d = [c[i] + x["done"] - x["cost"] + (far if x["auto"] else load if x["done"] != x["cost"] else 0) for i, x in enumerate(nodes)]
+            cases.append((c, d, [[(y, d[y] + (lag + cost[y] - cost[i] - nodes[y]["done"]) * wait) for y, lag in back[i] if y in x["deps"]]
+                                 for i, x in enumerate(nodes)]))
+
+        def worth(s):
+            total = max(s[i] + nodes[i]["done"] for i in range(n)) + 0.1 * sum(s[i] for i in stones)
+            seq = sorted(range(n), key=lambda i: (s[i], i))
+            for c, d, pre in cases:
+                free, at = dict.fromkeys("VSPGYA", 0.0), [0.0] * n
+                for i in seq:
+                    e = nodes[i]["e"]
+                    y = free[e] if e != "A" else 0.0
+                    for j, lag in pre[i]:
+                        if at[j] + lag > y:
+                            y = at[j] + lag
+                    at[i], free[e] = y, y + c[i]
+                total += max(at[i] + d[i] for i in range(n)) + 0.1 * sum(at[i] for i in stones)
+            return total / (1 + len(cases))
+
         seed = [1]
 
         def draw():
@@ -217,8 +242,9 @@ def rank_program(g, core, T, topo):
                 late = place(back, tail, [cost[i] - rank_[i] for i in range(n)])
                 rank_ = [late[i] + cost[i] for i in range(n)]
             start = place(succ, [0.0] * n, rank_)
-            if worth(start) <= now[0] + 60 * (1 - x / TRIES):
-                now = (worth(start), start)
+            value = worth(start)
+            if value <= now[0] + 60 * (1 - x / TRIES):
+                now = (value, start)
                 best = min(best, now)
         PLAN.append(max(best[1][i] + nodes[i]["done"] for i in range(n)))
         return sorted(range(n), key=lambda i: (best[1][i], i))
@@ -254,6 +280,8 @@ def rank_program(g, core, T, topo):
             for s2, c2 in best.items():
                 need(e, s2, c2)
             ins = x["fn"](*x["args"], **x["kw"])
+            for args in x["more"]:
+                ins = x["fn"](*args)
             if not x["auto"]:
                 ins.then_inc(T.sem[s], x["inc"])
             snap[x["tok"]] = dict(know[e])
@@ -271,9 +299,11 @@ def rank_program(g, core, T, topo):
 
     def span(e, o, ins, per=None):
         if o[4]:
+            kind.append("s")
             return 50 + o[2] * SCATTER * CYC
         if any(a[4] for a in ins):
-            return (50 if e == "V" else 65) + o[2] * GATHER * CYC
+            kind.append("e" if per else "g")
+            return (50 if e == "V" else 65) + o[2] * (BOTH if per else GATHER) * CYC
         if per is None:
             per = 0.5 if e == "V" and o[3] and all(a[3] for a in ins) else 1
         return max(VMIN if e == "V" else SMIN, o[2] * per) * CYC
@@ -306,60 +336,51 @@ def rank_program(g, core, T, topo):
     def memset(o, c):
         op("V", g.vector.memset, (o[0], c), {}, [], o[1], span("V", o, []))
 
-    def iota(o, pat, base=0, cm=0, fl=True):
-        op("G", g.iota, (o[0], pat, base, cm), dict(allow_small_or_imprecise_dtypes=True) if fl else {}, [], o[1], 130 + 2 * CYC * o[2], row="iota")
+    def iota(o, pat, base=0, cm=0, fl=True, row="iota"):
+        op("G", g.iota, (o[0], pat, base, cm), dict(allow_small_or_imprecise_dtypes=True) if fl else {}, [], o[1], 130 + 2 * CYC * o[2], row=row)
 
     def dma(e, out, in_, sem, rd, wr, done):
-        op(e, Q[e].dma_start, (out, in_), {}, rd, wr, 60, done, sem=sem, inc=16, row="dma" + e)
+        op(e, Q[e].dma_start, (out, in_), {}, rd, wr, 100, done, sem=sem, inc=16, row="dma" + e)
 
     def mm(o, l, r, start=False, stop=False):
-        op("P", g.tensor.matmul, (o[0], l[0], r[0], start, stop), {}, l[1] + r[1], o[1], max(PMIN, r[2]) * PCYC)
+        op("P", g.tensor.matmul, (o[0], l[0], r[0], start, stop), {}, l[1] + r[1], o[1], PFIX + max(16, r[2]) * PCYC)
 
     def whole(name):
         return R(T[name][:], name)
 
     Wn, WIn = {}, {}
 
-    def w(name, n=1, q=0, h=None):
-        if name not in Wn:
-            Wn[name] = sum(v[1] for v in Wn.values()), n
-        c = Wn[name][0] + q
+    def w(name, h=None):
+        c = Wn.setdefault(name, len(Wn))
         if h is not None:
             return R(T.W[:, 16 * c + 8 * h:16 * c + 8 * h + 8], "W.%d" % c)
-        return R(T.W[:, 16 * c:16 * (c + n)], *["W.%d" % (c + x) for x in range(n)])
+        return R(T.W[:, 16 * c:16 * c + 16], "W.%d" % c)
 
-    def wi(name, n=16):
+    def wi(name, h=None):
         c = WIn.setdefault(name, len(WIn))
-        return R(T.WI[:, 16 * c:16 * c + n], "WI.%d" % c)
+        if h is not None:
+            return R(T.WI[:, 16 * c + 8 * h:16 * c + 8 * h + 8], "WI.%d.%d" % (c, h))
+        return R(T.WI[:, 16 * c:16 * c + 16], "WI.%d.0" % c, "WI.%d.1" % c)
 
-    for name, n in (("col", 1), ("g0", 2), ("g1", 2), ("g2", 2), ("KK", 2), ("Ka", 2), ("kb", 2), ("FF", 2), ("KI", 2)):
-        w(name, n)
+    w("col")
 
     def col(i):
         return R(T.W[:, i:i + 1], "c%d" % i)
 
-    def me(q, n=1):
-        return R(T.M[:, 16 * q:16 * (q + n)], *["ME%d" % x for x in range(q, q + n)])
-
-    D0, NR, ON = 0, 16 * E, 32 * E
-    D0K = ["D0.%d" % e for e in range(E)]
-    D1K = ["D1.%d" % e for e in range(E)]
-
-    def sc(base, e, h=None, step=E):
-        a, b = (0, 16 * E) if h is None else (8 * E * h, 8 * E * (h + 1))
-        return R(T.SC[:, base + a + e:base + b:step], *(["SC%d" % base] if base else D0K[e::step]))
-
-    def d1(e, h=None):
-        a, b = (0, 16 * E) if h is None else (8 * E * h, 8 * E * (h + 1))
-        return R(T.D1[:, a + e:b:E], D1K[e])
-
     def tile(name, q, n=1):
         return R(T[name][:, 16 * q:16 * (q + n)], *["%s.%d" % (name, x) for x in range(q, q + n)])
 
+    N_, K_, M1, M3, M2, LK, X1, X2, RR, K2, K4 = 0, 1, 2, 3, 4, 5, 7, 9, 11, 12, 13
+    me = lambda q, n=1: tile("M", q, n)
+    sc = lambda q: R(T.SC[:, q, 5::6], "SC%d" % q)
+    nok4 = R(T.NK[:], "NK0", "NK1")
     part = [T.cores[rank ^ 1], T.cores[rank ^ 2]]
     XK = ["X.0", "X.1"]
-    nok4 = sc(D0, 14)
-    ID, NID, IB = whole("ID"), whole("NID"), whole("IB")
+    ID, NID, IB, ONES = whole("ID"), whole("NID"), whole("IB"), whole("ONES")
+
+    def sums_of(at, terms, start=True, stop=True):
+        for x, (q, l, r) in enumerate(terms):
+            mm(at(q, r[2] // 16), whole(l), r, start and x == 0, stop and x == len(terms) - 1)
 
     def send(t, h, p):
         rid, pid, _ = topo.addr(part[h])
@@ -367,102 +388,129 @@ def rank_program(g, core, T, topo):
         i = 4 * t + (2 if p == "v" else 0) + h
         a, b = (0, 128) if p == "n" else (128, 384)
         op("G", g.remote_dma, (T.Q[:, 2 * t + h, a:b], T.RP[:, h, RW + a:RW + b], T.sem["da%d" % i], T.sem["dl%d" % i], pid, rid, topo.mask(core, part[h])), {},
-           ["Pn%d" % h] if p == "n" else ["PA%d" % h], ["sent%d" % i], ISSUE, REMOTE, sem="dl%d" % i, inc=ne, auto=True)
+           ["Pn%d" % h] if p == "n" else ["PA%d" % h], ["sent%d" % i], ISSUE, REMOTE + BYTE * 256 * (b - a), sem="dl%d" % i, inc=ne, auto=True)
+        mark("send%s%d" % (p, h), t)
         op("A", None, (), {}, ["sent%d" % i], ["Q%d%d%s" % (t, h, p)], 0, sem="da%d" % i, inc=ne)
 
     def send_lengths(t):
         trs, tot = [], 0
+        src = me(0, 4) if t else whole("MZ")
         for h in (0, 1):
             rid, pid, _ = topo.addr(part[h])
             en = topo.engines(core, part[h])
             en = en[:len(en) // 2] if h == 0 else en[len(en) // 2:]
             tot += len(en)
             trs.append(RemoteDMATransfer(dst_ids=[DstId(rid=rid, pnc=pid)], dma_engine_mask=sum(1 << x for x in en),
-                                         remote_sem=T.sem["ma%d" % t], src=me(0, 4)[0], dst=T.QM[:, 2 * t + h, 8 - 8 * h:72 - 8 * h]))
+                                         remote_sem=T.sem["ma%d" % t], src=src[0], dst=T.QM[:, 2 * t + h, 8 - 8 * h:72 - 8 * h]))
         late = FIRST if t == 0 else 0
-        op("G", g.remote_dma_fused, (trs,), dict(local_sem=T.sem["ml%d" % t]), me(0, 4)[1], ["sentm%d" % t], ISSUE + late, REMOTE + late,
-           sem="ml%d" % t, inc=tot, auto=True)
+        op("G", g.remote_dma_fused, (trs,), dict(local_sem=T.sem["ml%d" % t]), src[1], ["sentm%d" % t], ISSUE + late,
+           REMOTE + BYTE * 32768 + late, sem="ml%d" % t, inc=tot, auto=True)
+        mark("sendm", t)
         op("A", None, (), {}, ["sentm%d" % t], ["Q%dm" % t], 0, sem="ma%d" % t, inc=tot)
 
     dma("S", T.sdi[:], T.sd[:], "ld2", [], ["sdi"], SMALL)
-    dma("Y", T.tri[:], T.tr[:], "ld3", [], ["tri"], SMALL + 300)
-    dma("S", T.ki[:], T.k0[:], "ld1", [], ["ki"], SMALL + 200)
-    dma("Y", T.ni[:], T.n0[:], "ld0", [], ["ni"], SMALL + 400)
+    dma("Y", T.tri[:], T.tr[:], "ld3", [], ["tri"], SMALL + 200)
+    dma("S", T.ki[:], T.k0[:], "ld1", [], ["ki"], SMALL)
+    dma("Y", T.ni[:], T.n0[:], "ld0", [], ["ni"], SMALL)
     dma("Y", T.X[:, TB:TB + 4096], T.xt[:], "ld4", [], XK, LOAD)
     dma("S", T.wi[:, 0:1], T.wt[:], "ld6", [], ["wi0"], LOAD + 200)
     dma("S", T.thi[:], T.th[:], "ld5", [], ["thi"], LOAD + 200)
 
     iota(whole("PI"), [[0, 16]], 0, 1, fl=False)
+    iota(whole("XR"), [[1, 144]])
     iota(whole("JJ"), [[1, 16], [0, 16]])
     iota(whole("PC"), [[0, 2], [16, 8]])
-    iota(whole("XR"), [[1, 144]])
+    for q, n, c in ((14, 1, -147456.0), (K_, 1, -B), (LK, 2, -34816.0), (X1, 4, -B), (RR, 1, -18432.0), (K2, 1, 384.0), (K4, 1, 768.0)):
+        memset(tile("CH", q, n), c)
+    iota(whole("BK2"), [[16, 9], [0, 4], [-128, 4]], 15 + 3 * 128)
+    iota(whole("DG"), [[1, 8], [4096, 8]])
     for l in LSU:
-        memset(R(T.V[:, VOFF[l]:VOFF[l] + 256 * l:l], "Vz%d" % l), -256.0)
-    for name, c in (("C2080", 2080.0), ("ZR", 0.0), ("C2048", 2048.0), ("M192", -192.0), ("D1R", 0.0), ("ONES", 1.0),
-                    ("ONEQ", 1.0 / 4096), ("NONE", -1.0), ("VV", 0.0), ("OL", 0.0)):
+        lead = R(T.V[:, VOFF[l]:VOFF[l] + 256 * l:l], "Vz%d" % l)
+        if l == LS[0]:
+            memset(lead, -256.0)
+        else:
+            iota(lead, [[0, 256]], -256, row=None)
+            mark("lead", LS.index(l) - 2)
+            mark("led", LS.index(l) - 1)
+    memset(whole("NONE"), -1.0)
+    for name, c in (("C2080", 2080.0), ("ZR", 0.0), ("C2048", 2048.0), ("M192", -192.0), ("ONES", 1.0), ("ONEQ", 1.0 / 4096),
+                    ("AW", 0.0), ("TH", 0.0), ("DZ", 0.0)):
         memset(whole(name), c)
+    memset(nok4, 4096.0)
+    memset(R(T.DZ[:, 0::6], "DZ"), 1.0)
     memset(R(T.X[:, TB + 4096:TB + 4112], "Xz"), 0.0)
     memset(col(9), 0.0)
+    memset(tile("CL", 0, 14), 0.0)
+    for q, n, c in ((0, 2, 1.0), (3, 1, 1.0), (LK, 2, -560.0), (RR, 1, -255.0), (K2, 1, -0.6875), (K4, 1, -0.1875), (14, 1, -318.5), (15, 1, 894.0),
+                    (16, 1, 2045.0), (17, 1, 1023.0), (18, 1, 2174.0)):
+        memset(tile("CL", q, n), c)
     PI1 = R(T.PI[:, 0:1], "PI")
     cp(col(0), PI1)
     ts(wi("a"), whole("PI"), 15, A.bitwise_and)
-    ts(R(T.wj[:, 0:1], "wj0"), PI1, 112, A.bitwise_and)
+    one = lambda x: R(T.wj[:, x:x + 1], "wj%d" % x)
+    ts(one(0), PI1, 112, A.bitwise_and)
     ts(ID, R(T.XR[:, :128], "XR"), col(0)[0], A.is_equal, extra=["c0"])
-    for name, c in (("I2080", 2080.0), ("NID", -1.0), ("IB", 512.0), ("I1184", 1184.0), ("I2", 2.0), ("IG", 2.0625)):
-        aff(whole(name), ID, c)
-    ts(col(1), R(T.wj[:, 0:1], "wj0"), 15.0, A.add)
+    for x, (name, c) in enumerate(DIAG.items()):
+        if name in VD:
+            ts(whole(name), ID, c, A.mult)
+        else:
+            aff(whole(name), ID, c)
+    ts(col(1), one(0), 15.0, A.add)
     ts(whole("Z"), whole("XR"), col(1)[0], A.is_equal, extra=["c1"])
-    for name, c in (("Z2", 2.0), ("NZ", -1.0)) if any(VMAX) else ():
-        aff(whole(name), whole("Z"), c)
-    tt(w("li"), whole("PC"), wi("a"), A.add)
-    cp(whole("BC"), wi("a"))
+    ts(whole("BK"), whole("BK2"), col(1)[0], A.is_equal, -B, A.mult, extra=["c1"])
+    ts(whole("BK2"), whole("BK"), -2.0, A.mult)
+    a1 = R(T.WI[:, 0:1], "WI.0.0")
+    tt(whole("LI"), whole("PC"), wi("a"), A.add)
     aff(whole("J1184"), whole("JJ"), 1184.0)
     aff(whole("JB"), whole("JJ"), -1.0)
-    oc = lambda t, q: R(T.OC[:, 2 * t:2 * t + 2, 8 * q:8 * q + 8], "OC%d.%d" % (t, q))
-    base = lambda t: R(T.OL[:, 2 * t:2 * t + 2, 8:16], "OL%d" % t)
-    for t in range(RO):
-        l = float(LS[t])
-        aff(oc(t, 0), w("li"), *((l, 0.0) if t == 0 else (1.0, 128 * l - 1)))
-        aff(oc(t, 1), w("li"), l, -1.0)
-        aff(base(t), w("li"), l, extra=["OL"])
-    aff(w("ci", h=0), w("li", h=0), 16.0, 4096.0)
-    aff(w("ci", h=1), w("li", h=1), 16.0)
-
-    ts(wi("a2"), wi("a"), 1, A.arith_shift_right)
-    memset(R(T.SC[:, 0:16 * E], *D0K), 1.0)
-    memset(R(T.D1[:], *D1K), 0.0)
-    memset(tile("CA", 0), 0.0)
-    memset(sc(D0, 0), 0.0)
-    memset(sc(D0, 10), 1.0 / 4096)
-    memset(R(T.D1R[:, 0::E], "D1R"), 1.0)
-    for h in (0, 1):
-        ts(R(T.BV[:, h:h + 1], "BV%d" % h), wi("a2", 1), float(E), A.mult, NR + 14.0 + 8 * E * h, A.add)
-    ts(R(T.BR[:, 0:8], "BR0"), wi("a", 8), float(E), A.mult, NR + 14.0, A.add)
-    ts(R(T.BR[:, 8:10], "BR8"), wi("a", 2), float(E), A.mult, D0 + 14.0, A.add)
-    ts(R(T.BY[:], "BY"), wi("a", 4), float(E), A.mult, ON + 15.0, A.add)
-    memset(R(T.BY[:, 1:2], "BY"), D0 + 2)
+    for x, l in enumerate(LSU):
+        aff(R(T.OB[:, x], "OB%d" % l), whole("LI"), float(l))
+        aff(R(T.OD[:, x], "OD%d" % l), whole("LI"), 1.0, 128.0 * l - 1)
+    aff(w("ci", h=0), R(T.LI[:, 0:8], "LI"), 16.0, float(TB))
+    aff(w("ci", h=1), R(T.LI[:, 0:8], "LI"), 16.0)
+    ts(one(1), a1, 2, A.arith_shift_right)
+    ts(one(2), a1, 3, A.arith_shift_right)
+    ts(col(11), one(1), -8192.0, A.mult, -4096.0, A.add)
+    ts(col(3), a1, 8.0, A.mult, 7.0, A.add)
+    ts(col(4), a1, 8.0, A.mult, float(SP), A.add)
+    cp(col(5), one(2))
+    ts(whole("BS"), R(T.XR[:, :8], "XR"), 2.0, A.mult, col(5)[0], A.add, extra=["c5"])
+    act(whole("DG"), whole("DG"), F.Abs, 1.0, col(11)[0], extra=["c11"])
+    aff(whole("DH"), whole("DG"), 1.0, -8.0)
+    aff(w("th"), whole("thi"), 1.0, 0.5)
+    for h, s in ((0, -1.0), (1, 1.0)):
+        cs = lambda a, step=1: R(T.CS[:, 64 * h + a:64 * h + 64:step], "CS%d" % h)
+        aff(cs(0), whole("DG"), s, col(3 + h)[0], extra=["c%d" % (3 + h)])
+        for x in (2, 4):
+            aff(cs(x, 8), R(T.XR[:, :8], "XR"), s, col(3 + h)[0], extra=["c%d" % (3 + h)])
+        tt(R(T.THD[:, 64 * h:64 * h + 64], "THD%d" % h), IX(w("th")[0], T.BS[:, 4 * h:4 * h + 4], "BS", *w("th")[1]), whole("DH"), A.max)
+    memset(R(T.THD[:, 0::8], "THD0", "THD1"), -B)
+    for x in (2, 4):
+        memset(R(T.THD[:, x::8], "THD0", "THD1"), 0.5)
     WT = R(T.wi[:, 0:1], "wi0")
     ts(col(6), WT, 2048.0, A.is_ge, -4096.0, A.mult)
     tt(col(7), col(6), WT, A.add)
     aff(whole("ZW"), whole("Z"), col(7)[0], extra=["c7"])
-    aff(R(T.TH[:, 0:16], "TH"), whole("thi"))
     for q in range(4):
-        aff(R(T.TH[:, 16 + q:80:4], "TH%d" % q), whole("thi"))
+        aff(R(T.TH[:, 1 + q::6], "TH%d" % q), whole("thi"), extra=["TH"])
+    fixed[0] = len(nodes)
 
     def tn(t, a, b):
         return R(T.TN[:, t % 2, 16 * a:16 * b], *(["TN%d" % (t % 2)] * (a < 10 + t) + ["NP%d" % (t % 2)] * (b > 10 + t)))
 
     def seeds(t, nb):
         n = 16 * nb
-        mm(R(T.pY[:, :n + 16], "pY"), ID, R(T.C2080[:, :n + 16], "C2080"), start=True)
+        e = n + 16 * (t > 0)
+        mm(R(T.pY[:, :e], "pY"), ID, R(T.C2080[:, :e], "C2080"), start=True)
         mm(R(T.pY[:, 256:256 + n], "pY"), ID, R(T.J1184[:, :n], "J1184"))
         sr = lambda k: R(T.SR[:, t, :k], "SR0", "SR1", "SR2", "SR3")
-        for c in range(0, n + 16, 64):
-            mm(R(T.pY[:, c:min(c + 64, n + 16)], "pY"), ID, sr(min(64, n + 16 - c)))
+        for c in range(0, e, 64):
+            mm(R(T.pY[:, c:min(c + 64, e)], "pY"), ID, sr(min(64, e - c)))
         for c in range(0, n, 64):
-            mm(R(T.pY[:, 256 + c:256 + min(c + 64, n)], "pY"), whole("I2080"), sr(min(64, n - c)))
-        mm(R(T.pY[:, 256 + n:272 + n], "pY"), whole("I2080"), sr(16))
-        mm(R(T.pY[:, 256 + n:272 + n], "pY"), whole("I1184"), me(0), stop=True)
+            mm(R(T.pY[:, 256 + c:256 + min(c + 64, n)], "pY"), whole("I2080"), sr(min(64, n - c)), stop=t == 0 and c + 64 >= n)
+        if t:
+            mm(R(T.pY[:, 256 + n:272 + n], "pY"), whole("I2080"), sr(16))
+            mm(R(T.pY[:, 256 + n:272 + n], "pY"), whole("I1184"), me(0), stop=True)
 
     def columns(src, a, b, key):
         part_ = lambda name: R(T[name][:, 16 * a:16 * b], name + key)
@@ -484,96 +532,132 @@ def rank_program(g, core, T, topo):
             mm(R(T.pT[:, 256:512], "pT"), ID, whole("C2048"))
         for j in range(nb):
             mm(R(T.pT[:, 16 * j:16 * j + 16], "pT"), ID, new, stop=j == nb - 1)
-        if MKP and t < RO:
-            tt(whole("SB"), me(0), nok4, A.add)
-            mm(R(T.pN[:, :n], "pN"), ID, R(T.JB[:, :n], "JB"), start=True)
+        bk = "pY" if t == RO else "pN"
+        mm(R(T[bk][:, :n], bk), ID, R(T.JB[:, :n], "JB"), start=True)
+        for x, r in enumerate((me(0), nok4)):
             for j in range(nb):
-                mm(R(T.pN[:, 16 * j:16 * j + 16], "pN"), ID, whole("SB"), stop=j == nb - 1)
-            ts(R(T.MK[:, :n], "MK"), R(T.pN[:, :n], "pN"), 0.0, A.is_equal)
-        else:
-            tt(whole("SIG"), me(0), nok4, A.add)
-            tt(R(T.MK[:, :n], "MK"), IX(T.SIG[:], T.BC[:, 0:nb], "SIG", "BC"), R(T.JJ[:, :n], "JJ"), A.is_equal)
+                mm(R(T[bk][:, 16 * j:16 * j + 16], bk), ID, r, stop=x == 1 and j == nb - 1)
+        ts(R(T.MK[:, :n], "MK"), R(T[bk][:, :n], bk), 0.0, A.is_equal)
         tt(R(T.WW[:, :n], "WW"), R(T.pT[:, :n], "pT"), R(T.MK[:, :n], "MK"), A.mult)
         tt(whole("YT") if t == RO else tn(t, 0, nb), R(T.pT[:, 256:256 + n], "pT"), R(T.WW[:, :n], "WW"), A.add)
 
-    def offsets(t):
-        of = lambda q: R(T.pK[:, :, 8 * q:8 * q + 8], "pK")
-        tt(whole("OFN"), sc(ON, 14) if t else me(0), base(t), A.add)
-        mm(R(T.pK[:, :, 0:16], "pK"), ID, R(T.OC[:, 2 * t:2 * t + 2, :], "OC%d.0" % t, "OC%d.1" % t), start=True)
-        terms = ((0, d1(14)), (0, sc(ON, 15)), (1, sc(ON, 15)), (0, tile("RES", 8)), (0, tile("RES", 9)), (0, tile("RES", 2)), (1, tile("RES", 3)))
-        terms = terms if t else ((0, me(2)), (1, me(3)))
-        for x, (q, r) in enumerate(terms):
-            mm(of(q), NID if t and x == 0 else ID, r, stop=x == len(terms) - 1)
-        tt(whole("OFU"), R(T.pK[:, :, 0:16], "pK"), R(T.OL[:, 2 * t:2 * t + 2, :], "OL", "OL%d" % t), A.max)
-
     for r in range(4):
-        aff(R(T.SR[:, :, 16 * r:16 * r + 16], "SR%d" % r), whole("sdi"), 1.0, -2048.0)
+        if r % 2:
+            ts(R(T.SR[:, :, 16 * r:16 * r + 16], "SR%d" % r), whole("sdi"), -2048.0, A.add)
+        else:
+            aff(R(T.SR[:, :, 16 * r:16 * r + 16], "SR%d" % r), whole("sdi"), 1.0, -2048.0)
     aff(R(T.TP[:, 160:], "TP"), R(T.tri[:, 160:], "tri"), 1.0, -2048.0)
     aff(tn(0, 0, 10), R(T.tri[:, :160], "tri"), 1.0, -2048.0)
-    first = lambda name, key="a": R(T[name][:, :160], name + key)
-    s0 = R(T.sdi[:, 0:16], "sdi")
-    ts(w("s0"), s0, 32.0, A.add)
-    ts(w("b0"), s0, -2048.0, A.add, 2080.0, A.mult)
-    ts(first("WW", ""), first("tri", ""), -2048.0, A.add)
-    tt(first("MK", ""), IX(w("b0")[0], T.BC[:, 0:10], "BC", *w("b0")[1]), first("J1184", ""), A.add)
-    tt(first("Y0"), IX(w("s0")[0], T.BC[:, 0:10], "BC", *w("s0")[1]), first("WW", ""), A.mult)
-    tt(first("NI"), first("Y0"), first("MK", ""), A.add)
-    ts(first("NJ"), first("NI"), 5, A.arith_shift_right, 4095, A.bitwise_and)
-    cp(ct(0, 10), first("NJ"))
-    gt = lambda q, n=1: R(T.GG[:, 16 * q:16 * (q + n)], *["GG%d" % x for x in range(q, q + n)])
-    for x in range(3):
-        ts(gt(x), whole("ki"), 2.0 ** (x + 1), A.is_ge, 2.0 ** x, A.mult)
-        aff(gt(3 + x), gt(x), -0.5 / 4 ** x)
-        ts(R(T.NB[:, 16 * x:16 * x + 16], "NB%d" % x), whole("ni"), x, A.arith_shift_right, 1, A.bitwise_and)
-    tt(gt(6, 3), gt(0, 3), R(T.NB[:], "NB0", "NB1", "NB2"), A.mult)
-    aff(me(0), whole("ni"))
-    aff(me(1), whole("ki"))
+    seeds(0, 10)
+    for a, b, key in ((0, FS, "a"), (FS, 10, "b")):
+        cp(R(T.CT[:, 16 * a:16 * b], "CT0" + key), columns(tn(0, a, b), a, b, key))
 
-    def tiles(bank, terms):
-        for x, (q, l, r) in enumerate(terms):
-            mm(R(T[bank][:, 16 * q:16 * q + 16], bank), l, r, x == 0, x == len(terms) - 1)
+    pS = lambda r, a=0, b=6: R(T.pS[:, r:r + 16, a:b], "pS")
+    pX = R(T.pS[:, 80:84, 0:4], "pS")
+    ah = lambda x: R(T.AH[:, x::4], "AH")
+    m1x = whole("MX")
+    floor_terms = [("ID", me(N_)), ("IF", me(K2)), ("IF", me(K4))]
+    base = lambda t: R(T.OB[:, LSU.index(LS[t])], "OB%d" % LS[t])
+    votes = [("ID", me(X1, 2)), ("NID", me(X2, 2))]
+    grown = [(p, ah(x)) for p, xs in ((0, (2, 3)), (1, (0, 1))) for x in xs]
 
-    tiles("pT", [(0, ID, me(0)), (1, ID, me(0))] + [(1, NID, gt(x)) for x in range(3)] + [(q, NID, gt(x)) for x in (6, 7, 8) for q in (0, 1)])
-    aff(me(2, 2), R(T.pT[:, 0:32], "pT"))
-    act(me(4), R(T.pT[:, 16:32], "pT"), F.Relu, 1.0, -1.0)
-    offsets(0)
-    tiles("pY", [(4, ID, gt(x)) for x in range(3)] + [(5, ID, gt(x)) for x in (3, 4, 5)] + [(q, NID, me(1)) for q in (6, 7)]
-          + [(q, ID, whole("ONES")) for q in (6, 7)] + [(7, whole("I2"), gt(x)) for x in range(3)]
-          + [(6, whole("IG" if x else "I2"), gt(x)) for x in range(3)])
-    aff(tile("RES", 4, 2), R(T.pY[:, 64:96], "pY"))
-    aff(tile("RES", 6), R(T.pY[:, 96:112], "pY"), 8.0)
-    aff(tile("RES", 7), R(T.pY[:, 112:128], "pY"))
-    tt(tile("RES", 2), me(2), me(0), A.subtract)
-
-    pC = R(T.pN[:, 256:288], "pN")
-    sums = R(T.pS[:, 16:80], "pS")
+    def choices(t):
+        last = t == RO - 1
+        if not last:
+            sums_of(lambda q, n: pX, [(0, l, r) for l, r in [("ID", tile("CL", 14)), ("ID", tile("CH", 14))] + floor_terms])
+            (aff if UX == "S" else cp)(m1x, pX)
+        at = lambda q, n=1: pS(16 + 16 * (q // 6), q % 6, q % 6 + 1)
+        lim = [(q, l, r) for l in ("I8", "NID") for q in (1, 2, 3, 4) for r in [sc(3) if l == "I8" else me(LK + (q < 3))]]
+        terms = [(6, "ID", me(N_)), (6, "NID", me(M2)), (8, "ID", me(M2)), (8, "NID", me(M1)), (10, "ID", me(M1)), (10, "NID", me(N_)), (11, "ID", me(N_))]
+        if last:
+            terms += [(12, "ID", me(K_)), (12, "ID", ONES), (17, "ID", ONES)]
+        else:
+            more = [(10, "NID", ONES), (6, "NID", tile("CH", 14)), (6, "N129", me(K2)), (6, "N129", me(K4))]
+            terms += [(q + o, l, r) for o in (6, 12) for q, l, r in terms[1:] + more]
+            terms += [(12, "ID", tile("CL", 15)), (17, "ID", ONES), (18, "ID", tile("CL", 16)), (18, "NID", me(K2)), (18, "NID", me(K4))]
+            terms += [(q, "ID", base(t + 1)) for q in (11, 23)] + [(q, "ID", m1x) for q in (12, 18)]
+        if t == 0 or last:
+            mm(R(T.pS[:, 16:80], "pS"), ID, R(T.ZR[:, :384], "ZR"), True, True)
+        sums_of(at, lim + terms)
+        aff(R(T.D1[:, :3 - last], "D1"), R(T.pS[:, 32:80 - 16 * last], "pS"))
+        mark("terms", t)
+        aff(whole("LIM"), pS(16), B, col(9)[0], extra=["c9"])
 
     def post(t):
-        last = t == RO - 1
-        tt(sc(D0, 1, step=4), sums, R(T.LIM[:], "LIM0", "LIM1"), A.is_gt)
-        scan(R(T.SC[:, ON:ON + 16 * E], "SC%d" % ON), R(T.SC[:, 0:16 * E], *D0K), R(T.D1[:], *D1K), A.mult, A.add)
-        scan(R(T.SC[:, NR:NR + 16 * E], "SC%d" % NR), R(T.SC[:, 0:16 * E], *D0K), whole("D1R"), A.mult, A.add)
-        ts(whole("AH"), sums, col(9)[0], A.is_le, extra=["c9"])
-        if not last:
-            mm(R(T.pU[:, 16:32], "pU"), whole("ONEQ"), nok4, start=True)
-            mm(R(T.pU[:, 16:32], "pU"), whole("NONE"), sc(NR, 14), stop=True)
-            act(w("junk"), R(T.pU[:, 16:32], "pU"), F.Identity, 1.0, 1100.0, accum=col(8))
-            aff(R(T.FL[:, 0:1], "FL"), col(8), 0.0625, -0.46875)
-            aff(col(9), R(T.FL[:, 0:1], "FL"), -16.0, col(8)[0], extra=["c8"])
-        mm(pC, ID, whole("VV"), start=True)
-        for x in (0, 1):
-            mm(pC, ID, R(T.AH[:, x::2], "AH"), stop=x == 1)
-        tt(whole("VC"), pC, R(T.NF2[:], "NF0", "NF1"), A.min)
+        first, last = t < 0, t == RO - 1
+        z = sc(3)
+        if not first:
+            tt(whole("D0"), pS(0), whole("LIM"), A.is_gt)
+            mark("cmp", t + 1)
+            scan(R(T.SC[:, 3], "SC3"), whole("D0"), whole("DZ"), A.mult, A.add)
+            for q in range(3 - last):
+                scan(R(T.SC[:, q], "SC%d" % q), whole("D0"), R(T.D1[:, q], "D1"), A.mult, A.add)
+            ts(whole("AH"), pS(0, 1, 5), col(9)[0], A.is_le, extra=["c9"])
+        pM = lambda q, n=1: R(T.pU[:, 64 + 16 * q:64 + 16 * (q + n)], "pU")
         if last:
+            ys = lambda q: tile("YS", q)
+            ts(m1x, me(RR), 0.0, A.is_equal)
+            sums_of(pM, [(0, l, r) for l, r in votes] + [(p, "N8", m1x) for p in (0, 1)] + [(p, "ID", r) for p, r in grown])
+            ts(whole("VC"), pM(0, 2), 0.0, A.max)
+            aff(w("ok"), nok4, -1.0 / 4096, 1.0)
+            tt(ys(0), sc(0), w("ok"), A.add)
+            cp(ys(1), sc(1))
+            for p in (0, 1):
+                tt(ys(2 + p), z, R(T.VC[:, 16 * p:16 * p + 16], "VC"), A.mult)
             return
-        tt(whole("VV"), IX(T.SC[:, 0:ON], T.BV[:], "SC%d" % NR, "BV0", "BV1", *D0K), whole("VC"), A.mult)
-        tt(tile("RES", 0, 10), IX(T.SC[:, 0:ON], T.BR[:], "SC%d" % NR, "BR0", "BR8", *D0K), tile("CA", 0, 10), A.mult)
-        offsets(t + 1)
-        tt(me(0, 4), IX(T.SC[:], T.BY[:], "SC%d" % ON, "SC%d" % NR, "BY", *D0K), tile("RES", 0, 4), A.add)
-        ts(me(4), me(3), -1.0, A.add, 0.0, A.max)
+        of = lambda q: R(T.OF[:, :, 8 * q:8 * q + 8], "OF%d" % q)
+        cp(of(0), sc(0))
+        pB = R(T.pK[:, 0:16], "pK")
+        sums_of(lambda q, n: pB, [(0, "ID", R(T.OD[:, LSU.index(LS[t + 1])], "OD%d" % LS[t + 1])), (0, "NID", me(N_)), (0, "NID", nok4)])
+        tt(w("bp"), pB, base(t + 1), A.max)
+        tt(of(1), sc(1), w("bp"), A.add)
+        tt(of(2), sc(2), base(t + 1), A.max)
+        if not first:
+            mm(pX, whole("ONEQ"), nok4, start=True)
+            mm(pX, whole("NONE"), z, stop=True)
+            fl = R(T.FL[:, 0:1], "FL")
+            act(w("junk"), pX, F.Identity, 1.0, 1100.0, accum=col(8))
+            aff(fl, col(8), 0.0625, -0.46875)
+            aff(col(9), fl, -16.0, col(8)[0], extra=["c8"])
+            aff(whole("AW"), R(T.XR[:, :32], "XR"), 0.0, col(9)[0], extra=["c9"])
+        terms = [(0, "ID", tile("CL", 0, 14)), (K_, "ID", tile("CH", K_)), (LK, "ID", tile("CH", LK, 9)), (K_, "ID", me(K_)), (RR, "NID", me(K_))]
+        terms += [(q, "IE", me(K_)) for q in (K2, K4)] + [(q, "N8", me(K_)) for q in (LK, LK + 1)]
+        terms += [(q, l, me(x)) for q, l in ((LK, "IL"), (LK + 1, "IL"), (RR, "I2")) for x in (K2, K4)]
+        terms += [(q, "NID", base(t + 1)) for q in (N_, M3, M2)]
+        if not first:
+            terms += [(q, l, r) for q in (X1, X2) for l, r in votes] + [(LK, "NID", me(X1, 2)), (LK, "ID", me(X2, 2))]
+            terms += [(X2 + p, "N8", me(RR)) for p in (0, 1)]
+        terms += [(N_, "NQ", nok4)]
+        if not first:
+            terms += [(q + p, l, r) for q, l in ((LK, "NID"), (X1, "ID"), (X2, "ID")) for p, r in grown]
+        terms += [(q, "IP", z) for q in (K_, LK, LK + 1, X1, X1 + 1, X2, X2 + 1, RR)] + [(q, "I13", z) for q in (K2, K4)]
+        terms += [(N_, "ID", sc(0)), (M1, "ID", sc(1)), (M3, "ID", sc(2)), (M2, "ID", sc(2))]
+        sums_of(pM, terms)
+        act(me(0, 14), pM(0, 14), F.Relu)
+        mark("state", t + 1)
+        choices(t + 1)
+
+    cp(me(N_), whole("ni"))
+    tt(sc(0), whole("ni"), base(0), A.add)
+    ts(me(K_), whole("ki"), -2.0, A.add)
+    ts(me(K2), whole("ki"), 0.125, A.mult, 384.5625, A.add)
+    ts(me(K4), whole("ki"), 0.125, A.mult, 769.0625, A.add)
+    ts(sc(3), whole("ki"), 2.0, A.is_ge)
+    pT = lambda q, n=1: R(T.pT[:, 16 * q:16 * q + 16 * n], "pT")
+    sums_of(pT, [(0, l, r) for l, r in floor_terms + [("IF", sc(3))]])
+    ts(m1x, pT(0), -147903.0, A.add)
+    ks = (me(K2), me(K4), sc(3))
+    sums_of(pT, [(0, "ID", me(N_)), (1, "ID", me(K_)), (1, "ID", ONES), (3, "ID", ONES)] + [(q, "N129", x) for q in (2, 3) for x in ks]
+            + [(3, "NID", x) for x in ks]
+            + [(q, l, r) for q in (2, 3) for l, r in (("NID", tile("CH", 14)), ("ID", tile("CL", 15 + q)), ("ID", m1x))])
+    ts(whole("MZ"), pT(0, 4), 0.0, A.max)
+    cp(sc(1), pT(2))
+    tt(w("m2"), pT(3), base(0), A.add)
+    ts(sc(2), w("m2"), -1.0, A.add)
+    post(-1)
 
     for t in range(RO):
-        S_, L, last = SL[t], LS[t], t == RO - 1
+        S_, L, last, nb = SL[t], LS[t], t == RO - 1, 10 + t
         vo = VOFF[L]
 
         runs = {"a": (0, CUT), "b": (CUT, 128), "c": (128, 256)}
@@ -582,99 +666,112 @@ def rank_program(g, core, T, topo):
             a, b = runs[xs[0]][0], runs[xs[-1]][1]
             c = 256 * (t % 2) + 16 * j
             (cp if e == "V" else scp)(R(T.V[:, vo + L * a + 1 + j:vo + L * b:L], *["V%d.%d.%s" % (L, j, x) for x in xs]),
-                                      IX(T.X[:, TB:TB + 4096], T.CT[:, c + a // 16:c + b // 16], "CT%d" % (t % 2), *XK))
+                                      IX(T.X[:, TB:TB + 4096], T.CT[:, c + a // 16:c + b // 16], "CT%d" % (t % 2) + ("" if t else "ab"[j >= FS]), *XK))
             mark("g" + e + xs, t)
 
         pn = lambda h, a=0, s=1: R(T.RP[:, h, RW + a:RW + 128:s], "Pn%d" % h)
 
         def folds(h):
             r0 = RW - 128 * L
-            for xs in ["c"] if h else ["a", "b"] if N2[t] else ["ab"]:
-                a, b = runs[xs[0]][0], runs[xs[-1]][1]
-                scan(R(T.RP[:, h, r0 + (a - 128 * h) * L:r0 + (b - 128 * h) * L], *["R" + x for x in xs]),
-                     R(T.V[:, vo + a * L:vo + b * L], "Vz%d" % L, *["V%d.%d.%s" % (L, j, x) for j in range(S_) for x in xs]),
-                     R(T.ZR[:, :(b - a) * L], "ZR"), A.add, A.max)
-                mark("scan" + xs, t)
-            rk = ["Rc"] if h else ["Ra", "Rb"]
-            src = IX(T.RP[:, h, r0:RW], T.OFN[:, 8 * h:8 * h + 8], "OFN", *rk)
+            for x, a in (("c", 128), ("c", 192)) if h else (("a", 0), ("b", 64)):
+                scan(R(T.RP[:, h, r0 + a % 128 * L:r0 + (a % 128 + 64) * L], "R%d" % a),
+                     R(T.V[:, vo + a * L:vo + (a + 64) * L], "Vz%d" % L, *["V%d.%d.%s" % (L, j, x) for j in range(S_)]),
+                     R(T.ZR[:, :64 * L], "ZR"), A.add, A.max)
+                mark("scan" + x, t)
+            rk = ["R%d" % (128 * h), "R%d" % (128 * h + 64)]
+            src = IX(T.RP[:, h, r0:RW], T.OF[:, h, 0:8], "OF0", *rk)
             if t > 0:
                 tt(pn(h), src, R(T.VN[:, 128 * h:128 * h + 128], "VN"), A.add)
             else:
                 cp(pn(h), src)
             mark("pick%d" % h, t)
             send(t, h, "n")
-            scp(R(T.RP[:, h, PA:PA + 256], "PA%d" % h), IX(T.RP[:, h, r0:RW + 128], T.OFU[:, h, :], "Pn%d" % h, "OFU", *rk))
+            scp(R(T.RP[:, h, PA:PA + 256], "PA%d" % h), IX(T.RP[:, h, r0:RW + 128], T.OF[:, h, 8:24], "Pn%d" % h, "OF1", "OF2", *rk))
             mark("points%d" % h, t)
             send(t, h, "v")
             aff(R(T.VT[:, 128 * h:128 * h + 128], "VT%d" % h), pn(h), 0.0625, 191.53125)
 
+        def weighted(bk, h):
+            pu = R(T[bk][:, 400:408 if HALF else 416], bk)
+            for a in range(16):
+                mm(pu, R(T.ZW[:, 15 - a:143 - a], "ZW"), pn(h, a, 16) if HALF else R(T.RP[:, :, RW + a:RW + 128:16], "Pn0", "Pn1"), a == 0, a == 15)
+            h = h if HALF else None
+            (aff if UY == "S" else cp)(wi("y", h), pu)
+            ts(wi("ul", h), wi("y", h), 15, A.bitwise_and)
+            tt(R(T.CS[:, 64 * h:64 * h + 64:8], "CS%d" % h) if HALF else R(T.CS[:, 0::8], "CS0", "CS1"), wi("ul", h), w("ci", h), A.add)
+
+        def appended():
+            ts(wi("u"), wi("y"), 4095, A.bitwise_and)
+            if USQ:
+                act(w("ua"), wi("u"), F.Square, 1.0, 592.0)
+                aff(wi("uw"), w("ua"), 1.0, 42752.0)
+            else:
+                ts(w("ua"), wi("u"), 4096.0, A.add)
+                ts(w("ub"), wi("u"), -2912.0, A.add)
+                tt(wi("uw"), w("ua"), w("ub"), A.mult)
+            ts(wi("new"), wi("uw"), 5, A.arith_shift_right, 4095, A.bitwise_and)
+            if UT == "S":
+                aff(tn(t, nb, nb + 1), wi("new"), 1.0, -2048.0)
+            else:
+                ts(tn(t, nb, nb + 1), wi("new"), -2048.0, A.add)
+
         def compare_lengths():
-            pl = lambda a, n=1: R(T.pV0[:, a:a + n, 0, :], "pV0")
-            mm(pl(0, 2), ID, me(0, 2), start=True)
-            for c, q in ((2, 4), (3, 4), (4, 2), (5, 2)):
-                mm(pl(c), ID, me(q))
-            for c in (2, 5):
-                mm(pl(c), ID, whole("ONES"))
-            for c, q in enumerate((0, 1, 3, 2, 2, 3)):
-                mm(pl(c), NID, R(T.QM[:, 2 * t:2 * t + 2, 8 + 16 * q:16 + 16 * q], "Q%dm" % t), stop=c == 5)
-            act(whole("DL"), pl(0, 6), F.Abs)
+            pl = lambda a, n=1: R(T.pN[:, 256 + 16 * a:256 + 16 * (a + n)], "pN")
+            terms = [(c, "ID", me(q)) for c, q in enumerate((M2, M2, M1, M1))] + [(c, "ID", ONES) for c in (0, 3)]
+            terms += [(c, "NID", R(T.QM[:, 2 * t:2 * t + 2, 8 + 16 * q:16 + 16 * q], "Q%dm" % t)) for c, q in enumerate((3, 2, 2, 3))]
+            sums_of(pl, terms)
+            act(whole("DL"), pl(0, 4), F.Abs)
             mark("lengths", t)
 
         def compare_n(h):
             qn = lambda a=0, s=1: R(T.Q[:, 2 * t + h, a:128:s], "Q%d%dn" % (t, h))
-            dn = lambda a, s, *xs: R(T.DN[:, h, a:128:s], *["DN%d.%d" % (h, x) for x in xs])
-            rows = lambda name, x: R(T[name][:, 15 - x:143 - x], name)
-            o = R(T.pS[:, 0:8], "pS") if h else R(T.pK[:, 0, 32:40], "pK")
-            mm(o, NID, R(T.TH[:, 8 * h:8 * h + 8], "TH"), start=True)
-            if VMAX[h]:
-                for x in range(16):
-                    mm(o, rows("NZ", x), pn(h, x, 16))
-            def lengths(stop):
-                for q in (0, 1):
-                    mm(o, IB, R(T.DL[:, 16 * q + 8 * h:16 * q + 8 * h + 8], "DL"), stop=stop and q == 1)
+            dn = lambda a=0, s=1: R(T.DN[:, h, a:128:s], "DN%d" % h)
+            bk, lim = ("pU", whole("IN")) if h else ("pK", whole("IP"))
+            o = lambda a=0, s=1: R(T[bk][:, 320 + a:384:s], bk)
+            own = R(T.pN[:, 0:128], "pN") if h else R(T.pV0[:, 0:8], "pV0")
 
-            if h == 0:
-                lengths(False)
-            if VMAX[h]:
-                for x in range(16):
-                    mm(o, rows("NZ", x), qn(x, 16))
-                    mark("diff%d" % h, t)
-                for x in (0, 1):
-                    tt(dn(x, 2, x), pn(h, x, 2), qn(x, 2), A.max)
-                    mark("max%d" % h, t)
-            else:
-                pn_ = R(T.pN[:, 0:128], "pN")
-                mm(pn_, ID, pn(h), start=True)
-                mm(pn_, NID, qn(), stop=True)
-                mark("diff%d" % h, t)
-                act(dn(0, 1, 0, 1), pn_, F.Abs)
-                mark("size%d" % h, t)
-            for x in list(range(0, 16, 2)) + list(range(1, 16, 2)):
-                mm(o, rows("Z2" if VMAX[h] else "Z", x), dn(x, 16, x % 2), stop=x == 15 and h == 0)
-                mark("sum%d" % h, t)
-            if h == 1:
-                lengths(True)
-            so = R(T.SOU[:, 8 * h:8 * h + 8], "SOU%d" % h)
-            ts(sc(D0, 14, h), o, col(9)[0], A.is_gt, 4096.0, A.mult, extra=["c9"])
+            def rows(name, src, stop=False):
+                for x in range(4):
+                    mm(o(1, 2), R(T[name][:, 3 - x:131 - x], name), src(x, 4), stop=stop and x == 3)
+
+            mm(own, ID, pn(h), True, True)
+            if HALF:
+                weighted("pN" if h else bk, h)
+                if h == 0:
+                    appended()
+            mm(o(), lim, R(T.THD[:, 64 * h:64 * h + 64], "THD%d" % h), start=True)
+            rows("BK", lambda a, s: pn(h, a, s))
+            mm(o(1, 2), lim, whole("AW"))
+            for x, (l, r) in enumerate((("P", "N"), ("N", "P"))):
+                for q, i in enumerate("JI"):
+                    mm(o(2 + 2 * x, 8), whole(i + l), R(T.M[:, 16 * q + 8 * h:16 * q + 8 * h + 8], "M.%d" % q))
+                    mm(o(2 + 2 * x, 8), whole(i + r), R(T.QM[:, 2 * t + h, 8 + 16 * q:16 + 16 * q], "Q%dm" % t))
+            rows("BK", qn)
+            tt(dn(), own, qn(), A.max if h else A.min)
+            mark("max%d" % h, t)
+            rows("BK2", dn, True)
+            mark("sum%d" % h, t)
+            scan(R(T.SO[:, 64 * h:64 * h + 64], "SO%d" % h), o(), R(T.CS[:, 64 * h:64 * h + 64], "CS%d" % h),
+                 *((A.max, A.min) if h else (A.min, A.max)))
             mark("ok%d" % h, t)
-            tt(so, w("colx", h=h), sc(D0, 14, h), A.subtract if h == 0 else A.add)
+            so, end = R(T.SOU[:, 8 * h:8 * h + 8], "SOU%d" % h), R(T.SO[:, 64 * h + 7:64 * h + 64:8], "SO%d" % h)
+            cp(so, end)
+            ts(R(T.NK[:, 8 * h:8 * h + 8], "NK%d" % h), end, *((float(SP), A.is_ge) if h else (float(TB), A.is_lt)), 4096.0, A.mult)
             if last and h == 0:
-                tt(IX(T.X[:, 0:6144], T.SOU[:, 4:8], "X.0", "X.0b"), R(T.VT[:, 64:128], "VT0", *so[1]), R(T.M192[:, :64], "M192"), A.add)
-                dma("Y", T.yx[:, 1024:2048], T.X[:, TB + 1024:TB + 2048], "st4", ["X.0b"], [], STORE + 250)
-                tt(IX(T.X[:, 0:5120], T.SOU[:, 0:4], "X.0"), R(T.VT[:, 0:64], "VT0", *so[1]), R(T.M192[:, :64], "M192"), A.add)
+                tt(IX(T.X[:, 0:TB + 2048], T.SOU[:, 4:8], "X.0", "X.0b"), R(T.VT[:, 64:128], "VT0", *so[1]), R(T.M192[:, :64], "M192"), A.add)
+                dma("Y", T.yx[:, 1024:2048], T.X[:, TB + 1024:TB + 2048], "st4", ["X.0b"], [], STORE + 400)
+                tt(IX(T.X[:, 0:TB + 1024], T.SOU[:, 0:4], "X.0"), R(T.VT[:, 0:64], "VT0", *so[1]), R(T.M192[:, :64], "M192"), A.add)
             else:
-                tt(IX(T.X[:, 6144 * h:6144 * h + 6144], so[0], XK[h], *["Xz"] * h),
+                tt(IX(T.X[:, TB + 2048:] if h else T.X[:, :TB + 2048], so[0], XK[h], *["Xz"] * h),
                    R(T.VT[:, 128 * h:128 * h + 128], "VT%d" % h, *so[1]), whole("M192"), A.add)
             mark("write%d" % h, t)
 
         def compare_v(h):
             bk = "pV%d" % h
             for x, a in enumerate((128, 128, 0, 0)):
-                mm(R(T[bk][:, :, x, :], bk), ID, R(T.RP[:, h, PA + a:PA + a + 128], "PA%d" % h), start=x == 0)
-                mark("own%d" % h, t)
+                mm(R(T[bk][:, x::4, :], bk), ID, R(T.RP[:, h, PA + a:PA + a + 128], "PA%d" % h), start=x == 0)
             for x, a in enumerate((256, 128, 128, 256)):
-                mm(R(T[bk][:, :, x, :], bk), NID, R(T.Q[:, 2 * t + h, a:a + 128], "Q%d%dv" % (t, h)), stop=x == 3)
-                mark("diffs%d" % h, t)
+                mm(R(T[bk][:, x::4, :], bk), NID, R(T.Q[:, 2 * t + h, a:a + 128], "Q%d%dv" % (t, h)), stop=x == 3)
             act(R(T.DV[:, 512 * h:512 * h + 512], "DV%d" % h), whole(bk), F.Abs)
             mark("sizes%d" % h, t)
 
@@ -689,87 +786,35 @@ def rank_program(g, core, T, topo):
                 gather("V" if j < NV[t] else "S", j, "abc")
             else:
                 gather("S", j, "c")
-                if j >= S_ - N2[t]:
-                    gather("S", j, "a")
-                    gather("S", j, "b")
-                else:
-                    gather("V" if j < NV[t] + NS[t] + NH[t] else "S", j, "ab")
+                for xs in ("a", "b") if j >= S_ - N2[t] else ("ab",):
+                    gather("S", j, xs)
         if not last:
-            seeds(t + 1, 10 + t)
-            aff(ct(t + 1, 10 + t), columns(tn(t, 0, 10 + t), 0, 10 + t, "a"))
+            seeds(t + 1, nb)
+            aff(ct(t + 1, nb), columns(tn(t, 0, nb), 0, nb, "a"))
         folds(1)
         folds(0)
-        for a in range(16):
-            mm(R(T.pU[:, 0:16], "pU"), R(T.ZW[:, 15 - a:143 - a], "ZW"), R(T.RP[:, :, RW + a:RW + 128:16], "Pn0", "Pn1"), a == 0, a == 15)
-        cp(wi("y"), R(T.pU[:, 0:16], "pU"))
-        ts(wi("u"), wi("y"), 4095, A.bitwise_and)
-        ts(wi("ul"), wi("y"), 15, A.bitwise_and)
-        tt(w("colx"), wi("ul"), w("ci"), A.add)
-        ts(w("ua"), wi("u"), 4096.0, A.add)
-        ts(w("ub"), wi("u"), -2912.0, A.add)
-        tt(wi("uw"), w("ua"), w("ub"), A.mult)
-        ts(wi("new"), wi("uw"), 5, A.arith_shift_right, 4095, A.bitwise_and)
-        ts(tn(t, 10 + t, 11 + t), wi("new"), -2048.0, A.add)
-        for x, (o, l, q) in enumerate(((0, ID, 0), (1, ID, 4), (0, NID, 4), (1, NID, 2))):
-            mm(R(T.pV1[:, 0, 0:2, o::2], "pV1"), l, me(q), x == 0, x == 3)
-        aff(R(T.D1[:, 0::8], D1K[0], D1K[8]), R(T.pV1[:, 0, 0:2, :], "pV1"))
-        aff(d1(13), tile("RES", 2), 1.0 / 4096)
-        aff(d1(14), me(0))
-        for x in (0, 1):
-            aff(R(T.NF2[:, x::2], "NF%d" % x), tile("RES", 7), 8.0)
-            tt(R(T.ND[:, x::2], "ND%d" % x), tile("RES", 6), R(T.VV[:, x::2], "VV"), A.subtract)
-        for x in (0, 1):
-            aff(R(T.LIM[:, x::2], "LIM%d" % x), R(T.ND[:], "ND0", "ND1"), -16384.0, col(9)[0], extra=["c9"])
-        if last:
-            aff(sc(D0, 15), me(1))
-            memset(R(T.D1R[:, 15::E], "D1R"), 1.0)
-        else:
-            ts(w("FF", 1, 0), tile("RES", 7), 0.0, A.is_equal, 1.0, A.add)
-            ts(w("FF", 1, 1), tile("RES", 7), 0.0, A.not_equal, 1.0, A.add)
-            aff(w("KI", 1, 0), tile("RES", 4), 1.0, 1.0)
-            aff(w("KI", 1, 1), tile("RES", 5), 0.5, 0.5)
-            tt(w("KK", 2), w("KI", 2), w("FF", 2), A.mult)
-            aff(tile("CA", 4, 2), w("KK", 2), 1.0, -1.0)
-            tt(w("x1"), me(0), w("KK", 1, 1), A.mult)
-            ts(wi("fl"), w("x1"), -0.4375, A.add)
-            tt(w("x3"), wi("fl"), w("KK", 1, 0), A.mult)
-            tt(tile("CA", 2), w("x3"), me(0), A.subtract)
-            aff(w("n1"), me(0), 1.0, -1.0)
-            tt(w("nK"), w("n1"), w("KK", 1, 0), A.add)
-            tt(tile("CA", 3), w("x3"), w("nK"), A.subtract)
-            aff(tile("CA", 1), me(1))
-            aff(w("kb", 1, 0), me(1), 8.0)
-            aff(w("kb", 1, 1), me(1))
-            aff(w("Ka", 1, 0), w("KK", 1, 0), 16.5, -17.0)
-            aff(w("Ka", 1, 1), w("KK", 1, 0), 2.0, -2.0)
-            tt(tile("CA", 6, 2), w("Ka", 2), w("kb", 2), A.subtract)
-            aff(tile("CA", 8), w("li"), (LS[t + 1] - 1) / 4096, -LS[t + 1] / 32)
-            aff(tile("CA", 9), me(0), 1.0 / 4096, 1.0 / 4096)
-        compare_lengths()
+        if not HALF:
+            weighted("pK", 0)
+            appended()
         compare_n(1)
+        compare_lengths()
         if last:
-            dma("Y", T.yx[:, 2048:4096], T.X[:, TB + 2048:TB + 4096], "st0", ["X.1"], [], STORE + 700)
+            dma("Y", T.yx[:, 2048:4096], T.X[:, TB + 2048:TB + 4096], "st0", ["X.1"], [], STORE + 800)
         compare_v(1)
         compare_n(0)
         if not last:
-            tt(whole("VOU"), columns(tn(t, 10 + t, 11 + t), 10 + t, 11 + t, "b"), nok4, A.max)
-        aff(d1(15), nok4, -1.0 / 4096, 1.0)
+            tt(whole("VOU"), columns(tn(t, nb, nb + 1), nb, nb + 1, "b"), nok4, A.max)
         compare_v(0)
-        mm(sums, NID, R(T.TH[:, 16:80], "TH0", "TH1", "TH2", "TH3"), start=True)
-        mark("votes", t)
+        mm(pS(0), NID, R(T.TH[:], "TH", "TH0", "TH1", "TH2", "TH3"), start=True)
         for x in range(4):
-            mm(R(T.pS[:, 16 + x:80:4], "pS"), IB, R(T.DL[:, 32 + 16 * x:48 + 16 * x], "DL"))
+            mm(pS(0, 1 + x, 2 + x), IB, R(T.DL[:, 16 * x:16 * x + 16], "DL"))
+        mm(pS(0, 5, 6), ID, nok4)
         for x in range(16):
-            mm(sums, R(T.Z[:, 15 - x:143 - x], "Z"), R(T.DV[:, x::16], "DV0", "DV1"), stop=x == 15)
+            mm(pS(0, 1, 5), R(T.Z[:, 15 - x:143 - x], "Z"), R(T.DV[:, x::16], "DV0", "DV1"), stop=x == 15)
 
-    dma("Y", T.yx[:, 0:1024], T.X[:, TB:TB + 1024], "st1", ["X.0"], [], STORE + 250)
+    dma("Y", T.yx[:, 0:1024], T.X[:, TB:TB + 1024], "st1", ["X.0"], [], STORE + 400)
     update(RO)
     post(RO - 1)
-    dma("S", T.yt[:], T.YT[:], "st3", ["YT"], [], STORE + 100)
-    ys = lambda q: R(T.YS[:, 16 * q:16 * q + 16], "YS%d" % q)
-    tt(ys(0), sc(ON, 14), d1(15), A.add)
-    cp(ys(1), sc(NR, 15))
-    tt(ys(2), sc(NR, 14), R(T.VC[:, 1::2], "VC"), A.mult)
-    tt(ys(3), sc(NR, 14), R(T.VC[:, 0::2], "VC"), A.mult)
-    dma("Y", T.yst[:], T.YS[:], "st2", ["YS0", "YS1", "YS2", "YS3"], [], STORE)
+    dma("S", T.yt[:], T.YT[:], "st3", ["YT"], [], STORE + 200)
+    dma("Y", T.yst[:], T.YS[:], "st2", ["YS.0", "YS.1", "YS.2", "YS.3"], [], STORE)
     emit()

from concourse.bass import DstId, RemoteDMATransfer
from concourse.mybir import AluOpType as A, ActivationFunctionType as F
import comms_topo

RO = 6
SL = [10, 10, 11, 12, 13, 14]
LS = [s + 1 for s in SL]
LSU = sorted(set(LS))
VOFF = {l: 256 * sum(LSU[:x]) for x, l in enumerate(LSU)}
RW = 1920
PA = RW + 128
TB = 128
SP = 2064
B = 16384.0
NV = [4, 4, 5, 5, 5, 6]
NS = [2, 2, 2, 3, 4, 4]
N2, CUT = [2] * 6, 64
UY, USQ, UT, UX, HALF = "V", 1, "V", "S", 1
ROWS = ["gSabc gSc new gSab gSa gSb", "pick1 scanab scana scanb", "write1 ok0", "points0 lengths", "sizes1 sizes0", "sendv0 lead", "led sendm"]
CYC, PCYC, GATHER, SCATTER, VMIN, SMIN, PFIX, BOTH = 0.84, 0.42, 1.44, 3.3, 36, 50, 7, 2.0
LAG = {"V": 205, "S": 180, "P": 220, "G": 200}
CROSS, WAKE, ISSUE, REMOTE, BYTE, FIRST, SMALL, LOAD = 50, 150, 250, 760, 0.004, 2000, 1200, 3000
STORE = 1200
RUN, FS = 8, 6
CASES = ((0.8, 0.7, 1.2, 0.9, 400, 500), (1.2, 1.3, 0.9, 1.15, -150, -200))
VD = ("I2080", "IF", "N129", "NID")
PASSES, WIDE, TRIES = 6, 8, 7000
PLAN, ORDER = [], []

f32, bf, f16, i32, u16 = "float32", "bfloat16", "float16", "int32", "uint16"
DIAG = {"NID": -1.0, "I2": 2.0, "I8": 8.0, "N8": -8.0, "IE": 0.125, "I13": 1.625, "IL": 16.5, "IF": 128.5, "N129": -129.0, "IB": 512.0,
        "I1184": 1184.0, "I2080": 2080.0, "NQ": -1.0 / 4096, "IP": B, "IN": -B, "JP": 16 * B, "JN": -16 * B}
SCRATCH = {
    "X": ("sbuf", [128, TB + 2048 + SP + 128], bf), "V": ("sbuf", [128, 256 * sum(LSU)], bf), "ZR": ("sbuf", [128, 960], bf),
    "RP": ("sbuf", [128, 2, RW + 384], bf), "Q": ("sbuf", [128, 2 * RO, 384], bf),
    "THD": ("sbuf", [128, 128], f16), "CS": ("sbuf", [128, 128], f32), "SO": ("sbuf", [128, 128], f32),
    "AW": ("sbuf", [128, 32], bf), "DG": ("sbuf", [128, 64], f32), "DH": ("sbuf", [128, 64], f32), "BS": ("sbuf", [128, 8], u16),
    "DN": ("sbuf", [128, 2, 128], bf), "DV": ("sbuf", [128, 1024], bf),
    "VN": ("sbuf", [128, 256], bf), "VT": ("sbuf", [128, 256], bf), "M192": ("sbuf", [128, 128], bf),
    "tri": ("sbuf", [128, 256], i32), "sdi": ("sbuf", [128, 96], i32), "ni": ("sbuf", [128, 16], i32),
    "ki": ("sbuf", [128, 16], i32), "thi": ("sbuf", [128, 16], i32), "wi": ("sbuf", [128, 4], i32), "wj": ("sbuf", [128, 4], i32),
    "TP": ("sbuf", [128, 256], f16), "TN": ("sbuf", [128, 2, 256], f16), "SR": ("sbuf", [128, RO, 64], f16),
    "JJ": ("sbuf", [128, 256], f32), "J1184": ("sbuf", [128, 256], f16), "C2080": ("sbuf", [128, 256], f16), "C2048": ("sbuf", [128, 256], f16),
    "MK": ("sbuf", [128, 256], f32), "WW": ("sbuf", [128, 256], f32), "Y0": ("sbuf", [128, 256], f32),
    "NI": ("sbuf", [128, 256], i32), "NJ": ("sbuf", [128, 256], i32),
    "CT": ("sbuf", [128, 512], u16), "OF": ("sbuf", [128, 2, 24], u16), "SOU": ("sbuf", [128, 16], u16), "VOU": ("sbuf", [128, 16], u16),
    "OB": ("sbuf", [128, len(LSU), 16], f16), "OD": ("sbuf", [128, len(LSU), 16], f16), "LI": ("sbuf", [128, 16], f32),
    "TH": ("sbuf", [128, 96], bf), "LIM": ("sbuf", [128, 96], f32), "D0": ("sbuf", [128, 96], bf), "DZ": ("sbuf", [128, 96], bf),
    "D1": ("sbuf", [128, 3, 96], f16), "SC": ("sbuf", [128, 4, 96], f16), "VC": ("sbuf", [128, 32], f32), "AH": ("sbuf", [128, 64], bf),
    "ONES": ("sbuf", [128, 16], bf), "JB": ("sbuf", [128, 256], bf), "SB": ("sbuf", [128, 16], bf), "NK": ("sbuf", [128, 16], bf),
    "M": ("sbuf", [128, 224], bf), "MZ": ("sbuf", [128, 64], bf), "MX": ("sbuf", [128, 16], bf), "QM": ("sbuf", [128, 2 * RO, 80], bf),
    "DL": ("sbuf", [128, 64], bf), "CH": ("sbuf", [128, 240], bf), "CL": ("sbuf", [128, 304], f16), "FL": ("sbuf", [128, 16], f16),
    "W": ("sbuf", [128, 16 * 16], f32), "WI": ("sbuf", [128, 16 * 16], i32),
    "PI": ("sbuf", [128, 16], i32), "PC": ("sbuf", [128, 16], f32), "XR": ("sbuf", [128, 144], f32),
    "Z": ("sbuf", [128, 144], bf), "ZW": ("sbuf", [128, 144], f16), "BK": ("sbuf", [128, 144], bf), "BK2": ("sbuf", [128, 144], bf),
    "ID": ("sbuf", [128, 128], bf), "ONEQ": ("sbuf", [128, 128], bf), "NONE": ("sbuf", [128, 128], bf),
    "YT": ("sbuf", [128, 256], f32), "YS": ("sbuf", [128, 64], f32),
    "pN": ("psum", [128, 512], f32), "pV0": ("psum", [128, 32, 16], f32), "pV1": ("psum", [128, 32, 16], f32),
    "pS": ("psum", [128, 85, 6], f32), "pU": ("psum", [128, 512], f32),
    "pT": ("psum", [128, 512], f32), "pY": ("psum", [128, 512], f32), "pK": ("psum", [128, 512], f32),
}
SCRATCH.update({name: ("sbuf", [128, 128], f16 if name == "IF" else bf) for name in DIAG})
SEMAPHORES = (["cV", "cS", "cP", "cG"] + ["ld%d" % i for i in range(8)] + ["st%d" % i for i in range(5)]
              + ["ml%d" % t for t in range(RO)] + ["ma%d" % t for t in range(RO)]
              + ["dl%d" % i for i in range(4 * RO)] + ["da%d" % i for i in range(4 * RO)])


def rank_program(g, core, T, topo):
    rank = T.rank_of(core)
    if rank is None:
        return
    Q = {"V": g.vector, "S": g.scalar, "P": g.tensor, "G": g, "Y": g.sync}
    CS = {"V": "cV", "S": "cS", "P": "cP", "G": "cG"}
    nodes, lastw, readers, chain, marks, fixed, kind = [], {}, {}, {}, {}, [0], []

    def op(e, fn, args, kw, rd, wr, cost, done=None, sem=None, inc=1, auto=False, row=None):
        deps = set()
        for k in rd:
            deps.add(lastw[k])
            if k[0] == "p":
                deps.update(x for x in readers.get(k, []) if nodes[x]["e"] != e)
        for k in wr:
            if k in lastw:
                deps.add(lastw[k])
            deps.update(readers.get(k, []))
        i = len(nodes)
        y = nodes[-1] if nodes else None
        if e == "P" and y["e"] == "P" and y["wr"] == wr and len(y["more"]) < RUN - 1 and all(d in y["deps"] or d == i - 1 or d < fixed[0] for d in deps):
            y["more"].append(args)
            y["deps"] = sorted(set(y["deps"]) | deps - {i - 1})
            y["cost"] = y["done"] = y["cost"] + cost
            for k in rd:
                readers.setdefault(k, []).append(i - 1)
            return
        nodes.append(dict(e=e, fn=fn, args=args, kw=kw, deps=sorted(deps), wr=wr, more=[], kind=kind.pop() if kind else e, cost=cost, done=cost if done is None else done,
                          sem=sem or CS.get(e), inc=inc, auto=auto, after=[chain[row]] if row in chain else []))
        if row:
            chain[row] = i
        for k in rd:
            readers.setdefault(k, []).append(i)
        for k in wr:
            lastw[k] = i
            readers[k] = []

    def mark(name, t):
        marks.setdefault((name, t), []).append(len(nodes) - 1)

    def order():
        for t in range(RO):
            for row in ROWS:
                row = [marks[x, t] for x in row.split() if (x, t) in marks]
                for a, b in zip(row, row[1:]):
                    for i in b:
                        nodes[i]["after"] += a
        n = len(nodes)
        cost = [x["cost"] for x in nodes]
        succ, back = [[] for _ in range(n)], [[] for _ in range(n)]
        for i, x in enumerate(nodes):
            pre = [(d, cost[d]) for d in x["after"]]
            for d in x["deps"]:
                y = nodes[d]
                if y["e"] == x["e"] == "P" or x["e"] == "A":
                    lag = 0
                elif y["done"] != y["cost"] or y["e"] == "A":
                    lag = WAKE
                else:
                    lag = LAG[y["e"]] + (0 if y["e"] == x["e"] else CROSS)
                pre.append((d, y["done"] + lag))
            for d, lag in pre:
                succ[d].append((i, lag))
                back[i].append((d, lag + cost[i] - cost[d]))
        left = [0.0] * n
        for _ in range(3):
            for i in range(n - 1, -1, -1):
                left[i] = max([nodes[i]["done"]] + [lag + left[j] for j, lag in succ[i]])

        def counts(nxt):
            todo = [0] * n
            for i in range(n):
                for j, _ in nxt[i]:
                    todo[j] += 1
            return todo

        def place(nxt, ready, left):
            ready, todo = list(ready), counts(nxt)
            pool = sorted((-left[i], i) for i in range(n) if not todo[i])
            busy = {e: [] for e in "VSPGYA"}
            start = [0.0] * n
            while pool:
                i = pool.pop(0)[1]
                b, s0 = busy[nodes[i]["e"]], ready[i]
                k = len(b)
                while k and b[k - 1][1] > s0:
                    k -= 1
                while k < len(b) and b[k][0] < s0 + cost[i]:
                    s0 = max(s0, b[k][1])
                    k += 1
                b.insert(k, (s0, s0 + cost[i]))
                start[i] = s0
                new = []
                for j, lag in nxt[i]:
                    ready[j] = max(ready[j], s0 + lag)
                    todo[j] -= 1
                    if not todo[j]:
                        new.append((-left[j], j))
                if new:
                    pool = sorted(pool + new)
            return start

        def follow(nxt, ready, left):
            ready, todo = list(ready), counts(nxt)
            pool = {e: [i for i in range(n) if nodes[i]["e"] == e and not todo[i]] for e in "VSPGYA"}
            free = {e: 0.0 for e in pool}
            start, pick = [0.0] * n, {}
            for _ in range(n):
                for e, c in pool.items():
                    if e not in pick and c:
                        c.sort(key=lambda i: -left[i])
                        top = c[:WIDE] + [min(c, key=lambda i: ready[i])]
                        pick[e] = min((max([max(free[e], ready[i]) + left[i]]
                                           + [max(max(free[e], ready[i]) + cost[i], ready[j]) + left[j] for j in top if j != i]),
                                       max(free[e], ready[i]), -left[i], i) for i in top)
                e = min(pick, key=lambda e: pick[e][1])
                _, s0, _, i = pick.pop(e)
                pool[e].remove(i)
                start[i], free[e] = s0, s0 + cost[i]
                for j, lag in nxt[i]:
                    ready[j] = max(ready[j], s0 + lag)
                    todo[j] -= 1
                    if not todo[j]:
                        pool[nodes[j]["e"]].append(j)
                        pick.pop(nodes[j]["e"], None)
            return start

        best = None
        tail = [nodes[i]["done"] - cost[i] for i in range(n)]
        for x in range(PASSES):
            way = follow if x % 2 else place
            start = way(succ, [0.0] * n, left)
            end = max(start[i] + nodes[i]["done"] for i in range(n))
            if best is None or end < best[0]:
                best = (end, start)
            late = way(back, tail, [best[1][i] + cost[i] for i in range(n)])
            left = [late[i] + cost[i] for i in range(n)]
        stones = [marks[x, t][-1] for t in range(RO) for x in ("write0", "pick0", "pick1", "write1")]
        cases = []
        for ga, sc_, pe, wait, far, load in CASES:
            c = [x["cost"] * {"g": ga, "s": sc_, "P": pe}.get(x["kind"], 1) for x in nodes]
            d = [c[i] + x["done"] - x["cost"] + (far if x["auto"] else load if x["done"] != x["cost"] else 0) for i, x in enumerate(nodes)]
            cases.append((c, d, [[(y, d[y] + (lag + cost[y] - cost[i] - nodes[y]["done"]) * wait) for y, lag in back[i] if y in x["deps"]]
                                 for i, x in enumerate(nodes)]))

        def worth(s):
            total = max(s[i] + nodes[i]["done"] for i in range(n)) + 0.1 * sum(s[i] for i in stones)
            seq = sorted(range(n), key=lambda i: (s[i], i))
            for c, d, pre in cases:
                free, at = dict.fromkeys("VSPGYA", 0.0), [0.0] * n
                for i in seq:
                    e = nodes[i]["e"]
                    y = free[e] if e != "A" else 0.0
                    for j, lag in pre[i]:
                        if at[j] + lag > y:
                            y = at[j] + lag
                    at[i], free[e] = y, y + c[i]
                total += max(at[i] + d[i] for i in range(n)) + 0.1 * sum(at[i] for i in stones)
            return total / (1 + len(cases))

        seed = [1]

        def draw():
            seed[0] = (seed[0] * 1103515245 + 12345) % 2147483648
            return seed[0] / 2147483648

        pick = lambda xs: xs[int(draw() * len(xs))]
        now = best = (worth(best[1]), best[1])
        for x in range(TRIES):
            mid, wide, step = draw() * end, pick((1000, 2500, 5000, 60000)), pick((100, 300, 800, 1500))
            queues, share = pick(("V", "S", "P", "VS", "VSP")), pick((0.05, 0.3))
            rank_ = [-s + (step * (2 * draw() - 1) if abs(s - mid) < wide and y["e"] in queues and draw() < share else 0)
                     for s, y in zip(now[1], nodes)]
            if x % 4 == 3:
                late = place(back, tail, [cost[i] - rank_[i] for i in range(n)])
                rank_ = [late[i] + cost[i] for i in range(n)]
            start = place(succ, [0.0] * n, rank_)
            value = worth(start)
            if value <= now[0] + 60 * (1 - x / TRIES):
                now = (value, start)
                best = min(best, now)
        PLAN.append(max(best[1][i] + nodes[i]["done"] for i in range(n)))
        return sorted(range(n), key=lambda i: (best[1][i], i))

    def emit():
        cnt = {}
        know = {e: {} for e in Q}
        snap = {}

        def need(e, s, c):
            if know[e].get(s, 0) >= c:
                return
            Q[e].wait_ge(T.sem[s], c)
            know[e][s] = c
            for s2, c2 in snap.get((s, c), {}).items():
                if know[e].get(s2, 0) < c2:
                    know[e][s2] = c2

        if not ORDER:
            ORDER.extend(order())
        for i in ORDER:
            x = nodes[i]
            e, s = x["e"], x["sem"]
            cnt[s] = cnt.get(s, 0) + x["inc"]
            x["tok"] = (s, cnt[s])
            if e == "A":
                continue
            best = {}
            for d in x["deps"]:
                s2, c2 = nodes[d]["tok"]
                if not (e == "P" and s2 == "cP"):
                    best[s2] = max(best.get(s2, 0), c2)
            for s2, c2 in best.items():
                need(e, s2, c2)
            ins = x["fn"](*x["args"], **x["kw"])
            for args in x["more"]:
                ins = x["fn"](*args)
            if not x["auto"]:
                ins.then_inc(T.sem[s], x["inc"])
            snap[x["tok"]] = dict(know[e])
        for s, c in cnt.items():
            need("G", s, c)

    def R(ap, *keys):
        n = 1
        for x in ap.shape[1:]:
            n *= x
        return (ap, list(keys), n, "16" in str(ap.dtype), False)

    def IX(win, offs, *keys):
        return (win.indirect(offs), list(keys), 16 * offs.shape[1], False, True)

    def span(e, o, ins, per=None):
        if o[4]:
            kind.append("s")
            return 50 + o[2] * SCATTER * CYC
        if any(a[4] for a in ins):
            kind.append("e" if per else "g")
            return (50 if e == "V" else 65) + o[2] * (BOTH if per else GATHER) * CYC
        if per is None:
            per = 0.5 if e == "V" and o[3] and all(a[3] for a in ins) else 1
        return max(VMIN if e == "V" else SMIN, o[2] * per) * CYC

    def tt(o, a, b, alu):
        per = 1 if a[1][0][0] == "p" or b[1][0][0] == "p" else 2
        op("V", g.vector.tensor_tensor, (o[0], a[0], b[0], alu), {}, a[1] + b[1], o[1], span("V", o, [a, b], per))

    def ts(o, a, s1, op0, s2=None, op1=None, extra=()):
        op("V", g.vector.tensor_scalar, (o[0], a[0], s1, s2, op0) + ((op1,) if op1 is not None else ()), {}, a[1] + list(extra), o[1], span("V", o, [a]))

    def cp(o, a):
        op("V", g.vector.tensor_copy, (o[0], a[0]), {}, a[1], o[1], span("V", o, [a]))

    def scan(o, a, b, op0, op1):
        op("V", g.vector.tensor_tensor_scan, (o[0], a[0], b[0], 0.0, op0, op1), {}, a[1] + b[1], o[1], span("V", o, [a, b]))

    def act(o, a, fn, scale=1.0, bias=0.0, extra=(), accum=None):
        kw = dict(bias=bias, scale=scale)
        if accum:
            kw["accum_out"] = accum[0]
        op("S", g.scalar.activation, (o[0], a[0], fn), kw, a[1] + list(extra), o[1] + (accum[1] if accum else []), span("S", o, [a]))

    def aff(o, a, scale=1.0, bias=0.0, extra=()):
        act(o, a, F.Identity, scale, bias, extra)

    def scp(o, a):
        op("S", g.scalar.activation, (o[0], a[0], F.Copy), {}, a[1], o[1], span("S", o, [a]))

    def memset(o, c):
        op("V", g.vector.memset, (o[0], c), {}, [], o[1], span("V", o, []))

    def iota(o, pat, base=0, cm=0, fl=True, row="iota"):
        op("G", g.iota, (o[0], pat, base, cm), dict(allow_small_or_imprecise_dtypes=True) if fl else {}, [], o[1], 130 + 2 * CYC * o[2], row=row)

    def dma(e, out, in_, sem, rd, wr, done):
        op(e, Q[e].dma_start, (out, in_), {}, rd, wr, 100, done, sem=sem, inc=16, row="dma" + e)

    def mm(o, l, r, start=False, stop=False):
        op("P", g.tensor.matmul, (o[0], l[0], r[0], start, stop), {}, l[1] + r[1], o[1], PFIX + max(16, r[2]) * PCYC)

    def whole(name):
        return R(T[name][:], name)

    Wn, WIn = {}, {}

    def w(name, h=None):
        c = Wn.setdefault(name, len(Wn))
        if h is not None:
            return R(T.W[:, 16 * c + 8 * h:16 * c + 8 * h + 8], "W.%d" % c)
        return R(T.W[:, 16 * c:16 * c + 16], "W.%d" % c)

    def wi(name, h=None):
        c = WIn.setdefault(name, len(WIn))
        if h is not None:
            return R(T.WI[:, 16 * c + 8 * h:16 * c + 8 * h + 8], "WI.%d.%d" % (c, h))
        return R(T.WI[:, 16 * c:16 * c + 16], "WI.%d.0" % c, "WI.%d.1" % c)

    w("col")

    def col(i):
        return R(T.W[:, i:i + 1], "c%d" % i)

    def tile(name, q, n=1):
        return R(T[name][:, 16 * q:16 * (q + n)], *["%s.%d" % (name, x) for x in range(q, q + n)])

    N_, K_, M1, M3, M2, LK, X1, X2, RR, K2, K4 = 0, 1, 2, 3, 4, 5, 7, 9, 11, 12, 13
    me = lambda q, n=1: tile("M", q, n)
    sc = lambda q: R(T.SC[:, q, 5::6], "SC%d" % q)
    nok4 = R(T.NK[:], "NK0", "NK1")
    part = [T.cores[rank ^ 1], T.cores[rank ^ 2]]
    XK = ["X.0", "X.1"]
    ID, NID, IB, ONES = whole("ID"), whole("NID"), whole("IB"), whole("ONES")

    def sums_of(at, terms, start=True, stop=True):
        for x, (q, l, r) in enumerate(terms):
            mm(at(q, r[2] // 16), whole(l), r, start and x == 0, stop and x == len(terms) - 1)

    def send(t, h, p):
        rid, pid, _ = topo.addr(part[h])
        ne = len(topo.engines(core, part[h]))
        i = 4 * t + (2 if p == "v" else 0) + h
        a, b = (0, 128) if p == "n" else (128, 384)
        op("G", g.remote_dma, (T.Q[:, 2 * t + h, a:b], T.RP[:, h, RW + a:RW + b], T.sem["da%d" % i], T.sem["dl%d" % i], pid, rid, topo.mask(core, part[h])), {},
           ["Pn%d" % h] if p == "n" else ["PA%d" % h], ["sent%d" % i], ISSUE, REMOTE + BYTE * 256 * (b - a), sem="dl%d" % i, inc=ne, auto=True)
        mark("send%s%d" % (p, h), t)
        op("A", None, (), {}, ["sent%d" % i], ["Q%d%d%s" % (t, h, p)], 0, sem="da%d" % i, inc=ne)

    def send_lengths(t):
        trs, tot = [], 0
        src = me(0, 4) if t else whole("MZ")
        for h in (0, 1):
            rid, pid, _ = topo.addr(part[h])
            en = topo.engines(core, part[h])
            en = en[:len(en) // 2] if h == 0 else en[len(en) // 2:]
            tot += len(en)
            trs.append(RemoteDMATransfer(dst_ids=[DstId(rid=rid, pnc=pid)], dma_engine_mask=sum(1 << x for x in en),
                                         remote_sem=T.sem["ma%d" % t], src=src[0], dst=T.QM[:, 2 * t + h, 8 - 8 * h:72 - 8 * h]))
        late = FIRST if t == 0 else 0
        op("G", g.remote_dma_fused, (trs,), dict(local_sem=T.sem["ml%d" % t]), src[1], ["sentm%d" % t], ISSUE + late,
           REMOTE + BYTE * 32768 + late, sem="ml%d" % t, inc=tot, auto=True)
        mark("sendm", t)
        op("A", None, (), {}, ["sentm%d" % t], ["Q%dm" % t], 0, sem="ma%d" % t, inc=tot)

    dma("S", T.sdi[:], T.sd[:], "ld2", [], ["sdi"], SMALL)
    dma("Y", T.tri[:], T.tr[:], "ld3", [], ["tri"], SMALL + 200)
    dma("S", T.ki[:], T.k0[:], "ld1", [], ["ki"], SMALL)
    dma("Y", T.ni[:], T.n0[:], "ld0", [], ["ni"], SMALL)
    dma("Y", T.X[:, TB:TB + 4096], T.xt[:], "ld4", [], XK, LOAD)
    dma("S", T.wi[:, 0:1], T.wt[:], "ld6", [], ["wi0"], LOAD + 200)
    dma("S", T.thi[:], T.th[:], "ld5", [], ["thi"], LOAD + 200)

    iota(whole("PI"), [[0, 16]], 0, 1, fl=False)
    iota(whole("XR"), [[1, 144]])
    iota(whole("JJ"), [[1, 16], [0, 16]])
    iota(whole("PC"), [[0, 2], [16, 8]])
    for q, n, c in ((14, 1, -147456.0), (K_, 1, -B), (LK, 2, -34816.0), (X1, 4, -B), (RR, 1, -18432.0), (K2, 1, 384.0), (K4, 1, 768.0)):
        memset(tile("CH", q, n), c)
    iota(whole("BK2"), [[16, 9], [0, 4], [-128, 4]], 15 + 3 * 128)
    iota(whole("DG"), [[1, 8], [4096, 8]])
    for l in LSU:
        lead = R(T.V[:, VOFF[l]:VOFF[l] + 256 * l:l], "Vz%d" % l)
        if l == LS[0]:
            memset(lead, -256.0)
        else:
            iota(lead, [[0, 256]], -256, row=None)
            mark("lead", LS.index(l) - 2)
            mark("led", LS.index(l) - 1)
    memset(whole("NONE"), -1.0)
    for name, c in (("C2080", 2080.0), ("ZR", 0.0), ("C2048", 2048.0), ("M192", -192.0), ("ONES", 1.0), ("ONEQ", 1.0 / 4096),
                    ("AW", 0.0), ("TH", 0.0), ("DZ", 0.0)):
        memset(whole(name), c)
    memset(nok4, 4096.0)
    memset(R(T.DZ[:, 0::6], "DZ"), 1.0)
    memset(R(T.X[:, TB + 4096:TB + 4112], "Xz"), 0.0)
    memset(col(9), 0.0)
    memset(tile("CL", 0, 14), 0.0)
    for q, n, c in ((0, 2, 1.0), (3, 1, 1.0), (LK, 2, -560.0), (RR, 1, -255.0), (K2, 1, -0.6875), (K4, 1, -0.1875), (14, 1, -318.5), (15, 1, 894.0),
                    (16, 1, 2045.0), (17, 1, 1023.0), (18, 1, 2174.0)):
        memset(tile("CL", q, n), c)
    PI1 = R(T.PI[:, 0:1], "PI")
    cp(col(0), PI1)
    ts(wi("a"), whole("PI"), 15, A.bitwise_and)
    one = lambda x: R(T.wj[:, x:x + 1], "wj%d" % x)
    ts(one(0), PI1, 112, A.bitwise_and)
    ts(ID, R(T.XR[:, :128], "XR"), col(0)[0], A.is_equal, extra=["c0"])
    for x, (name, c) in enumerate(DIAG.items()):
        if name in VD:
            ts(whole(name), ID, c, A.mult)
        else:
            aff(whole(name), ID, c)
    ts(col(1), one(0), 15.0, A.add)
    ts(whole("Z"), whole("XR"), col(1)[0], A.is_equal, extra=["c1"])
    ts(whole("BK"), whole("BK2"), col(1)[0], A.is_equal, -B, A.mult, extra=["c1"])
    ts(whole("BK2"), whole("BK"), -2.0, A.mult)
    a1 = R(T.WI[:, 0:1], "WI.0.0")
    tt(whole("LI"), whole("PC"), wi("a"), A.add)
    aff(whole("J1184"), whole("JJ"), 1184.0)
    aff(whole("JB"), whole("JJ"), -1.0)
    for x, l in enumerate(LSU):
        aff(R(T.OB[:, x], "OB%d" % l), whole("LI"), float(l))
        aff(R(T.OD[:, x], "OD%d" % l), whole("LI"), 1.0, 128.0 * l - 1)
    aff(w("ci", h=0), R(T.LI[:, 0:8], "LI"), 16.0, float(TB))
    aff(w("ci", h=1), R(T.LI[:, 0:8], "LI"), 16.0)
    ts(one(1), a1, 2, A.arith_shift_right)
    ts(one(2), a1, 3, A.arith_shift_right)
    ts(col(11), one(1), -8192.0, A.mult, -4096.0, A.add)
    ts(col(3), a1, 8.0, A.mult, 7.0, A.add)
    ts(col(4), a1, 8.0, A.mult, float(SP), A.add)
    cp(col(5), one(2))
    ts(whole("BS"), R(T.XR[:, :8], "XR"), 2.0, A.mult, col(5)[0], A.add, extra=["c5"])
    act(whole("DG"), whole("DG"), F.Abs, 1.0, col(11)[0], extra=["c11"])
    aff(whole("DH"), whole("DG"), 1.0, -8.0)
    aff(w("th"), whole("thi"), 1.0, 0.5)
    for h, s in ((0, -1.0), (1, 1.0)):
        cs = lambda a, step=1: R(T.CS[:, 64 * h + a:64 * h + 64:step], "CS%d" % h)
        aff(cs(0), whole("DG"), s, col(3 + h)[0], extra=["c%d" % (3 + h)])
        for x in (2, 4):
            aff(cs(x, 8), R(T.XR[:, :8], "XR"), s, col(3 + h)[0], extra=["c%d" % (3 + h)])
        tt(R(T.THD[:, 64 * h:64 * h + 64], "THD%d" % h), IX(w("th")[0], T.BS[:, 4 * h:4 * h + 4], "BS", *w("th")[1]), whole("DH"), A.max)
    memset(R(T.THD[:, 0::8], "THD0", "THD1"), -B)
    for x in (2, 4):
        memset(R(T.THD[:, x::8], "THD0", "THD1"), 0.5)
    WT = R(T.wi[:, 0:1], "wi0")
    ts(col(6), WT, 2048.0, A.is_ge, -4096.0, A.mult)
    tt(col(7), col(6), WT, A.add)
    aff(whole("ZW"), whole("Z"), col(7)[0], extra=["c7"])
    for q in range(4):
        aff(R(T.TH[:, 1 + q::6], "TH%d" % q), whole("thi"), extra=["TH"])
    fixed[0] = len(nodes)

    def tn(t, a, b):
        return R(T.TN[:, t % 2, 16 * a:16 * b], *(["TN%d" % (t % 2)] * (a < 10 + t) + ["NP%d" % (t % 2)] * (b > 10 + t)))

    def seeds(t, nb):
        n = 16 * nb
        e = n + 16 * (t > 0)
        mm(R(T.pY[:, :e], "pY"), ID, R(T.C2080[:, :e], "C2080"), start=True)
        mm(R(T.pY[:, 256:256 + n], "pY"), ID, R(T.J1184[:, :n], "J1184"))
        sr = lambda k: R(T.SR[:, t, :k], "SR0", "SR1", "SR2", "SR3")
        for c in range(0, e, 64):
            mm(R(T.pY[:, c:min(c + 64, e)], "pY"), ID, sr(min(64, e - c)))
        for c in range(0, n, 64):
            mm(R(T.pY[:, 256 + c:256 + min(c + 64, n)], "pY"), whole("I2080"), sr(min(64, n - c)), stop=t == 0 and c + 64 >= n)
        if t:
            mm(R(T.pY[:, 256 + n:272 + n], "pY"), whole("I2080"), sr(16))
            mm(R(T.pY[:, 256 + n:272 + n], "pY"), whole("I1184"), me(0), stop=True)

    def columns(src, a, b, key):
        part_ = lambda name: R(T[name][:, 16 * a:16 * b], name + key)
        tt(part_("Y0"), R(T.pY[:, 16 * a:16 * b], "pY"), src, A.mult)
        tt(part_("NI"), R(T.pY[:, 256 + 16 * a:256 + 16 * b], "pY"), part_("Y0"), A.add)
        ts(part_("NJ"), part_("NI"), 5, A.arith_shift_right, 4095, A.bitwise_and)
        return part_("NJ")

    ct = lambda t, nb: R(T.CT[:, 256 * (t % 2):256 * (t % 2) + 16 * nb], "CT%d" % (t % 2))

    def update(t):
        nb = 10 + t
        n = 16 * nb
        old, last, new = tn(t - 1, 0, nb - 1), R(T.TP[:, n - 16:n], "TP"), tn(t - 1, nb - 1, nb)
        for x, (o, l) in enumerate(((0, NID), (256, ID))):
            mm(R(T.pT[:, o:o + n - 16], "pT"), l, old, start=x == 0)
            mm(R(T.pT[:, o + n - 16:o + n], "pT"), l, last)
        if t == RO:
            mm(R(T.pT[:, 256:512], "pT"), ID, whole("C2048"))
        for j in range(nb):
            mm(R(T.pT[:, 16 * j:16 * j + 16], "pT"), ID, new, stop=j == nb - 1)
        bk = "pY" if t == RO else "pN"
        mm(R(T[bk][:, :n], bk), ID, R(T.JB[:, :n], "JB"), start=True)
        for x, r in enumerate((me(0), nok4)):
            for j in range(nb):
                mm(R(T[bk][:, 16 * j:16 * j + 16], bk), ID, r, stop=x == 1 and j == nb - 1)
        ts(R(T.MK[:, :n], "MK"), R(T[bk][:, :n], bk), 0.0, A.is_equal)
        tt(R(T.WW[:, :n], "WW"), R(T.pT[:, :n], "pT"), R(T.MK[:, :n], "MK"), A.mult)
        tt(whole("YT") if t == RO else tn(t, 0, nb), R(T.pT[:, 256:256 + n], "pT"), R(T.WW[:, :n], "WW"), A.add)

    for r in range(4):
        if r % 2:
            ts(R(T.SR[:, :, 16 * r:16 * r + 16], "SR%d" % r), whole("sdi"), -2048.0, A.add)
        else:
            aff(R(T.SR[:, :, 16 * r:16 * r + 16], "SR%d" % r), whole("sdi"), 1.0, -2048.0)
    aff(R(T.TP[:, 160:], "TP"), R(T.tri[:, 160:], "tri"), 1.0, -2048.0)
    aff(tn(0, 0, 10), R(T.tri[:, :160], "tri"), 1.0, -2048.0)
    seeds(0, 10)
    for a, b, key in ((0, FS, "a"), (FS, 10, "b")):
        cp(R(T.CT[:, 16 * a:16 * b], "CT0" + key), columns(tn(0, a, b), a, b, key))

    pS = lambda r, a=0, b=6: R(T.pS[:, r:r + 16, a:b], "pS")
    pX = R(T.pS[:, 80:84, 0:4], "pS")
    ah = lambda x: R(T.AH[:, x::4], "AH")
    m1x = whole("MX")
    floor_terms = [("ID", me(N_)), ("IF", me(K2)), ("IF", me(K4))]
    base = lambda t: R(T.OB[:, LSU.index(LS[t])], "OB%d" % LS[t])
    votes = [("ID", me(X1, 2)), ("NID", me(X2, 2))]
    grown = [(p, ah(x)) for p, xs in ((0, (2, 3)), (1, (0, 1))) for x in xs]

    def choices(t):
        last = t == RO - 1
        if not last:
            sums_of(lambda q, n: pX, [(0, l, r) for l, r in [("ID", tile("CL", 14)), ("ID", tile("CH", 14))] + floor_terms])
            (aff if UX == "S" else cp)(m1x, pX)
        at = lambda q, n=1: pS(16 + 16 * (q // 6), q % 6, q % 6 + 1)
        lim = [(q, l, r) for l in ("I8", "NID") for q in (1, 2, 3, 4) for r in [sc(3) if l == "I8" else me(LK + (q < 3))]]
        terms = [(6, "ID", me(N_)), (6, "NID", me(M2)), (8, "ID", me(M2)), (8, "NID", me(M1)), (10, "ID", me(M1)), (10, "NID", me(N_)), (11, "ID", me(N_))]
        if last:
            terms += [(12, "ID", me(K_)), (12, "ID", ONES), (17, "ID", ONES)]
        else:
            more = [(10, "NID", ONES), (6, "NID", tile("CH", 14)), (6, "N129", me(K2)), (6, "N129", me(K4))]
            terms += [(q + o, l, r) for o in (6, 12) for q, l, r in terms[1:] + more]
            terms += [(12, "ID", tile("CL", 15)), (17, "ID", ONES), (18, "ID", tile("CL", 16)), (18, "NID", me(K2)), (18, "NID", me(K4))]
            terms += [(q, "ID", base(t + 1)) for q in (11, 23)] + [(q, "ID", m1x) for q in (12, 18)]
        if t == 0 or last:
            mm(R(T.pS[:, 16:80], "pS"), ID, R(T.ZR[:, :384], "ZR"), True, True)
        sums_of(at, lim + terms)
        aff(R(T.D1[:, :3 - last], "D1"), R(T.pS[:, 32:80 - 16 * last], "pS"))
        mark("terms", t)
        aff(whole("LIM"), pS(16), B, col(9)[0], extra=["c9"])

    def post(t):
        first, last = t < 0, t == RO - 1
        z = sc(3)
        if not first:
            tt(whole("D0"), pS(0), whole("LIM"), A.is_gt)
            mark("cmp", t + 1)
            scan(R(T.SC[:, 3], "SC3"), whole("D0"), whole("DZ"), A.mult, A.add)
            for q in range(3 - last):
                scan(R(T.SC[:, q], "SC%d" % q), whole("D0"), R(T.D1[:, q], "D1"), A.mult, A.add)
            ts(whole("AH"), pS(0, 1, 5), col(9)[0], A.is_le, extra=["c9"])
        pM = lambda q, n=1: R(T.pU[:, 64 + 16 * q:64 + 16 * (q + n)], "pU")
        if last:
            ys = lambda q: tile("YS", q)
            ts(m1x, me(RR), 0.0, A.is_equal)
            sums_of(pM, [(0, l, r) for l, r in votes] + [(p, "N8", m1x) for p in (0, 1)] + [(p, "ID", r) for p, r in grown])
            ts(whole("VC"), pM(0, 2), 0.0, A.max)
            aff(w("ok"), nok4, -1.0 / 4096, 1.0)
            tt(ys(0), sc(0), w("ok"), A.add)
            cp(ys(1), sc(1))
            for p in (0, 1):
                tt(ys(2 + p), z, R(T.VC[:, 16 * p:16 * p + 16], "VC"), A.mult)
            return
        of = lambda q: R(T.OF[:, :, 8 * q:8 * q + 8], "OF%d" % q)
        cp(of(0), sc(0))
        pB = R(T.pK[:, 0:16], "pK")
        sums_of(lambda q, n: pB, [(0, "ID", R(T.OD[:, LSU.index(LS[t + 1])], "OD%d" % LS[t + 1])), (0, "NID", me(N_)), (0, "NID", nok4)])
        tt(w("bp"), pB, base(t + 1), A.max)
        tt(of(1), sc(1), w("bp"), A.add)
        tt(of(2), sc(2), base(t + 1), A.max)
        if not first:
            mm(pX, whole("ONEQ"), nok4, start=True)
            mm(pX, whole("NONE"), z, stop=True)
            fl = R(T.FL[:, 0:1], "FL")
            act(w("junk"), pX, F.Identity, 1.0, 1100.0, accum=col(8))
            aff(fl, col(8), 0.0625, -0.46875)
            aff(col(9), fl, -16.0, col(8)[0], extra=["c8"])
            aff(whole("AW"), R(T.XR[:, :32], "XR"), 0.0, col(9)[0], extra=["c9"])
        terms = [(0, "ID", tile("CL", 0, 14)), (K_, "ID", tile("CH", K_)), (LK, "ID", tile("CH", LK, 9)), (K_, "ID", me(K_)), (RR, "NID", me(K_))]
        terms += [(q, "IE", me(K_)) for q in (K2, K4)] + [(q, "N8", me(K_)) for q in (LK, LK + 1)]
        terms += [(q, l, me(x)) for q, l in ((LK, "IL"), (LK + 1, "IL"), (RR, "I2")) for x in (K2, K4)]
        terms += [(q, "NID", base(t + 1)) for q in (N_, M3, M2)]
        if not first:
            terms += [(q, l, r) for q in (X1, X2) for l, r in votes] + [(LK, "NID", me(X1, 2)), (LK, "ID", me(X2, 2))]
            terms += [(X2 + p, "N8", me(RR)) for p in (0, 1)]
        terms += [(N_, "NQ", nok4)]
        if not first:
            terms += [(q + p, l, r) for q, l in ((LK, "NID"), (X1, "ID"), (X2, "ID")) for p, r in grown]
        terms += [(q, "IP", z) for q in (K_, LK, LK + 1, X1, X1 + 1, X2, X2 + 1, RR)] + [(q, "I13", z) for q in (K2, K4)]
        terms += [(N_, "ID", sc(0)), (M1, "ID", sc(1)), (M3, "ID", sc(2)), (M2, "ID", sc(2))]
        sums_of(pM, terms)
        act(me(0, 14), pM(0, 14), F.Relu)
        mark("state", t + 1)
        choices(t + 1)

    cp(me(N_), whole("ni"))
    tt(sc(0), whole("ni"), base(0), A.add)
    ts(me(K_), whole("ki"), -2.0, A.add)
    ts(me(K2), whole("ki"), 0.125, A.mult, 384.5625, A.add)
    ts(me(K4), whole("ki"), 0.125, A.mult, 769.0625, A.add)
    ts(sc(3), whole("ki"), 2.0, A.is_ge)
    pT = lambda q, n=1: R(T.pT[:, 16 * q:16 * q + 16 * n], "pT")
    sums_of(pT, [(0, l, r) for l, r in floor_terms + [("IF", sc(3))]])
    ts(m1x, pT(0), -147903.0, A.add)
    ks = (me(K2), me(K4), sc(3))
    sums_of(pT, [(0, "ID", me(N_)), (1, "ID", me(K_)), (1, "ID", ONES), (3, "ID", ONES)] + [(q, "N129", x) for q in (2, 3) for x in ks]
            + [(3, "NID", x) for x in ks]
            + [(q, l, r) for q in (2, 3) for l, r in (("NID", tile("CH", 14)), ("ID", tile("CL", 15 + q)), ("ID", m1x))])
    ts(whole("MZ"), pT(0, 4), 0.0, A.max)
    cp(sc(1), pT(2))
    tt(w("m2"), pT(3), base(0), A.add)
    ts(sc(2), w("m2"), -1.0, A.add)
    post(-1)

    for t in range(RO):
        S_, L, last, nb = SL[t], LS[t], t == RO - 1, 10 + t
        vo = VOFF[L]

        runs = {"a": (0, CUT), "b": (CUT, 128), "c": (128, 256)}

        def gather(e, j, xs):
            a, b = runs[xs[0]][0], runs[xs[-1]][1]
            c = 256 * (t % 2) + 16 * j
            (cp if e == "V" else scp)(R(T.V[:, vo + L * a + 1 + j:vo + L * b:L], *["V%d.%d.%s" % (L, j, x) for x in xs]),
                                      IX(T.X[:, TB:TB + 4096], T.CT[:, c + a // 16:c + b // 16], "CT%d" % (t % 2) + ("" if t else "ab"[j >= FS]), *XK))
            mark("g" + e + xs, t)

        pn = lambda h, a=0, s=1: R(T.RP[:, h, RW + a:RW + 128:s], "Pn%d" % h)

        def folds(h):
            r0 = RW - 128 * L
            for x, a in (("c", 128), ("c", 192)) if h else (("a", 0), ("b", 64)):
                scan(R(T.RP[:, h, r0 + a % 128 * L:r0 + (a % 128 + 64) * L], "R%d" % a),
                     R(T.V[:, vo + a * L:vo + (a + 64) * L], "Vz%d" % L, *["V%d.%d.%s" % (L, j, x) for j in range(S_)]),
                     R(T.ZR[:, :64 * L], "ZR"), A.add, A.max)
                mark("scan" + x, t)
            rk = ["R%d" % (128 * h), "R%d" % (128 * h + 64)]
            src = IX(T.RP[:, h, r0:RW], T.OF[:, h, 0:8], "OF0", *rk)
            if t > 0:
                tt(pn(h), src, R(T.VN[:, 128 * h:128 * h + 128], "VN"), A.add)
            else:
                cp(pn(h), src)
            mark("pick%d" % h, t)
            send(t, h, "n")
            scp(R(T.RP[:, h, PA:PA + 256], "PA%d" % h), IX(T.RP[:, h, r0:RW + 128], T.OF[:, h, 8:24], "Pn%d" % h, "OF1", "OF2", *rk))
            mark("points%d" % h, t)
            send(t, h, "v")
            aff(R(T.VT[:, 128 * h:128 * h + 128], "VT%d" % h), pn(h), 0.0625, 191.53125)

        def weighted(bk, h):
            pu = R(T[bk][:, 400:408 if HALF else 416], bk)
            for a in range(16):
                mm(pu, R(T.ZW[:, 15 - a:143 - a], "ZW"), pn(h, a, 16) if HALF else R(T.RP[:, :, RW + a:RW + 128:16], "Pn0", "Pn1"), a == 0, a == 15)
            h = h if HALF else None
            (aff if UY == "S" else cp)(wi("y", h), pu)
            ts(wi("ul", h), wi("y", h), 15, A.bitwise_and)
            tt(R(T.CS[:, 64 * h:64 * h + 64:8], "CS%d" % h) if HALF else R(T.CS[:, 0::8], "CS0", "CS1"), wi("ul", h), w("ci", h), A.add)

        def appended():
            ts(wi("u"), wi("y"), 4095, A.bitwise_and)
            if USQ:
                act(w("ua"), wi("u"), F.Square, 1.0, 592.0)
                aff(wi("uw"), w("ua"), 1.0, 42752.0)
            else:
                ts(w("ua"), wi("u"), 4096.0, A.add)
                ts(w("ub"), wi("u"), -2912.0, A.add)
                tt(wi("uw"), w("ua"), w("ub"), A.mult)
            ts(wi("new"), wi("uw"), 5, A.arith_shift_right, 4095, A.bitwise_and)
            if UT == "S":
                aff(tn(t, nb, nb + 1), wi("new"), 1.0, -2048.0)
            else:
                ts(tn(t, nb, nb + 1), wi("new"), -2048.0, A.add)

        def compare_lengths():
            pl = lambda a, n=1: R(T.pN[:, 256 + 16 * a:256 + 16 * (a + n)], "pN")
            terms = [(c, "ID", me(q)) for c, q in enumerate((M2, M2, M1, M1))] + [(c, "ID", ONES) for c in (0, 3)]
            terms += [(c, "NID", R(T.QM[:, 2 * t:2 * t + 2, 8 + 16 * q:16 + 16 * q], "Q%dm" % t)) for c, q in enumerate((3, 2, 2, 3))]
            sums_of(pl, terms)
            act(whole("DL"), pl(0, 4), F.Abs)
            mark("lengths", t)

        def compare_n(h):
            qn = lambda a=0, s=1: R(T.Q[:, 2 * t + h, a:128:s], "Q%d%dn" % (t, h))
            dn = lambda a=0, s=1: R(T.DN[:, h, a:128:s], "DN%d" % h)
            bk, lim = ("pU", whole("IN")) if h else ("pK", whole("IP"))
            o = lambda a=0, s=1: R(T[bk][:, 320 + a:384:s], bk)
            own = R(T.pN[:, 0:128], "pN") if h else R(T.pV0[:, 0:8], "pV0")

            def rows(name, src, stop=False):
                for x in range(4):
                    mm(o(1, 2), R(T[name][:, 3 - x:131 - x], name), src(x, 4), stop=stop and x == 3)

            mm(own, ID, pn(h), True, True)
            if HALF:
                weighted("pN" if h else bk, h)
                if h == 0:
                    appended()
            mm(o(), lim, R(T.THD[:, 64 * h:64 * h + 64], "THD%d" % h), start=True)
            rows("BK", lambda a, s: pn(h, a, s))
            mm(o(1, 2), lim, whole("AW"))
            for x, (l, r) in enumerate((("P", "N"), ("N", "P"))):
                for q, i in enumerate("JI"):
                    mm(o(2 + 2 * x, 8), whole(i + l), R(T.M[:, 16 * q + 8 * h:16 * q + 8 * h + 8], "M.%d" % q))
                    mm(o(2 + 2 * x, 8), whole(i + r), R(T.QM[:, 2 * t + h, 8 + 16 * q:16 + 16 * q], "Q%dm" % t))
            rows("BK", qn)
            tt(dn(), own, qn(), A.max if h else A.min)
            mark("max%d" % h, t)
            rows("BK2", dn, True)
            mark("sum%d" % h, t)
            scan(R(T.SO[:, 64 * h:64 * h + 64], "SO%d" % h), o(), R(T.CS[:, 64 * h:64 * h + 64], "CS%d" % h),
                 *((A.max, A.min) if h else (A.min, A.max)))
            mark("ok%d" % h, t)
            so, end = R(T.SOU[:, 8 * h:8 * h + 8], "SOU%d" % h), R(T.SO[:, 64 * h + 7:64 * h + 64:8], "SO%d" % h)
            cp(so, end)
            ts(R(T.NK[:, 8 * h:8 * h + 8], "NK%d" % h), end, *((float(SP), A.is_ge) if h else (float(TB), A.is_lt)), 4096.0, A.mult)
            if last and h == 0:
                tt(IX(T.X[:, 0:TB + 2048], T.SOU[:, 4:8], "X.0", "X.0b"), R(T.VT[:, 64:128], "VT0", *so[1]), R(T.M192[:, :64], "M192"), A.add)
                dma("Y", T.yx[:, 1024:2048], T.X[:, TB + 1024:TB + 2048], "st4", ["X.0b"], [], STORE + 400)
                tt(IX(T.X[:, 0:TB + 1024], T.SOU[:, 0:4], "X.0"), R(T.VT[:, 0:64], "VT0", *so[1]), R(T.M192[:, :64], "M192"), A.add)
            else:
                tt(IX(T.X[:, TB + 2048:] if h else T.X[:, :TB + 2048], so[0], XK[h], *["Xz"] * h),
                   R(T.VT[:, 128 * h:128 * h + 128], "VT%d" % h, *so[1]), whole("M192"), A.add)
            mark("write%d" % h, t)

        def compare_v(h):
            bk = "pV%d" % h
            for x, a in enumerate((128, 128, 0, 0)):
                mm(R(T[bk][:, x::4, :], bk), ID, R(T.RP[:, h, PA + a:PA + a + 128], "PA%d" % h), start=x == 0)
            for x, a in enumerate((256, 128, 128, 256)):
                mm(R(T[bk][:, x::4, :], bk), NID, R(T.Q[:, 2 * t + h, a:a + 128], "Q%d%dv" % (t, h)), stop=x == 3)
            act(R(T.DV[:, 512 * h:512 * h + 512], "DV%d" % h), whole(bk), F.Abs)
            mark("sizes%d" % h, t)

        if t > 0:
            scp(whole("VN"), IX(T.X[:, TB:TB + 4112], T.VOU[:], "Xz", "VOU", *XK))
            mark("new", t)
            update(t)
            post(t - 1)
        send_lengths(t)
        for j in range(S_):
            if j < NV[t] + NS[t]:
                gather("V" if j < NV[t] else "S", j, "abc")
            else:
                gather("S", j, "c")
                for xs in ("a", "b") if j >= S_ - N2[t] else ("ab",):
                    gather("S", j, xs)
        if not last:
            seeds(t + 1, nb)
            aff(ct(t + 1, nb), columns(tn(t, 0, nb), 0, nb, "a"))
        folds(1)
        folds(0)
        if not HALF:
            weighted("pK", 0)
            appended()
        compare_n(1)
        compare_lengths()
        if last:
            dma("Y", T.yx[:, 2048:4096], T.X[:, TB + 2048:TB + 4096], "st0", ["X.1"], [], STORE + 800)
        compare_v(1)
        compare_n(0)
        if not last:
            tt(whole("VOU"), columns(tn(t, nb, nb + 1), nb, nb + 1, "b"), nok4, A.max)
        compare_v(0)
        mm(pS(0), NID, R(T.TH[:], "TH", "TH0", "TH1", "TH2", "TH3"), start=True)
        for x in range(4):
            mm(pS(0, 1 + x, 2 + x), IB, R(T.DL[:, 16 * x:16 * x + 16], "DL"))
        mm(pS(0, 5, 6), ID, nok4)
        for x in range(16):
            mm(pS(0, 1, 5), R(T.Z[:, 15 - x:143 - x], "Z"), R(T.DV[:, x::16], "DV0", "DV1"), stop=x == 15)

    dma("Y", T.yx[:, 0:1024], T.X[:, TB:TB + 1024], "st1", ["X.0"], [], STORE + 400)
    update(RO)
    post(RO - 1)
    dma("S", T.yt[:], T.YT[:], "st3", ["YT"], [], STORE + 200)
    dma("Y", T.yst[:], T.YS[:], "st2", ["YS.0", "YS.1", "YS.2", "YS.3"], [], STORE)
    emit()
